import numpy as np
import ml_dtypes


def mxq(x, axis, fmt="e4m3"):
    dtype, down = {"e4m3": (ml_dtypes.float8_e4m3fn, 7), "e5m2": (ml_dtypes.float8_e5m2, 14)}[fmt]
    v = np.moveaxis(np.asarray(x, np.float32).astype(ml_dtypes.bfloat16).astype(np.float64), axis, -1)
    blocks = v.reshape(v.shape[:-1] + (-1, 32))
    amax = np.abs(blocks).max(-1, keepdims=True)
    byte = np.maximum(np.where(amax > 0, np.frexp(amax)[1] - 1 + 127, 0) - down, 1)
    scale = np.exp2(byte - 127.0)
    codes = (blocks / scale).astype(np.float32).astype(dtype).astype(np.float64)
    return np.moveaxis((codes * scale).reshape(v.shape), -1, axis)


WIDE = False


def mx_kscale(k):
    if not WIDE:
        return np.ones(k)
    levels = np.array([10, -10, 5, -5, 0])
    if k % 512:
        return np.exp2(np.random.permutation(np.resize(levels, k // 32))).repeat(32)
    a = np.empty((k // 512, 16))
    for p in range(k // 512):
        a[p, :8] = np.random.permutation(np.resize(levels, 8))
        for g in range(8):
            far = levels[np.abs(levels - a[p, g]) >= 10]
            a[p, g + 8] = far[np.random.randint(len(far))]
    return np.exp2(a.ravel()).repeat(32)


BF16 = ml_dtypes.bfloat16


def bf(x):
    return np.asarray(x, np.float32).astype(BF16)


def f64(x):
    return np.asarray(x).astype(np.float64)


E2M1 = np.array([0.0, 0.5, 1.0, 1.5, 2.0, 3.0, 4.0, 6.0, -0.0, -0.5, -1.0, -1.5, -2.0, -3.0, -4.0, -6.0])


def pack_weight(w, fmt):
    k, n = w.shape
    w = f64(bf(w)).reshape(k // 32, 32, n)
    amax = np.abs(w).max(1)
    if fmt == "e4m3":
        byte = np.frexp(amax)[1] - 1 + 127 - 7
    else:
        mant, ex = np.frexp(amax / 6.0)
        byte = np.where(mant > 0.5, ex, ex - 1) + 127
    byte = np.clip(np.where(amax > 0, byte, 1), 1, 254)
    scaled = (w * np.exp2(127.0 - byte)[:, None, :]).reshape(k, n).astype(np.float32)
    by_word = np.ascontiguousarray(scaled.reshape(k // 512, 128, 4, n).transpose(0, 1, 3, 2))
    if fmt == "e4m3":
        words = by_word.astype(ml_dtypes.float8_e4m3fn).view(np.uint8)
    else:
        c = by_word.astype(ml_dtypes.float4_e2m1fn).view(np.uint8) & 0xF
        words = c[..., 0::2] | (c[..., 1::2] << 4)
    return np.ascontiguousarray(words), np.ascontiguousarray(byte.astype(np.uint8).reshape(k // 512, 16, n))


def unpack_weight(words, scales, fmt):
    g, p, n, _ = words.shape
    if fmt == "e4m3":
        vals = np.ascontiguousarray(words).view(ml_dtypes.float8_e4m3fn).astype(np.float64)
    else:
        nib = np.empty((g, p, n, 4), np.uint8)
        nib[..., 0::2] = words & 0xF
        nib[..., 1::2] = words >> 4
        vals = E2M1[nib]
    vals = vals * np.repeat(np.exp2(scales.astype(np.float64) - 127.0), 8, axis=1)[..., None]
    return vals.transpose(0, 1, 3, 2).reshape(g * 512, n)
def pack4(w):
    words, scales = pack_weight(w, "e2m1")
    return words.reshape(words.shape[0], 128, -1), scales


def unpack4(words, scales):
    return unpack_weight(words.reshape(words.shape[0], 128, -1, 2), scales, "e2m1")


T, IN, R, OUT = 1024, 2048, 512, 1536


def draw0():
    s = mx_kscale(R)
    t = mx_kscale(IN)
    x = np.random.standard_normal((T, IN)) / np.sqrt(IN)
    x_words, x_scales = pack4(x.T / t[:, None])
    a = np.random.standard_normal((IN, R)) / np.sqrt(R) * s * t[:, None]
    bmat = np.random.standard_normal((R, OUT)) / s[:, None]
    w0 = np.random.standard_normal((IN, OUT)) * t[:, None]
    return {"x_words": x_words,
            "x_scales": x_scales,
            "a": bf(a),
            "bmat": bf(bmat),
            "d_gain": bf(1 + 0.3 * np.random.standard_normal(R)),
            "b_gain": bf(1 + 0.3 * np.random.standard_normal(OUT)),
            "w0": bf(w0)}


def core(x_words, x_scales, a, bmat, d_gain, b_gain, w0):
    xt = unpack4(x_words, x_scales)
    ad = f64(a) * f64(d_gain)
    delta = mxq(ad, 1, "e4m3") @ mxq(f64(bmat), 0, "e4m3")
    wm = f64(w0) + delta * f64(b_gain)
    y = xt.T @ mxq(wm, 0, "e4m3")
    return y


def e4m3fn_bytes(y):
    return np.clip(np.asarray(y, np.float64), -448.0, 448.0).astype(np.float32).astype(ml_dtypes.float8_e4m3fn).view(np.uint8)


def e4m3fn_values(b):
    return np.asarray(b, np.uint8).view(ml_dtypes.float8_e4m3fn).astype(np.float64)


def setup_inputs():
    d = draw0()
    x0 = np.asarray(d['bmat']).astype(np.float64)
    s = (np.max(np.abs(x0), axis=(1,), keepdims=True) / 448.0).astype(np.float32)
    out = {}
    for k, v in d.items():
        if k == 'bmat':
            out['bmat_bytes'] = e4m3fn_bytes(x0 / s.astype(np.float64))
            out['bmat_scale'] = s
        else:
            out[k] = v
    return out


def reference(x_words, x_scales, a, bmat_bytes, bmat_scale, d_gain, b_gain, w0):
    return core(x_words, x_scales, a, e4m3fn_values(bmat_bytes) * bmat_scale.astype(np.float64), d_gain, b_gain, w0)

@@ -1,0 +1,388 @@
+from contextlib import ExitStack
+
+import concourse.mybir as mybir
+from concourse.masks import make_identity
+
+F32 = mybir.dt.float32
+BF16 = mybir.dt.bfloat16
+I32 = mybir.dt.int32
+U32 = mybir.dt.uint32
+U8 = mybir.dt.uint8
+E4M3 = mybir.dt.float8_e4m3fn
+E4M3X4 = mybir.dt.float8_e4m3fn_x4
+E2M1X4 = mybir.dt.float4_e2m1fn_x4
+MULT = mybir.AluOpType.mult
+ADD = mybir.AluOpType.add
+COPY = mybir.ActivationFunctionType.Copy
+
+T, IN, R, OUT = 1024, 2048, 512, 1536
+P = 128
+PACK = 4
+GROUPS = IN // (P * PACK)
+CHUNK = 512
+CHUNKS = OUT // CHUNK
+HALF = 256
+BLOCKS = OUT // P
+T_TILES = T // P
+
+FLOPS = 2 * IN * R * OUT + 2 * T * IN * OUT
+
+PANELS = [[0, 1], [2, 3], [4, 5, 6, 7], [8, 9], [10], [11]]
+PATTERNS = ["TTTT","TTTP","TTTP","PPTP","TTTP","TTTT","PPPP","TTPP","PPPP","PPTP","PPPP","PPPP"]
+BPREP = {0: 1, 1: 2, 2: 3, 4: 4, 6: 5}
+DP, DT, TB, YB = 2, 2, 1, 3
+HP = 64
+
+
+def tile_vera_merged_layer_s13_kernel(tc, x_words, x_scales, a, bmat_bytes, bmat_scale, d_gain, b_gain, w0, out):
+    nc = tc.nc
+    with ExitStack() as ctx:
+        keep = ctx.enter_context(tc.tile_pool(name="keep", bufs=1))
+        work = ctx.enter_context(tc.tile_pool(name="work", bufs=2))
+        psum = ctx.enter_context(tc.psum_pool(name="psum", bufs=2))
+
+        b_row = keep.tile([P, OUT], BF16, name="b_row")
+        ones = keep.tile([P, P], BF16, name="ones")
+        warm = keep.tile([P, 8], F32, name="warm")
+        ident = keep.tile([P, P], F32, name="ident")
+        b_sc = keep.tile([P, PACK], F32, name="b_sc")
+        b_raw = keep.tile([P, PACK, OUT], U8, name="b_raw", align_bytes=64)
+        b_wide = keep.tile([P, PACK, OUT], BF16, name="b_wide", align_bytes=64)
+        b_grp = keep.tile([P, OUT, PACK], BF16, name="b_grp", align_bytes=64)
+        b_cod = keep.tile([P, OUT], U32, name="b_cod", align_bytes=64)
+        b_pla = keep.tile([P, OUT], U8, name="b_pla", align_bytes=64)
+        a_raw = keep.tile([P, GROUPS, PACK, R], BF16, name="a_raw", align_bytes=64)
+        a_cod = keep.tile([P, GROUPS, P * PACK], U32, name="a_cod", align_bytes=64)
+        a_pla = keep.tile([P, GROUPS, P * PACK], U8, name="a_pla", align_bytes=64)
+        w_raw = keep.tile([P, GROUPS, PACK, OUT], BF16, name="w_raw", align_bytes=64)
+        w_cod = keep.tile([P, GROUPS * OUT], U32, name="w_cod", align_bytes=64)
+        w_pla = keep.tile([P, GROUPS * OUT], U8, name="w_pla", align_bytes=64)
+        x_cod = keep.tile([P, GROUPS, 2 * T], U8, name="x_cod", align_bytes=64)
+        x_pla = keep.tile([P, GROUPS, T], U8, name="x_pla", align_bytes=64)
+        d_col = keep.tile([P, PACK], BF16, name="d_col")
+        bg = keep.tile([P, OUT], F32, name="bg")
+        b_col = keep.tile([P, BLOCKS], F32, name="b_col")
+
+        a_view = a.rearrange("(g p t) r -> g p t r", p=P, t=PACK)
+        w_view = w0.rearrange("(g p t) o -> g p t o", p=P, t=PACK)
+        b_view = bmat_bytes.rearrange("(p t) o -> p t o", t=PACK)
+
+        nc.scalar.dma_start(out=d_col[:], in_=d_gain.rearrange("(p t) -> p t", t=PACK))
+        nc.vector.memset(warm[:], 0.0)
+        nc.scalar.activation(out=warm[:, 0:4], in_=warm[:, 4:8], func=COPY)
+        nc.vector.memset(ones[:], 1.0)
+        nc.gpsimd.memset(b_row[:], 0.0)
+        make_identity(nc, ident[:])
+        nc.gpsimd.memset(x_pla[:].rearrange("p g n -> p (g n)").bitcast(U32), 0)
+
+        nc.sync.dma_start(out=b_sc[:], in_=bmat_scale.rearrange("(p t) o -> p (t o)", t=PACK))
+        nc.sync.dma_start(out=b_raw[:, :, 0:CHUNK], in_=b_view[:, :, 0:CHUNK])
+        for h in range(2):
+            nc.sync.dma_start(out=a_raw[:, 0, 2 * h : 2 * h + 2, :], in_=a_view[0][:, 2 * h : 2 * h + 2, :])
+
+        def load_a(g):
+            nc.sync.dma_start(out=a_raw[:, g, :, :], in_=a_view[g])
+
+        def load_w(c, g):
+            cols = slice(c * CHUNK, (c + 1) * CHUNK)
+            nc.sync.dma_start(out=w_raw[:, g, :, cols], in_=w_view[g][:, :, cols])
+
+        nc.sync.dma_start(out=b_row[0:1, :], in_=b_gain.rearrange("(o r) -> o r", o=1))
+        load_a(1)
+        load_w(0, 0)
+        load_a(2)
+        load_w(0, 1)
+        load_a(3)
+        load_w(0, 2)
+        load_w(0, 3)
+        nc.sync.dma_start(out=b_raw[:, :, CHUNK:OUT], in_=b_view[:, :, CHUNK:OUT])
+        for g in range(GROUPS):
+            load_w(1, g)
+        nc.sync.dma_start(out=x_cod[:].bitcast(I32), in_=x_words.bitcast(I32).rearrange("g p n -> p g n"))
+        for q in range(4):
+            nc.sync.dma_start(
+                out=x_pla[32 * q : 32 * q + 4, :, :].bitcast(I32),
+                in_=x_scales[:, 4 * q : 4 * q + 4, :].bitcast(I32).rearrange("g q n -> q g n"),
+            )
+        for g in range(GROUPS):
+            load_w(2, g)
+
+        ad_tiles = {}
+        grp_tiles = {}
+
+        def ad_turn(g, h):
+            if h == 0:
+                grp_tiles[g] = work.tile([P, P * PACK, PACK], BF16, name="ad_grp", tag="ad_grp", align_bytes=64)
+            bank = psum.tile([P, 2, HALF], F32, name="bank_a", tag="y", bufs=YB)
+            ad_tiles[(g, h)] = bank
+            if g >= 1:
+                turned_words = work.tile([P, 2, 2, P], F32, name="a_words", tag="a_words")
+                nc.scalar.copy(
+                    out=turned_words[:],
+                    in_=a_raw[:, g, 2 * h : 2 * h + 2, :].bitcast(F32).rearrange("p i (m u) -> p i u m", u=2),
+                )
+            for i in range(2):
+                words = a_raw[:, g, 2 * h + i, :].bitcast(F32)
+                for u in range(2):
+                    in_words = turned_words[:, i, u, :] if g >= 1 else words[:, u::2]
+                    nc.tensor.transpose(bank[:, u, i * P : (i + 1) * P], in_words, ident[:])
+
+        def ad_product(g, h):
+            nc.vector.tensor_tensor(
+                out=grp_tiles[g][:, h * HALF : (h + 1) * HALF, :].rearrange("p n (u e) -> p n u e", u=2),
+                in0=ad_tiles[(g, h)][:].bitcast(BF16).rearrange("p u (n e) -> p n u e", e=2),
+                in1=d_col[:].rearrange("p (u e) -> p u e", u=2).unsqueeze(1).to_broadcast([P, HALF, 2, 2]),
+                op=MULT,
+            )
+
+        def ad_quantise(g):
+            nc.vector.quantize_mx(
+                out=a_cod[:, g, :].bitcast(E4M3X4), scales=a_pla[:, g, :], in_=grp_tiles[g][:].rearrange("p n t -> p (n t)")
+            )
+
+        def b_widen(k):
+            cols = slice(k * HALF, (k + 1) * HALF)
+            for t in range(PACK):
+                nc.scalar.activation(out=b_wide[:, t, cols], in_=b_raw[:, t, cols].bitcast(E4M3), func=COPY, scale=b_sc[:, t : t + 1])
+
+        def b_interleave(k, copy):
+            cols = slice(k * HALF, (k + 1) * HALF)
+            copy(out=b_grp[:, cols, :], in_=b_wide[:, :, cols].rearrange("p t c -> p c t"))
+
+        def b_quantise(k):
+            cols = slice(k * HALF, (k + 1) * HALF)
+            nc.vector.quantize_mx(
+                out=b_cod[:, cols].bitcast(E4M3X4), scales=b_pla[:, cols], in_=b_grp[:, cols, :].rearrange("p c t -> p (c t)")
+            )
+
+        periods = []
+        last_period = {}
+        bases = {}
+        base = 0
+        for pi, panel in enumerate(PANELS):
+            bases[pi] = base
+            order = [(g, ob) for g in range(GROUPS) for ob in panel]
+            for i in range(0, len(order), 4):
+                periods.append((order[i : i + 4], base + i * P, PATTERNS[len(periods)]))
+            last_period[len(periods) - 1] = pi
+            base += GROUPS * len(panel) * P
+        banks, scaled, turned, prods, wm = {}, {}, {}, {}, {}
+
+        def first_product(k, u):
+            (g, ob), kind = periods[k][0][u], periods[k][2][u]
+            cols = slice(ob * P, (ob + 1) * P)
+            bank = psum.tile([P, PACK, P], F32, name="bank_d", tag="dt" if kind == "T" else "dp", bufs=DT if kind == "T" else DP)
+            banks[(k, u)] = bank
+            if kind == "T":
+                nc.tensor.matmul_mx(
+                    out=bank[:].rearrange("p t o -> p (t o)"),
+                    lhsT=b_cod[:, cols].bitcast(E4M3X4),
+                    lhsT_scale=b_pla[:, cols],
+                    rhs=a_cod[:, g, :].bitcast(E4M3X4),
+                    rhs_scale=a_pla[:, g, :],
+                    start=True,
+                    stop=True,
+                )
+                tile = work.tile([P, PACK, P], F32, name="scaled", tag="scaled", bufs=6)
+                scaled[(k, u)] = tile
+                nc.scalar.activation(out=tile[:], in_=bank[:], func=COPY, scale=b_col[:, ob : ob + 1])
+            else:
+                for t in range(PACK):
+                    nc.tensor.matmul_mx(
+                        out=bank[:, t, :],
+                        lhsT=a_cod[:, g, t * P : (t + 1) * P].bitcast(E4M3X4),
+                        lhsT_scale=a_pla[:, g, t * P : (t + 1) * P],
+                        rhs=b_cod[:, cols].bitcast(E4M3X4),
+                        rhs_scale=b_pla[:, cols],
+                        start=True,
+                        stop=True,
+                    )
+
+        def turn_back(k, u):
+            if periods[k][2][u] == "T":
+                bank = psum.tile([P, PACK, P], F32, name="bank_t", tag="t", bufs=TB)
+                turned[(k, u)] = bank
+                for t in range(PACK):
+                    nc.tensor.transpose(bank[:, t, :], scaled[(k, u)][:, t, :], ident[:])
+
+        def scale_plain(k, u):
+            g, ob = periods[k][0][u]
+            nc.vector.tensor_tensor(
+                out=prods[k][:, u * P : (u + 1) * P, :],
+                in0=banks[(k, u)][:].rearrange("p t o -> p o t"),
+                in1=bg[:, ob * P : (ob + 1) * P].unsqueeze(2).to_broadcast([P, P, PACK]),
+                op=MULT,
+            )
+
+        def add_turned(k, u):
+            g, ob = periods[k][0][u]
+            nc.vector.tensor_tensor(
+                out=wm[k][:, u * P : (u + 1) * P, :],
+                in0=turned[(k, u)][:].rearrange("p t o -> p o t"),
+                in1=w_raw[:, g, :, ob * P : (ob + 1) * P].rearrange("p t o -> p o t"),
+                op=ADD,
+            )
+
+        def add_plain(engine, k, lo, hi):
+            g, ob = periods[k][0][lo // P]
+            o0 = ob * P + lo % P
+            engine.tensor_tensor(
+                out=wm[k][:, lo:hi, :],
+                in0=prods[k][:, lo:hi, :],
+                in1=w_raw[:, g, :, o0 : o0 + hi - lo].rearrange("p t o -> p o t"),
+                op=ADD,
+            )
+
+        def plain_runs(k):
+            units, at, pattern = periods[k]
+            runs = []
+            for u in range(4):
+                if pattern[u] not in "Pg":
+                    continue
+                lo = u * P + (HP if pattern[u] == "g" else 0)
+                hi = (u + 1) * P
+                if runs and runs[-1][1] == lo and units[u][0] == units[u - 1][0]:
+                    runs[-1][1] = hi
+                else:
+                    runs.append([lo, hi])
+            return runs
+
+        def wm_quantise(k, lo=0, hi=4 * P):
+            at = periods[k][1]
+            nc.vector.quantize_mx(
+                out=w_cod[:, at + lo : at + hi].bitcast(E4M3X4),
+                scales=w_pla[:, at + lo : at + hi],
+                in_=wm[k][:, lo:hi, :].rearrange("p o t -> p (o t)"),
+            )
+
+        y_banks = {}
+
+        def y_product(pi, j):
+            width = len(PANELS[pi]) * P
+            n = min(width, CHUNK) if width == CHUNK else P
+            tiles = CHUNK // width
+            bank = psum.tile([P, tiles, width], F32, name="bank_y", tag="y", bufs=YB)
+            y_banks[(pi, j)] = bank
+            for i in range(tiles):
+                tt = j * tiles + i
+                for o in range(0, width, n):
+                    for g in range(GROUPS):
+                        at = bases[pi] + g * width + o
+                        nc.tensor.matmul_mx(
+                            out=bank[:, i, o : o + n],
+                            lhsT=x_cod[:, g, tt * 2 * P : (tt + 1) * 2 * P].bitcast(E2M1X4),
+                            lhsT_scale=x_pla[:, g, tt * P : (tt + 1) * P],
+                            rhs=w_cod[:, at : at + n].bitcast(E4M3X4),
+                            rhs_scale=w_pla[:, at : at + n],
+                            start=g == 0,
+                            stop=g == GROUPS - 1,
+                        )
+
+        out_view = out.rearrange("(m p) o -> p m o", p=P)
+
+        def y_store(pi, j, engine=None):
+            width = len(PANELS[pi]) * P
+            tiles = CHUNK // width
+            o0 = PANELS[pi][0] * P
+            res = work.tile([P, tiles, width], F32, name="res", tag="res", bufs=6)
+            if engine is None:
+                nc.scalar.copy(out=res[:], in_=y_banks[(pi, j)][:])
+            else:
+                engine(out=res[:], in_=y_banks[(pi, j)][:])
+            nc.sync.dma_start(out=out_view[:, j * tiles : (j + 1) * tiles, o0 : o0 + width], in_=res[:])
+
+        for i in range(0):
+            bank = psum.tile([P, R], F32, name="bank_w", tag="y", bufs=YB)
+            nc.tensor.matmul(bank[:], lhsT=ones[:], rhs=b_row[:, 0:R], start=True, stop=True)
+        b_widen(0)
+        ad_turn(0, 0)
+        ad_turn(0, 1)
+        ad_product(0, 0)
+        ad_product(0, 1)
+        b_interleave(0, nc.scalar.copy)
+        ad_quantise(0)
+        b_quantise(0)
+        ad_turn(1, 0)
+        ad_turn(1, 1)
+        bank = psum.tile([P, BLOCKS], F32, name="bank_c", tag="t", bufs=TB)
+        for ob in range(BLOCKS):
+            nc.tensor.matmul(bank[:, ob : ob + 1], lhsT=b_row[:, ob * P : (ob + 1) * P], rhs=ones[:, 0:1], start=True, stop=True)
+        nc.scalar.copy(out=b_col[:], in_=bank[:])
+        ad_product(1, 0)
+        ad_product(1, 1)
+        for u in range(2):
+            first_product(0, u)
+        for u in range(2):
+            turn_back(0, u)
+        ad_quantise(1)
+        ad_turn(2, 0)
+        ad_turn(2, 1)
+        ad_product(2, 0)
+        ad_product(2, 1)
+        for u in range(2, 4):
+            first_product(0, u)
+        for u in range(2, 4):
+            turn_back(0, u)
+        ad_turn(3, 0)
+        ad_turn(3, 1)
+        ad_quantise(2)
+        ad_product(3, 0)
+        ad_product(3, 1)
+        for j in range(3):
+            bank = psum.tile([P, CHUNK], F32, name="bank_b", tag="y", bufs=YB)
+            nc.tensor.matmul(bank[:], lhsT=ones[:], rhs=b_row[:, j * CHUNK : (j + 1) * CHUNK], start=True, stop=True)
+            nc.scalar.copy(out=bg[:, j * CHUNK : (j + 1) * CHUNK], in_=bank[:])
+
+        n = len(periods)
+        todo = []
+        open_item = None
+        for k in range(n + 1):
+            if k < n:
+                units, at, pattern = periods[k]
+                prods[k] = work.tile([P, 4 * P, PACK], F32, name="prod", tag="prod", bufs=2)
+                wm[k] = work.tile([P, 4 * P, PACK], BF16, name="wm", tag="wm", bufs=3, align_bytes=64)
+                for kind in "GgP":
+                    for u in range(4):
+                        if pattern[u] == kind:
+                            scale_plain(k, u)
+                for u in range(4):
+                    if pattern[u] == "G":
+                        add_plain(nc.gpsimd, k, u * P, (u + 1) * P)
+                    if pattern[u] == "g":
+                        add_plain(nc.gpsimd, k, u * P, u * P + HP)
+                for u in range(4):
+                    if pattern[u] == "T":
+                        add_turned(k, u)
+            if k == 0:
+                ad_quantise(3)
+            if k > 0:
+                wm_quantise(k - 1)
+                if k - 1 in last_period:
+                    pi = last_period[k - 1]
+                    todo.extend((pi, j) for j in range(2 * len(PANELS[pi])))
+            if k == n:
+                break
+            for lo, hi in plain_runs(k):
+                add_plain(nc.vector, k, lo, hi)
+            if k - 1 in BPREP:
+                b_quantise(BPREP[k - 1])
+            if k in BPREP:
+                b_widen(BPREP[k])
+                b_interleave(BPREP[k], nc.scalar.copy)
+            if k + 1 < n:
+                for u in range(4):
+                    first_product(k + 1, u)
+                for u in range(4):
+                    turn_back(k + 1, u)
+            for item in todo[:1]:
+                if open_item is not None:
+                    y_store(*open_item)
+                y_product(*item)
+                open_item = item
+            todo = todo[1:]
+        for item in todo:
+            if open_item is not None:
+                y_store(*open_item)
+            y_product(*item)
+            open_item = item
+        y_store(*open_item)

@@ -27,11 +27,9 @@ T_TILES = T // P
 
 FLOPS = 2 * IN * R * OUT + 2 * T * IN * OUT
 
-PANELS = [[0, 1], [2, 3], [4, 5, 6, 7], [8, 9], [10], [11]]
-PATTERNS = ["TTTT","TTTP","TTTP","PPTP","TTTP","TTTT","PPPP","TTPP","PPPP","PPTP","PPPP","PPPP"]
-BPREP = {0: 1, 1: 2, 2: 3, 4: 4, 6: 5}
-DP, DT, TB, YB = 2, 2, 1, 3
-HP = 64
+
+STEPS = CHUNKS * GROUPS * 2
+TURNED = ["TTTT", "TTPP", "PPPP"]
 
 
 def tile_vera_merged_layer_s13_kernel(tc, x_words, x_scales, a, bmat_bytes, bmat_scale, d_gain, b_gain, w0, out):
@@ -39,350 +37,346 @@ def tile_vera_merged_layer_s13_kernel(tc, x_words, x_scales, a, bmat_bytes, bmat
     with ExitStack() as ctx:
         keep = ctx.enter_context(tc.tile_pool(name="keep", bufs=1))
         work = ctx.enter_context(tc.tile_pool(name="work", bufs=2))
-        psum = ctx.enter_context(tc.psum_pool(name="psum", bufs=2))
+        psum = ctx.enter_context(tc.psum_pool(name="psum", bufs=1))
+        ctx.enter_context(tc.manual_schedule())
 
-        b_row = keep.tile([P, OUT], BF16, name="b_row")
-        ones = keep.tile([P, P], BF16, name="ones")
-        warm = keep.tile([P, 8], F32, name="warm")
+        gain_rows = keep.tile([P, P], BF16, name="gain_rows")
         ident = keep.tile([P, P], F32, name="ident")
+        ident_bf = keep.tile([P, P], BF16, name="ident_bf")
         b_sc = keep.tile([P, PACK], F32, name="b_sc")
-        b_raw = keep.tile([P, PACK, OUT], U8, name="b_raw", align_bytes=64)
-        b_wide = keep.tile([P, PACK, OUT], BF16, name="b_wide", align_bytes=64)
-        b_grp = keep.tile([P, OUT, PACK], BF16, name="b_grp", align_bytes=64)
+        d_col = keep.tile([P, PACK], BF16, name="d_col")
+        b_col = keep.tile([P, BLOCKS], F32, name="b_col")
+        bg = keep.tile([P, OUT - CHUNK], BF16, name="bg")
+        b_raw = [keep.tile([P, PACK, CHUNK], U8, name="b_raw%d" % c, align_bytes=64) for c in range(CHUNKS)]
         b_cod = keep.tile([P, OUT], U32, name="b_cod", align_bytes=64)
         b_pla = keep.tile([P, OUT], U8, name="b_pla", align_bytes=64)
-        a_raw = keep.tile([P, GROUPS, PACK, R], BF16, name="a_raw", align_bytes=64)
-        a_cod = keep.tile([P, GROUPS, P * PACK], U32, name="a_cod", align_bytes=64)
-        a_pla = keep.tile([P, GROUPS, P * PACK], U8, name="a_pla", align_bytes=64)
-        w_raw = keep.tile([P, GROUPS, PACK, OUT], BF16, name="w_raw", align_bytes=64)
+        a_raw = {(g, h): keep.tile([P, 2, R], BF16, name="a_raw%d%d" % (g, h), align_bytes=64) for g in range(GROUPS) for h in range(2)}
+        a_cod = keep.tile([P, GROUPS * CHUNK], U32, name="a_cod", align_bytes=64)
+        a_pla = keep.tile([P, GROUPS * CHUNK], U8, name="a_pla", align_bytes=64)
+        w_raw = {(c, g): keep.tile([P, PACK, CHUNK], BF16, name="w_raw%d%d" % (c, g), align_bytes=64) for c in range(CHUNKS) for g in range(GROUPS)}
         w_cod = keep.tile([P, GROUPS * OUT], U32, name="w_cod", align_bytes=64)
         w_pla = keep.tile([P, GROUPS * OUT], U8, name="w_pla", align_bytes=64)
         x_cod = keep.tile([P, GROUPS, 2 * T], U8, name="x_cod", align_bytes=64)
         x_pla = keep.tile([P, GROUPS, T], U8, name="x_pla", align_bytes=64)
-        d_col = keep.tile([P, PACK], BF16, name="d_col")
-        bg = keep.tile([P, OUT], F32, name="bg")
-        b_col = keep.tile([P, BLOCKS], F32, name="b_col")
 
         a_view = a.rearrange("(g p t) r -> g p t r", p=P, t=PACK)
         w_view = w0.rearrange("(g p t) o -> g p t o", p=P, t=PACK)
         b_view = bmat_bytes.rearrange("(p t) o -> p t o", t=PACK)
+        out_view = out.rearrange("(m p) o -> m p o", p=P)
 
-        nc.scalar.dma_start(out=d_col[:], in_=d_gain.rearrange("(p t) -> p t", t=PACK))
-        nc.vector.memset(warm[:], 0.0)
-        nc.scalar.activation(out=warm[:, 0:4], in_=warm[:, 4:8], func=COPY)
-        nc.vector.memset(ones[:], 1.0)
-        nc.gpsimd.memset(b_row[:], 0.0)
+        ring = [0]
+
+        def s_bank(shape, dtype=F32):
+            ring[0] = (ring[0] + 1) % 4
+            return psum.tile(shape, dtype, name="s_bank", tag="s_bank%d" % ring[0])
+
+        def v_bank(s, i, shape=(P, PACK, P)):
+            return psum.tile(list(shape), F32, name="v_bank", tag="v_bank%d" % (2 * (s % 2) + i))
+
+        nc.vector.memset(gain_rows[:], 0.0)
         make_identity(nc, ident[:])
         nc.gpsimd.memset(x_pla[:].rearrange("p g n -> p (g n)").bitcast(U32), 0)
-
-        nc.sync.dma_start(out=b_sc[:], in_=bmat_scale.rearrange("(p t) o -> p (t o)", t=PACK))
-        nc.sync.dma_start(out=b_raw[:, :, 0:CHUNK], in_=b_view[:, :, 0:CHUNK])
-        for h in range(2):
-            nc.sync.dma_start(out=a_raw[:, 0, 2 * h : 2 * h + 2, :], in_=a_view[0][:, 2 * h : 2 * h + 2, :])
+        nc.scalar.dma_start(out=b_sc[:], in_=bmat_scale.rearrange("(p t) o -> p (t o)", t=PACK))
+        nc.scalar.dma_start(out=d_col[:], in_=d_gain.rearrange("(p t) -> p t", t=PACK))
+        nc.scalar.dma_start(out=gain_rows[0:BLOCKS, :], in_=b_gain.rearrange("(c p) -> c p", p=P))
 
         def load_a(g):
-            nc.sync.dma_start(out=a_raw[:, g, :, :], in_=a_view[g])
+            for h in range(2):
+                nc.sync.dma_start(out=a_raw[(g, h)][:], in_=a_view[g][:, 2 * h : 2 * h + 2, :])
+
+        def load_b(c):
+            nc.sync.dma_start(out=b_raw[c][:], in_=b_view[:, :, c * CHUNK : (c + 1) * CHUNK])
 
         def load_w(c, g):
-            cols = slice(c * CHUNK, (c + 1) * CHUNK)
-            nc.sync.dma_start(out=w_raw[:, g, :, cols], in_=w_view[g][:, :, cols])
+            nc.sync.dma_start(out=w_raw[(c, g)][:], in_=w_view[g][:, :, c * CHUNK : (c + 1) * CHUNK])
 
-        nc.sync.dma_start(out=b_row[0:1, :], in_=b_gain.rearrange("(o r) -> o r", o=1))
+        load_b(0)
+        load_a(0)
         load_a(1)
         load_w(0, 0)
         load_a(2)
+        load_b(1)
         load_w(0, 1)
         load_a(3)
         load_w(0, 2)
         load_w(0, 3)
-        nc.sync.dma_start(out=b_raw[:, :, CHUNK:OUT], in_=b_view[:, :, CHUNK:OUT])
-        for g in range(GROUPS):
-            load_w(1, g)
-        nc.sync.dma_start(out=x_cod[:].bitcast(I32), in_=x_words.bitcast(I32).rearrange("g p n -> p g n"))
         for q in range(4):
             nc.sync.dma_start(
                 out=x_pla[32 * q : 32 * q + 4, :, :].bitcast(I32),
                 in_=x_scales[:, 4 * q : 4 * q + 4, :].bitcast(I32).rearrange("g q n -> q g n"),
             )
+        load_w(1, 0)
+        load_w(1, 1)
+        nc.sync.dma_start(out=x_cod[:].bitcast(I32), in_=x_words.bitcast(I32).rearrange("g p n -> p g n"))
+        load_w(1, 2)
+        load_w(1, 3)
+        load_b(2)
         for g in range(GROUPS):
             load_w(2, g)
 
-        ad_tiles = {}
-        grp_tiles = {}
+        ad_banks, ad_grp = {}, {}
 
-        def ad_turn(g, h):
-            if h == 0:
-                grp_tiles[g] = work.tile([P, P * PACK, PACK], BF16, name="ad_grp", tag="ad_grp", align_bytes=64)
-            bank = psum.tile([P, 2, HALF], F32, name="bank_a", tag="y", bufs=YB)
-            ad_tiles[(g, h)] = bank
-            if g >= 1:
-                turned_words = work.tile([P, 2, 2, P], F32, name="a_words", tag="a_words")
-                nc.scalar.copy(
-                    out=turned_words[:],
-                    in_=a_raw[:, g, 2 * h : 2 * h + 2, :].bitcast(F32).rearrange("p i (m u) -> p i u m", u=2),
-                )
-            for i in range(2):
-                words = a_raw[:, g, 2 * h + i, :].bitcast(F32)
-                for u in range(2):
-                    in_words = turned_words[:, i, u, :] if g >= 1 else words[:, u::2]
-                    nc.tensor.transpose(bank[:, u, i * P : (i + 1) * P], in_words, ident[:])
+        def ad_turn(g):
+            ad_grp[g] = work.tile([P, CHUNK, PACK], BF16, name="ad_grp", tag="ad_grp", align_bytes=64)
+            for h in range(2):
+                bank = s_bank([P, 2, HALF])
+                ad_banks[(g, h)] = bank
+                for i in range(2):
+                    words = a_raw[(g, h)][:, i, :].bitcast(F32)
+                    for u in range(2):
+                        nc.tensor.transpose(bank[:, u, i * P : (i + 1) * P], words[:, u::2], ident[:])
 
         def ad_product(g, h):
             nc.vector.tensor_tensor(
-                out=grp_tiles[g][:, h * HALF : (h + 1) * HALF, :].rearrange("p n (u e) -> p n u e", u=2),
-                in0=ad_tiles[(g, h)][:].bitcast(BF16).rearrange("p u (n e) -> p n u e", e=2),
+                out=ad_grp[g][:, h * HALF : (h + 1) * HALF, :].rearrange("p n (u e) -> p n u e", u=2),
+                in0=ad_banks[(g, h)][:].bitcast(BF16).rearrange("p u (n e) -> p n u e", e=2),
                 in1=d_col[:].rearrange("p (u e) -> p u e", u=2).unsqueeze(1).to_broadcast([P, HALF, 2, 2]),
                 op=MULT,
             )
 
         def ad_quantise(g):
-            nc.vector.quantize_mx(
-                out=a_cod[:, g, :].bitcast(E4M3X4), scales=a_pla[:, g, :], in_=grp_tiles[g][:].rearrange("p n t -> p (n t)")
-            )
+            cols = slice(g * CHUNK, (g + 1) * CHUNK)
+            nc.vector.quantize_mx(out=a_cod[:, cols].bitcast(E4M3X4), scales=a_pla[:, cols], in_=ad_grp[g][:].rearrange("p n t -> p (n t)"))
 
-        def b_widen(k):
-            cols = slice(k * HALF, (k + 1) * HALF)
-            for t in range(PACK):
-                nc.scalar.activation(out=b_wide[:, t, cols], in_=b_raw[:, t, cols].bitcast(E4M3), func=COPY, scale=b_sc[:, t : t + 1])
+        b_wide, b_grp = {}, {}
 
-        def b_interleave(k, copy):
-            cols = slice(k * HALF, (k + 1) * HALF)
-            copy(out=b_grp[:, cols, :], in_=b_wide[:, :, cols].rearrange("p t c -> p c t"))
+        def b_tiles(c):
+            b_wide[c] = work.tile([P, PACK, CHUNK], BF16, name="b_wide", tag="b_wide", bufs=1, align_bytes=64)
+            b_grp[c] = work.tile([P, CHUNK, PACK], BF16, name="b_grp", tag="b_grp", bufs=1, align_bytes=64)
 
-        def b_quantise(k):
-            cols = slice(k * HALF, (k + 1) * HALF)
-            nc.vector.quantize_mx(
-                out=b_cod[:, cols].bitcast(E4M3X4), scales=b_pla[:, cols], in_=b_grp[:, cols, :].rearrange("p c t -> p (c t)")
-            )
+        def b_widen_scalar(c, t):
+            nc.scalar.activation(out=b_wide[c][:, t, :], in_=b_raw[c][:, t, :].bitcast(E4M3), func=COPY, scale=b_sc[:, t : t + 1])
 
-        periods = []
-        last_period = {}
-        bases = {}
-        base = 0
-        for pi, panel in enumerate(PANELS):
-            bases[pi] = base
-            order = [(g, ob) for g in range(GROUPS) for ob in panel]
-            for i in range(0, len(order), 4):
-                periods.append((order[i : i + 4], base + i * P, PATTERNS[len(periods)]))
-            last_period[len(periods) - 1] = pi
-            base += GROUPS * len(panel) * P
-        banks, scaled, turned, prods, wm = {}, {}, {}, {}, {}
+        def b_widen_vector(c, t):
+            nc.vector.tensor_scalar(out=b_wide[c][:, t, :], in0=b_raw[c][:, t, :].bitcast(E4M3), scalar1=b_sc[:, t : t + 1], scalar2=None, op0=MULT)
 
-        def first_product(k, u):
-            (g, ob), kind = periods[k][0][u], periods[k][2][u]
-            cols = slice(ob * P, (ob + 1) * P)
-            bank = psum.tile([P, PACK, P], F32, name="bank_d", tag="dt" if kind == "T" else "dp", bufs=DT if kind == "T" else DP)
-            banks[(k, u)] = bank
-            if kind == "T":
-                nc.tensor.matmul_mx(
-                    out=bank[:].rearrange("p t o -> p (t o)"),
-                    lhsT=b_cod[:, cols].bitcast(E4M3X4),
-                    lhsT_scale=b_pla[:, cols],
-                    rhs=a_cod[:, g, :].bitcast(E4M3X4),
-                    rhs_scale=a_pla[:, g, :],
-                    start=True,
-                    stop=True,
-                )
-                tile = work.tile([P, PACK, P], F32, name="scaled", tag="scaled", bufs=6)
-                scaled[(k, u)] = tile
-                nc.scalar.activation(out=tile[:], in_=bank[:], func=COPY, scale=b_col[:, ob : ob + 1])
-            else:
-                for t in range(PACK):
+        def b_interleave(copy, c, h):
+            cols = slice(h * HALF, (h + 1) * HALF)
+            copy(out=b_grp[c][:, cols, :], in_=b_wide[c][:, :, cols].rearrange("p t c -> p c t"))
+
+        def b_quantise(c, lo, hi):
+            cols = slice(c * CHUNK + lo, c * CHUNK + hi)
+            nc.vector.quantize_mx(out=b_cod[:, cols].bitcast(E4M3X4), scales=b_pla[:, cols], in_=b_grp[c][:, lo:hi, :].rearrange("p c t -> p (c t)"))
+
+        def place(s, i):
+            c, g = divmod(s // 2, GROUPS)
+            u = 2 * (s % 2) + i
+            return c, g, u, TURNED[c][u]
+
+        banks, scaled, prods, wm = {}, {}, {}, {}
+
+        def turned_product(s):
+            for i in range(2):
+                c, g, u, kind = place(s, i)
+                if kind == "T":
+                    cols = slice(c * CHUNK + u * P, c * CHUNK + (u + 1) * P)
+                    rows = slice(g * CHUNK, (g + 1) * CHUNK)
+                    bank = s_bank([P, CHUNK])
+                    banks[(s, i)] = bank
                     nc.tensor.matmul_mx(
-                        out=bank[:, t, :],
-                        lhsT=a_cod[:, g, t * P : (t + 1) * P].bitcast(E4M3X4),
-                        lhsT_scale=a_pla[:, g, t * P : (t + 1) * P],
-                        rhs=b_cod[:, cols].bitcast(E4M3X4),
-                        rhs_scale=b_pla[:, cols],
+                        out=bank[:],
+                        lhsT=b_cod[:, cols].bitcast(E4M3X4),
+                        lhsT_scale=b_pla[:, cols],
+                        rhs=a_cod[:, rows].bitcast(E4M3X4),
+                        rhs_scale=a_pla[:, rows],
                         start=True,
                         stop=True,
                     )
 
-        def turn_back(k, u):
-            if periods[k][2][u] == "T":
-                bank = psum.tile([P, PACK, P], F32, name="bank_t", tag="t", bufs=TB)
-                turned[(k, u)] = bank
-                for t in range(PACK):
-                    nc.tensor.transpose(bank[:, t, :], scaled[(k, u)][:, t, :], ident[:])
+        def turned_scale(s):
+            for i in range(2):
+                c, g, u, kind = place(s, i)
+                if kind == "T":
+                    tile = work.tile([P, CHUNK], F32, name="scaled", tag="scaled", bufs=4)
+                    scaled[(s, i)] = tile
+                    ob = c * PACK + u
+                    nc.scalar.activation(out=tile[:], in_=banks[(s, i)][:], func=COPY, scale=b_col[:, ob : ob + 1])
 
-        def scale_plain(k, u):
-            g, ob = periods[k][0][u]
-            nc.vector.tensor_tensor(
-                out=prods[k][:, u * P : (u + 1) * P, :],
-                in0=banks[(k, u)][:].rearrange("p t o -> p o t"),
-                in1=bg[:, ob * P : (ob + 1) * P].unsqueeze(2).to_broadcast([P, P, PACK]),
-                op=MULT,
-            )
+        def plain_product(s):
+            for i in range(2):
+                c, g, u, kind = place(s, i)
+                if kind == "P":
+                    cols = slice(c * CHUNK + u * P, c * CHUNK + (u + 1) * P)
+                    bank = v_bank(s, i)
+                    banks[(s, i)] = bank
+                    for t in range(PACK):
+                        rows = slice(g * CHUNK + t * P, g * CHUNK + (t + 1) * P)
+                        nc.tensor.matmul_mx(
+                            out=bank[:, t, :],
+                            lhsT=a_cod[:, rows].bitcast(E4M3X4),
+                            lhsT_scale=a_pla[:, rows],
+                            rhs=b_cod[:, cols].bitcast(E4M3X4),
+                            rhs_scale=b_pla[:, cols],
+                            start=True,
+                            stop=True,
+                        )
 
-        def add_turned(k, u):
-            g, ob = periods[k][0][u]
-            nc.vector.tensor_tensor(
-                out=wm[k][:, u * P : (u + 1) * P, :],
-                in0=turned[(k, u)][:].rearrange("p t o -> p o t"),
-                in1=w_raw[:, g, :, ob * P : (ob + 1) * P].rearrange("p t o -> p o t"),
-                op=ADD,
-            )
+        def turn_back(s):
+            for i in range(2):
+                if place(s, i)[3] == "T":
+                    bank = v_bank(s, i)
+                    banks[(s, i)] = bank
+                    for t in range(PACK):
+                        nc.tensor.transpose(bank[:, t, :], scaled[(s, i)][:, t * P : (t + 1) * P], ident[:])
 
-        def add_plain(engine, k, lo, hi):
-            g, ob = periods[k][0][lo // P]
-            o0 = ob * P + lo % P
-            engine.tensor_tensor(
-                out=wm[k][:, lo:hi, :],
-                in0=prods[k][:, lo:hi, :],
-                in1=w_raw[:, g, :, o0 : o0 + hi - lo].rearrange("p t o -> p o t"),
-                op=ADD,
-            )
+        def empty_block(s, i):
+            c, g, u, kind = place(s, i)
+            row = s // 2
+            if u == 0:
+                wm[row] = work.tile([P, CHUNK, PACK], BF16, name="wm", tag="wm", bufs=3, align_bytes=64)
+            if i == 0:
+                prods[s] = work.tile([P, HALF, PACK], F32, name="prod", tag="prod", bufs=2) if "P" in TURNED[c][u : u + 2] else None
+            delta = banks[(s, i)][:].rearrange("p t o -> p o t")
+            if kind == "T":
+                nc.vector.tensor_tensor(
+                    out=wm[row][:, u * P : (u + 1) * P, :],
+                    in0=delta,
+                    in1=w_raw[(c, g)][:, :, u * P : (u + 1) * P].rearrange("p t o -> p o t"),
+                    op=ADD,
+                )
+            else:
+                o0 = (c - 1) * CHUNK + u * P
+                nc.vector.tensor_tensor(
+                    out=prods[s][:, i * P : (i + 1) * P, :],
+                    in0=delta,
+                    in1=bg[:, o0 : o0 + P].unsqueeze(2).to_broadcast([P, P, PACK]),
+                    op=MULT,
+                )
 
-        def plain_runs(k):
-            units, at, pattern = periods[k]
-            runs = []
-            for u in range(4):
-                if pattern[u] not in "Pg":
-                    continue
-                lo = u * P + (HP if pattern[u] == "g" else 0)
-                hi = (u + 1) * P
-                if runs and runs[-1][1] == lo and units[u][0] == units[u - 1][0]:
-                    runs[-1][1] = hi
-                else:
-                    runs.append([lo, hi])
-            return runs
+        def add_plain(s):
+            plain = [i for i in range(2) if place(s, i)[3] == "P"]
+            if plain:
+                c, g, u, kind = place(s, 0)
+                lo, hi = plain[0] * P, (plain[-1] + 1) * P
+                nc.vector.tensor_tensor(
+                    out=wm[s // 2][:, u * P + lo : u * P + hi, :],
+                    in0=prods[s][:, lo:hi, :],
+                    in1=w_raw[(c, g)][:, :, u * P + lo : u * P + hi].rearrange("p t o -> p o t"),
+                    op=ADD,
+                )
 
-        def wm_quantise(k, lo=0, hi=4 * P):
-            at = periods[k][1]
-            nc.vector.quantize_mx(
-                out=w_cod[:, at + lo : at + hi].bitcast(E4M3X4),
-                scales=w_pla[:, at + lo : at + hi],
-                in_=wm[k][:, lo:hi, :].rearrange("p o t -> p (o t)"),
-            )
+        def wm_quantise(row):
+            cols = slice(row * CHUNK, (row + 1) * CHUNK)
+            nc.vector.quantize_mx(out=w_cod[:, cols].bitcast(E4M3X4), scales=w_pla[:, cols], in_=wm[row][:].rearrange("p o t -> p (o t)"))
 
         y_banks = {}
 
-        def y_product(pi, j):
-            width = len(PANELS[pi]) * P
-            n = min(width, CHUNK) if width == CHUNK else P
-            tiles = CHUNK // width
-            bank = psum.tile([P, tiles, width], F32, name="bank_y", tag="y", bufs=YB)
-            y_banks[(pi, j)] = bank
-            for i in range(tiles):
-                tt = j * tiles + i
-                for o in range(0, width, n):
-                    for g in range(GROUPS):
-                        at = bases[pi] + g * width + o
-                        nc.tensor.matmul_mx(
-                            out=bank[:, i, o : o + n],
-                            lhsT=x_cod[:, g, tt * 2 * P : (tt + 1) * 2 * P].bitcast(E2M1X4),
-                            lhsT_scale=x_pla[:, g, tt * P : (tt + 1) * P],
-                            rhs=w_cod[:, at : at + n].bitcast(E4M3X4),
-                            rhs_scale=w_pla[:, at : at + n],
-                            start=g == 0,
-                            stop=g == GROUPS - 1,
-                        )
+        def y_passes(c, m, groups, bank=None):
+            if groups[0] == 0:
+                y_banks[(c, m)] = bank if bank is not None else s_bank([P, CHUNK])
+            for g in groups:
+                cols = slice((c * GROUPS + g) * CHUNK, (c * GROUPS + g + 1) * CHUNK)
+                nc.tensor.matmul_mx(
+                    out=y_banks[(c, m)][:],
+                    lhsT=x_cod[:, g, m * 2 * P : (m + 1) * 2 * P].bitcast(E2M1X4),
+                    lhsT_scale=x_pla[:, g, m * P : (m + 1) * P],
+                    rhs=w_cod[:, cols].bitcast(E4M3X4),
+                    rhs_scale=w_pla[:, cols],
+                    start=g == 0,
+                    stop=g == GROUPS - 1,
+                )
 
-        out_view = out.rearrange("(m p) o -> p m o", p=P)
+        def y_store(c, m, copy):
+            res = work.tile([P, CHUNK], F32, name="res", tag="res", bufs=8)
+            copy(out=res[:], in_=y_banks[(c, m)][:])
+            nc.sync.dma_start(out=out_view[m][:, c * CHUNK : (c + 1) * CHUNK], in_=res[:])
 
-        def y_store(pi, j, engine=None):
-            width = len(PANELS[pi]) * P
-            tiles = CHUNK // width
-            o0 = PANELS[pi][0] * P
-            res = work.tile([P, tiles, width], F32, name="res", tag="res", bufs=6)
-            if engine is None:
-                nc.scalar.copy(out=res[:], in_=y_banks[(pi, j)][:])
-            else:
-                engine(out=res[:], in_=y_banks[(pi, j)][:])
-            nc.sync.dma_start(out=out_view[:, j * tiles : (j + 1) * tiles, o0 : o0 + width], in_=res[:])
-
-        for i in range(0):
-            bank = psum.tile([P, R], F32, name="bank_w", tag="y", bufs=YB)
-            nc.tensor.matmul(bank[:], lhsT=ones[:], rhs=b_row[:, 0:R], start=True, stop=True)
-        b_widen(0)
-        ad_turn(0, 0)
-        ad_turn(0, 1)
+        nc.scalar.activation(out=ident_bf[:], in_=ident[:], func=COPY)
+        b_tiles(0)
+        for t in range(2):
+            b_widen_vector(0, t)
+            b_widen_scalar(0, t + 2)
+        gain_banks = []
+        for c in range(1, CHUNKS):
+            bank = v_bank(0, c - 1)
+            gain_banks.append(bank)
+            for u in range(PACK):
+                ob = c * PACK + u
+                nc.tensor.matmul(bank[:, u, :], lhsT=ident_bf[:, ob : ob + 1].to_broadcast([P, P]), rhs=gain_rows[:], start=True, stop=True)
+        col_bank = v_bank(1, 0)
+        nc.tensor.matmul(col_bank[:, 0, 0:BLOCKS], lhsT=gain_rows[:], rhs=ident_bf[:, 0:BLOCKS], start=True, stop=True)
+        ad_turn(0)
+        b_interleave(nc.vector.tensor_copy, 0, 0)
+        b_interleave(nc.scalar.copy, 0, 1)
+        nc.scalar.copy(out=b_col[:], in_=col_bank[:, 0, 0:BLOCKS])
+        for c in range(1, CHUNKS):
+            nc.scalar.copy(out=bg[:, (c - 1) * CHUNK : c * CHUNK], in_=gain_banks[c - 1][:].rearrange("p u o -> p (u o)"))
         ad_product(0, 0)
         ad_product(0, 1)
-        b_interleave(0, nc.scalar.copy)
+        ad_turn(1)
+        b_quantise(0, 0, HALF)
         ad_quantise(0)
-        b_quantise(0)
-        ad_turn(1, 0)
-        ad_turn(1, 1)
-        bank = psum.tile([P, BLOCKS], F32, name="bank_c", tag="t", bufs=TB)
-        for ob in range(BLOCKS):
-            nc.tensor.matmul(bank[:, ob : ob + 1], lhsT=b_row[:, ob * P : (ob + 1) * P], rhs=ones[:, 0:1], start=True, stop=True)
-        nc.scalar.copy(out=b_col[:], in_=bank[:])
+        b_quantise(0, HALF, CHUNK)
+        turned_product(0)
+        turned_scale(0)
         ad_product(1, 0)
         ad_product(1, 1)
-        for u in range(2):
-            first_product(0, u)
-        for u in range(2):
-            turn_back(0, u)
+        turned_product(1)
+        turn_back(0)
+        turned_scale(1)
         ad_quantise(1)
-        ad_turn(2, 0)
-        ad_turn(2, 1)
-        ad_product(2, 0)
-        ad_product(2, 1)
-        for u in range(2, 4):
-            first_product(0, u)
-        for u in range(2, 4):
-            turn_back(0, u)
-        ad_turn(3, 0)
-        ad_turn(3, 1)
-        ad_quantise(2)
-        ad_product(3, 0)
-        ad_product(3, 1)
-        for j in range(3):
-            bank = psum.tile([P, CHUNK], F32, name="bank_b", tag="y", bufs=YB)
-            nc.tensor.matmul(bank[:], lhsT=ones[:], rhs=b_row[:, j * CHUNK : (j + 1) * CHUNK], start=True, stop=True)
-            nc.scalar.copy(out=bg[:, j * CHUNK : (j + 1) * CHUNK], in_=bank[:])
+        ad_turn(2)
 
-        n = len(periods)
+        b_jobs = {}
+        for c in range(1, CHUNKS):
+            s0 = (c - 1) * 8
+            b_jobs[s0] = [lambda c=c: b_tiles(c), lambda c=c: b_widen_scalar(c, 0), lambda c=c: b_widen_scalar(c, 1)]
+            b_jobs[s0 + 1] = [lambda c=c: b_widen_scalar(c, 2), lambda c=c: b_widen_scalar(c, 3)]
+            b_jobs[s0 + 2] = [lambda c=c: b_interleave(nc.scalar.copy, c, 0)]
+            b_jobs[s0 + 3] = [lambda c=c: b_interleave(nc.scalar.copy, c, 1)]
         todo = []
-        open_item = None
-        for k in range(n + 1):
-            if k < n:
-                units, at, pattern = periods[k]
-                prods[k] = work.tile([P, 4 * P, PACK], F32, name="prod", tag="prod", bufs=2)
-                wm[k] = work.tile([P, 4 * P, PACK], BF16, name="wm", tag="wm", bufs=3, align_bytes=64)
-                for kind in "GgP":
-                    for u in range(4):
-                        if pattern[u] == kind:
-                            scale_plain(k, u)
-                for u in range(4):
-                    if pattern[u] == "G":
-                        add_plain(nc.gpsimd, k, u * P, (u + 1) * P)
-                    if pattern[u] == "g":
-                        add_plain(nc.gpsimd, k, u * P, u * P + HP)
-                for u in range(4):
-                    if pattern[u] == "T":
-                        add_turned(k, u)
-            if k == 0:
-                ad_quantise(3)
-            if k > 0:
-                wm_quantise(k - 1)
-                if k - 1 in last_period:
-                    pi = last_period[k - 1]
-                    todo.extend((pi, j) for j in range(2 * len(PANELS[pi])))
-            if k == n:
-                break
-            for lo, hi in plain_runs(k):
-                add_plain(nc.vector, k, lo, hi)
-            if k - 1 in BPREP:
-                b_quantise(BPREP[k - 1])
-            if k in BPREP:
-                b_widen(BPREP[k])
-                b_interleave(BPREP[k], nc.scalar.copy)
-            if k + 1 < n:
-                for u in range(4):
-                    first_product(k + 1, u)
-                for u in range(4):
-                    turn_back(k + 1, u)
-            for item in todo[:1]:
-                if open_item is not None:
-                    y_store(*open_item)
-                y_product(*item)
-                open_item = item
-            todo = todo[1:]
-        for item in todo:
-            if open_item is not None:
-                y_store(*open_item)
-            y_product(*item)
-            open_item = item
-        y_store(*open_item)
+        to_store = []
+        last = CHUNKS - 1
+        for s in range(STEPS):
+            if s in (0, 2):
+                ad_product(s // 2 + 2, 0)
+                ad_product(s // 2 + 2, 1)
+            empty_block(s, 0)
+            if s > 0:
+                add_plain(s - 1)
+            empty_block(s, 1)
+            if s in (0, 2):
+                ad_quantise(s // 2 + 2)
+            if s % 8 == 5 and s // 8 + 1 < CHUNKS:
+                b_quantise(s // 8 + 1, 0, CHUNK)
+            if s % 2 == 0 and s > 0:
+                wm_quantise(s // 2 - 1)
+                if s % 8 == 0:
+                    todo.extend((s // 8 - 1, m) for m in range(T_TILES))
+            if s + 1 < STEPS:
+                plain_product(s + 1)
+            if s + 2 < STEPS:
+                turned_product(s + 2)
+            if s + 1 < STEPS:
+                turn_back(s + 1)
+            if s == 1:
+                ad_turn(3)
+            if s + 2 < STEPS:
+                turned_scale(s + 2)
+            for item in to_store:
+                y_store(*item, nc.scalar.copy)
+            to_store = todo[: 2 if (s > 16 and s % 2) else 1]
+            todo = todo[len(to_store) :]
+            for item in to_store:
+                y_passes(*item, range(GROUPS))
+            for job in b_jobs.get(s, []):
+                job()
+            if s == STEPS - 2:
+                for item in to_store:
+                    y_store(*item, nc.scalar.copy)
+                to_store = []
+                for m in range(4):
+                    y_passes(last, m, range(2))
+            if s == STEPS - 1:
+                for m in range(4):
+                    y_passes(last, m, range(2, 3))
+        add_plain(STEPS - 1)
+        for m in range(4, 6):
+            y_passes(last, m, range(3), v_bank(0, m - 4, (P, CHUNK)))
+        wm_quantise(STEPS // 2 - 1)
+        for m in range(6):
+            y_passes(last, m, range(3, 4))
+            y_store(last, m, nc.scalar.copy if m % 2 == 0 else nc.vector.tensor_copy)
+        for m in range(6, 8):
+            y_passes(last, m, range(4), v_bank(1, m - 6, (P, CHUNK)))
+            y_store(last, m, nc.scalar.copy if m % 2 == 0 else nc.vector.tensor_copy)

@@ -29,7 +29,8 @@ FLOPS = 2 * IN * R * OUT + 2 * T * IN * OUT
 
 
 STEPS = CHUNKS * GROUPS * 2
-TURNED = ["TTTT", "TTPP", "PPPP"]
+KINDS = ["AAAA", "AAAA", "ATAT", "ATAT"] + ["TTPP"] * 4 + ["PPPP"] * 4
+WOVEN_FROM = 16
 
 
 def tile_vera_merged_layer_s13_kernel(tc, x_words, x_scales, a, bmat_bytes, bmat_scale, d_gain, b_gain, w0, out):
@@ -76,9 +77,6 @@ def tile_vera_merged_layer_s13_kernel(tc, x_words, x_scales, a, bmat_bytes, bmat
         nc.vector.memset(gain_rows[:], 0.0)
         make_identity(nc, ident[:])
         nc.gpsimd.memset(x_pla[:].rearrange("p g n -> p (g n)").bitcast(U32), 0)
-        nc.scalar.dma_start(out=b_sc[:], in_=bmat_scale.rearrange("(p t) o -> p (t o)", t=PACK))
-        nc.scalar.dma_start(out=d_col[:], in_=d_gain.rearrange("(p t) -> p t", t=PACK))
-        nc.scalar.dma_start(out=gain_rows[0:BLOCKS, :], in_=b_gain.rearrange("(c p) -> c p", p=P))
 
         def load_a(g):
             for h in range(2):
@@ -90,13 +88,16 @@ def tile_vera_merged_layer_s13_kernel(tc, x_words, x_scales, a, bmat_bytes, bmat
         def load_w(c, g):
             nc.sync.dma_start(out=w_raw[(c, g)][:], in_=w_view[g][:, :, c * CHUNK : (c + 1) * CHUNK])
 
-        load_b(0)
         load_a(0)
+        nc.sync.dma_start(out=b_sc[:], in_=bmat_scale.rearrange("(p t) o -> p (t o)", t=PACK))
+        nc.sync.dma_start(out=d_col[:], in_=d_gain.rearrange("(p t) -> p t", t=PACK))
+        load_b(0)
+        nc.sync.dma_start(out=gain_rows[0:BLOCKS, :], in_=b_gain.rearrange("(c p) -> c p", p=P))
         load_a(1)
         load_w(0, 0)
         load_a(2)
-        load_b(1)
         load_w(0, 1)
+        load_b(1)
         load_a(3)
         load_w(0, 2)
         load_w(0, 3)
@@ -161,14 +162,14 @@ def tile_vera_merged_layer_s13_kernel(tc, x_words, x_scales, a, bmat_bytes, bmat
         def place(s, i):
             c, g = divmod(s // 2, GROUPS)
             u = 2 * (s % 2) + i
-            return c, g, u, TURNED[c][u]
+            return c, g, u, KINDS[s // 2][u]
 
-        banks, scaled, prods, wm = {}, {}, {}, {}
+        banks, scaled, prods, wm, turned, woven = {}, {}, {}, {}, {}, {}
 
         def turned_product(s):
             for i in range(2):
                 c, g, u, kind = place(s, i)
-                if kind == "T":
+                if kind != "P":
                     cols = slice(c * CHUNK + u * P, c * CHUNK + (u + 1) * P)
                     rows = slice(g * CHUNK, (g + 1) * CHUNK)
                     bank = s_bank([P, CHUNK])
@@ -186,7 +187,7 @@ def tile_vera_merged_layer_s13_kernel(tc, x_words, x_scales, a, bmat_bytes, bmat
         def turned_scale(s):
             for i in range(2):
                 c, g, u, kind = place(s, i)
-                if kind == "T":
+                if kind != "P":
                     tile = work.tile([P, CHUNK], F32, name="scaled", tag="scaled", bufs=4)
                     scaled[(s, i)] = tile
                     ob = c * PACK + u
@@ -211,13 +212,42 @@ def tile_vera_merged_layer_s13_kernel(tc, x_words, x_scales, a, bmat_bytes, bmat
                             stop=True,
                         )
 
+        def lay_base(s):
+            for i in range(2):
+                c, g, u, kind = place(s, i)
+                if kind != "P":
+                    turned[(s, i)] = v_bank(s, i)
+                if kind == "A":
+                    nc.tensor.matmul(
+                        turned[(s, i)][:], lhsT=ident_bf[:], rhs=w_raw[(c, g)][:, :, u * P : (u + 1) * P], start=True, stop=False
+                    )
+
         def turn_back(s):
             for i in range(2):
-                if place(s, i)[3] == "T":
-                    bank = v_bank(s, i)
-                    banks[(s, i)] = bank
+                kind = place(s, i)[3]
+                if kind != "P":
+                    banks[(s, i)] = turned[(s, i)]
                     for t in range(PACK):
-                        nc.tensor.transpose(bank[:, t, :], scaled[(s, i)][:, t * P : (t + 1) * P], ident[:])
+                        nc.tensor.matmul(
+                            turned[(s, i)][:, t, :],
+                            lhsT=scaled[(s, i)][:, t * P : (t + 1) * P],
+                            rhs=ident[:],
+                            is_transpose=True,
+                            start=kind == "T",
+                            stop=kind == "T" or t == PACK - 1,
+                        )
+
+        def weave(s):
+            if s >= WOVEN_FROM:
+                c, g, u, kind = place(s, 0)
+                woven[s] = work.tile([P, HALF, PACK], BF16, name="woven", tag="woven", bufs=3, align_bytes=64)
+                nc.scalar.copy(out=woven[s][:], in_=w_raw[(c, g)][:, :, u * P : u * P + HALF].rearrange("p t o -> p o t"))
+
+        def base(s, lo, hi):
+            if s >= WOVEN_FROM:
+                return woven[s][:, lo:hi, :]
+            c, g, u, kind = place(s, 0)
+            return w_raw[(c, g)][:, :, u * P + lo : u * P + hi].rearrange("p t o -> p o t")
 
         def empty_block(s, i):
             c, g, u, kind = place(s, i)
@@ -225,15 +255,12 @@ def tile_vera_merged_layer_s13_kernel(tc, x_words, x_scales, a, bmat_bytes, bmat
             if u == 0:
                 wm[row] = work.tile([P, CHUNK, PACK], BF16, name="wm", tag="wm", bufs=3, align_bytes=64)
             if i == 0:
-                prods[s] = work.tile([P, HALF, PACK], F32, name="prod", tag="prod", bufs=2) if "P" in TURNED[c][u : u + 2] else None
+                prods[s] = work.tile([P, HALF, PACK], F32, name="prod", tag="prod", bufs=2) if "P" in KINDS[row][u : u + 2] else None
             delta = banks[(s, i)][:].rearrange("p t o -> p o t")
-            if kind == "T":
-                nc.vector.tensor_tensor(
-                    out=wm[row][:, u * P : (u + 1) * P, :],
-                    in0=delta,
-                    in1=w_raw[(c, g)][:, :, u * P : (u + 1) * P].rearrange("p t o -> p o t"),
-                    op=ADD,
-                )
+            if kind == "A":
+                nc.vector.tensor_copy(out=wm[row][:, u * P : (u + 1) * P, :], in_=delta)
+            elif kind == "T":
+                nc.vector.tensor_tensor(out=wm[row][:, u * P : (u + 1) * P, :], in0=delta, in1=base(s, i * P, (i + 1) * P), op=ADD)
             else:
                 o0 = (c - 1) * CHUNK + u * P
                 nc.vector.tensor_tensor(
@@ -251,7 +278,7 @@ def tile_vera_merged_layer_s13_kernel(tc, x_words, x_scales, a, bmat_bytes, bmat
                 nc.vector.tensor_tensor(
                     out=wm[s // 2][:, u * P + lo : u * P + hi, :],
                     in0=prods[s][:, lo:hi, :],
-                    in1=w_raw[(c, g)][:, :, u * P + lo : u * P + hi].rearrange("p t o -> p o t"),
+                    in1=base(s, lo, hi),
                     op=ADD,
                 )
 
@@ -282,38 +309,39 @@ def tile_vera_merged_layer_s13_kernel(tc, x_words, x_scales, a, bmat_bytes, bmat
             nc.sync.dma_start(out=out_view[m][:, c * CHUNK : (c + 1) * CHUNK], in_=res[:])
 
         nc.scalar.activation(out=ident_bf[:], in_=ident[:], func=COPY)
-        b_tiles(0)
-        for t in range(2):
-            b_widen_vector(0, t)
-            b_widen_scalar(0, t + 2)
+        ad_turn(0)
         gain_banks = []
         for c in range(1, CHUNKS):
-            bank = v_bank(0, c - 1)
+            bank = v_bank(1, c - 1)
             gain_banks.append(bank)
             for u in range(PACK):
                 ob = c * PACK + u
                 nc.tensor.matmul(bank[:, u, :], lhsT=ident_bf[:, ob : ob + 1].to_broadcast([P, P]), rhs=gain_rows[:], start=True, stop=True)
-        col_bank = v_bank(1, 0)
+        col_bank = v_bank(0, 0)
         nc.tensor.matmul(col_bank[:, 0, 0:BLOCKS], lhsT=gain_rows[:], rhs=ident_bf[:, 0:BLOCKS], start=True, stop=True)
-        ad_turn(0)
+        b_tiles(0)
+        ad_product(0, 0)
+        for t in range(2):
+            b_widen_vector(0, t)
+            b_widen_scalar(0, t + 2)
+        ad_product(0, 1)
+        ad_turn(1)
         b_interleave(nc.vector.tensor_copy, 0, 0)
         b_interleave(nc.scalar.copy, 0, 1)
         nc.scalar.copy(out=b_col[:], in_=col_bank[:, 0, 0:BLOCKS])
-        for c in range(1, CHUNKS):
-            nc.scalar.copy(out=bg[:, (c - 1) * CHUNK : c * CHUNK], in_=gain_banks[c - 1][:].rearrange("p u o -> p (u o)"))
-        ad_product(0, 0)
-        ad_product(0, 1)
-        ad_turn(1)
-        b_quantise(0, 0, HALF)
         ad_quantise(0)
-        b_quantise(0, HALF, CHUNK)
+        b_quantise(0, 0, HALF)
         turned_product(0)
+        lay_base(0)
         turned_scale(0)
         ad_product(1, 0)
+        b_quantise(0, HALF, CHUNK)
         ad_product(1, 1)
         turned_product(1)
-        turn_back(0)
         turned_scale(1)
+        for c in range(1, CHUNKS):
+            nc.scalar.copy(out=bg[:, (c - 1) * CHUNK : c * CHUNK], in_=gain_banks[c - 1][:].rearrange("p u o -> p (u o)"))
+        turn_back(0)
         ad_quantise(1)
         ad_turn(2)
 
@@ -328,14 +356,14 @@ def tile_vera_merged_layer_s13_kernel(tc, x_words, x_scales, a, bmat_bytes, bmat
         to_store = []
         last = CHUNKS - 1
         for s in range(STEPS):
-            if s in (0, 2):
-                ad_product(s // 2 + 2, 0)
-                ad_product(s // 2 + 2, 1)
             empty_block(s, 0)
             if s > 0:
                 add_plain(s - 1)
             empty_block(s, 1)
             if s in (0, 2):
+                ad_product(s // 2 + 2, 0)
+                ad_product(s // 2 + 2, 1)
+            if s in (1, 3):
                 ad_quantise(s // 2 + 2)
             if s % 8 == 5 and s // 8 + 1 < CHUNKS:
                 b_quantise(s // 8 + 1, 0, CHUNK)
@@ -348,6 +376,7 @@ def tile_vera_merged_layer_s13_kernel(tc, x_words, x_scales, a, bmat_bytes, bmat
             if s + 2 < STEPS:
                 turned_product(s + 2)
             if s + 1 < STEPS:
+                lay_base(s + 1)
                 turn_back(s + 1)
             if s == 1:
                 ad_turn(3)
@@ -359,6 +388,8 @@ def tile_vera_merged_layer_s13_kernel(tc, x_words, x_scales, a, bmat_bytes, bmat
             todo = todo[len(to_store) :]
             for item in to_store:
                 y_passes(*item, range(GROUPS))
+            if s + 1 < STEPS:
+                weave(s + 1)
             for job in b_jobs.get(s, []):
                 job()
             if s == STEPS - 2:
@@ -371,12 +402,9 @@ def tile_vera_merged_layer_s13_kernel(tc, x_words, x_scales, a, bmat_bytes, bmat
                 for m in range(4):
                     y_passes(last, m, range(2, 3))
         add_plain(STEPS - 1)
-        for m in range(4, 6):
-            y_passes(last, m, range(3), v_bank(0, m - 4, (P, CHUNK)))
+        for m in range(4, 8):
+            y_passes(last, m, range(3), v_bank(m // 2, m % 2, (P, CHUNK)))
         wm_quantise(STEPS // 2 - 1)
-        for m in range(6):
+        for m in range(T_TILES):
             y_passes(last, m, range(3, 4))
-            y_store(last, m, nc.scalar.copy if m % 2 == 0 else nc.vector.tensor_copy)
-        for m in range(6, 8):
-            y_passes(last, m, range(4), v_bank(1, m - 6, (P, CHUNK)))
             y_store(last, m, nc.scalar.copy if m % 2 == 0 else nc.vector.tensor_copy)

@@ -29,8 +29,14 @@ FLOPS = 2 * IN * R * OUT + 2 * T * IN * OUT
 
 
 STEPS = CHUNKS * GROUPS * 2
-KINDS = ["AAAA", "AAAA", "ATAT", "ATAT"] + ["TTPP"] * 4 + ["PPPP"] * 4
-WOVEN_FROM = 16
+KINDS = ["USUS","USUS","USUS","USUS","PPPS","PPPS","PPPS","PPPS","PPPS","PPPP","PPPP","PPPP"]
+B_QUANT = {1: 6,2: 14}
+WARM = [0,0,0]
+B_JOBS = {0: [[1,"w",0,"S"]],1: [[1,"w",1,"S"]],2: [[1,"w",2,"S"]],3: [[1,"w",3,"S"]],4: [[1,"i",0,"V"],[2,"w",0,"S"]],5: [[1,"i",1,"V"],[2,"w",1,"S"]],6: [[2,"w",2,"V"],[2,"w",3,"V"]],7: [[2,"i",0,"V"],[2,"i",1,"V"]]}
+UNWOVEN = ()
+G0 = 1
+OPEN = 6
+DOUBLE = (17, 19, 21)
 
 
 def tile_vera_merged_layer_s13_kernel(tc, x_words, x_scales, a, bmat_bytes, bmat_scale, d_gain, b_gain, w0, out):
@@ -42,12 +48,13 @@ def tile_vera_merged_layer_s13_kernel(tc, x_words, x_scales, a, bmat_bytes, bmat
         ctx.enter_context(tc.manual_schedule())
 
         gain_rows = keep.tile([P, P], BF16, name="gain_rows")
+        warm = keep.tile([P, P], BF16, name="warm")
         ident = keep.tile([P, P], F32, name="ident")
         ident_bf = keep.tile([P, P], BF16, name="ident_bf")
         b_sc = keep.tile([P, PACK], F32, name="b_sc")
         d_col = keep.tile([P, PACK], BF16, name="d_col")
         b_col = keep.tile([P, BLOCKS], F32, name="b_col")
-        bg = keep.tile([P, OUT - CHUNK], BF16, name="bg")
+        bg = keep.tile([P, OUT], BF16, name="bg")
         b_raw = [keep.tile([P, PACK, CHUNK], U8, name="b_raw%d" % c, align_bytes=64) for c in range(CHUNKS)]
         b_cod = keep.tile([P, OUT], U32, name="b_cod", align_bytes=64)
         b_pla = keep.tile([P, OUT], U8, name="b_pla", align_bytes=64)
@@ -106,26 +113,26 @@ def tile_vera_merged_layer_s13_kernel(tc, x_words, x_scales, a, bmat_bytes, bmat
                 out=x_pla[32 * q : 32 * q + 4, :, :].bitcast(I32),
                 in_=x_scales[:, 4 * q : 4 * q + 4, :].bitcast(I32).rearrange("g q n -> q g n"),
             )
+        load_b(2)
         load_w(1, 0)
         load_w(1, 1)
         nc.sync.dma_start(out=x_cod[:].bitcast(I32), in_=x_words.bitcast(I32).rearrange("g p n -> p g n"))
         load_w(1, 2)
         load_w(1, 3)
-        load_b(2)
         for g in range(GROUPS):
             load_w(2, g)
 
         ad_banks, ad_grp = {}, {}
 
-        def ad_turn(g):
-            ad_grp[g] = work.tile([P, CHUNK, PACK], BF16, name="ad_grp", tag="ad_grp", align_bytes=64)
-            for h in range(2):
-                bank = s_bank([P, 2, HALF])
-                ad_banks[(g, h)] = bank
-                for i in range(2):
-                    words = a_raw[(g, h)][:, i, :].bitcast(F32)
-                    for u in range(2):
-                        nc.tensor.transpose(bank[:, u, i * P : (i + 1) * P], words[:, u::2], ident[:])
+        def ad_turn(g, h):
+            if h == 0:
+                ad_grp[g] = work.tile([P, CHUNK, PACK], BF16, name="ad_grp", tag="ad_grp", align_bytes=64)
+            bank = s_bank([P, 2, HALF])
+            ad_banks[(g, h)] = bank
+            for i in range(2):
+                words = a_raw[(g, h)][:, i, :].bitcast(F32)
+                for u in range(2):
+                    nc.tensor.transpose(bank[:, u, i * P : (i + 1) * P], words[:, u::2], ident[:])
 
         def ad_product(g, h):
             nc.vector.tensor_tensor(
@@ -142,8 +149,8 @@ def tile_vera_merged_layer_s13_kernel(tc, x_words, x_scales, a, bmat_bytes, bmat
         b_wide, b_grp = {}, {}
 
         def b_tiles(c):
-            b_wide[c] = work.tile([P, PACK, CHUNK], BF16, name="b_wide", tag="b_wide", bufs=1, align_bytes=64)
-            b_grp[c] = work.tile([P, CHUNK, PACK], BF16, name="b_grp", tag="b_grp", bufs=1, align_bytes=64)
+            b_wide[c] = work.tile([P, PACK, CHUNK], BF16, name="b_wide", tag="b_wide", bufs=2, align_bytes=64)
+            b_grp[c] = work.tile([P, CHUNK, PACK], BF16, name="b_grp", tag="b_grp", bufs=2, align_bytes=64)
 
         def b_widen_scalar(c, t):
             nc.scalar.activation(out=b_wide[c][:, t, :], in_=b_raw[c][:, t, :].bitcast(E4M3), func=COPY, scale=b_sc[:, t : t + 1])
@@ -217,7 +224,7 @@ def tile_vera_merged_layer_s13_kernel(tc, x_words, x_scales, a, bmat_bytes, bmat
                 c, g, u, kind = place(s, i)
                 if kind != "P":
                     turned[(s, i)] = v_bank(s, i)
-                if kind == "A":
+                if kind in "AS":
                     nc.tensor.matmul(
                         turned[(s, i)][:], lhsT=ident_bf[:], rhs=w_raw[(c, g)][:, :, u * P : (u + 1) * P], start=True, stop=False
                     )
@@ -233,21 +240,23 @@ def tile_vera_merged_layer_s13_kernel(tc, x_words, x_scales, a, bmat_bytes, bmat
                             lhsT=scaled[(s, i)][:, t * P : (t + 1) * P],
                             rhs=ident[:],
                             is_transpose=True,
-                            start=kind == "T",
-                            stop=kind == "T" or t == PACK - 1,
+                            start=kind in "TU",
+                            stop=kind in "TU" or t == PACK - 1,
                         )
 
         def weave(s):
-            if s >= WOVEN_FROM:
+            wanted = [i for i in range(2) if place(s, i)[3] in "TP"]
+            if wanted and s not in UNWOVEN:
                 c, g, u, kind = place(s, 0)
-                woven[s] = work.tile([P, HALF, PACK], BF16, name="woven", tag="woven", bufs=3, align_bytes=64)
-                nc.scalar.copy(out=woven[s][:], in_=w_raw[(c, g)][:, :, u * P : u * P + HALF].rearrange("p t o -> p o t"))
+                lo, hi = wanted[0] * P, (wanted[-1] + 1) * P
+                woven[s] = work.tile([P, HALF, PACK], BF16, name="woven", tag="woven", bufs=4, align_bytes=64)
+                nc.scalar.copy(out=woven[s][:, lo:hi, :], in_=w_raw[(c, g)][:, :, u * P + lo : u * P + hi].rearrange("p t o -> p o t"))
 
         def base(s, lo, hi):
-            if s >= WOVEN_FROM:
-                return woven[s][:, lo:hi, :]
-            c, g, u, kind = place(s, 0)
-            return w_raw[(c, g)][:, :, u * P + lo : u * P + hi].rearrange("p t o -> p o t")
+            if s in UNWOVEN:
+                c, g, u, kind = place(s, 0)
+                return w_raw[(c, g)][:, :, u * P + lo : u * P + hi].rearrange("p t o -> p o t")
+            return woven[s][:, lo:hi, :]
 
         def empty_block(s, i):
             c, g, u, kind = place(s, i)
@@ -255,14 +264,19 @@ def tile_vera_merged_layer_s13_kernel(tc, x_words, x_scales, a, bmat_bytes, bmat
             if u == 0:
                 wm[row] = work.tile([P, CHUNK, PACK], BF16, name="wm", tag="wm", bufs=3, align_bytes=64)
             if i == 0:
-                prods[s] = work.tile([P, HALF, PACK], F32, name="prod", tag="prod", bufs=2) if "P" in KINDS[row][u : u + 2] else None
+                prods[s] = work.tile([P, HALF, PACK], F32, name="prod", tag="prod", bufs=3) if "P" in KINDS[row][u : u + 2] else None
             delta = banks[(s, i)][:].rearrange("p t o -> p o t")
             if kind == "A":
                 nc.vector.tensor_copy(out=wm[row][:, u * P : (u + 1) * P, :], in_=delta)
+            elif kind == "S":
+                nc.scalar.copy(out=wm[row][:, u * P : (u + 1) * P, :], in_=delta)
+            elif kind == "U":
+                raw = w_raw[(c, g)][:, :, u * P : (u + 1) * P].rearrange("p t o -> p o t")
+                nc.vector.tensor_tensor(out=wm[row][:, u * P : (u + 1) * P, :], in0=delta, in1=raw, op=ADD)
             elif kind == "T":
                 nc.vector.tensor_tensor(out=wm[row][:, u * P : (u + 1) * P, :], in0=delta, in1=base(s, i * P, (i + 1) * P), op=ADD)
             else:
-                o0 = (c - 1) * CHUNK + u * P
+                o0 = c * CHUNK + u * P
                 nc.vector.tensor_tensor(
                     out=prods[s][:, i * P : (i + 1) * P, :],
                     in0=delta,
@@ -308,11 +322,18 @@ def tile_vera_merged_layer_s13_kernel(tc, x_words, x_scales, a, bmat_bytes, bmat
             copy(out=res[:], in_=y_banks[(c, m)][:])
             nc.sync.dma_start(out=out_view[m][:, c * CHUNK : (c + 1) * CHUNK], in_=res[:])
 
+        def warm_up(count):
+            for i in range(count):
+                nc.tensor.matmul(v_bank(0, 1)[:], lhsT=warm[:], rhs=warm[:].unsqueeze(1).to_broadcast([P, PACK, P]), start=True, stop=True)
+
         nc.scalar.activation(out=ident_bf[:], in_=ident[:], func=COPY)
-        ad_turn(0)
+        warm_up(WARM[0])
+        ad_turn(0, 0)
+        ad_turn(0, 1)
+        warm_up(WARM[1])
         gain_banks = []
-        for c in range(1, CHUNKS):
-            bank = v_bank(1, c - 1)
+        for c in range(G0, CHUNKS):
+            bank = v_bank(1, c - 1) if c else v_bank(0, 1)
             gain_banks.append(bank)
             for u in range(PACK):
                 ob = c * PACK + u
@@ -325,73 +346,85 @@ def tile_vera_merged_layer_s13_kernel(tc, x_words, x_scales, a, bmat_bytes, bmat
             b_widen_vector(0, t)
             b_widen_scalar(0, t + 2)
         ad_product(0, 1)
-        ad_turn(1)
+        ad_turn(1, 0)
+        ad_turn(1, 1)
+        warm_up(WARM[2])
         b_interleave(nc.vector.tensor_copy, 0, 0)
         b_interleave(nc.scalar.copy, 0, 1)
         nc.scalar.copy(out=b_col[:], in_=col_bank[:, 0, 0:BLOCKS])
+        for c in range(G0, CHUNKS):
+            nc.scalar.copy(out=bg[:, c * CHUNK : (c + 1) * CHUNK], in_=gain_banks[c - G0][:].rearrange("p u o -> p (u o)"))
         ad_quantise(0)
         b_quantise(0, 0, HALF)
-        turned_product(0)
         lay_base(0)
+        turned_product(0)
         turned_scale(0)
         ad_product(1, 0)
         b_quantise(0, HALF, CHUNK)
         ad_product(1, 1)
         turned_product(1)
+        plain_product(0)
         turned_scale(1)
-        for c in range(1, CHUNKS):
-            nc.scalar.copy(out=bg[:, (c - 1) * CHUNK : c * CHUNK], in_=gain_banks[c - 1][:].rearrange("p u o -> p (u o)"))
+        weave(0)
+        weave(1)
         turn_back(0)
+        ad_turn(2, 0)
         ad_quantise(1)
-        ad_turn(2)
 
-        b_jobs = {}
-        for c in range(1, CHUNKS):
-            s0 = (c - 1) * 8
-            b_jobs[s0] = [lambda c=c: b_tiles(c), lambda c=c: b_widen_scalar(c, 0), lambda c=c: b_widen_scalar(c, 1)]
-            b_jobs[s0 + 1] = [lambda c=c: b_widen_scalar(c, 2), lambda c=c: b_widen_scalar(c, 3)]
-            b_jobs[s0 + 2] = [lambda c=c: b_interleave(nc.scalar.copy, c, 0)]
-            b_jobs[s0 + 3] = [lambda c=c: b_interleave(nc.scalar.copy, c, 1)]
+        def b_job(job):
+            c, what, part, engine = job
+            if c not in b_wide:
+                b_tiles(c)
+            if what == "w":
+                (b_widen_scalar if engine == "S" else b_widen_vector)(c, part)
+            else:
+                b_interleave(nc.scalar.copy if engine == "S" else nc.vector.tensor_copy, c, part)
+
         todo = []
         to_store = []
         last = CHUNKS - 1
         for s in range(STEPS):
             empty_block(s, 0)
+            if s < 4:
+                ad_product(s // 2 + 2, s % 2)
             if s > 0:
                 add_plain(s - 1)
             empty_block(s, 1)
-            if s in (0, 2):
-                ad_product(s // 2 + 2, 0)
-                ad_product(s // 2 + 2, 1)
             if s in (1, 3):
                 ad_quantise(s // 2 + 2)
-            if s % 8 == 5 and s // 8 + 1 < CHUNKS:
-                b_quantise(s // 8 + 1, 0, CHUNK)
+            for job in B_JOBS.get(s, []):
+                if job[3] == "V":
+                    b_job(job)
+            for c in range(1, CHUNKS):
+                if s == B_QUANT[c]:
+                    b_quantise(c, 0, CHUNK)
             if s % 2 == 0 and s > 0:
                 wm_quantise(s // 2 - 1)
-                if s % 8 == 0:
-                    todo.extend((s // 8 - 1, m) for m in range(T_TILES))
+
+            if s % 8 == 1 and s > 8:
+                todo.extend((s // 8 - 1, m) for m in range(T_TILES))
             if s + 1 < STEPS:
                 plain_product(s + 1)
             if s + 2 < STEPS:
                 turned_product(s + 2)
+            if s < 3:
+                ad_turn((s + 1) // 2 + 2, (s + 1) % 2)
             if s + 1 < STEPS:
                 lay_base(s + 1)
                 turn_back(s + 1)
-            if s == 1:
-                ad_turn(3)
             if s + 2 < STEPS:
                 turned_scale(s + 2)
             for item in to_store:
                 y_store(*item, nc.scalar.copy)
-            to_store = todo[: 2 if (s > 16 and s % 2) else 1]
+            to_store = todo[: 2 if s in DOUBLE else 1]
             todo = todo[len(to_store) :]
             for item in to_store:
                 y_passes(*item, range(GROUPS))
-            if s + 1 < STEPS:
-                weave(s + 1)
-            for job in b_jobs.get(s, []):
-                job()
+            if s + 2 < STEPS:
+                weave(s + 2)
+            for job in B_JOBS.get(s, []):
+                if job[3] == "S":
+                    b_job(job)
             if s == STEPS - 2:
                 for item in to_store:
                     y_store(*item, nc.scalar.copy)
@@ -402,9 +435,12 @@ def tile_vera_merged_layer_s13_kernel(tc, x_words, x_scales, a, bmat_bytes, bmat
                 for m in range(4):
                     y_passes(last, m, range(2, 3))
         add_plain(STEPS - 1)
-        for m in range(4, 8):
+        for m in range(4, OPEN):
             y_passes(last, m, range(3), v_bank(m // 2, m % 2, (P, CHUNK)))
         wm_quantise(STEPS // 2 - 1)
         for m in range(T_TILES):
-            y_passes(last, m, range(3, 4))
+            if m < OPEN:
+                y_passes(last, m, range(3, 4))
+            else:
+                y_passes(last, m, range(4), v_bank(m // 2, m % 2, (P, CHUNK)))
             y_store(last, m, nc.scalar.copy if m % 2 == 0 else nc.vector.tensor_copy)

@@ -29,12 +29,15 @@ FLOPS = 2 * IN * R * OUT + 2 * T * IN * OUT
 
 
 STEPS = CHUNKS * GROUPS * 2
-KINDS = ["USUS","USUS","USUS","USUS","PPPS","PPPS","PPPS","PPPS","PPPS","PPPP","PPPP","PPPP"]
+KINDS = ["USUS","USUS","ASAS","ASAS","PPPS","PPPS","PPPS","PPPS","PPPS","PPPP","PPPP","PPPP"]
 B_QUANT = {1: 6,2: 14}
 WARM = [0,0,0]
 B_JOBS = {0: [[1,"w",0,"S"]],1: [[1,"w",1,"S"]],2: [[1,"w",2,"S"]],3: [[1,"w",3,"S"]],4: [[1,"i",0,"V"],[2,"w",0,"S"]],5: [[1,"i",1,"V"],[2,"w",1,"S"]],6: [[2,"w",2,"V"],[2,"w",3,"V"]],7: [[2,"i",0,"V"],[2,"i",1,"V"]]}
-UNWOVEN = ()
+UNWOVEN = []
 G0 = 1
+BACK_FIRST = ()
+G_ROWS = ()
+Y_AT = 1
 OPEN = 6
 DOUBLE = (17, 19, 21)
 
@@ -249,14 +252,23 @@ def tile_vera_merged_layer_s13_kernel(tc, x_words, x_scales, a, bmat_bytes, bmat
             if wanted and s not in UNWOVEN:
                 c, g, u, kind = place(s, 0)
                 lo, hi = wanted[0] * P, (wanted[-1] + 1) * P
-                woven[s] = work.tile([P, HALF, PACK], BF16, name="woven", tag="woven", bufs=4, align_bytes=64)
-                nc.scalar.copy(out=woven[s][:, lo:hi, :], in_=w_raw[(c, g)][:, :, u * P + lo : u * P + hi].rearrange("p t o -> p o t"))
+                if s // 2 in G_ROWS and s % 2 == 0:
+                    woven[s] = work.tile([P, P, PACK], F32, name="woven", tag="shared%d" % (s // 2 % 2), bufs=1, align_bytes=64)
+                else:
+                    woven[s] = work.tile([P, P, PACK], F32, name="woven", tag="woven", bufs=3, align_bytes=64)
+                nc.scalar.copy(
+                    out=woven[s][:, lo // 2 : hi // 2, :],
+                    in_=w_raw[(c, g)][:].bitcast(F32)[:, :, (u * P + lo) // 2 : (u * P + hi) // 2].rearrange("p t m -> p m t"),
+                )
 
         def base(s, lo, hi):
             if s in UNWOVEN:
                 c, g, u, kind = place(s, 0)
-                return w_raw[(c, g)][:, :, u * P + lo : u * P + hi].rearrange("p t o -> p o t")
-            return woven[s][:, lo:hi, :]
+                return w_raw[(c, g)][:, :, u * P + lo : u * P + hi].rearrange("p t (m e) -> p m e t", e=2)
+            return woven[s][:].bitcast(BF16)[:, lo // 2 : hi // 2, :].rearrange("p m (t e) -> p m e t", e=2)
+
+        def pairs(ap):
+            return ap.rearrange("p (m e) t -> p m e t", e=2)
 
         def empty_block(s, i):
             c, g, u, kind = place(s, i)
@@ -264,7 +276,7 @@ def tile_vera_merged_layer_s13_kernel(tc, x_words, x_scales, a, bmat_bytes, bmat
             if u == 0:
                 wm[row] = work.tile([P, CHUNK, PACK], BF16, name="wm", tag="wm", bufs=3, align_bytes=64)
             if i == 0:
-                prods[s] = work.tile([P, HALF, PACK], F32, name="prod", tag="prod", bufs=3) if "P" in KINDS[row][u : u + 2] else None
+                prods[s] = work.tile([P, HALF, PACK], F32, name="prod", tag="prod", bufs=4) if "P" in KINDS[row][u : u + 2] else None
             delta = banks[(s, i)][:].rearrange("p t o -> p o t")
             if kind == "A":
                 nc.vector.tensor_copy(out=wm[row][:, u * P : (u + 1) * P, :], in_=delta)
@@ -274,7 +286,7 @@ def tile_vera_merged_layer_s13_kernel(tc, x_words, x_scales, a, bmat_bytes, bmat
                 raw = w_raw[(c, g)][:, :, u * P : (u + 1) * P].rearrange("p t o -> p o t")
                 nc.vector.tensor_tensor(out=wm[row][:, u * P : (u + 1) * P, :], in0=delta, in1=raw, op=ADD)
             elif kind == "T":
-                nc.vector.tensor_tensor(out=wm[row][:, u * P : (u + 1) * P, :], in0=delta, in1=base(s, i * P, (i + 1) * P), op=ADD)
+                nc.vector.tensor_tensor(out=pairs(wm[row][:, u * P : (u + 1) * P, :]), in0=pairs(delta), in1=base(s, i * P, (i + 1) * P), op=ADD)
             else:
                 o0 = c * CHUNK + u * P
                 nc.vector.tensor_tensor(
@@ -290,13 +302,24 @@ def tile_vera_merged_layer_s13_kernel(tc, x_words, x_scales, a, bmat_bytes, bmat
                 c, g, u, kind = place(s, 0)
                 lo, hi = plain[0] * P, (plain[-1] + 1) * P
                 nc.vector.tensor_tensor(
-                    out=wm[s // 2][:, u * P + lo : u * P + hi, :],
-                    in0=prods[s][:, lo:hi, :],
+                    out=pairs(wm[s // 2][:, u * P + lo : u * P + hi, :]),
+                    in0=pairs(prods[s][:, lo:hi, :]),
                     in1=base(s, lo, hi),
                     op=ADD,
                 )
 
+        late = {}
+
+        def add_late(row):
+            late[row] = work.tile([P, HALF, PACK], BF16, name="late", tag="shared%d" % (row % 2), bufs=1, align_bytes=64)
+            nc.gpsimd.tensor_tensor(out=pairs(late[row][:]), in0=pairs(prods[2 * row + 1][:]), in1=base(2 * row + 1, 0, HALF), op=ADD)
+
         def wm_quantise(row):
+            if row in late:
+                for h, tile in enumerate((wm[row][:, 0:HALF, :], late[row][:])):
+                    cols = slice(row * CHUNK + h * HALF, row * CHUNK + (h + 1) * HALF)
+                    nc.vector.quantize_mx(out=w_cod[:, cols].bitcast(E4M3X4), scales=w_pla[:, cols], in_=tile.rearrange("p o t -> p (o t)"))
+                return
             cols = slice(row * CHUNK, (row + 1) * CHUNK)
             nc.vector.quantize_mx(out=w_cod[:, cols].bitcast(E4M3X4), scales=w_pla[:, cols], in_=wm[row][:].rearrange("p o t -> p (o t)"))
 
@@ -387,9 +410,20 @@ def tile_vera_merged_layer_s13_kernel(tc, x_words, x_scales, a, bmat_bytes, bmat
             empty_block(s, 0)
             if s < 4:
                 ad_product(s // 2 + 2, s % 2)
-            if s > 0:
+            if s > 0 and s // 2 not in G_ROWS and (s - 1) // 2 not in G_ROWS:
                 add_plain(s - 1)
+            if s > 0 and s % 2 == 1 and s // 2 not in G_ROWS and s // 2 - 1 in G_ROWS:
+                wm_quantise(s // 2 - 1)
             empty_block(s, 1)
+            if s // 2 in G_ROWS and s % 2 == 1:
+                if s // 2 - 1 not in G_ROWS:
+                    add_plain(s - 2)
+                    add_plain(s - 1)
+                    wm_quantise(s // 2 - 1)
+                else:
+                    wm_quantise(s // 2 - 1)
+                    add_plain(s - 1)
+                add_late(s // 2)
             if s in (1, 3):
                 ad_quantise(s // 2 + 2)
             for job in B_JOBS.get(s, []):
@@ -398,18 +432,21 @@ def tile_vera_merged_layer_s13_kernel(tc, x_words, x_scales, a, bmat_bytes, bmat
             for c in range(1, CHUNKS):
                 if s == B_QUANT[c]:
                     b_quantise(c, 0, CHUNK)
-            if s % 2 == 0 and s > 0:
+            if s % 2 == 0 and s > 0 and s // 2 not in G_ROWS and s // 2 - 1 not in G_ROWS:
                 wm_quantise(s // 2 - 1)
 
-            if s % 8 == 1 and s > 8:
+            if s % 8 == Y_AT and s > 8:
                 todo.extend((s // 8 - 1, m) for m in range(T_TILES))
             if s + 1 < STEPS:
                 plain_product(s + 1)
+            if s in BACK_FIRST:
+                lay_base(s + 1)
+                turn_back(s + 1)
             if s + 2 < STEPS:
                 turned_product(s + 2)
             if s < 3:
                 ad_turn((s + 1) // 2 + 2, (s + 1) % 2)
-            if s + 1 < STEPS:
+            if s + 1 < STEPS and s not in BACK_FIRST:
                 lay_base(s + 1)
                 turn_back(s + 1)
             if s + 2 < STEPS:

@@ -29,10 +29,10 @@ FLOPS = 2 * IN * R * OUT + 2 * T * IN * OUT
 
 
 STEPS = CHUNKS * GROUPS * 2
-KINDS = ["USUS","USUS","ASAS","ASAS","PPPS","PPPS","PPPS","PPPS","PPPS","PPPP","PPPP","PPPP"]
-B_QUANT = {1: 6,2: 14}
+KINDS = ["UUUU","UUUU","UUUU","UUUU","UUUU","PPPS","PPPS","PPPS","PPPS","PPPP","PPPP","PPPP"]
+B_QUANT = {1: 5,2: 14}
 WARM = [0,0,0]
-B_JOBS = {0: [[1,"w",0,"S"]],1: [[1,"w",1,"S"]],2: [[1,"w",2,"S"]],3: [[1,"w",3,"S"]],4: [[1,"i",0,"V"],[2,"w",0,"S"]],5: [[1,"i",1,"V"],[2,"w",1,"S"]],6: [[2,"w",2,"V"],[2,"w",3,"V"]],7: [[2,"i",0,"V"],[2,"i",1,"V"]]}
+B_JOBS = {0: [[1,"w",0,"S"],[1,"w",1,"S"]],1: [[1,"w",2,"S"],[1,"w",3,"S"]],2: [[1,"i",0,"S"]],3: [[1,"i",1,"S"]],4: [[2,"w",0,"S"]],5: [[2,"w",1,"S"]],6: [[2,"w",2,"S"]],7: [[2,"w",3,"S"]],8: [[2,"i",0,"S"]],10: [[2,"i",1,"S"]]}
 UNWOVEN = []
 G0 = 1
 BACK_FIRST = ()
@@ -407,9 +407,13 @@ def tile_vera_merged_layer_s13_kernel(tc, x_words, x_scales, a, bmat_bytes, bmat
         to_store = []
         last = CHUNKS - 1
         for s in range(STEPS):
-            empty_block(s, 0)
-            if s < 4:
+            if s < 4 and s % 2 == 1:
                 ad_product(s // 2 + 2, s % 2)
+            empty_block(s, 0)
+            if s < 4 and s % 2 == 0:
+                ad_product(s // 2 + 2, s % 2)
+            if s in (1, 3):
+                ad_quantise(s // 2 + 2)
             if s > 0 and s // 2 not in G_ROWS and (s - 1) // 2 not in G_ROWS:
                 add_plain(s - 1)
             if s > 0 and s % 2 == 1 and s // 2 not in G_ROWS and s // 2 - 1 in G_ROWS:
@@ -424,8 +428,6 @@ def tile_vera_merged_layer_s13_kernel(tc, x_words, x_scales, a, bmat_bytes, bmat
                     wm_quantise(s // 2 - 1)
                     add_plain(s - 1)
                 add_late(s // 2)
-            if s in (1, 3):
-                ad_quantise(s // 2 + 2)
             for job in B_JOBS.get(s, []):
                 if job[3] == "V":
                     b_job(job)
@@ -457,8 +459,10 @@ def tile_vera_merged_layer_s13_kernel(tc, x_words, x_scales, a, bmat_bytes, bmat
             todo = todo[len(to_store) :]
             for item in to_store:
                 y_passes(*item, range(GROUPS))
-            if s + 2 < STEPS:
+            if s + 2 < STEPS and not (s % 2 == 0 and s // 2 + 1 in G_ROWS):
                 weave(s + 2)
+            if s % 2 == 1 and (s + 1) // 2 in G_ROWS:
+                weave(s + 1)
             for job in B_JOBS.get(s, []):
                 if job[3] == "S":
                     b_job(job)

@@ -283,8 +283,12 @@ def tile_vera_merged_layer_s13_kernel(tc, x_words, x_scales, a, bmat_bytes, bmat
             elif kind == "S":
                 nc.scalar.copy(out=wm[row][:, u * P : (u + 1) * P, :], in_=delta)
             elif kind == "U":
-                raw = w_raw[(c, g)][:, :, u * P : (u + 1) * P].rearrange("p t o -> p o t")
-                nc.vector.tensor_tensor(out=wm[row][:, u * P : (u + 1) * P, :], in0=delta, in1=raw, op=ADD)
+                nc.vector.tensor_tensor(
+                    out=wm[row][:, u * P : (u + 1) * P, :].rearrange("p (c i) t -> p c t i", i=4),
+                    in0=banks[(s, i)][:].rearrange("p t (c i) -> p c t i", i=4),
+                    in1=w_raw[(c, g)][:, :, u * P : (u + 1) * P].rearrange("p t (c i) -> p c t i", i=4),
+                    op=ADD,
+                )
             elif kind == "T":
                 nc.vector.tensor_tensor(out=pairs(wm[row][:, u * P : (u + 1) * P, :]), in0=pairs(delta), in1=base(s, i * P, (i + 1) * P), op=ADD)
             else:

@@ -39,7 +39,7 @@ BACK_FIRST = ()
 G_ROWS = ()
 Y_AT = 1
 OPEN = 6
-DOUBLE = (17, 19, 21)
+DOUBLE = [19,20,21]
 
 
 def tile_vera_merged_layer_s13_kernel(tc, x_words, x_scales, a, bmat_bytes, bmat_scale, d_gain, b_gain, w0, out):
@@ -163,11 +163,17 @@ def tile_vera_merged_layer_s13_kernel(tc, x_words, x_scales, a, bmat_bytes, bmat
 
         def b_interleave(copy, c, h):
             cols = slice(h * HALF, (h + 1) * HALF)
-            copy(out=b_grp[c][:, cols, :], in_=b_wide[c][:, :, cols].rearrange("p t c -> p c t"))
+            copy(
+                out=b_grp[c][:, cols, :].rearrange("p (c i) t -> p c t i", i=4),
+                in_=b_wide[c][:, :, cols].rearrange("p t (c i) -> p c t i", i=4),
+            )
 
         def b_quantise(c, lo, hi):
             cols = slice(c * CHUNK + lo, c * CHUNK + hi)
             nc.vector.quantize_mx(out=b_cod[:, cols].bitcast(E4M3X4), scales=b_pla[:, cols], in_=b_grp[c][:, lo:hi, :].rearrange("p c t -> p (c t)"))
+
+        def gpsimd_copy(out, in_):
+            nc.gpsimd.tensor_scalar(out=out, in0=in_, scalar1=1.0, scalar2=0.0, op0=MULT, op1=ADD)
 
         def place(s, i):
             c, g = divmod(s // 2, GROUPS)
@@ -257,8 +263,8 @@ def tile_vera_merged_layer_s13_kernel(tc, x_words, x_scales, a, bmat_bytes, bmat
                 else:
                     woven[s] = work.tile([P, P, PACK], F32, name="woven", tag="woven", bufs=3, align_bytes=64)
                 nc.scalar.copy(
-                    out=woven[s][:, lo // 2 : hi // 2, :],
-                    in_=w_raw[(c, g)][:].bitcast(F32)[:, :, (u * P + lo) // 2 : (u * P + hi) // 2].rearrange("p t m -> p m t"),
+                    out=woven[s][:, lo // 2 : hi // 2, :].rearrange("p (c i) t -> p c t i", i=2),
+                    in_=w_raw[(c, g)][:].bitcast(F32)[:, :, (u * P + lo) // 2 : (u * P + hi) // 2].rearrange("p t (c i) -> p c t i", i=2),
                 )
 
         def base(s, lo, hi):
@@ -405,7 +411,7 @@ def tile_vera_merged_layer_s13_kernel(tc, x_words, x_scales, a, bmat_bytes, bmat
             if what == "w":
                 (b_widen_scalar if engine == "S" else b_widen_vector)(c, part)
             else:
-                b_interleave(nc.scalar.copy if engine == "S" else nc.vector.tensor_copy, c, part)
+                b_interleave({"S": nc.scalar.copy, "V": nc.vector.tensor_copy, "G": gpsimd_copy}[engine], c, part)
 
         todo = []
         to_store = []
@@ -468,7 +474,7 @@ def tile_vera_merged_layer_s13_kernel(tc, x_words, x_scales, a, bmat_bytes, bmat
             if s % 2 == 1 and (s + 1) // 2 in G_ROWS:
                 weave(s + 1)
             for job in B_JOBS.get(s, []):
-                if job[3] == "S":
+                if job[3] in "SG":
                     b_job(job)
             if s == STEPS - 2:
                 for item in to_store:

@@ -37,7 +37,7 @@ UNWOVEN = []
 G0 = 1
 BACK_FIRST = ()
 G_ROWS = ()
-Y_AT = 1
+Y_AT = (9, 17)
 OPEN = 6
 DOUBLE = [19,20,21]
 
@@ -209,7 +209,28 @@ def tile_vera_merged_layer_s13_kernel(tc, x_words, x_scales, a, bmat_bytes, bmat
                     ob = c * PACK + u
                     nc.scalar.activation(out=tile[:], in_=banks[(s, i)][:], func=COPY, scale=b_col[:, ob : ob + 1])
 
+        def wide(s):
+            return KINDS[s // 2][2 * (s % 2) : 2 * (s % 2) + 2] == "PP"
+
         def plain_product(s):
+            if wide(s):
+                c, g, u, kind = place(s, 0)
+                cols = slice(c * CHUNK + u * P, c * CHUNK + u * P + HALF)
+                for i in range(2):
+                    bank = v_bank(s, i, (P, 2, HALF))
+                    banks[(s, i)] = bank
+                    for e in range(2):
+                        rows = slice(g * CHUNK + (2 * i + e) * P, g * CHUNK + (2 * i + e + 1) * P)
+                        nc.tensor.matmul_mx(
+                            out=bank[:, e, :],
+                            lhsT=a_cod[:, rows].bitcast(E4M3X4),
+                            lhsT_scale=a_pla[:, rows],
+                            rhs=b_cod[:, cols].bitcast(E4M3X4),
+                            rhs_scale=b_pla[:, cols],
+                            start=True,
+                            stop=True,
+                        )
+                return
             for i in range(2):
                 c, g, u, kind = place(s, i)
                 if kind == "P":
@@ -284,6 +305,15 @@ def tile_vera_merged_layer_s13_kernel(tc, x_words, x_scales, a, bmat_bytes, bmat
             if i == 0:
                 prods[s] = work.tile([P, HALF, PACK], F32, name="prod", tag="prod", bufs=4) if "P" in KINDS[row][u : u + 2] else None
             delta = banks[(s, i)][:].rearrange("p t o -> p o t")
+            if wide(s):
+                o0 = c * CHUNK + 2 * (s % 2) * P
+                nc.vector.tensor_tensor(
+                    out=prods[s][:].rearrange("p o t -> p (o t)").rearrange("p (u o e) -> p u o e", u=2, e=2)[:, i, :, :],
+                    in0=delta,
+                    in1=bg[:, o0 : o0 + HALF].unsqueeze(2).to_broadcast([P, HALF, 2]),
+                    op=MULT,
+                )
+                return
             if kind == "A":
                 nc.vector.tensor_copy(out=wm[row][:, u * P : (u + 1) * P, :], in_=delta)
             elif kind == "S":
@@ -308,7 +338,15 @@ def tile_vera_merged_layer_s13_kernel(tc, x_words, x_scales, a, bmat_bytes, bmat
 
         def add_plain(s):
             plain = [i for i in range(2) if place(s, i)[3] == "P"]
-            if plain:
+            if wide(s):
+                lo = s % 2 * HALF
+                nc.vector.tensor_tensor(
+                    out=wm[s // 2][:, lo : lo + HALF, :].rearrange("p (m f) (u e) -> p m f u e", f=2, u=2),
+                    in0=prods[s][:].rearrange("p o t -> p (o t)").rearrange("p (u m f e) -> p m f u e", u=2, f=2, e=2),
+                    in1=woven[s][:].bitcast(BF16).rearrange("p m (u e f) -> p m f u e", u=2, f=2),
+                    op=ADD,
+                )
+            elif plain:
                 c, g, u, kind = place(s, 0)
                 lo, hi = plain[0] * P, (plain[-1] + 1) * P
                 nc.vector.tensor_tensor(
@@ -332,6 +370,11 @@ def tile_vera_merged_layer_s13_kernel(tc, x_words, x_scales, a, bmat_bytes, bmat
                 return
             cols = slice(row * CHUNK, (row + 1) * CHUNK)
             nc.vector.quantize_mx(out=w_cod[:, cols].bitcast(E4M3X4), scales=w_pla[:, cols], in_=wm[row][:].rearrange("p o t -> p (o t)"))
+
+        def half_quantise(s):
+            cols = slice(s * HALF, (s + 1) * HALF)
+            part = wm[s // 2][:, s % 2 * HALF : (s % 2 + 1) * HALF, :]
+            nc.vector.quantize_mx(out=w_cod[:, cols].bitcast(E4M3X4), scales=w_pla[:, cols], in_=part.rearrange("p o t -> p (o t)"))
 
         y_banks = {}
 
@@ -447,7 +490,7 @@ def tile_vera_merged_layer_s13_kernel(tc, x_words, x_scales, a, bmat_bytes, bmat
             if s % 2 == 0 and s > 0 and s // 2 not in G_ROWS and s // 2 - 1 not in G_ROWS:
                 wm_quantise(s // 2 - 1)
 
-            if s % 8 == Y_AT and s > 8:
+            if s in Y_AT:
                 todo.extend((s // 8 - 1, m) for m in range(T_TILES))
             if s + 1 < STEPS:
                 plain_product(s + 1)
@@ -485,10 +528,11 @@ def tile_vera_merged_layer_s13_kernel(tc, x_words, x_scales, a, bmat_bytes, bmat
             if s == STEPS - 1:
                 for m in range(4):
                     y_passes(last, m, range(2, 3))
+        half_quantise(STEPS - 2)
         add_plain(STEPS - 1)
         for m in range(4, OPEN):
             y_passes(last, m, range(3), v_bank(m // 2, m % 2, (P, CHUNK)))
-        wm_quantise(STEPS // 2 - 1)
+        half_quantise(STEPS - 1)
         for m in range(T_TILES):
             if m < OPEN:
                 y_passes(last, m, range(3, 4))

@@ -17,29 +17,26 @@ COPY = mybir.ActivationFunctionType.Copy
 
 T, IN, R, OUT = 1024, 2048, 512, 1536
 P = 128
-PACK = 4
-GROUPS = IN // (P * PACK)
-CHUNK = 512
-CHUNKS = OUT // CHUNK
-HALF = 256
-BLOCKS = OUT // P
+SLOTS = 4
+GROUPS = IN // (P * SLOTS)
+PANEL = 512
+PANELS = OUT // PANEL
+HALF = PANEL // 2
+PIECES = OUT // P
 T_TILES = T // P
+ROWS = PANELS * GROUPS
+STEPS = 2 * ROWS
+PANEL_STEPS = 2 * GROUPS
+RUN = 4
 
 FLOPS = 2 * IN * R * OUT + 2 * T * IN * OUT
 
-
-STEPS = CHUNKS * GROUPS * 2
-KINDS = ["UUUU","UUUU","UUUU","UUUU","UUUU","PPPS","PPPS","PPPS","PPPS","PPPP","PPPP","PPPP"]
-B_QUANT = {1: 5,2: 14}
-WARM = [0,0,0]
-B_JOBS = {0: [[1,"w",0,"S"],[1,"w",1,"S"]],1: [[1,"w",2,"S"],[1,"w",3,"S"]],2: [[1,"i",0,"S"]],3: [[1,"i",1,"S"]],4: [[2,"w",0,"S"]],5: [[2,"w",1,"S"]],6: [[2,"w",2,"S"]],7: [[2,"w",3,"S"]],8: [[2,"i",0,"S"]],10: [[2,"i",1,"S"]]}
-UNWOVEN = []
-G0 = 1
-BACK_FIRST = ()
-G_ROWS = ()
-Y_AT = (9, 17)
-OPEN = 6
-DOUBLE = [19,20,21]
+TURNED_ROWS = 5
+MIXED_ROWS = 4
+KINDS = ["VVVV"] * TURNED_ROWS + ["PPPS"] * MIXED_ROWS + ["PPPP"] * (ROWS - TURNED_ROWS - MIXED_ROWS)
+EARLY_FIRST = 2
+EARLY_LAST = 6
+ALIGN = 64
 
 
 def tile_vera_merged_layer_s13_kernel(tc, x_words, x_scales, a, bmat_bytes, bmat_scale, d_gain, b_gain, w0, out):
@@ -51,38 +48,42 @@ def tile_vera_merged_layer_s13_kernel(tc, x_words, x_scales, a, bmat_bytes, bmat
         ctx.enter_context(tc.manual_schedule())
 
         gain_rows = keep.tile([P, P], BF16, name="gain_rows")
-        warm = keep.tile([P, P], BF16, name="warm")
         ident = keep.tile([P, P], F32, name="ident")
         ident_bf = keep.tile([P, P], BF16, name="ident_bf")
-        b_sc = keep.tile([P, PACK], F32, name="b_sc")
-        d_col = keep.tile([P, PACK], BF16, name="d_col")
-        b_col = keep.tile([P, BLOCKS], F32, name="b_col")
-        bg = keep.tile([P, OUT], BF16, name="bg")
-        b_raw = [keep.tile([P, PACK, CHUNK], U8, name="b_raw%d" % c, align_bytes=64) for c in range(CHUNKS)]
-        b_cod = keep.tile([P, OUT], U32, name="b_cod", align_bytes=64)
-        b_pla = keep.tile([P, OUT], U8, name="b_pla", align_bytes=64)
-        a_raw = {(g, h): keep.tile([P, 2, R], BF16, name="a_raw%d%d" % (g, h), align_bytes=64) for g in range(GROUPS) for h in range(2)}
-        a_cod = keep.tile([P, GROUPS * CHUNK], U32, name="a_cod", align_bytes=64)
-        a_pla = keep.tile([P, GROUPS * CHUNK], U8, name="a_pla", align_bytes=64)
-        w_raw = {(c, g): keep.tile([P, PACK, CHUNK], BF16, name="w_raw%d%d" % (c, g), align_bytes=64) for c in range(CHUNKS) for g in range(GROUPS)}
-        w_cod = keep.tile([P, GROUPS * OUT], U32, name="w_cod", align_bytes=64)
-        w_pla = keep.tile([P, GROUPS * OUT], U8, name="w_pla", align_bytes=64)
-        x_cod = keep.tile([P, GROUPS, 2 * T], U8, name="x_cod", align_bytes=64)
-        x_pla = keep.tile([P, GROUPS, T], U8, name="x_pla", align_bytes=64)
+        b_sc = keep.tile([P, SLOTS], F32, name="b_sc")
+        d_col = keep.tile([P, SLOTS], BF16, name="d_col")
+        gain_col = keep.tile([P, PIECES], F32, name="gain_col")
+        gain_all = keep.tile([P, OUT], BF16, name="gain_all")
+        b_raw = [keep.tile([P, SLOTS, PANEL], U8, name="b_raw%d" % c, align_bytes=ALIGN) for c in range(PANELS)]
+        b_cod = keep.tile([P, OUT], U32, name="b_cod", align_bytes=ALIGN)
+        b_pla = keep.tile([P, OUT], U8, name="b_pla", align_bytes=ALIGN)
+        a_raw = {(g, h): keep.tile([P, 2, R], BF16, name="a_raw%d%d" % (g, h), align_bytes=ALIGN) for g in range(GROUPS) for h in range(2)}
+        a_cod = keep.tile([P, IN], U32, name="a_cod", align_bytes=ALIGN)
+        a_pla = keep.tile([P, IN], U8, name="a_pla", align_bytes=ALIGN)
+        w_raw = {
+            (c, g): keep.tile([P, SLOTS, PANEL], BF16, name="w_raw%d%d" % (c, g), align_bytes=ALIGN) for c in range(PANELS) for g in range(GROUPS)
+        }
+        w_cod = keep.tile([P, ROWS * PANEL], U32, name="w_cod", align_bytes=ALIGN)
+        w_pla = keep.tile([P, ROWS * PANEL], U8, name="w_pla", align_bytes=ALIGN)
+        x_cod = keep.tile([P, GROUPS, 2 * T], U8, name="x_cod", align_bytes=ALIGN)
+        x_pla = keep.tile([P, GROUPS, T], U8, name="x_pla", align_bytes=ALIGN)
 
-        a_view = a.rearrange("(g p t) r -> g p t r", p=P, t=PACK)
-        w_view = w0.rearrange("(g p t) o -> g p t o", p=P, t=PACK)
-        b_view = bmat_bytes.rearrange("(p t) o -> p t o", t=PACK)
+        a_view = a.rearrange("(g p t) r -> g p t r", p=P, t=SLOTS)
+        w_view = w0.rearrange("(g p t) o -> g p t o", p=P, t=SLOTS)
+        b_view = bmat_bytes.rearrange("(p t) o -> p t o", t=SLOTS)
         out_view = out.rearrange("(m p) o -> m p o", p=P)
 
         ring = [0]
+        open_tiles = {}
 
-        def s_bank(shape, dtype=F32):
+        def ring_bank(shape):
             ring[0] = (ring[0] + 1) % 4
-            return psum.tile(shape, dtype, name="s_bank", tag="s_bank%d" % ring[0])
+            while ring[0] in open_tiles.values():
+                ring[0] = (ring[0] + 1) % 4
+            return psum.tile(shape, F32, name="ring_bank", tag="ring_bank%d" % ring[0])
 
-        def v_bank(s, i, shape=(P, PACK, P)):
-            return psum.tile(list(shape), F32, name="v_bank", tag="v_bank%d" % (2 * (s % 2) + i))
+        def step_bank(s, i, shape):
+            return psum.tile(shape, F32, name="step_bank", tag="step_bank%d" % (2 * (s % 2) + i))
 
         nc.vector.memset(gain_rows[:], 0.0)
         make_identity(nc, ident[:])
@@ -93,16 +94,16 @@ def tile_vera_merged_layer_s13_kernel(tc, x_words, x_scales, a, bmat_bytes, bmat
                 nc.sync.dma_start(out=a_raw[(g, h)][:], in_=a_view[g][:, 2 * h : 2 * h + 2, :])
 
         def load_b(c):
-            nc.sync.dma_start(out=b_raw[c][:], in_=b_view[:, :, c * CHUNK : (c + 1) * CHUNK])
+            nc.sync.dma_start(out=b_raw[c][:], in_=b_view[:, :, c * PANEL : (c + 1) * PANEL])
 
         def load_w(c, g):
-            nc.sync.dma_start(out=w_raw[(c, g)][:], in_=w_view[g][:, :, c * CHUNK : (c + 1) * CHUNK])
+            nc.sync.dma_start(out=w_raw[(c, g)][:], in_=w_view[g][:, :, c * PANEL : (c + 1) * PANEL])
 
         load_a(0)
-        nc.sync.dma_start(out=b_sc[:], in_=bmat_scale.rearrange("(p t) o -> p (t o)", t=PACK))
-        nc.sync.dma_start(out=d_col[:], in_=d_gain.rearrange("(p t) -> p t", t=PACK))
+        nc.sync.dma_start(out=b_sc[:], in_=bmat_scale.rearrange("(p t) o -> p (t o)", t=SLOTS))
+        nc.sync.dma_start(out=d_col[:], in_=d_gain.rearrange("(p t) -> p t", t=SLOTS))
         load_b(0)
-        nc.sync.dma_start(out=gain_rows[0:BLOCKS, :], in_=b_gain.rearrange("(c p) -> c p", p=P))
+        nc.sync.dma_start(out=gain_rows[0:PIECES, :], in_=b_gain.rearrange("(j p) -> j p", p=P))
         load_a(1)
         load_w(0, 0)
         load_a(2)
@@ -117,20 +118,24 @@ def tile_vera_merged_layer_s13_kernel(tc, x_words, x_scales, a, bmat_bytes, bmat
                 in_=x_scales[:, 4 * q : 4 * q + 4, :].bitcast(I32).rearrange("g q n -> q g n"),
             )
         load_b(2)
-        load_w(1, 0)
-        load_w(1, 1)
         nc.sync.dma_start(out=x_cod[:].bitcast(I32), in_=x_words.bitcast(I32).rearrange("g p n -> p g n"))
-        load_w(1, 2)
-        load_w(1, 3)
-        for g in range(GROUPS):
-            load_w(2, g)
+        for c in range(1, PANELS):
+            for g in range(GROUPS):
+                load_w(c, g)
+
+        def quantise(codes, plane, at, grouped):
+            cols = slice(at, at + grouped.shape[1])
+            nc.vector.quantize_mx(out=codes[:, cols].bitcast(E4M3X4), scales=plane[:, cols], in_=grouped.rearrange("p n t -> p (n t)"))
+
+        def mx_pass(bank, lhs, lhs_plane, rhs, rhs_plane, start=True, stop=True):
+            nc.tensor.matmul_mx(out=bank, lhsT=lhs, lhsT_scale=lhs_plane, rhs=rhs, rhs_scale=rhs_plane, start=start, stop=stop)
 
         ad_banks, ad_grp = {}, {}
 
         def ad_turn(g, h):
             if h == 0:
-                ad_grp[g] = work.tile([P, CHUNK, PACK], BF16, name="ad_grp", tag="ad_grp", align_bytes=64)
-            bank = s_bank([P, 2, HALF])
+                ad_grp[g] = work.tile([P, PANEL, SLOTS], BF16, name="ad_grp", tag="ad_grp", align_bytes=ALIGN)
+            bank = ring_bank([P, 2, HALF])
             ad_banks[(g, h)] = bank
             for i in range(2):
                 words = a_raw[(g, h)][:, i, :].bitcast(F32)
@@ -146,14 +151,13 @@ def tile_vera_merged_layer_s13_kernel(tc, x_words, x_scales, a, bmat_bytes, bmat
             )
 
         def ad_quantise(g):
-            cols = slice(g * CHUNK, (g + 1) * CHUNK)
-            nc.vector.quantize_mx(out=a_cod[:, cols].bitcast(E4M3X4), scales=a_pla[:, cols], in_=ad_grp[g][:].rearrange("p n t -> p (n t)"))
+            quantise(a_cod, a_pla, g * PANEL, ad_grp[g][:])
 
         b_wide, b_grp = {}, {}
 
         def b_tiles(c):
-            b_wide[c] = work.tile([P, PACK, CHUNK], BF16, name="b_wide", tag="b_wide", bufs=2, align_bytes=64)
-            b_grp[c] = work.tile([P, CHUNK, PACK], BF16, name="b_grp", tag="b_grp", bufs=2, align_bytes=64)
+            b_wide[c] = work.tile([P, SLOTS, PANEL], BF16, name="b_wide", tag="b_wide", align_bytes=ALIGN)
+            b_grp[c] = work.tile([P, PANEL, SLOTS], BF16, name="b_grp", tag="b_grp", align_bytes=ALIGN)
 
         def b_widen_scalar(c, t):
             nc.scalar.activation(out=b_wide[c][:, t, :], in_=b_raw[c][:, t, :].bitcast(E4M3), func=COPY, scale=b_sc[:, t : t + 1])
@@ -164,258 +168,188 @@ def tile_vera_merged_layer_s13_kernel(tc, x_words, x_scales, a, bmat_bytes, bmat
         def b_interleave(copy, c, h):
             cols = slice(h * HALF, (h + 1) * HALF)
             copy(
-                out=b_grp[c][:, cols, :].rearrange("p (c i) t -> p c t i", i=4),
-                in_=b_wide[c][:, :, cols].rearrange("p t (c i) -> p c t i", i=4),
+                out=b_grp[c][:, cols, :].rearrange("p (n i) t -> p n t i", i=RUN),
+                in_=b_wide[c][:, :, cols].rearrange("p t (n i) -> p n t i", i=RUN),
             )
 
         def b_quantise(c, lo, hi):
-            cols = slice(c * CHUNK + lo, c * CHUNK + hi)
-            nc.vector.quantize_mx(out=b_cod[:, cols].bitcast(E4M3X4), scales=b_pla[:, cols], in_=b_grp[c][:, lo:hi, :].rearrange("p c t -> p (c t)"))
-
-        def gpsimd_copy(out, in_):
-            nc.gpsimd.tensor_scalar(out=out, in0=in_, scalar1=1.0, scalar2=0.0, op0=MULT, op1=ADD)
+            quantise(b_cod, b_pla, c * PANEL + lo, b_grp[c][:, lo:hi, :])
 
         def place(s, i):
             c, g = divmod(s // 2, GROUPS)
             u = 2 * (s % 2) + i
             return c, g, u, KINDS[s // 2][u]
 
-        banks, scaled, prods, wm, turned, woven = {}, {}, {}, {}, {}, {}
+        def both_plain(s):
+            return place(s, 0)[3] == "P" and place(s, 1)[3] == "P"
+
+        products, scaled, banks, gained, woven, wm = {}, {}, {}, {}, {}, {}
+
+        def a_operand(lo, hi):
+            return a_cod[:, lo:hi].bitcast(E4M3X4), a_pla[:, lo:hi]
+
+        def b_operand(lo, hi):
+            return b_cod[:, lo:hi].bitcast(E4M3X4), b_pla[:, lo:hi]
 
         def turned_product(s):
             for i in range(2):
                 c, g, u, kind = place(s, i)
                 if kind != "P":
-                    cols = slice(c * CHUNK + u * P, c * CHUNK + (u + 1) * P)
-                    rows = slice(g * CHUNK, (g + 1) * CHUNK)
-                    bank = s_bank([P, CHUNK])
-                    banks[(s, i)] = bank
-                    nc.tensor.matmul_mx(
-                        out=bank[:],
-                        lhsT=b_cod[:, cols].bitcast(E4M3X4),
-                        lhsT_scale=b_pla[:, cols],
-                        rhs=a_cod[:, rows].bitcast(E4M3X4),
-                        rhs_scale=a_pla[:, rows],
-                        start=True,
-                        stop=True,
-                    )
+                    o0 = c * PANEL + u * P
+                    products[(s, i)] = ring_bank([P, PANEL])
+                    mx_pass(products[(s, i)][:], *b_operand(o0, o0 + P), *a_operand(g * PANEL, (g + 1) * PANEL))
 
         def turned_scale(s):
             for i in range(2):
                 c, g, u, kind = place(s, i)
                 if kind != "P":
-                    tile = work.tile([P, CHUNK], F32, name="scaled", tag="scaled", bufs=4)
-                    scaled[(s, i)] = tile
-                    ob = c * PACK + u
-                    nc.scalar.activation(out=tile[:], in_=banks[(s, i)][:], func=COPY, scale=b_col[:, ob : ob + 1])
-
-        def wide(s):
-            return KINDS[s // 2][2 * (s % 2) : 2 * (s % 2) + 2] == "PP"
-
-        def plain_product(s):
-            if wide(s):
-                c, g, u, kind = place(s, 0)
-                cols = slice(c * CHUNK + u * P, c * CHUNK + u * P + HALF)
-                for i in range(2):
-                    bank = v_bank(s, i, (P, 2, HALF))
-                    banks[(s, i)] = bank
-                    for e in range(2):
-                        rows = slice(g * CHUNK + (2 * i + e) * P, g * CHUNK + (2 * i + e + 1) * P)
-                        nc.tensor.matmul_mx(
-                            out=bank[:, e, :],
-                            lhsT=a_cod[:, rows].bitcast(E4M3X4),
-                            lhsT_scale=a_pla[:, rows],
-                            rhs=b_cod[:, cols].bitcast(E4M3X4),
-                            rhs_scale=b_pla[:, cols],
-                            start=True,
-                            stop=True,
-                        )
-                return
-            for i in range(2):
-                c, g, u, kind = place(s, i)
-                if kind == "P":
-                    cols = slice(c * CHUNK + u * P, c * CHUNK + (u + 1) * P)
-                    bank = v_bank(s, i)
-                    banks[(s, i)] = bank
-                    for t in range(PACK):
-                        rows = slice(g * CHUNK + t * P, g * CHUNK + (t + 1) * P)
-                        nc.tensor.matmul_mx(
-                            out=bank[:, t, :],
-                            lhsT=a_cod[:, rows].bitcast(E4M3X4),
-                            lhsT_scale=a_pla[:, rows],
-                            rhs=b_cod[:, cols].bitcast(E4M3X4),
-                            rhs_scale=b_pla[:, cols],
-                            start=True,
-                            stop=True,
-                        )
-
-        def lay_base(s):
-            for i in range(2):
-                c, g, u, kind = place(s, i)
-                if kind != "P":
-                    turned[(s, i)] = v_bank(s, i)
-                if kind in "AS":
-                    nc.tensor.matmul(
-                        turned[(s, i)][:], lhsT=ident_bf[:], rhs=w_raw[(c, g)][:, :, u * P : (u + 1) * P], start=True, stop=False
-                    )
+                    j = c * SLOTS + u
+                    scaled[(s, i)] = work.tile([P, PANEL], F32, name="scaled", tag="scaled", bufs=4)
+                    nc.scalar.activation(out=scaled[(s, i)][:], in_=products[(s, i)][:], func=COPY, scale=gain_col[:, j : j + 1])
 
         def turn_back(s):
             for i in range(2):
+                c, g, u, kind = place(s, i)
+                if kind != "P":
+                    banks[(s, i)] = step_bank(s, i, [P, SLOTS, P])
+                if kind == "S":
+                    nc.tensor.matmul(banks[(s, i)][:], lhsT=ident_bf[:], rhs=w_raw[(c, g)][:, :, u * P : (u + 1) * P], start=True, stop=False)
+            for i in range(2):
                 kind = place(s, i)[3]
                 if kind != "P":
-                    banks[(s, i)] = turned[(s, i)]
-                    for t in range(PACK):
+                    for t in range(SLOTS):
                         nc.tensor.matmul(
-                            turned[(s, i)][:, t, :],
+                            banks[(s, i)][:, t, :],
                             lhsT=scaled[(s, i)][:, t * P : (t + 1) * P],
                             rhs=ident[:],
                             is_transpose=True,
-                            start=kind in "TU",
-                            stop=kind in "TU" or t == PACK - 1,
+                            start=kind == "V",
+                            stop=kind == "V" or t == SLOTS - 1,
                         )
 
+        def plain_product(s):
+            for i in range(2):
+                c, g, u, kind = place(s, i)
+                if both_plain(s):
+                    o0 = c * PANEL + (u - i) * P
+                    banks[(s, i)] = step_bank(s, i, [P, 2, HALF])
+                    for e in range(2):
+                        at = g * PANEL + (2 * i + e) * P
+                        mx_pass(banks[(s, i)][:, e, :], *a_operand(at, at + P), *b_operand(o0, o0 + HALF))
+                elif kind == "P":
+                    o0 = c * PANEL + u * P
+                    banks[(s, i)] = step_bank(s, i, [P, SLOTS, P])
+                    for t in range(SLOTS):
+                        at = g * PANEL + t * P
+                        mx_pass(banks[(s, i)][:, t, :], *a_operand(at, at + P), *b_operand(o0, o0 + P))
+
+        def plain_width(s):
+            return P * sum(place(s, i)[3] == "P" for i in range(2))
+
         def weave(s):
-            wanted = [i for i in range(2) if place(s, i)[3] in "TP"]
-            if wanted and s not in UNWOVEN:
+            words = plain_width(s) // 2
+            if words:
                 c, g, u, kind = place(s, 0)
-                lo, hi = wanted[0] * P, (wanted[-1] + 1) * P
-                if s // 2 in G_ROWS and s % 2 == 0:
-                    woven[s] = work.tile([P, P, PACK], F32, name="woven", tag="shared%d" % (s // 2 % 2), bufs=1, align_bytes=64)
-                else:
-                    woven[s] = work.tile([P, P, PACK], F32, name="woven", tag="woven", bufs=3, align_bytes=64)
+                woven[s] = work.tile([P, P, SLOTS], F32, name="woven", tag="woven", bufs=3, align_bytes=ALIGN)
                 nc.scalar.copy(
-                    out=woven[s][:, lo // 2 : hi // 2, :].rearrange("p (c i) t -> p c t i", i=2),
-                    in_=w_raw[(c, g)][:].bitcast(F32)[:, :, (u * P + lo) // 2 : (u * P + hi) // 2].rearrange("p t (c i) -> p c t i", i=2),
+                    out=woven[s][:, 0:words, :].rearrange("p (n i) t -> p n t i", i=RUN // 2),
+                    in_=w_raw[(c, g)][:].bitcast(F32)[:, :, u * P // 2 : u * P // 2 + words].rearrange("p t (n i) -> p n t i", i=RUN // 2),
                 )
 
-        def base(s, lo, hi):
-            if s in UNWOVEN:
-                c, g, u, kind = place(s, 0)
-                return w_raw[(c, g)][:, :, u * P + lo : u * P + hi].rearrange("p t (m e) -> p m e t", e=2)
-            return woven[s][:].bitcast(BF16)[:, lo // 2 : hi // 2, :].rearrange("p m (t e) -> p m e t", e=2)
-
-        def pairs(ap):
-            return ap.rearrange("p (m e) t -> p m e t", e=2)
-
-        def empty_block(s, i):
+        def empty_bank(s, i):
             c, g, u, kind = place(s, i)
             row = s // 2
             if u == 0:
-                wm[row] = work.tile([P, CHUNK, PACK], BF16, name="wm", tag="wm", bufs=3, align_bytes=64)
-            if i == 0:
-                prods[s] = work.tile([P, HALF, PACK], F32, name="prod", tag="prod", bufs=4) if "P" in KINDS[row][u : u + 2] else None
-            delta = banks[(s, i)][:].rearrange("p t o -> p o t")
-            if wide(s):
-                o0 = c * CHUNK + 2 * (s % 2) * P
+                wm[row] = work.tile([P, PANEL, SLOTS], BF16, name="wm", tag="wm", bufs=3, align_bytes=ALIGN)
+            if i == 0 and kind == "P":
+                gained[s] = work.tile([P, HALF * SLOTS], F32, name="gained", tag="gained", bufs=4)
+            cols = slice(u * P, (u + 1) * P)
+            by_column = banks[(s, i)][:].rearrange("p t o -> p o t")
+            if both_plain(s):
+                o0 = c * PANEL + (u - i) * P
                 nc.vector.tensor_tensor(
-                    out=prods[s][:].rearrange("p o t -> p (o t)").rearrange("p (u o e) -> p u o e", u=2, e=2)[:, i, :, :],
-                    in0=delta,
-                    in1=bg[:, o0 : o0 + HALF].unsqueeze(2).to_broadcast([P, HALF, 2]),
+                    out=gained[s][:].rearrange("p (h o e) -> p h o e", h=2, e=2)[:, i, :, :],
+                    in0=by_column,
+                    in1=gain_all[:, o0 : o0 + HALF].unsqueeze(2).to_broadcast([P, HALF, 2]),
                     op=MULT,
                 )
-                return
-            if kind == "A":
-                nc.vector.tensor_copy(out=wm[row][:, u * P : (u + 1) * P, :], in_=delta)
+            elif kind == "P":
+                o0 = c * PANEL + u * P
+                nc.vector.tensor_tensor(
+                    out=gained[s][:].rearrange("p (o t) -> p o t", t=SLOTS)[:, 0:P, :],
+                    in0=by_column,
+                    in1=gain_all[:, o0 : o0 + P].unsqueeze(2).to_broadcast([P, P, SLOTS]),
+                    op=MULT,
+                )
             elif kind == "S":
-                nc.scalar.copy(out=wm[row][:, u * P : (u + 1) * P, :], in_=delta)
-            elif kind == "U":
-                nc.vector.tensor_tensor(
-                    out=wm[row][:, u * P : (u + 1) * P, :].rearrange("p (c i) t -> p c t i", i=4),
-                    in0=banks[(s, i)][:].rearrange("p t (c i) -> p c t i", i=4),
-                    in1=w_raw[(c, g)][:, :, u * P : (u + 1) * P].rearrange("p t (c i) -> p c t i", i=4),
-                    op=ADD,
-                )
-            elif kind == "T":
-                nc.vector.tensor_tensor(out=pairs(wm[row][:, u * P : (u + 1) * P, :]), in0=pairs(delta), in1=base(s, i * P, (i + 1) * P), op=ADD)
+                nc.scalar.copy(out=wm[row][:, cols, :], in_=by_column)
             else:
-                o0 = c * CHUNK + u * P
                 nc.vector.tensor_tensor(
-                    out=prods[s][:, i * P : (i + 1) * P, :],
-                    in0=delta,
-                    in1=bg[:, o0 : o0 + P].unsqueeze(2).to_broadcast([P, P, PACK]),
-                    op=MULT,
+                    out=wm[row][:, cols, :].rearrange("p (n i) t -> p n t i", i=RUN),
+                    in0=banks[(s, i)][:].rearrange("p t (n i) -> p n t i", i=RUN),
+                    in1=w_raw[(c, g)][:, :, cols].rearrange("p t (n i) -> p n t i", i=RUN),
+                    op=ADD,
                 )
 
         def add_plain(s):
-            plain = [i for i in range(2) if place(s, i)[3] == "P"]
-            if wide(s):
-                lo = s % 2 * HALF
+            lo = s % 2 * HALF
+            if both_plain(s):
                 nc.vector.tensor_tensor(
-                    out=wm[s // 2][:, lo : lo + HALF, :].rearrange("p (m f) (u e) -> p m f u e", f=2, u=2),
-                    in0=prods[s][:].rearrange("p o t -> p (o t)").rearrange("p (u m f e) -> p m f u e", u=2, f=2, e=2),
-                    in1=woven[s][:].bitcast(BF16).rearrange("p m (u e f) -> p m f u e", u=2, f=2),
+                    out=wm[s // 2][:, lo : lo + HALF, :].rearrange("p (m f) (h e) -> p m f h e", f=2, h=2),
+                    in0=gained[s][:].rearrange("p (h m f e) -> p m f h e", h=2, f=2, e=2),
+                    in1=woven[s][:].bitcast(BF16).rearrange("p m (h e f) -> p m f h e", h=2, f=2),
                     op=ADD,
                 )
-            elif plain:
-                c, g, u, kind = place(s, 0)
-                lo, hi = plain[0] * P, (plain[-1] + 1) * P
+            elif plain_width(s):
                 nc.vector.tensor_tensor(
-                    out=pairs(wm[s // 2][:, u * P + lo : u * P + hi, :]),
-                    in0=pairs(prods[s][:, lo:hi, :]),
-                    in1=base(s, lo, hi),
+                    out=wm[s // 2][:, lo : lo + P, :].rearrange("p (m f) t -> p m f t", f=2),
+                    in0=gained[s][:].rearrange("p (m f t) -> p m f t", f=2, t=SLOTS)[:, 0 : P // 2, :, :],
+                    in1=woven[s][:].bitcast(BF16)[:, 0 : P // 2, :].rearrange("p m (t f) -> p m f t", f=2),
                     op=ADD,
                 )
 
-        late = {}
-
-        def add_late(row):
-            late[row] = work.tile([P, HALF, PACK], BF16, name="late", tag="shared%d" % (row % 2), bufs=1, align_bytes=64)
-            nc.gpsimd.tensor_tensor(out=pairs(late[row][:]), in0=pairs(prods[2 * row + 1][:]), in1=base(2 * row + 1, 0, HALF), op=ADD)
-
-        def wm_quantise(row):
-            if row in late:
-                for h, tile in enumerate((wm[row][:, 0:HALF, :], late[row][:])):
-                    cols = slice(row * CHUNK + h * HALF, row * CHUNK + (h + 1) * HALF)
-                    nc.vector.quantize_mx(out=w_cod[:, cols].bitcast(E4M3X4), scales=w_pla[:, cols], in_=tile.rearrange("p o t -> p (o t)"))
-                return
-            cols = slice(row * CHUNK, (row + 1) * CHUNK)
-            nc.vector.quantize_mx(out=w_cod[:, cols].bitcast(E4M3X4), scales=w_pla[:, cols], in_=wm[row][:].rearrange("p o t -> p (o t)"))
-
-        def half_quantise(s):
-            cols = slice(s * HALF, (s + 1) * HALF)
-            part = wm[s // 2][:, s % 2 * HALF : (s % 2 + 1) * HALF, :]
-            nc.vector.quantize_mx(out=w_cod[:, cols].bitcast(E4M3X4), scales=w_pla[:, cols], in_=part.rearrange("p o t -> p (o t)"))
+        def wm_quantise(row, lo=0, hi=PANEL):
+            quantise(w_cod, w_pla, row * PANEL + lo, wm[row][:, lo:hi, :])
 
         y_banks = {}
 
         def y_passes(c, m, groups, bank=None):
             if groups[0] == 0:
-                y_banks[(c, m)] = bank if bank is not None else s_bank([P, CHUNK])
+                if bank is None:
+                    bank = ring_bank([P, PANEL])
+                    if len(groups) < GROUPS:
+                        open_tiles[(c, m)] = ring[0]
+                y_banks[(c, m)] = bank
             for g in groups:
-                cols = slice((c * GROUPS + g) * CHUNK, (c * GROUPS + g + 1) * CHUNK)
-                nc.tensor.matmul_mx(
-                    out=y_banks[(c, m)][:],
-                    lhsT=x_cod[:, g, m * 2 * P : (m + 1) * 2 * P].bitcast(E2M1X4),
-                    lhsT_scale=x_pla[:, g, m * P : (m + 1) * P],
-                    rhs=w_cod[:, cols].bitcast(E4M3X4),
-                    rhs_scale=w_pla[:, cols],
+                cols = slice((c * GROUPS + g) * PANEL, (c * GROUPS + g + 1) * PANEL)
+                mx_pass(
+                    y_banks[(c, m)][:],
+                    x_cod[:, g, m * 2 * P : (m + 1) * 2 * P].bitcast(E2M1X4),
+                    x_pla[:, g, m * P : (m + 1) * P],
+                    w_cod[:, cols].bitcast(E4M3X4),
+                    w_pla[:, cols],
                     start=g == 0,
                     stop=g == GROUPS - 1,
                 )
 
         def y_store(c, m, copy):
-            res = work.tile([P, CHUNK], F32, name="res", tag="res", bufs=8)
+            res = work.tile([P, PANEL], F32, name="res", tag="res", bufs=T_TILES)
             copy(out=res[:], in_=y_banks[(c, m)][:])
-            nc.sync.dma_start(out=out_view[m][:, c * CHUNK : (c + 1) * CHUNK], in_=res[:])
-
-        def warm_up(count):
-            for i in range(count):
-                nc.tensor.matmul(v_bank(0, 1)[:], lhsT=warm[:], rhs=warm[:].unsqueeze(1).to_broadcast([P, PACK, P]), start=True, stop=True)
+            open_tiles[(c, m)] = None
+            nc.sync.dma_start(out=out_view[m][:, c * PANEL : (c + 1) * PANEL], in_=res[:])
 
         nc.scalar.activation(out=ident_bf[:], in_=ident[:], func=COPY)
-        warm_up(WARM[0])
         ad_turn(0, 0)
         ad_turn(0, 1)
-        warm_up(WARM[1])
-        gain_banks = []
-        for c in range(G0, CHUNKS):
-            bank = v_bank(1, c - 1) if c else v_bank(0, 1)
-            gain_banks.append(bank)
-            for u in range(PACK):
-                ob = c * PACK + u
-                nc.tensor.matmul(bank[:, u, :], lhsT=ident_bf[:, ob : ob + 1].to_broadcast([P, P]), rhs=gain_rows[:], start=True, stop=True)
-        col_bank = v_bank(0, 0)
-        nc.tensor.matmul(col_bank[:, 0, 0:BLOCKS], lhsT=gain_rows[:], rhs=ident_bf[:, 0:BLOCKS], start=True, stop=True)
+        gain_banks = {}
+        for c in range(1, PANELS):
+            count = max(kinds.count("P") for kinds in KINDS[c * GROUPS : (c + 1) * GROUPS])
+            gain_banks[c] = step_bank(1, c - 1, [P, count, P])
+            for u in range(count):
+                j = c * SLOTS + u
+                nc.tensor.matmul(gain_banks[c][:, u, :], lhsT=ident_bf[:, j : j + 1].to_broadcast([P, P]), rhs=gain_rows[:], start=True, stop=True)
+        col_bank = step_bank(0, 0, [P, PIECES])
+        nc.tensor.matmul(col_bank[:], lhsT=gain_rows[:], rhs=ident_bf[:, 0:PIECES], start=True, stop=True)
         b_tiles(0)
         ad_product(0, 0)
         for t in range(2):
@@ -424,118 +358,101 @@ def tile_vera_merged_layer_s13_kernel(tc, x_words, x_scales, a, bmat_bytes, bmat
         ad_product(0, 1)
         ad_turn(1, 0)
         ad_turn(1, 1)
-        warm_up(WARM[2])
         b_interleave(nc.vector.tensor_copy, 0, 0)
         b_interleave(nc.scalar.copy, 0, 1)
-        nc.scalar.copy(out=b_col[:], in_=col_bank[:, 0, 0:BLOCKS])
-        for c in range(G0, CHUNKS):
-            nc.scalar.copy(out=bg[:, c * CHUNK : (c + 1) * CHUNK], in_=gain_banks[c - G0][:].rearrange("p u o -> p (u o)"))
+        nc.scalar.copy(out=gain_col[:], in_=col_bank[:])
+        for c in range(1, PANELS):
+            spread = gain_banks[c][:].rearrange("p u o -> p (u o)")
+            nc.scalar.copy(out=gain_all[:, c * PANEL : c * PANEL + spread.shape[1]], in_=spread)
         ad_quantise(0)
         b_quantise(0, 0, HALF)
-        lay_base(0)
         turned_product(0)
         turned_scale(0)
         ad_product(1, 0)
-        b_quantise(0, HALF, CHUNK)
+        b_quantise(0, HALF, PANEL)
         ad_product(1, 1)
         turned_product(1)
-        plain_product(0)
         turned_scale(1)
-        weave(0)
-        weave(1)
         turn_back(0)
         ad_turn(2, 0)
         ad_quantise(1)
 
-        def b_job(job):
-            c, what, part, engine = job
-            if c not in b_wide:
-                b_tiles(c)
-            if what == "w":
-                (b_widen_scalar if engine == "S" else b_widen_vector)(c, part)
-            else:
-                b_interleave({"S": nc.scalar.copy, "V": nc.vector.tensor_copy, "G": gpsimd_copy}[engine], c, part)
+        def b_prepare(s):
+            if s in (0, 4):
+                b_tiles(s // 4 + 1)
+            if s < 2:
+                b_widen_scalar(1, 2 * s)
+                b_widen_scalar(1, 2 * s + 1)
+            elif s < 4:
+                b_interleave(nc.scalar.copy, 1, s - 2)
+            elif s < 8:
+                b_widen_scalar(2, s - 4)
+            elif s in (8, 10):
+                b_interleave(nc.scalar.copy, 2, (s - 8) // 2)
 
-        todo = []
+        b_due = {PANEL_STEPS - 3: 1, 2 * PANEL_STEPS - 2: 2}
+        early_group = {max(4, 2 * g + 3): g for g in range(GROUPS)}
+        whole_tiles = {s: 2 if s in (19, 21) else 1 for s in range(10, STEPS - 2)}
+        todo = [(0, m) for m in range(EARLY_FIRST, T_TILES)] + [(1, m) for m in range(T_TILES)]
+
         to_store = []
-        last = CHUNKS - 1
+        last = PANELS - 1
         for s in range(STEPS):
-            if s < 4 and s % 2 == 1:
-                ad_product(s // 2 + 2, s % 2)
-            empty_block(s, 0)
-            if s < 4 and s % 2 == 0:
-                ad_product(s // 2 + 2, s % 2)
-            if s in (1, 3):
-                ad_quantise(s // 2 + 2)
-            if s > 0 and s // 2 not in G_ROWS and (s - 1) // 2 not in G_ROWS:
+            ad_group, ad_half = s // 2 + 2, s % 2
+            if ad_group < GROUPS and ad_half == 1:
+                ad_product(ad_group, 1)
+            empty_bank(s, 0)
+            if ad_group < GROUPS and ad_half == 0:
+                ad_product(ad_group, 0)
+            if ad_group < GROUPS and ad_half == 1:
+                ad_quantise(ad_group)
+            if s > 0:
                 add_plain(s - 1)
-            if s > 0 and s % 2 == 1 and s // 2 not in G_ROWS and s // 2 - 1 in G_ROWS:
-                wm_quantise(s // 2 - 1)
-            empty_block(s, 1)
-            if s // 2 in G_ROWS and s % 2 == 1:
-                if s // 2 - 1 not in G_ROWS:
-                    add_plain(s - 2)
-                    add_plain(s - 1)
-                    wm_quantise(s // 2 - 1)
-                else:
-                    wm_quantise(s // 2 - 1)
-                    add_plain(s - 1)
-                add_late(s // 2)
-            for job in B_JOBS.get(s, []):
-                if job[3] == "V":
-                    b_job(job)
-            for c in range(1, CHUNKS):
-                if s == B_QUANT[c]:
-                    b_quantise(c, 0, CHUNK)
-            if s % 2 == 0 and s > 0 and s // 2 not in G_ROWS and s // 2 - 1 not in G_ROWS:
+            empty_bank(s, 1)
+            if s in b_due:
+                b_quantise(b_due[s], 0, PANEL)
+            if s % 2 == 0 and s > 0:
                 wm_quantise(s // 2 - 1)
 
-            if s in Y_AT:
-                todo.extend((s // 8 - 1, m) for m in range(T_TILES))
             if s + 1 < STEPS:
                 plain_product(s + 1)
-            if s in BACK_FIRST:
-                lay_base(s + 1)
-                turn_back(s + 1)
             if s + 2 < STEPS:
                 turned_product(s + 2)
-            if s < 3:
+            if (s + 1) // 2 + 2 < GROUPS:
                 ad_turn((s + 1) // 2 + 2, (s + 1) % 2)
-            if s + 1 < STEPS and s not in BACK_FIRST:
-                lay_base(s + 1)
+            if s + 1 < STEPS:
                 turn_back(s + 1)
             if s + 2 < STEPS:
                 turned_scale(s + 2)
-            for item in to_store:
-                y_store(*item, nc.scalar.copy)
-            to_store = todo[: 2 if s in DOUBLE else 1]
+            for c, m in to_store:
+                y_store(c, m, nc.scalar.copy)
+            to_store = todo[: whole_tiles.get(s, 0)]
             todo = todo[len(to_store) :]
-            for item in to_store:
-                y_passes(*item, range(GROUPS))
-            if s + 2 < STEPS and not (s % 2 == 0 and s // 2 + 1 in G_ROWS):
+            for c, m in to_store:
+                y_passes(c, m, range(GROUPS))
+            if s in early_group:
+                for m in range(EARLY_FIRST):
+                    y_passes(0, m, [early_group[s]])
+                if early_group[s] == GROUPS - 1:
+                    to_store = [(0, m) for m in range(EARLY_FIRST)]
+            if s + 2 < STEPS:
                 weave(s + 2)
-            if s % 2 == 1 and (s + 1) // 2 in G_ROWS:
-                weave(s + 1)
-            for job in B_JOBS.get(s, []):
-                if job[3] in "SG":
-                    b_job(job)
+            b_prepare(s)
             if s == STEPS - 2:
-                for item in to_store:
-                    y_store(*item, nc.scalar.copy)
-                to_store = []
                 for m in range(4):
-                    y_passes(last, m, range(2))
+                    y_passes(last, m, range(0, 2))
             if s == STEPS - 1:
                 for m in range(4):
                     y_passes(last, m, range(2, 3))
-        half_quantise(STEPS - 2)
+
+        wm_quantise(ROWS - 1, 0, HALF)
         add_plain(STEPS - 1)
-        for m in range(4, OPEN):
-            y_passes(last, m, range(3), v_bank(m // 2, m % 2, (P, CHUNK)))
-        half_quantise(STEPS - 1)
+        for m in range(4, EARLY_LAST):
+            y_passes(last, m, range(0, 3), step_bank(m // 2, m % 2, [P, PANEL]))
+        wm_quantise(ROWS - 1, HALF, PANEL)
         for m in range(T_TILES):
-            if m < OPEN:
+            if m < EARLY_LAST:
                 y_passes(last, m, range(3, 4))
             else:
-                y_passes(last, m, range(4), v_bank(m // 2, m % 2, (P, CHUNK)))
+                y_passes(last, m, range(GROUPS), step_bank(m // 2, m % 2, [P, PANEL]))
             y_store(last, m, nc.scalar.copy if m % 2 == 0 else nc.vector.tensor_copy)

@@ -47,6 +47,10 @@ def tile_vera_merged_layer_s13_kernel(tc, x_words, x_scales, a, bmat_bytes, bmat
         psum = ctx.enter_context(tc.psum_pool(name="psum", bufs=1))
         ctx.enter_context(tc.manual_schedule())
 
+        def staggered(name, columns, dtype, size, start):
+            tile = keep.tile([P, columns + 256 // size], dtype, name=name, align_bytes=256)
+            return tile[:, start // size : start // size + columns]
+
         gain_rows = keep.tile([P, P], BF16, name="gain_rows")
         ident = keep.tile([P, P], F32, name="ident")
         ident_bf = keep.tile([P, P], BF16, name="ident_bf")
@@ -55,18 +59,18 @@ def tile_vera_merged_layer_s13_kernel(tc, x_words, x_scales, a, bmat_bytes, bmat
         gain_col = keep.tile([P, PIECES], F32, name="gain_col")
         gain_all = keep.tile([P, OUT], BF16, name="gain_all")
         b_raw = [keep.tile([P, SLOTS, PANEL], U8, name="b_raw%d" % c, align_bytes=ALIGN) for c in range(PANELS)]
-        b_cod = keep.tile([P, OUT], U32, name="b_cod", align_bytes=ALIGN)
-        b_pla = keep.tile([P, OUT], U8, name="b_pla", align_bytes=ALIGN)
+        b_cod = staggered("b_cod", OUT, U32, 4, 64)
+        b_pla = staggered("b_pla", OUT, U8, 1, 192)
         a_raw = {(g, h): keep.tile([P, 2, R], BF16, name="a_raw%d%d" % (g, h), align_bytes=ALIGN) for g in range(GROUPS) for h in range(2)}
-        a_cod = keep.tile([P, IN], U32, name="a_cod", align_bytes=ALIGN)
-        a_pla = keep.tile([P, IN], U8, name="a_pla", align_bytes=ALIGN)
+        a_cod = staggered("a_cod", IN, U32, 4, 0)
+        a_pla = staggered("a_pla", IN, U8, 1, 128)
         w_raw = {
             (c, g): keep.tile([P, SLOTS, PANEL], BF16, name="w_raw%d%d" % (c, g), align_bytes=ALIGN) for c in range(PANELS) for g in range(GROUPS)
         }
-        w_cod = keep.tile([P, ROWS * PANEL], U32, name="w_cod", align_bytes=ALIGN)
-        w_pla = keep.tile([P, ROWS * PANEL], U8, name="w_pla", align_bytes=ALIGN)
-        x_cod = keep.tile([P, GROUPS, 2 * T], U8, name="x_cod", align_bytes=ALIGN)
-        x_pla = keep.tile([P, GROUPS, T], U8, name="x_pla", align_bytes=ALIGN)
+        w_cod = staggered("w_cod", ROWS * PANEL, U32, 4, 0)
+        w_pla = staggered("w_pla", ROWS * PANEL, U8, 1, 128)
+        x_cod = staggered("x_cod", GROUPS * 2 * T, U8, 1, 64).rearrange("p (g n) -> p g n", g=GROUPS)
+        x_pla = staggered("x_pla", GROUPS * T, U8, 1, 192).rearrange("p (g n) -> p g n", g=GROUPS)
 
         a_view = a.rearrange("(g p t) r -> g p t r", p=P, t=SLOTS)
         w_view = w0.rearrange("(g p t) o -> g p t o", p=P, t=SLOTS)

@@ -25,18 +25,22 @@ HALF = PANEL // 2
 PIECES = OUT // P
 T_TILES = T // P
 ROWS = PANELS * GROUPS
-STEPS = 2 * ROWS
-PANEL_STEPS = 2 * GROUPS
 RUN = 4
 
 FLOPS = 2 * IN * R * OUT + 2 * T * IN * OUT
 
-TURNED_ROWS = 5
-MIXED_ROWS = 4
-KINDS = ["VVVV"] * TURNED_ROWS + ["PPPS"] * MIXED_ROWS + ["PPPP"] * (ROWS - TURNED_ROWS - MIXED_ROWS)
-EARLY_FIRST = 2
-EARLY_LAST = 6
 ALIGN = 64
+PIECE_BANKS = 4
+RES_BUFS = 8
+KINDS = ["PPVV"] * 4 + ["PPPP"] * 8
+G_COLS = [256] * 11 + [128]
+B_DUE = {2: (1, 0), 3: (1, 1), 5: (2, 0), 6: (2, 1)}
+B_WORK = {-2: [("tiles", 1, 0), ("widen", 1, 0), ("widen", 1, 1)], -1: [("gain", 1, 0), ("widen", 1, 2), ("widen", 1, 3)], 0: [("weave", 1, 0)], 1: [("weave", 1, 1), ("tiles", 2, 0), ("widen", 2, 0)], 2: [("widen", 2, 1), ("widen", 2, 2)],
+          3: [("widen", 2, 3), ("weave", 2, 0)], 4: [("weave", 2, 1), ("gain", 2, 0)]}
+AD_AT = {-1: [0, 0], 0: [1, 3]}
+Y_RATE = {-1: [0], 0: [0, 0, 1], 1: [1, 1, 2, 2], 2: [1], 3: [2], 4: [3], 5: [3], 6: [3], 7: [3], 8: [3], 9: [3], 10: [4]}
+Y_OPEN = {-1: 0, 0: 2, 1: 4, 2: 4, 3: 4, 4: 3, 5: 4, 6: 4, 7: 4, 8: 4, 9: 4, 10: 8}
+TAIL_EARLY = 12
 
 
 def tile_vera_merged_layer_s13_kernel(tc, x_words, x_scales, a, bmat_bytes, bmat_scale, d_gain, b_gain, w0, out):
@@ -47,47 +51,37 @@ def tile_vera_merged_layer_s13_kernel(tc, x_words, x_scales, a, bmat_bytes, bmat
         psum = ctx.enter_context(tc.psum_pool(name="psum", bufs=1))
         ctx.enter_context(tc.manual_schedule())
 
-        def staggered(name, columns, dtype, size, start):
-            tile = keep.tile([P, columns + 256 // size], dtype, name=name, align_bytes=256)
-            return tile[:, start // size : start // size + columns]
-
         gain_rows = keep.tile([P, P], BF16, name="gain_rows")
         ident = keep.tile([P, P], F32, name="ident")
         ident_bf = keep.tile([P, P], BF16, name="ident_bf")
         b_sc = keep.tile([P, SLOTS], F32, name="b_sc")
         d_col = keep.tile([P, SLOTS], BF16, name="d_col")
         gain_col = keep.tile([P, PIECES], F32, name="gain_col")
-        gain_all = keep.tile([P, OUT], BF16, name="gain_all")
+        gain_all = [keep.tile([P, PANEL], BF16, name="gain_all%d" % c) for c in range(PANELS)]
         b_raw = [keep.tile([P, SLOTS, PANEL], U8, name="b_raw%d" % c, align_bytes=ALIGN) for c in range(PANELS)]
-        b_cod = staggered("b_cod", OUT, U32, 4, 64)
-        b_pla = staggered("b_pla", OUT, U8, 1, 192)
+        b_cod = keep.tile([P, OUT], U32, name="b_cod", align_bytes=ALIGN)
+        b_pla = keep.tile([P, OUT], U8, name="b_pla", align_bytes=ALIGN)
         a_raw = {(g, h): keep.tile([P, 2, R], BF16, name="a_raw%d%d" % (g, h), align_bytes=ALIGN) for g in range(GROUPS) for h in range(2)}
-        a_cod = staggered("a_cod", IN, U32, 4, 0)
-        a_pla = staggered("a_pla", IN, U8, 1, 128)
-        w_raw = {
-            (c, g): keep.tile([P, SLOTS, PANEL], BF16, name="w_raw%d%d" % (c, g), align_bytes=ALIGN) for c in range(PANELS) for g in range(GROUPS)
-        }
-        w_cod = staggered("w_cod", ROWS * PANEL, U32, 4, 0)
-        w_pla = staggered("w_pla", ROWS * PANEL, U8, 1, 128)
-        x_cod = staggered("x_cod", GROUPS * 2 * T, U8, 1, 64).rearrange("p (g n) -> p g n", g=GROUPS)
-        x_pla = staggered("x_pla", GROUPS * T, U8, 1, 192).rearrange("p (g n) -> p g n", g=GROUPS)
+        a_cod = keep.tile([P, IN], U32, name="a_cod", align_bytes=ALIGN)
+        a_pla = keep.tile([P, IN], U8, name="a_pla", align_bytes=ALIGN)
+        w_raw = [keep.tile([P, SLOTS, PANEL], BF16, name="w_raw%d" % r, align_bytes=ALIGN) for r in range(ROWS)]
+        w_cod = keep.tile([P, ROWS * PANEL], U32, name="w_cod", align_bytes=ALIGN)
+        w_pla = keep.tile([P, ROWS * PANEL], U8, name="w_pla", align_bytes=ALIGN)
+        x_cod = [keep.tile([P, 2 * T], U8, name="x_cod%d" % g, align_bytes=ALIGN) for g in range(GROUPS)]
+        x_pla = keep.tile([P, GROUPS, T], U8, name="x_pla", align_bytes=ALIGN)
 
         a_view = a.rearrange("(g p t) r -> g p t r", p=P, t=SLOTS)
         w_view = w0.rearrange("(g p t) o -> g p t o", p=P, t=SLOTS)
         b_view = bmat_bytes.rearrange("(p t) o -> p t o", t=SLOTS)
         out_view = out.rearrange("(m p) o -> m p o", p=P)
 
-        ring = [0]
-        open_tiles = {}
+        piece_free = list(range(PIECE_BANKS))
+        ring_free = list(range(PIECE_BANKS, 8))
 
-        def ring_bank(shape):
-            ring[0] = (ring[0] + 1) % 4
-            while ring[0] in open_tiles.values():
-                ring[0] = (ring[0] + 1) % 4
-            return psum.tile(shape, F32, name="ring_bank", tag="ring_bank%d" % ring[0])
-
-        def step_bank(s, i, shape):
-            return psum.tile(shape, F32, name="step_bank", tag="step_bank%d" % (2 * (s % 2) + i))
+        def take(free, shape):
+            b = free[0]
+            free.remove(b)
+            return b, psum.tile(shape, F32, name="bank", tag="bank%d" % b)
 
         nc.vector.memset(gain_rows[:], 0.0)
         make_identity(nc, ident[:])
@@ -100,32 +94,44 @@ def tile_vera_merged_layer_s13_kernel(tc, x_words, x_scales, a, bmat_bytes, bmat
         def load_b(c):
             nc.sync.dma_start(out=b_raw[c][:], in_=b_view[:, :, c * PANEL : (c + 1) * PANEL])
 
-        def load_w(c, g):
-            nc.sync.dma_start(out=w_raw[(c, g)][:], in_=w_view[g][:, :, c * PANEL : (c + 1) * PANEL])
+        def load_w(r):
+            c, g = divmod(r, GROUPS)
+            nc.sync.dma_start(out=w_raw[r][:], in_=w_view[g][:, :, c * PANEL : (c + 1) * PANEL])
 
+        def load_x_scales():
+            for q in range(4):
+                nc.sync.dma_start(
+                    out=x_pla[32 * q : 32 * q + 4, :, :].bitcast(I32),
+                    in_=x_scales[:, 4 * q : 4 * q + 4, :].bitcast(I32).rearrange("g q n -> q g n"),
+                )
+
+        def load_x(g):
+            nc.sync.dma_start(out=x_cod[g][:].bitcast(I32), in_=x_words[g].bitcast(I32))
+
+        gain_view = b_gain.rearrange("(j p) -> j p", p=P)
         load_a(0)
         nc.sync.dma_start(out=b_sc[:], in_=bmat_scale.rearrange("(p t) o -> p (t o)", t=SLOTS))
         nc.sync.dma_start(out=d_col[:], in_=d_gain.rearrange("(p t) -> p t", t=SLOTS))
         load_b(0)
-        nc.sync.dma_start(out=gain_rows[0:PIECES, :], in_=b_gain.rearrange("(j p) -> j p", p=P))
+        nc.sync.dma_start(out=gain_rows[0:8, :], in_=gain_view[0:8])
+        nc.sync.dma_start(out=gain_rows[8:PIECES, :], in_=gain_view[8:PIECES])
         load_a(1)
-        load_w(0, 0)
+        load_w(0)
         load_a(2)
-        load_w(0, 1)
         load_b(1)
+        load_w(1)
         load_a(3)
-        load_w(0, 2)
-        load_w(0, 3)
-        for q in range(4):
-            nc.sync.dma_start(
-                out=x_pla[32 * q : 32 * q + 4, :, :].bitcast(I32),
-                in_=x_scales[:, 4 * q : 4 * q + 4, :].bitcast(I32).rearrange("g q n -> q g n"),
-            )
+        load_x_scales()
+        load_x(0)
+        load_w(2)
+        load_x(1)
+        load_w(3)
+        load_x(2)
         load_b(2)
-        nc.sync.dma_start(out=x_cod[:].bitcast(I32), in_=x_words.bitcast(I32).rearrange("g p n -> p g n"))
-        for c in range(1, PANELS):
-            for g in range(GROUPS):
-                load_w(c, g)
+        load_w(4)
+        load_x(3)
+        for r in range(5, ROWS):
+            load_w(r)
 
         def quantise(codes, plane, at, grouped):
             cols = slice(at, at + grouped.shape[1])
@@ -134,30 +140,32 @@ def tile_vera_merged_layer_s13_kernel(tc, x_words, x_scales, a, bmat_bytes, bmat
         def mx_pass(bank, lhs, lhs_plane, rhs, rhs_plane, start=True, stop=True):
             nc.tensor.matmul_mx(out=bank, lhsT=lhs, lhsT_scale=lhs_plane, rhs=rhs, rhs_scale=rhs_plane, start=start, stop=stop)
 
-        ad_banks, ad_grp = {}, {}
+        ad_banks, ad_grp, ad_done = {}, {}, []
 
         def ad_turn(g, h):
             if h == 0:
                 ad_grp[g] = work.tile([P, PANEL, SLOTS], BF16, name="ad_grp", tag="ad_grp", align_bytes=ALIGN)
-            bank = ring_bank([P, 2, HALF])
-            ad_banks[(g, h)] = bank
+            ad_banks[(g, h)] = take(ring_free, [P, 2, HALF])
             for i in range(2):
                 words = a_raw[(g, h)][:, i, :].bitcast(F32)
                 for u in range(2):
-                    nc.tensor.transpose(bank[:, u, i * P : (i + 1) * P], words[:, u::2], ident[:])
+                    nc.tensor.transpose(ad_banks[(g, h)][1][:, u, i * P : (i + 1) * P], words[:, u::2], ident[:])
 
         def ad_product(g, h):
+            b, bank = ad_banks[(g, h)]
             nc.vector.tensor_tensor(
                 out=ad_grp[g][:, h * HALF : (h + 1) * HALF, :].rearrange("p n (u e) -> p n u e", u=2),
-                in0=ad_banks[(g, h)][:].bitcast(BF16).rearrange("p u (n e) -> p n u e", e=2),
+                in0=bank[:].bitcast(BF16).rearrange("p u (n e) -> p n u e", e=2),
                 in1=d_col[:].rearrange("p (u e) -> p u e", u=2).unsqueeze(1).to_broadcast([P, HALF, 2, 2]),
                 op=MULT,
             )
+            ring_free.append(b)
 
         def ad_quantise(g):
             quantise(a_cod, a_pla, g * PANEL, ad_grp[g][:])
+            ad_done.append(g)
 
-        b_wide, b_grp = {}, {}
+        b_wide, b_grp, b_done = {}, {}, []
 
         def b_tiles(c):
             b_wide[c] = work.tile([P, SLOTS, PANEL], BF16, name="b_wide", tag="b_wide", align_bytes=ALIGN)
@@ -176,18 +184,9 @@ def tile_vera_merged_layer_s13_kernel(tc, x_words, x_scales, a, bmat_bytes, bmat
                 in_=b_wide[c][:, :, cols].rearrange("p t (n i) -> p n t i", i=RUN),
             )
 
-        def b_quantise(c, lo, hi):
-            quantise(b_cod, b_pla, c * PANEL + lo, b_grp[c][:, lo:hi, :])
-
-        def place(s, i):
-            c, g = divmod(s // 2, GROUPS)
-            u = 2 * (s % 2) + i
-            return c, g, u, KINDS[s // 2][u]
-
-        def both_plain(s):
-            return place(s, 0)[3] == "P" and place(s, 1)[3] == "P"
-
-        products, scaled, banks, gained, woven, wm = {}, {}, {}, {}, {}, {}
+        def b_quantise(c, h):
+            quantise(b_cod, b_pla, c * PANEL + h * HALF, b_grp[c][:, h * HALF : (h + 1) * HALF, :])
+            b_done.append((c, h))
 
         def a_operand(lo, hi):
             return a_cod[:, lo:hi].bitcast(E4M3X4), a_pla[:, lo:hi]
@@ -195,164 +194,187 @@ def tile_vera_merged_layer_s13_kernel(tc, x_words, x_scales, a, bmat_bytes, bmat
         def b_operand(lo, hi):
             return b_cod[:, lo:hi].bitcast(E4M3X4), b_pla[:, lo:hi]
 
-        def turned_product(s):
-            for i in range(2):
-                c, g, u, kind = place(s, i)
-                if kind != "P":
-                    o0 = c * PANEL + u * P
-                    products[(s, i)] = ring_bank([P, PANEL])
-                    mx_pass(products[(s, i)][:], *b_operand(o0, o0 + P), *a_operand(g * PANEL, (g + 1) * PANEL))
+        scaled, banks, gained, woven = {}, {}, {}, {}
+        wm_first = keep.tile([P, HALF, SLOTS], BF16, name="wm_first", align_bytes=ALIGN)
+        wm_second = [keep.tile([P, HALF, SLOTS], BF16, name="wm_second%d" % i, align_bytes=ALIGN) for i in range(2)]
 
-        def turned_scale(s):
-            for i in range(2):
-                c, g, u, kind = place(s, i)
-                if kind != "P":
-                    j = c * SLOTS + u
-                    scaled[(s, i)] = work.tile([P, PANEL], F32, name="scaled", tag="scaled", bufs=4)
-                    nc.scalar.activation(out=scaled[(s, i)][:], in_=products[(s, i)][:], func=COPY, scale=gain_col[:, j : j + 1])
+        def pieces(r, kinds):
+            return [u for u in range(SLOTS) if 0 <= r < ROWS and KINDS[r][u] in kinds]
 
-        def turn_back(s):
-            for i in range(2):
-                c, g, u, kind = place(s, i)
-                if kind != "P":
-                    banks[(s, i)] = step_bank(s, i, [P, SLOTS, P])
-                if kind == "S":
-                    nc.tensor.matmul(banks[(s, i)][:], lhsT=ident_bf[:], rhs=w_raw[(c, g)][:, :, u * P : (u + 1) * P], start=True, stop=False)
-            for i in range(2):
-                kind = place(s, i)[3]
-                if kind != "P":
-                    for t in range(SLOTS):
-                        nc.tensor.matmul(
-                            banks[(s, i)][:, t, :],
-                            lhsT=scaled[(s, i)][:, t * P : (t + 1) * P],
-                            rhs=ident[:],
-                            is_transpose=True,
-                            start=kind == "V",
-                            stop=kind == "V" or t == SLOTS - 1,
-                        )
+        unturned = []
 
-        def plain_product(s):
-            for i in range(2):
-                c, g, u, kind = place(s, i)
-                if both_plain(s):
-                    o0 = c * PANEL + (u - i) * P
-                    banks[(s, i)] = step_bank(s, i, [P, 2, HALF])
-                    for e in range(2):
-                        at = g * PANEL + (2 * i + e) * P
-                        mx_pass(banks[(s, i)][:, e, :], *a_operand(at, at + P), *b_operand(o0, o0 + HALF))
-                elif kind == "P":
-                    o0 = c * PANEL + u * P
-                    banks[(s, i)] = step_bank(s, i, [P, SLOTS, P])
-                    for t in range(SLOTS):
-                        at = g * PANEL + t * P
-                        mx_pass(banks[(s, i)][:, t, :], *a_operand(at, at + P), *b_operand(o0, o0 + P))
+        def fill(r, u):
+            c, g = divmod(r, GROUPS)
+            j = c * SLOTS + u
+            if KINDS[r][u] == "P":
+                banks[(r, u)] = take(piece_free, [P, SLOTS, P])
+                for t in range(SLOTS):
+                    at = g * PANEL + t * P
+                    mx_pass(banks[(r, u)][1][:, t, :], *a_operand(at, at + P), *b_operand(j * P, (j + 1) * P))
+            else:
+                b, bank = take(piece_free, [P, PANEL])
+                mx_pass(bank[:], *b_operand(j * P, (j + 1) * P), *a_operand(g * PANEL, (g + 1) * PANEL))
+                scaled[(r, u)] = work.tile([P, PANEL], F32, name="scaled", tag="scaled", bufs=4)
+                nc.scalar.activation(out=scaled[(r, u)][:], in_=bank[:], func=COPY, scale=gain_col[:, j : j + 1])
+                unturned.append((r, u, b))
 
-        def plain_width(s):
-            return P * sum(place(s, i)[3] == "P" for i in range(2))
+        def turn_back():
+            for r, u, b in unturned:
+                banks[(r, u)] = take([b], [P, SLOTS, P])
+                if KINDS[r][u] == "S":
+                    nc.tensor.matmul(banks[(r, u)][1][:], lhsT=ident_bf[:], rhs=w_raw[r][:, :, u * P : (u + 1) * P], start=True, stop=False)
+            for r, u, b in unturned:
+                kind = KINDS[r][u]
+                for t in range(SLOTS):
+                    nc.tensor.matmul(
+                        banks[(r, u)][1][:, t, :],
+                        lhsT=scaled[(r, u)][:, t * P : (t + 1) * P],
+                        rhs=ident[:],
+                        is_transpose=True,
+                        start=kind == "V",
+                        stop=kind == "V" or t == SLOTS - 1,
+                    )
+            unturned.clear()
 
-        def weave(s):
-            words = plain_width(s) // 2
-            if words:
-                c, g, u, kind = place(s, 0)
-                woven[s] = work.tile([P, P, SLOTS], F32, name="woven", tag="woven", bufs=3, align_bytes=ALIGN)
+        def weave(r, lo, hi):
+            if 0 <= r < ROWS and lo < hi:
+                if lo == 0:
+                    woven[r] = work.tile([P, HALF, SLOTS], F32, name="woven", tag="woven", bufs=3, align_bytes=ALIGN)
                 nc.scalar.copy(
-                    out=woven[s][:, 0:words, :].rearrange("p (n i) t -> p n t i", i=RUN // 2),
-                    in_=w_raw[(c, g)][:].bitcast(F32)[:, :, u * P // 2 : u * P // 2 + words].rearrange("p t (n i) -> p n t i", i=RUN // 2),
+                    out=woven[r][:, lo // 2 : hi // 2, :].rearrange("p (n i) t -> p n t i", i=RUN // 2),
+                    in_=w_raw[r][:].bitcast(F32)[:, :, lo // 2 : hi // 2].rearrange("p t (n i) -> p n t i", i=RUN // 2),
                 )
 
-        def empty_bank(s, i):
-            c, g, u, kind = place(s, i)
-            row = s // 2
-            if u == 0:
-                wm[row] = work.tile([P, PANEL, SLOTS], BF16, name="wm", tag="wm", bufs=3, align_bytes=ALIGN)
-            if i == 0 and kind == "P":
-                gained[s] = work.tile([P, HALF * SLOTS], F32, name="gained", tag="gained", bufs=4)
+        def wm_cols(r, lo, hi):
+            if lo < HALF:
+                return wm_first[:, lo:hi, :]
+            return wm_second[r % 2][:, lo - HALF : hi - HALF, :]
+
+        def empty(r, u):
+            c = r // GROUPS
+            kind = KINDS[r][u]
+            b, bank = banks[(r, u)]
             cols = slice(u * P, (u + 1) * P)
-            by_column = banks[(s, i)][:].rearrange("p t o -> p o t")
-            if both_plain(s):
-                o0 = c * PANEL + (u - i) * P
+            by_column = bank[:].rearrange("p t o -> p o t")
+            if kind == "P":
+                if u == 0:
+                    gained[r] = work.tile([P, PANEL, SLOTS], F32, name="gained", tag="gained", bufs=3)
                 nc.vector.tensor_tensor(
-                    out=gained[s][:].rearrange("p (h o e) -> p h o e", h=2, e=2)[:, i, :, :],
-                    in0=by_column,
-                    in1=gain_all[:, o0 : o0 + HALF].unsqueeze(2).to_broadcast([P, HALF, 2]),
-                    op=MULT,
-                )
-            elif kind == "P":
-                o0 = c * PANEL + u * P
-                nc.vector.tensor_tensor(
-                    out=gained[s][:].rearrange("p (o t) -> p o t", t=SLOTS)[:, 0:P, :],
-                    in0=by_column,
-                    in1=gain_all[:, o0 : o0 + P].unsqueeze(2).to_broadcast([P, P, SLOTS]),
-                    op=MULT,
+                    out=gained[r][:, cols, :], in0=by_column, in1=gain_all[c][:, cols].unsqueeze(2).to_broadcast([P, P, SLOTS]), op=MULT
                 )
             elif kind == "S":
-                nc.scalar.copy(out=wm[row][:, cols, :], in_=by_column)
+                nc.scalar.copy(out=wm_cols(r, u * P, (u + 1) * P), in_=by_column)
             else:
                 nc.vector.tensor_tensor(
-                    out=wm[row][:, cols, :].rearrange("p (n i) t -> p n t i", i=RUN),
-                    in0=banks[(s, i)][:].rearrange("p t (n i) -> p n t i", i=RUN),
-                    in1=w_raw[(c, g)][:, :, cols].rearrange("p t (n i) -> p n t i", i=RUN),
+                    out=wm_cols(r, u * P, (u + 1) * P).rearrange("p (n i) t -> p n t i", i=RUN),
+                    in0=bank[:].rearrange("p t (n i) -> p n t i", i=RUN),
+                    in1=w_raw[r][:, :, cols].rearrange("p t (n i) -> p n t i", i=RUN),
+                    op=ADD,
+                )
+            piece_free.append(b)
+
+        def add_plain(engine, r, lo, hi):
+            if 0 <= r < ROWS and lo < hi:
+                engine.tensor_tensor(
+                    out=wm_cols(r, lo, hi).rearrange("p (m f) t -> p m f t", f=2),
+                    in0=gained[r][:, lo:hi, :].rearrange("p (m f) t -> p m f t", f=2),
+                    in1=woven[r][:].bitcast(BF16)[:, lo // 2 : hi // 2, :].rearrange("p m (t f) -> p m f t", f=2),
                     op=ADD,
                 )
 
-        def add_plain(s):
-            lo = s % 2 * HALF
-            if both_plain(s):
-                nc.vector.tensor_tensor(
-                    out=wm[s // 2][:, lo : lo + HALF, :].rearrange("p (m f) (h e) -> p m f h e", f=2, h=2),
-                    in0=gained[s][:].rearrange("p (h m f e) -> p m f h e", h=2, f=2, e=2),
-                    in1=woven[s][:].bitcast(BF16).rearrange("p m (h e f) -> p m f h e", h=2, f=2),
-                    op=ADD,
-                )
-            elif plain_width(s):
-                nc.vector.tensor_tensor(
-                    out=wm[s // 2][:, lo : lo + P, :].rearrange("p (m f) t -> p m f t", f=2),
-                    in0=gained[s][:].rearrange("p (m f t) -> p m f t", f=2, t=SLOTS)[:, 0 : P // 2, :, :],
-                    in1=woven[s][:].bitcast(BF16)[:, 0 : P // 2, :].rearrange("p m (t f) -> p m f t", f=2),
-                    op=ADD,
-                )
+        quantised = []
 
-        def wm_quantise(row, lo=0, hi=PANEL):
-            quantise(w_cod, w_pla, row * PANEL + lo, wm[row][:, lo:hi, :])
+        def wm_quantise(r, lo=0, hi=PANEL):
+            quantise(w_cod, w_pla, r * PANEL + lo, wm_cols(r, lo, hi))
+            if hi == PANEL:
+                quantised.append(r)
 
-        y_banks = {}
+        waiting = [(c, m) for c in range(PANELS) for m in range(T_TILES)]
+        opened, y_banks, y_next, closed = [], {}, {}, []
 
-        def y_passes(c, m, groups, bank=None):
-            if groups[0] == 0:
-                if bank is None:
-                    bank = ring_bank([P, PANEL])
-                    if len(groups) < GROUPS:
-                        open_tiles[(c, m)] = ring[0]
-                y_banks[(c, m)] = bank
-            for g in groups:
-                cols = slice((c * GROUPS + g) * PANEL, (c * GROUPS + g + 1) * PANEL)
-                mx_pass(
-                    y_banks[(c, m)][:],
-                    x_cod[:, g, m * 2 * P : (m + 1) * 2 * P].bitcast(E2M1X4),
-                    x_pla[:, g, m * P : (m + 1) * P],
-                    w_cod[:, cols].bitcast(E4M3X4),
-                    w_pla[:, cols],
-                    start=g == 0,
-                    stop=g == GROUPS - 1,
-                )
+        def y_pass(most_open):
+            ready = [k for k in opened if k[0] * GROUPS + y_next[k] in quantised]
+            if not ready:
+                if not waiting or not ring_free or len(opened) >= most_open or waiting[0][0] * GROUPS not in quantised:
+                    return
+                k = waiting[0]
+                waiting.remove(k)
+                opened.append(k)
+                y_banks[k] = take(ring_free, [P, PANEL])
+                y_next[k] = 0
+                ready = [k]
+            k = ready[0]
+            c, m = k
+            g = y_next[k]
+            cols = slice((c * GROUPS + g) * PANEL, (c * GROUPS + g + 1) * PANEL)
+            mx_pass(
+                y_banks[k][1][:],
+                x_cod[g][:, m * 2 * P : (m + 1) * 2 * P].bitcast(E2M1X4),
+                x_pla[:, g, m * P : (m + 1) * P],
+                w_cod[:, cols].bitcast(E4M3X4),
+                w_pla[:, cols],
+                start=g == 0,
+                stop=g == GROUPS - 1,
+            )
+            y_next[k] = g + 1
+            if g == GROUPS - 1:
+                opened.remove(k)
+                closed.append(k)
 
-        def y_store(c, m, copy):
-            res = work.tile([P, PANEL], F32, name="res", tag="res", bufs=T_TILES)
-            copy(out=res[:], in_=y_banks[(c, m)][:])
-            open_tiles[(c, m)] = None
+        def y_store(copy):
+            k = closed[0]
+            closed.remove(k)
+            c, m = k
+            res = work.tile([P, PANEL], F32, name="res", tag="res", bufs=RES_BUFS)
+            copy(out=res[:], in_=y_banks[k][1][:])
+            ring_free.append(y_banks[k][0])
             nc.sync.dma_start(out=out_view[m][:, c * PANEL : (c + 1) * PANEL], in_=res[:])
+
+        def store_closed():
+            for k in list(closed):
+                y_store(nc.scalar.copy)
+
+        def y_passes(count, most_open):
+            for i in range(count):
+                store_closed()
+                y_pass(most_open)
+
+        def spread_gain(c):
+            count = max(kinds.count("P") for kinds in KINDS[c * GROUPS : (c + 1) * GROUPS])
+            if count:
+                store_closed()
+                b, bank = take(ring_free, [P, count, P])
+                for u in range(count):
+                    j = c * SLOTS + u
+                    nc.tensor.matmul(bank[:, u, :], lhsT=ident_bf[:, j : j + 1].to_broadcast([P, P]), rhs=gain_rows[:], start=True, stop=True)
+                nc.scalar.copy(out=gain_all[c][:, 0 : count * P], in_=bank[:].rearrange("p u o -> p (u o)"))
+                ring_free.append(b)
+
+        def early(r, u):
+            return u * P < G_COLS[r] and KINDS[r][u] == "P"
+
+        def emptied(w):
+            soon = [(w + 2, u) for u in pieces(w + 2, "P") if early(w + 2, u)]
+            rest = [(w + 1, u) for u in pieces(w + 1, "PVS") if not early(w + 1, u)]
+            return rest + soon
+
+        unfilled = [k for w in range(-2, ROWS - 1) for k in emptied(w)]
+
+        def fill_next():
+            if unfilled and piece_free:
+                r, u = unfilled[0]
+                if r % GROUPS in ad_done and (r // GROUPS, u // 2) in b_done:
+                    unfilled.remove((r, u))
+                    fill(r, u)
+
+        def fill_all():
+            for i in range(PIECE_BANKS):
+                fill_next()
 
         nc.scalar.activation(out=ident_bf[:], in_=ident[:], func=COPY)
         ad_turn(0, 0)
         ad_turn(0, 1)
-        gain_banks = {}
-        for c in range(1, PANELS):
-            count = max(kinds.count("P") for kinds in KINDS[c * GROUPS : (c + 1) * GROUPS])
-            gain_banks[c] = step_bank(1, c - 1, [P, count, P])
-            for u in range(count):
-                j = c * SLOTS + u
-                nc.tensor.matmul(gain_banks[c][:, u, :], lhsT=ident_bf[:, j : j + 1].to_broadcast([P, P]), rhs=gain_rows[:], start=True, stop=True)
-        col_bank = step_bank(0, 0, [P, PIECES])
+        col_b, col_bank = take(piece_free, [P, PIECES])
         nc.tensor.matmul(col_bank[:], lhsT=gain_rows[:], rhs=ident_bf[:, 0:PIECES], start=True, stop=True)
         b_tiles(0)
         ad_product(0, 0)
@@ -360,103 +382,86 @@ def tile_vera_merged_layer_s13_kernel(tc, x_words, x_scales, a, bmat_bytes, bmat
             b_widen_vector(0, t)
             b_widen_scalar(0, t + 2)
         ad_product(0, 1)
-        ad_turn(1, 0)
-        ad_turn(1, 1)
         b_interleave(nc.vector.tensor_copy, 0, 0)
         b_interleave(nc.scalar.copy, 0, 1)
         nc.scalar.copy(out=gain_col[:], in_=col_bank[:])
-        for c in range(1, PANELS):
-            spread = gain_banks[c][:].rearrange("p u o -> p (u o)")
-            nc.scalar.copy(out=gain_all[:, c * PANEL : c * PANEL + spread.shape[1]], in_=spread)
+        piece_free.append(col_b)
+        spread_gain(0)
+        ad_turn(1, 0)
+        ad_turn(1, 1)
         ad_quantise(0)
-        b_quantise(0, 0, HALF)
-        turned_product(0)
-        turned_scale(0)
+        b_quantise(0, 0)
+        fill_all()
         ad_product(1, 0)
-        b_quantise(0, HALF, PANEL)
         ad_product(1, 1)
-        turned_product(1)
-        turned_scale(1)
-        turn_back(0)
+        b_quantise(0, 1)
+        weave(0, 0, HALF)
+        fill_all()
         ad_turn(2, 0)
-        ad_quantise(1)
+        ad_turn(2, 1)
+        turn_back()
+        for r, u in emptied(-2):
+            empty(r, u)
 
-        def b_prepare(s):
-            if s in (0, 4):
-                b_tiles(s // 4 + 1)
-            if s < 2:
-                b_widen_scalar(1, 2 * s)
-                b_widen_scalar(1, 2 * s + 1)
-            elif s < 4:
-                b_interleave(nc.scalar.copy, 1, s - 2)
-            elif s < 8:
-                b_widen_scalar(2, s - 4)
-            elif s in (8, 10):
-                b_interleave(nc.scalar.copy, 2, (s - 8) // 2)
+        def scalar_extras(w):
+            for kind, c, i in B_WORK.get(w, []):
+                if kind == "tiles":
+                    b_tiles(c)
+                elif kind == "gain":
+                    spread_gain(c)
+                elif kind == "widen":
+                    b_widen_scalar(c, i)
+                else:
+                    b_interleave(nc.scalar.copy, c, i)
 
-        b_due = {PANEL_STEPS - 3: 1, 2 * PANEL_STEPS - 2: 2}
-        early_group = {max(4, 2 * g + 3): g for g in range(GROUPS)}
-        whole_tiles = {s: 2 if s in (19, 21) else 1 for s in range(10, STEPS - 2)}
-        todo = [(0, m) for m in range(EARLY_FIRST, T_TILES)] + [(1, m) for m in range(T_TILES)]
+        def plain_cols(r):
+            return P * len(pieces(r, "P"))
 
-        to_store = []
-        last = PANELS - 1
-        for s in range(STEPS):
-            ad_group, ad_half = s // 2 + 2, s % 2
-            if ad_group < GROUPS and ad_half == 1:
-                ad_product(ad_group, 1)
-            empty_bank(s, 0)
-            if ad_group < GROUPS and ad_half == 0:
-                ad_product(ad_group, 0)
-            if ad_group < GROUPS and ad_half == 1:
-                ad_quantise(ad_group)
-            if s > 0:
-                add_plain(s - 1)
-            empty_bank(s, 1)
-            if s in b_due:
-                b_quantise(b_due[s], 0, PANEL)
-            if s % 2 == 0 and s > 0:
-                wm_quantise(s // 2 - 1)
+        def g_cols(r):
+            return G_COLS[r] if 0 <= r < ROWS else 0
 
-            if s + 1 < STEPS:
-                plain_product(s + 1)
-            if s + 2 < STEPS:
-                turned_product(s + 2)
-            if (s + 1) // 2 + 2 < GROUPS:
-                ad_turn((s + 1) // 2 + 2, (s + 1) % 2)
-            if s + 1 < STEPS:
-                turn_back(s + 1)
-            if s + 2 < STEPS:
-                turned_scale(s + 2)
-            for c, m in to_store:
-                y_store(c, m, nc.scalar.copy)
-            to_store = todo[: whole_tiles.get(s, 0)]
-            todo = todo[len(to_store) :]
-            for c, m in to_store:
-                y_passes(c, m, range(GROUPS))
-            if s in early_group:
-                for m in range(EARLY_FIRST):
-                    y_passes(0, m, [early_group[s]])
-                if early_group[s] == GROUPS - 1:
-                    to_store = [(0, m) for m in range(EARLY_FIRST)]
-            if s + 2 < STEPS:
-                weave(s + 2)
-            b_prepare(s)
-            if s == STEPS - 2:
-                for m in range(4):
-                    y_passes(last, m, range(0, 2))
-            if s == STEPS - 1:
-                for m in range(4):
-                    y_passes(last, m, range(2, 3))
+        def locked(w):
+            if w in B_DUE:
+                b_quantise(*B_DUE[w])
+            if w + 2 < GROUPS:
+                ad_quantise(w + 2)
+            if w >= 0:
+                add_plain(nc.vector, w, g_cols(w), min(HALF, plain_cols(w)))
+                add_plain(nc.vector, w, max(HALF, g_cols(w)), plain_cols(w))
+                wm_quantise(w, 0, HALF)
+                wm_quantise(w, HALF, PANEL)
 
-        wm_quantise(ROWS - 1, 0, HALF)
-        add_plain(STEPS - 1)
-        for m in range(4, EARLY_LAST):
-            y_passes(last, m, range(0, 3), step_bank(m // 2, m % 2, [P, PANEL]))
-        wm_quantise(ROWS - 1, HALF, PANEL)
-        for m in range(T_TILES):
-            if m < EARLY_LAST:
-                y_passes(last, m, range(3, 4))
-            else:
-                y_passes(last, m, range(GROUPS), step_bank(m // 2, m % 2, [P, PANEL]))
-            y_store(last, m, nc.scalar.copy if m % 2 == 0 else nc.vector.tensor_copy)
+        scalar_extras(-2)
+        for w in range(-1, ROWS - 1):
+            locked(w)
+            add_plain(nc.gpsimd, w + 1, 0, g_cols(w + 1))
+            weave(w + 2, 0, min(HALF, plain_cols(w + 2)))
+            weave(w + 2, HALF, plain_cols(w + 2))
+            fill_all()
+            todo = emptied(w)
+            for i, (r, u) in enumerate(todo):
+                if w + 3 < GROUPS and i in AD_AT[w]:
+                    ad_product(w + 3, AD_AT[w].index(i))
+                    if AD_AT[w] == [i, i]:
+                        ad_product(w + 3, 1)
+                empty(r, u)
+                fill_next()
+                y_passes(Y_RATE[w][min(i, len(Y_RATE[w]) - 1)], Y_OPEN[w])
+            if w + 4 < GROUPS:
+                ad_turn(w + 4, 0)
+                ad_turn(w + 4, 1)
+            turn_back()
+            scalar_extras(w)
+            if not unfilled:
+                ring_free.extend(piece_free)
+                piece_free.clear()
+
+        y_passes(TAIL_EARLY, 8)
+        locked(ROWS - 1)
+        for k in list(closed):
+            y_store(nc.scalar.copy)
+        for i in range(T_TILES * GROUPS):
+            y_pass(8)
+            if closed:
+                y_store(nc.scalar.copy if closed[0][1] % 2 == 0 else nc.vector.tensor_copy)
+        assert not waiting and not opened and not closed

@@ -32,15 +32,17 @@ FLOPS = 2 * IN * R * OUT + 2 * T * IN * OUT
 ALIGN = 64
 PIECE_BANKS = 4
 RES_BUFS = 8
-KINDS = ["PPVV"] * 4 + ["PPPP"] * 8
-G_COLS = [256] * 11 + [128]
-B_DUE = {2: (1, 0), 3: (1, 1), 5: (2, 0), 6: (2, 1)}
-B_WORK = {-2: [("tiles", 1, 0), ("widen", 1, 0), ("widen", 1, 1)], -1: [("gain", 1, 0), ("widen", 1, 2), ("widen", 1, 3)], 0: [("weave", 1, 0)], 1: [("weave", 1, 1), ("tiles", 2, 0), ("widen", 2, 0)], 2: [("widen", 2, 1), ("widen", 2, 2)],
-          3: [("widen", 2, 3), ("weave", 2, 0)], 4: [("weave", 2, 1), ("gain", 2, 0)]}
+KINDS = ["PPVV"] * 4 + ["PPPP", "PPVV", "PPPP", "PPVV", "PPPP", "PPVV", "PPPP", "PPVV"]
+G_COLS = [256] * 2 + [192] * 9 + [64]
+B_DUE = {2: (1, 0), 3: (1, 1), 6: (2, 0), 7: (2, 1)}
+B_WORK = {-2: [("tiles", 1, 0), ("widen", 1, 0), ("widen", 1, 1)], -0.5: [("widen", 1, 2)], -1: [("widen", 1, 3), ("weave", 1, 0), ("gain", 1, 0)], 0: [("weave", 1, 1)], 1: [("tiles", 2, 0), ("widen", 2, 0), ("widen", 2, 1)], 2: [("widen", 2, 2), ("widen", 2, 3)],
+          4.5: [("weave", 2, 0)], 6.5: [("weave", 2, 1)]}
 AD_AT = {-1: [0, 0], 0: [1, 3]}
-Y_RATE = {-1: [0], 0: [0, 0, 1], 1: [1, 1, 2, 2], 2: [1], 3: [2], 4: [3], 5: [3], 6: [3], 7: [3], 8: [3], 9: [3], 10: [4]}
+Y_RATE = {-1: [0], 0: [0, 0, 1], 1: [1, 1, 2, 2], 2: [1], 3: [1, 3, 0, 4], 4: [2, 2, 2, 3], 5: [1, 3, 0, 4], 6: [2, 2, 2, 3], 7: [1, 3, 0, 4], 8: [2, 2, 2, 3], 9: [1, 3, 0, 4], 10: [3]}
 Y_OPEN = {-1: 0, 0: 2, 1: 4, 2: 4, 3: 4, 4: 3, 5: 4, 6: 4, 7: 4, 8: 4, 9: 4, 10: 8}
-TAIL_EARLY = 12
+TAIL_EARLY = 4
+TURN_AT = {3: 2, 5: 2, 7: 2, 9: 2}
+PAIRS = True
 
 
 def tile_vera_merged_layer_s13_kernel(tc, x_words, x_scales, a, bmat_bytes, bmat_scale, d_gain, b_gain, w0, out):
@@ -124,14 +126,15 @@ def tile_vera_merged_layer_s13_kernel(tc, x_words, x_scales, a, bmat_bytes, bmat
         load_x_scales()
         load_x(0)
         load_w(2)
+        load_b(2)
         load_x(1)
         load_w(3)
         load_x(2)
-        load_b(2)
         load_w(4)
         load_x(3)
         for r in range(5, ROWS):
             load_w(r)
+        nc.sync.dma_start(out=gain_all[2][:], in_=b_gain[2 * PANEL : 3 * PANEL].partition_broadcast(P))
 
         def quantise(codes, plane, at, grouped):
             cols = slice(at, at + grouped.shape[1])
@@ -201,12 +204,20 @@ def tile_vera_merged_layer_s13_kernel(tc, x_words, x_scales, a, bmat_bytes, bmat
         def pieces(r, kinds):
             return [u for u in range(SLOTS) if 0 <= r < ROWS and KINDS[r][u] in kinds]
 
+        def paired(r, u):
+            return PAIRS and u >= 2 and KINDS[r] == "PPPP"
+
         unturned = []
 
         def fill(r, u):
             c, g = divmod(r, GROUPS)
             j = c * SLOTS + u
-            if KINDS[r][u] == "P":
+            if paired(r, u):
+                banks[(r, u)] = take(piece_free, [P, 2, HALF])
+                for e in range(2):
+                    at = g * PANEL + (2 * (u - 2) + e) * P
+                    mx_pass(banks[(r, u)][1][:, e, :], *a_operand(at, at + P), *b_operand(c * PANEL + HALF, (c + 1) * PANEL))
+            elif KINDS[r][u] == "P":
                 banks[(r, u)] = take(piece_free, [P, SLOTS, P])
                 for t in range(SLOTS):
                     at = g * PANEL + t * P
@@ -256,9 +267,16 @@ def tile_vera_merged_layer_s13_kernel(tc, x_words, x_scales, a, bmat_bytes, bmat
             b, bank = banks[(r, u)]
             cols = slice(u * P, (u + 1) * P)
             by_column = bank[:].rearrange("p t o -> p o t")
-            if kind == "P":
-                if u == 0:
-                    gained[r] = work.tile([P, PANEL, SLOTS], F32, name="gained", tag="gained", bufs=3)
+            if kind == "P" and u == 0:
+                gained[r] = work.tile([P, PANEL, SLOTS], F32, name="gained", tag="gained", bufs=3)
+            if paired(r, u):
+                nc.vector.tensor_tensor(
+                    out=gained[r][:, HALF:PANEL, :].rearrange("p o t -> p (o t)").rearrange("p (h o e) -> p h o e", h=2, e=2)[:, u - 2, :, :],
+                    in0=by_column,
+                    in1=gain_all[c][:, HALF:PANEL].unsqueeze(2).to_broadcast([P, HALF, 2]),
+                    op=MULT,
+                )
+            elif kind == "P":
                 nc.vector.tensor_tensor(
                     out=gained[r][:, cols, :], in0=by_column, in1=gain_all[c][:, cols].unsqueeze(2).to_broadcast([P, P, SLOTS]), op=MULT
                 )
@@ -274,7 +292,14 @@ def tile_vera_merged_layer_s13_kernel(tc, x_words, x_scales, a, bmat_bytes, bmat
             piece_free.append(b)
 
         def add_plain(engine, r, lo, hi):
-            if 0 <= r < ROWS and lo < hi:
+            if 0 <= r < ROWS and lo == HALF and paired(r, 2):
+                engine.tensor_tensor(
+                    out=wm_cols(r, lo, hi).rearrange("p (m f) (h e) -> p m f h e", f=2, h=2),
+                    in0=gained[r][:, HALF:PANEL, :].rearrange("p o t -> p (o t)").rearrange("p (h m f e) -> p m f h e", h=2, f=2, e=2),
+                    in1=woven[r][:].bitcast(BF16)[:, lo // 2 : hi // 2, :].rearrange("p m (h e f) -> p m f h e", h=2, f=2),
+                    op=ADD,
+                )
+            elif 0 <= r < ROWS and lo < hi:
                 engine.tensor_tensor(
                     out=wm_cols(r, lo, hi).rearrange("p (m f) t -> p m f t", f=2),
                     in0=gained[r][:, lo:hi, :].rearrange("p (m f) t -> p m f t", f=2),
@@ -334,9 +359,10 @@ def tile_vera_merged_layer_s13_kernel(tc, x_words, x_scales, a, bmat_bytes, bmat
             for k in list(closed):
                 y_store(nc.scalar.copy)
 
-        def y_passes(count, most_open):
+        def y_passes(count, most_open, store=True):
             for i in range(count):
-                store_closed()
+                if store:
+                    store_closed()
                 y_pass(most_open)
 
         def spread_gain(c):
@@ -421,12 +447,12 @@ def tile_vera_merged_layer_s13_kernel(tc, x_words, x_scales, a, bmat_bytes, bmat
             return G_COLS[r] if 0 <= r < ROWS else 0
 
         def locked(w):
+            add_plain(nc.vector, w, g_cols(w), min(HALF, plain_cols(w)))
             if w in B_DUE:
                 b_quantise(*B_DUE[w])
             if w + 2 < GROUPS:
                 ad_quantise(w + 2)
             if w >= 0:
-                add_plain(nc.vector, w, g_cols(w), min(HALF, plain_cols(w)))
                 add_plain(nc.vector, w, max(HALF, g_cols(w)), plain_cols(w))
                 wm_quantise(w, 0, HALF)
                 wm_quantise(w, HALF, PANEL)
@@ -435,6 +461,7 @@ def tile_vera_merged_layer_s13_kernel(tc, x_words, x_scales, a, bmat_bytes, bmat
         for w in range(-1, ROWS - 1):
             locked(w)
             add_plain(nc.gpsimd, w + 1, 0, g_cols(w + 1))
+            scalar_extras(w + 0.5)
             weave(w + 2, 0, min(HALF, plain_cols(w + 2)))
             weave(w + 2, HALF, plain_cols(w + 2))
             fill_all()
@@ -445,8 +472,10 @@ def tile_vera_merged_layer_s13_kernel(tc, x_words, x_scales, a, bmat_bytes, bmat
                     if AD_AT[w] == [i, i]:
                         ad_product(w + 3, 1)
                 empty(r, u)
+                if i == TURN_AT.get(w):
+                    turn_back()
                 fill_next()
-                y_passes(Y_RATE[w][min(i, len(Y_RATE[w]) - 1)], Y_OPEN[w])
+                y_passes(Y_RATE[w][min(i, len(Y_RATE[w]) - 1)], Y_OPEN[w], i > 0 or w not in TURN_AT)
             if w + 4 < GROUPS:
                 ad_turn(w + 4, 0)
                 ad_turn(w + 4, 1)

@@ -32,16 +32,16 @@ FLOPS = 2 * IN * R * OUT + 2 * T * IN * OUT
 ALIGN = 64
 PIECE_BANKS = 4
 RES_BUFS = 8
-KINDS = ["PPVV"] * 4 + ["PPPP", "PPVV", "PPPP", "PPVV", "PPPP", "PPVV", "PPPP", "PPVV"]
-G_COLS = [256] * 2 + [192] * 9 + [64]
-B_DUE = {2: (1, 0), 3: (1, 1), 6: (2, 0), 7: (2, 1)}
-B_WORK = {-2: [("tiles", 1, 0), ("widen", 1, 0), ("widen", 1, 1)], -0.5: [("widen", 1, 2)], -1: [("widen", 1, 3), ("weave", 1, 0), ("gain", 1, 0)], 0: [("weave", 1, 1)], 1: [("tiles", 2, 0), ("widen", 2, 0), ("widen", 2, 1)], 2: [("widen", 2, 2), ("widen", 2, 3)],
-          4.5: [("weave", 2, 0)], 6.5: [("weave", 2, 1)]}
+KINDS = ["PPVV"] * 4 + ["PPPP", "PPPP", "PPPP", "PPVV", "PPPP", "PPVV", "PPPP", "PPPP"]
+G_COLS = [256] * 2 + [192] * 9 + [128]
+B_DUE = {2: [(1, 0), (1, 1)], 5: [(2, 0)], 6: [(2, 1)]}
+B_WORK = {-2: [("tiles", 1, 0), ("widen", 1, 0), ("widen", 1, 1)], -0.5: [("widen", 1, 2)], -1: [("widen", 1, 3), ("weave", 1, 0)], 0: [("weave", 1, 1)], 1: [("tiles", 2, 0), ("widen", 2, 0), ("widen", 2, 1)], 2: [("widen", 2, 2), ("widen", 2, 3)],
+          4.5: [("weave", 2, 0)], 5.5: [("weave", 2, 1)]}
 AD_AT = {-1: [0, 0], 0: [1, 3]}
-Y_RATE = {-1: [0], 0: [0, 0, 1], 1: [1, 1, 2, 2], 2: [1], 3: [1, 3, 0, 4], 4: [2, 2, 2, 3], 5: [1, 3, 0, 4], 6: [2, 2, 2, 3], 7: [1, 3, 0, 4], 8: [2, 2, 2, 3], 9: [1, 3, 0, 4], 10: [3]}
+Y_RATE = {-1: [0], 0: [0, 0, 1], 1: [1, 1, 2, 2], 2: [1], 3: [2, 2, 2, 4], 4: [2, 2, 2, 4], 5: [1, 3, 0, 4], 6: [2, 2, 2, 3], 7: [1, 3, 0, 4], 8: [2, 2, 2, 3], 9: [2, 2, 2, 4], 10: [3]}
 Y_OPEN = {-1: 0, 0: 2, 1: 4, 2: 4, 3: 4, 4: 3, 5: 4, 6: 4, 7: 4, 8: 4, 9: 4, 10: 8}
 TAIL_EARLY = 4
-TURN_AT = {3: 2, 5: 2, 7: 2, 9: 2}
+TURN_AT = {5: 2, 7: 2}
 PAIRS = True
 
 
@@ -415,6 +415,7 @@ def tile_vera_merged_layer_s13_kernel(tc, x_words, x_scales, a, bmat_bytes, bmat
         spread_gain(0)
         ad_turn(1, 0)
         ad_turn(1, 1)
+        spread_gain(1)
         ad_quantise(0)
         b_quantise(0, 0)
         fill_all()
@@ -448,8 +449,8 @@ def tile_vera_merged_layer_s13_kernel(tc, x_words, x_scales, a, bmat_bytes, bmat
 
         def locked(w):
             add_plain(nc.vector, w, g_cols(w), min(HALF, plain_cols(w)))
-            if w in B_DUE:
-                b_quantise(*B_DUE[w])
+            for c, h in B_DUE.get(w, []):
+                b_quantise(c, h)
             if w + 2 < GROUPS:
                 ad_quantise(w + 2)
             if w >= 0:

@@ -33,16 +33,19 @@ ALIGN = 64
 PIECE_BANKS = 4
 RES_BUFS = 8
 KINDS = ["PPVV"] * 4 + ["PPPP", "PPPP", "PPPP", "PPVV", "PPPP", "PPVV", "PPPP", "PPPP"]
-G_COLS = [256] * 2 + [192] * 9 + [128]
+G_COLS = [256] * 2 + [208] * 9 + [144]
 B_DUE = {2: [(1, 0), (1, 1)], 5: [(2, 0)], 6: [(2, 1)]}
 B_WORK = {-2: [("tiles", 1, 0), ("widen", 1, 0), ("widen", 1, 1)], -0.5: [("widen", 1, 2)], -1: [("widen", 1, 3), ("weave", 1, 0)], 0: [("weave", 1, 1)], 1: [("tiles", 2, 0), ("widen", 2, 0), ("widen", 2, 1)], 2: [("widen", 2, 2), ("widen", 2, 3)],
           4.5: [("weave", 2, 0)], 5.5: [("weave", 2, 1)]}
-AD_AT = {-1: [0, 0], 0: [1, 3]}
+AD_AT = {-1: [0, 0], 0: [0, 1]}
 Y_RATE = {-1: [0], 0: [0, 0, 1], 1: [1, 1, 2, 2], 2: [1], 3: [2, 2, 2, 4], 4: [2, 2, 2, 4], 5: [1, 3, 0, 4], 6: [2, 2, 2, 3], 7: [1, 3, 0, 4], 8: [2, 2, 2, 3], 9: [2, 2, 2, 4], 10: [3]}
 Y_OPEN = {-1: 0, 0: 2, 1: 4, 2: 4, 3: 4, 4: 3, 5: 4, 6: 4, 7: 4, 8: 4, 9: 4, 10: 8}
 TAIL_EARLY = 4
 TURN_AT = {5: 2, 7: 2}
 PAIRS = True
+SPLIT_SOON = []
+LEND_AT = None
+RETURN_AT = None
 
 
 def tile_vera_merged_layer_s13_kernel(tc, x_words, x_scales, a, bmat_bytes, bmat_scale, d_gain, b_gain, w0, out):
@@ -177,8 +180,9 @@ def tile_vera_merged_layer_s13_kernel(tc, x_words, x_scales, a, bmat_bytes, bmat
         def b_widen_scalar(c, t):
             nc.scalar.activation(out=b_wide[c][:, t, :], in_=b_raw[c][:, t, :].bitcast(E4M3), func=COPY, scale=b_sc[:, t : t + 1])
 
-        def b_widen_vector(c, t):
-            nc.vector.tensor_scalar(out=b_wide[c][:, t, :], in0=b_raw[c][:, t, :].bitcast(E4M3), scalar1=b_sc[:, t : t + 1], scalar2=None, op0=MULT)
+        def b_widen_halves(t):
+            nc.vector.tensor_scalar(out=b_wide[0][:, t, 0:HALF], in0=b_raw[0][:, t, 0:HALF].bitcast(E4M3), scalar1=b_sc[:, t : t + 1], scalar2=None, op0=MULT)
+            nc.scalar.activation(out=b_wide[0][:, t, HALF:PANEL], in_=b_raw[0][:, t, HALF:PANEL].bitcast(E4M3), func=COPY, scale=b_sc[:, t : t + 1])
 
         def b_interleave(copy, c, h):
             cols = slice(h * HALF, (h + 1) * HALF)
@@ -382,7 +386,7 @@ def tile_vera_merged_layer_s13_kernel(tc, x_words, x_scales, a, bmat_bytes, bmat
         def emptied(w):
             soon = [(w + 2, u) for u in pieces(w + 2, "P") if early(w + 2, u)]
             rest = [(w + 1, u) for u in pieces(w + 1, "PVS") if not early(w + 1, u)]
-            return rest + soon
+            return soon[:1] + rest + soon[1:] if w in SPLIT_SOON else rest + soon
 
         unfilled = [k for w in range(-2, ROWS - 1) for k in emptied(w)]
 
@@ -404,9 +408,8 @@ def tile_vera_merged_layer_s13_kernel(tc, x_words, x_scales, a, bmat_bytes, bmat
         nc.tensor.matmul(col_bank[:], lhsT=gain_rows[:], rhs=ident_bf[:, 0:PIECES], start=True, stop=True)
         b_tiles(0)
         ad_product(0, 0)
-        for t in range(2):
-            b_widen_vector(0, t)
-            b_widen_scalar(0, t + 2)
+        for t in range(SLOTS):
+            b_widen_halves(t)
         ad_product(0, 1)
         b_interleave(nc.vector.tensor_copy, 0, 0)
         b_interleave(nc.scalar.copy, 0, 1)
@@ -473,6 +476,13 @@ def tile_vera_merged_layer_s13_kernel(tc, x_words, x_scales, a, bmat_bytes, bmat
                     if AD_AT[w] == [i, i]:
                         ad_product(w + 3, 1)
                 empty(r, u)
+                if (w, i) == LEND_AT:
+                    ring_free.append(piece_free[-1])
+                    piece_free.remove(piece_free[-1])
+                if (w, i) == RETURN_AT:
+                    store_closed()
+                    piece_free.append(ring_free[0])
+                    ring_free.remove(ring_free[0])
                 if i == TURN_AT.get(w):
                     turn_back()
                 fill_next()

@@ -32,16 +32,16 @@ FLOPS = 2 * IN * R * OUT + 2 * T * IN * OUT
 ALIGN = 64
 PIECE_BANKS = 4
 RES_BUFS = 8
-KINDS = ["PPVV"] * 4 + ["PPPP", "PPPP", "PPPP", "PPVV", "PPPP", "PPVV", "PPPP", "PPPP"]
-G_COLS = [256] * 2 + [208] * 9 + [144]
-B_DUE = {2: [(1, 0), (1, 1)], 5: [(2, 0)], 6: [(2, 1)]}
+KINDS = ["PPVV"] * 4 + ["PPPP", "PPVV", "PPPP", "PPVV", "PPPP", "PPVV", "PPPP", "PPPP"]
+G_COLS = [256, 256, 256, 256, 208, 256, 208, 256, 208, 256, 160, 128]
+B_DUE = {2: 1, 5: 2}
 B_WORK = {-2: [("tiles", 1, 0), ("widen", 1, 0), ("widen", 1, 1)], -0.5: [("widen", 1, 2)], -1: [("widen", 1, 3), ("weave", 1, 0)], 0: [("weave", 1, 1)], 1: [("tiles", 2, 0), ("widen", 2, 0), ("widen", 2, 1)], 2: [("widen", 2, 2), ("widen", 2, 3)],
-          4.5: [("weave", 2, 0)], 5.5: [("weave", 2, 1)]}
+          3.5: [("weave", 2, 0)], 4.5: [("weave", 2, 1)]}
 AD_AT = {-1: [0, 0], 0: [0, 1]}
-Y_RATE = {-1: [0], 0: [0, 0, 1], 1: [1, 1, 2, 2], 2: [1], 3: [2, 2, 2, 4], 4: [2, 2, 2, 4], 5: [1, 3, 0, 4], 6: [2, 2, 2, 3], 7: [1, 3, 0, 4], 8: [2, 2, 2, 3], 9: [2, 2, 2, 4], 10: [3]}
+Y_RATE = {-1: [0], 0: [0, 0, 1], 1: [1, 1, 2, 2], 2: [1], 3: [1, 3, 0, 4], 4: [2, 2, 2, 3], 5: [1, 3, 0, 4], 6: [2, 2, 2, 3], 7: [1, 3, 0, 4], 8: [2, 2, 2, 3], 9: [2, 2, 2, 4], 10: [3]}
 Y_OPEN = {-1: 0, 0: 2, 1: 4, 2: 4, 3: 4, 4: 3, 5: 4, 6: 4, 7: 4, 8: 4, 9: 4, 10: 8}
 TAIL_EARLY = 4
-TURN_AT = {5: 2, 7: 2}
+TURN_AT = {3: 2, 5: 2, 7: 2}
 PAIRS = True
 SPLIT_SOON = []
 LEND_AT = None
@@ -72,7 +72,7 @@ def tile_vera_merged_layer_s13_kernel(tc, x_words, x_scales, a, bmat_bytes, bmat
         w_raw = [keep.tile([P, SLOTS, PANEL], BF16, name="w_raw%d" % r, align_bytes=ALIGN) for r in range(ROWS)]
         w_cod = keep.tile([P, ROWS * PANEL], U32, name="w_cod", align_bytes=ALIGN)
         w_pla = keep.tile([P, ROWS * PANEL], U8, name="w_pla", align_bytes=ALIGN)
-        x_cod = [keep.tile([P, 2 * T], U8, name="x_cod%d" % g, align_bytes=ALIGN) for g in range(GROUPS)]
+        x_cod = {(i, j): keep.tile([P, 2, T], U8, name="x_cod%d%d" % (i, j), align_bytes=ALIGN) for i in range(2) for j in range(2)}
         x_pla = keep.tile([P, GROUPS, T], U8, name="x_pla", align_bytes=ALIGN)
 
         a_view = a.rearrange("(g p t) r -> g p t r", p=P, t=SLOTS)
@@ -110,8 +110,11 @@ def tile_vera_merged_layer_s13_kernel(tc, x_words, x_scales, a, bmat_bytes, bmat
                     in_=x_scales[:, 4 * q : 4 * q + 4, :].bitcast(I32).rearrange("g q n -> q g n"),
                 )
 
-        def load_x(g):
-            nc.sync.dma_start(out=x_cod[g][:].bitcast(I32), in_=x_words[g].bitcast(I32))
+        def load_x(n):
+            i, j = divmod(n, 2)
+            nc.sync.dma_start(
+                out=x_cod[(i, j)][:].bitcast(I32), in_=x_words[2 * j : 2 * j + 2, :, i * T : (i + 1) * T].bitcast(I32).rearrange("g p n -> p g n")
+            )
 
         gain_view = b_gain.rearrange("(j p) -> j p", p=P)
         load_a(0)
@@ -126,14 +129,14 @@ def tile_vera_merged_layer_s13_kernel(tc, x_words, x_scales, a, bmat_bytes, bmat
         load_b(1)
         load_w(1)
         load_a(3)
+        load_w(2)
         load_x_scales()
         load_x(0)
-        load_w(2)
+        load_w(3)
         load_b(2)
         load_x(1)
-        load_w(3)
-        load_x(2)
         load_w(4)
+        load_x(2)
         load_x(3)
         for r in range(5, ROWS):
             load_w(r)
@@ -194,6 +197,10 @@ def tile_vera_merged_layer_s13_kernel(tc, x_words, x_scales, a, bmat_bytes, bmat
         def b_quantise(c, h):
             quantise(b_cod, b_pla, c * PANEL + h * HALF, b_grp[c][:, h * HALF : (h + 1) * HALF, :])
             b_done.append((c, h))
+
+        def b_quantise_whole(c):
+            quantise(b_cod, b_pla, c * PANEL, b_grp[c][:])
+            b_done.extend([(c, 0), (c, 1)])
 
         def a_operand(lo, hi):
             return a_cod[:, lo:hi].bitcast(E4M3X4), a_pla[:, lo:hi]
@@ -338,7 +345,7 @@ def tile_vera_merged_layer_s13_kernel(tc, x_words, x_scales, a, bmat_bytes, bmat
             cols = slice((c * GROUPS + g) * PANEL, (c * GROUPS + g + 1) * PANEL)
             mx_pass(
                 y_banks[k][1][:],
-                x_cod[g][:, m * 2 * P : (m + 1) * 2 * P].bitcast(E2M1X4),
+                x_cod[(m // 4, g // 2)][:, g % 2, m % 4 * 2 * P : (m % 4 + 1) * 2 * P].bitcast(E2M1X4),
                 x_pla[:, g, m * P : (m + 1) * P],
                 w_cod[:, cols].bitcast(E4M3X4),
                 w_pla[:, cols],
@@ -452,8 +459,8 @@ def tile_vera_merged_layer_s13_kernel(tc, x_words, x_scales, a, bmat_bytes, bmat
 
         def locked(w):
             add_plain(nc.vector, w, g_cols(w), min(HALF, plain_cols(w)))
-            for c, h in B_DUE.get(w, []):
-                b_quantise(c, h)
+            if w in B_DUE:
+                b_quantise_whole(B_DUE[w])
             if w + 2 < GROUPS:
                 ad_quantise(w + 2)
             if w >= 0:

@@ -32,11 +32,10 @@ FLOPS = 2 * IN * R * OUT + 2 * T * IN * OUT
 ALIGN = 64
 PIECE_BANKS = 4
 RES_BUFS = 8
-KINDS = ["PPVV"] * 4 + ["PPPP", "PPVV", "PPPP", "PPVV", "PPPP", "PPVV", "PPPP", "PPPP"]
+KINDS = ["PPVS", "PPVS", "PPVV", "PPVV"] + ["PPPP", "PPVV", "PPPP", "PPVV", "PPPP", "PPVV", "PPPP", "PPPP"]
 G_COLS = [256, 256, 256, 256, 208, 256, 208, 256, 208, 256, 160, 128]
 B_DUE = {2: 1, 5: 2}
-B_WORK = {-2: [("tiles", 1, 0), ("widen", 1, 0), ("widen", 1, 1)], -0.5: [("widen", 1, 2)], -1: [("widen", 1, 3), ("weave", 1, 0)], 0: [("weave", 1, 1)], 1: [("tiles", 2, 0), ("widen", 2, 0), ("widen", 2, 1)], 2: [("widen", 2, 2), ("widen", 2, 3)],
-          3.5: [("weave", 2, 0)], 4.5: [("weave", 2, 1)]}
+B_WORK = {-2: [("tiles", 1, 0), ("widen", 1, 0), ("widen", 1, 1)], -0.5: [("widen", 1, 2)], 0.5: [("widen", 1, 3)], 0: [("weave", 1, 0)], 1.5: [("weave", 1, 1)], 2.5: [("tiles", 2, 0), ("widen", 2, 0), ("widen", 2, 1)], 2: [("widen", 2, 2), ("widen", 2, 3)], 3.5: [("weave", 2, 0)], 4.5: [("weave", 2, 1)]}
 AD_AT = {-1: [0, 0], 0: [0, 1]}
 Y_RATE = {-1: [0], 0: [0, 0, 1], 1: [1, 1, 2, 2], 2: [1], 3: [1, 3, 0, 4], 4: [2, 2, 2, 3], 5: [1, 3, 0, 4], 6: [2, 2, 2, 3], 7: [1, 3, 0, 4], 8: [2, 2, 2, 3], 9: [2, 2, 2, 4], 10: [3]}
 Y_OPEN = {-1: 0, 0: 2, 1: 4, 2: 4, 3: 4, 4: 3, 5: 4, 6: 4, 7: 4, 8: 4, 9: 4, 10: 8}
@@ -245,7 +244,7 @@ def tile_vera_merged_layer_s13_kernel(tc, x_words, x_scales, a, bmat_bytes, bmat
                 banks[(r, u)] = take([b], [P, SLOTS, P])
                 if KINDS[r][u] == "S":
                     nc.tensor.matmul(banks[(r, u)][1][:], lhsT=ident_bf[:], rhs=w_raw[r][:, :, u * P : (u + 1) * P], start=True, stop=False)
-            for r, u, b in unturned:
+            for r, u, b in sorted(unturned):
                 kind = KINDS[r][u]
                 for t in range(SLOTS):
                     nc.tensor.matmul(
@@ -260,8 +259,7 @@ def tile_vera_merged_layer_s13_kernel(tc, x_words, x_scales, a, bmat_bytes, bmat
 
         def weave(r, lo, hi):
             if 0 <= r < ROWS and lo < hi:
-                if lo == 0:
-                    woven[r] = work.tile([P, HALF, SLOTS], F32, name="woven", tag="woven", bufs=3, align_bytes=ALIGN)
+                woven[r] = work.tile([P, HALF, SLOTS], F32, name="woven", tag="woven", align_bytes=ALIGN)
                 nc.scalar.copy(
                     out=woven[r][:, lo // 2 : hi // 2, :].rearrange("p (n i) t -> p n t i", i=RUN // 2),
                     in_=w_raw[r][:].bitcast(F32)[:, :, lo // 2 : hi // 2].rearrange("p t (n i) -> p n t i", i=RUN // 2),
@@ -315,6 +313,16 @@ def tile_vera_merged_layer_s13_kernel(tc, x_words, x_scales, a, bmat_bytes, bmat
                     out=wm_cols(r, lo, hi).rearrange("p (m f) t -> p m f t", f=2),
                     in0=gained[r][:, lo:hi, :].rearrange("p (m f) t -> p m f t", f=2),
                     in1=woven[r][:].bitcast(BF16)[:, lo // 2 : hi // 2, :].rearrange("p m (t f) -> p m f t", f=2),
+                    op=ADD,
+                )
+
+        def add_gpsimd(r):
+            cols = g_cols(r)
+            if cols:
+                nc.gpsimd.tensor_tensor(
+                    out=wm_cols(r, 0, cols).rearrange("p (m f) t -> p m t f", f=2),
+                    in0=gained[r][:, 0:cols, :].rearrange("p (m f) t -> p m t f", f=2),
+                    in1=w_raw[r][:, :, 0:cols].rearrange("p t (m f) -> p m t f", f=2),
                     op=ADD,
                 )
 
@@ -392,7 +400,7 @@ def tile_vera_merged_layer_s13_kernel(tc, x_words, x_scales, a, bmat_bytes, bmat
 
         def emptied(w):
             soon = [(w + 2, u) for u in pieces(w + 2, "P") if early(w + 2, u)]
-            rest = [(w + 1, u) for u in pieces(w + 1, "PVS") if not early(w + 1, u)]
+            rest = [(w + 1, u) for u in pieces(w + 1, "S") + pieces(w + 1, "PV") if not early(w + 1, u)]
             return soon[:1] + rest + soon[1:] if w in SPLIT_SOON else rest + soon
 
         unfilled = [k for w in range(-2, ROWS - 1) for k in emptied(w)]
@@ -432,7 +440,6 @@ def tile_vera_merged_layer_s13_kernel(tc, x_words, x_scales, a, bmat_bytes, bmat
         ad_product(1, 0)
         ad_product(1, 1)
         b_quantise(0, 1)
-        weave(0, 0, HALF)
         fill_all()
         ad_turn(2, 0)
         ad_turn(2, 1)
@@ -471,12 +478,13 @@ def tile_vera_merged_layer_s13_kernel(tc, x_words, x_scales, a, bmat_bytes, bmat
         scalar_extras(-2)
         for w in range(-1, ROWS - 1):
             locked(w)
-            add_plain(nc.gpsimd, w + 1, 0, g_cols(w + 1))
+            add_gpsimd(w + 1)
+            for u in pieces(w + 1, "S"):
+                empty(w + 1, u)
             scalar_extras(w + 0.5)
-            weave(w + 2, 0, min(HALF, plain_cols(w + 2)))
-            weave(w + 2, HALF, plain_cols(w + 2))
+            weave(w + 2, g_cols(w + 2), plain_cols(w + 2))
             fill_all()
-            todo = emptied(w)
+            todo = [(r, u) for r, u in emptied(w) if KINDS[r][u] != "S"]
             for i, (r, u) in enumerate(todo):
                 if w + 3 < GROUPS and i in AD_AT[w]:
                     ad_product(w + 3, AD_AT[w].index(i))

@@ -33,9 +33,9 @@ ALIGN = 64
 PIECE_BANKS = 4
 RES_BUFS = 8
 KINDS = ["PPVS", "PPVS", "PPVV", "PPVV"] + ["PPPP", "PPVV", "PPPP", "PPVV", "PPPP", "PPVV", "PPPP", "PPPP"]
-G_COLS = [256, 256, 256, 256, 208, 256, 208, 256, 208, 256, 160, 128]
+G_COLS = [256, 256, 232, 232, 208, 256, 208, 256, 208, 256, 160, 128]
 B_DUE = {2: 1, 5: 2}
-B_WORK = {-2: [("tiles", 1, 0), ("widen", 1, 0), ("widen", 1, 1)], -0.5: [("widen", 1, 2)], 0.5: [("widen", 1, 3)], 0: [("weave", 1, 0)], 1.5: [("weave", 1, 1)], 2.5: [("tiles", 2, 0), ("widen", 2, 0), ("widen", 2, 1)], 2: [("widen", 2, 2), ("widen", 2, 3)], 3.5: [("weave", 2, 0)], 4.5: [("weave", 2, 1)]}
+B_WORK = {-2: [("tiles", 1, 0), ("widen", 1, 0), ("widen", 1, 1)], -0.5: [("widen", 1, 2)], -1: [("widen", 1, 3)], 0: [("weave", 1, 0), ("weave", 1, 1)], 1: [("tiles", 2, 0), ("widen", 2, 0), ("widen", 2, 1)], 2: [("widen", 2, 2), ("widen", 2, 3)], 3.5: [("weave", 2, 0)], 4.5: [("weave", 2, 1)]}
 AD_AT = {-1: [0, 0], 0: [0, 1]}
 Y_RATE = {-1: [0], 0: [0, 0, 1], 1: [1, 1, 2, 2], 2: [1], 3: [1, 3, 0, 4], 4: [2, 2, 2, 3], 5: [1, 3, 0, 4], 6: [2, 2, 2, 3], 7: [1, 3, 0, 4], 8: [2, 2, 2, 3], 9: [2, 2, 2, 4], 10: [3]}
 Y_OPEN = {-1: 0, 0: 2, 1: 4, 2: 4, 3: 4, 4: 3, 5: 4, 6: 4, 7: 4, 8: 4, 9: 4, 10: 8}
@@ -45,6 +45,7 @@ PAIRS = True
 SPLIT_SOON = []
 LEND_AT = None
 RETURN_AT = None
+RAW_ROWS = [0, 1, 2, 3]
 
 
 def tile_vera_merged_layer_s13_kernel(tc, x_words, x_scales, a, bmat_bytes, bmat_scale, d_gain, b_gain, w0, out):
@@ -116,10 +117,10 @@ def tile_vera_merged_layer_s13_kernel(tc, x_words, x_scales, a, bmat_bytes, bmat
             )
 
         gain_view = b_gain.rearrange("(j p) -> j p", p=P)
-        load_a(0)
         nc.sync.dma_start(out=b_sc[:], in_=bmat_scale.rearrange("(p t) o -> p (t o)", t=SLOTS))
-        nc.sync.dma_start(out=d_col[:], in_=d_gain.rearrange("(p t) -> p t", t=SLOTS))
         load_b(0)
+        load_a(0)
+        nc.sync.dma_start(out=d_col[:], in_=d_gain.rearrange("(p t) -> p t", t=SLOTS))
         nc.sync.dma_start(out=gain_rows[0:8, :], in_=gain_view[0:8])
         nc.sync.dma_start(out=gain_rows[8:PIECES, :], in_=gain_view[8:PIECES])
         load_a(1)
@@ -139,7 +140,6 @@ def tile_vera_merged_layer_s13_kernel(tc, x_words, x_scales, a, bmat_bytes, bmat
         load_x(3)
         for r in range(5, ROWS):
             load_w(r)
-        nc.sync.dma_start(out=gain_all[2][:], in_=b_gain[2 * PANEL : 3 * PANEL].partition_broadcast(P))
 
         def quantise(codes, plane, at, grouped):
             cols = slice(at, at + grouped.shape[1])
@@ -259,7 +259,8 @@ def tile_vera_merged_layer_s13_kernel(tc, x_words, x_scales, a, bmat_bytes, bmat
 
         def weave(r, lo, hi):
             if 0 <= r < ROWS and lo < hi:
-                woven[r] = work.tile([P, HALF, SLOTS], F32, name="woven", tag="woven", align_bytes=ALIGN)
+                if r not in woven:
+                    woven[r] = work.tile([P, HALF, SLOTS], F32, name="woven", tag="woven", bufs=3, align_bytes=ALIGN)
                 nc.scalar.copy(
                     out=woven[r][:, lo // 2 : hi // 2, :].rearrange("p (n i) t -> p n t i", i=RUN // 2),
                     in_=w_raw[r][:].bitcast(F32)[:, :, lo // 2 : hi // 2].rearrange("p t (n i) -> p n t i", i=RUN // 2),
@@ -387,13 +388,12 @@ def tile_vera_merged_layer_s13_kernel(tc, x_words, x_scales, a, bmat_bytes, bmat
         def spread_gain(c):
             count = max(kinds.count("P") for kinds in KINDS[c * GROUPS : (c + 1) * GROUPS])
             if count:
-                store_closed()
-                b, bank = take(ring_free, [P, count, P])
+                b, bank = take(piece_free, [P, count, P])
                 for u in range(count):
                     j = c * SLOTS + u
                     nc.tensor.matmul(bank[:, u, :], lhsT=ident_bf[:, j : j + 1].to_broadcast([P, P]), rhs=gain_rows[:], start=True, stop=True)
                 nc.scalar.copy(out=gain_all[c][:, 0 : count * P], in_=bank[:].rearrange("p u o -> p (u o)"))
-                ring_free.append(b)
+                piece_free.append(b)
 
         def early(r, u):
             return u * P < G_COLS[r] and KINDS[r][u] == "P"
@@ -422,25 +422,24 @@ def tile_vera_merged_layer_s13_kernel(tc, x_words, x_scales, a, bmat_bytes, bmat
         col_b, col_bank = take(piece_free, [P, PIECES])
         nc.tensor.matmul(col_bank[:], lhsT=gain_rows[:], rhs=ident_bf[:, 0:PIECES], start=True, stop=True)
         b_tiles(0)
-        ad_product(0, 0)
         for t in range(SLOTS):
             b_widen_halves(t)
-        ad_product(0, 1)
         b_interleave(nc.vector.tensor_copy, 0, 0)
         b_interleave(nc.scalar.copy, 0, 1)
+        ad_product(0, 0)
+        b_quantise(0, 0)
+        ad_product(0, 1)
+        b_quantise(0, 1)
         nc.scalar.copy(out=gain_col[:], in_=col_bank[:])
         piece_free.append(col_b)
-        spread_gain(0)
+        for c in range(PANELS):
+            spread_gain(c)
         ad_turn(1, 0)
         ad_turn(1, 1)
-        spread_gain(1)
         ad_quantise(0)
-        b_quantise(0, 0)
         fill_all()
         ad_product(1, 0)
         ad_product(1, 1)
-        b_quantise(0, 1)
-        fill_all()
         ad_turn(2, 0)
         ad_turn(2, 1)
         turn_back()
@@ -478,11 +477,18 @@ def tile_vera_merged_layer_s13_kernel(tc, x_words, x_scales, a, bmat_bytes, bmat
         scalar_extras(-2)
         for w in range(-1, ROWS - 1):
             locked(w)
-            add_gpsimd(w + 1)
+            if w + 1 in RAW_ROWS:
+                add_gpsimd(w + 1)
+            else:
+                add_plain(nc.gpsimd, w + 1, 0, g_cols(w + 1))
             for u in pieces(w + 1, "S"):
                 empty(w + 1, u)
             scalar_extras(w + 0.5)
-            weave(w + 2, g_cols(w + 2), plain_cols(w + 2))
+            if w + 2 in RAW_ROWS:
+                weave(w + 2, g_cols(w + 2), plain_cols(w + 2))
+            else:
+                weave(w + 2, 0, min(HALF, plain_cols(w + 2)))
+                weave(w + 2, HALF, plain_cols(w + 2))
             fill_all()
             todo = [(r, u) for r, u in emptied(w) if KINDS[r][u] != "S"]
             for i, (r, u) in enumerate(todo):

@@ -417,6 +417,16 @@ def tile_vera_merged_layer_s13_kernel(tc, x_words, x_scales, a, bmat_bytes, bmat
                 fill_next()
 
         nc.scalar.activation(out=ident_bf[:], in_=ident[:], func=COPY)
+        warm = keep.tile([P, PANEL], BF16, name="warm")
+        nc.vector.memset(warm[:], 0.0)
+
+        def warm_up(count):
+            b, bank = take(piece_free, [P, PANEL])
+            for i in range(count):
+                nc.tensor.matmul(bank[:], lhsT=warm[:, 0:P], rhs=warm[:], start=True, stop=True)
+            piece_free.append(b)
+
+        warm_up(4)
         ad_turn(0, 0)
         ad_turn(0, 1)
         col_b, col_bank = take(piece_free, [P, PIECES])

@@ -37,8 +37,8 @@ G_COLS = [256, 256, 232, 232, 208, 256, 208, 256, 208, 256, 160, 128]
 B_DUE = {2: 1, 5: 2}
 B_WORK = {-2: [("tiles", 1, 0), ("widen", 1, 0), ("widen", 1, 1)], -0.5: [("widen", 1, 2)], -1: [("widen", 1, 3)], 0: [("weave", 1, 0), ("weave", 1, 1)], 1: [("tiles", 2, 0), ("widen", 2, 0), ("widen", 2, 1)], 2: [("widen", 2, 2), ("widen", 2, 3)], 3.5: [("weave", 2, 0)], 4.5: [("weave", 2, 1)]}
 AD_AT = {-1: [0, 0], 0: [0, 1]}
-Y_RATE = {-1: [0], 0: [0, 0, 1], 1: [1, 1, 2, 2], 2: [1], 3: [1, 3, 0, 4], 4: [2, 2, 2, 3], 5: [1, 3, 0, 4], 6: [2, 2, 2, 3], 7: [1, 3, 0, 4], 8: [2, 2, 2, 3], 9: [2, 2, 2, 4], 10: [3]}
-Y_OPEN = {-1: 0, 0: 2, 1: 4, 2: 4, 3: 4, 4: 3, 5: 4, 6: 4, 7: 4, 8: 4, 9: 4, 10: 8}
+Y_RATE = {-1: [0], 0: [0, 0, 2], 1: [1, 1, 2, 2], 2: [1], 3: [1, 3, 0, 4], 4: [2, 2, 3, 3], 5: [1, 3, 0, 4], 6: [2, 2, 2, 3], 7: [1, 3, 0, 4], 8: [2, 2, 2, 3], 9: [2, 2, 2, 4], 10: [3]}
+Y_OPEN = {-1: 0, 0: 2, 1: 4, 2: 4, 3: 4, 4: 4, 5: 4, 6: 4, 7: 4, 8: 4, 9: 4, 10: 8}
 TAIL_EARLY = 4
 TURN_AT = {3: 2, 5: 2, 7: 2}
 PAIRS = True
@@ -73,7 +73,7 @@ def tile_vera_merged_layer_s13_kernel(tc, x_words, x_scales, a, bmat_bytes, bmat
         w_cod = keep.tile([P, ROWS * PANEL], U32, name="w_cod", align_bytes=ALIGN)
         w_pla = keep.tile([P, ROWS * PANEL], U8, name="w_pla", align_bytes=ALIGN)
         x_cod = {(i, j): keep.tile([P, 2, T], U8, name="x_cod%d%d" % (i, j), align_bytes=ALIGN) for i in range(2) for j in range(2)}
-        x_pla = keep.tile([P, GROUPS, T], U8, name="x_pla", align_bytes=ALIGN)
+        x_pla = [keep.tile([P, GROUPS, T // 2], U8, name="x_pla%d" % i, align_bytes=ALIGN) for i in range(2)]
 
         a_view = a.rearrange("(g p t) r -> g p t r", p=P, t=SLOTS)
         w_view = w0.rearrange("(g p t) o -> g p t o", p=P, t=SLOTS)
@@ -90,7 +90,8 @@ def tile_vera_merged_layer_s13_kernel(tc, x_words, x_scales, a, bmat_bytes, bmat
 
         nc.vector.memset(gain_rows[:], 0.0)
         make_identity(nc, ident[:])
-        nc.gpsimd.memset(x_pla[:].rearrange("p g n -> p (g n)").bitcast(U32), 0)
+        for plane in x_pla:
+            nc.gpsimd.memset(plane[:].rearrange("p g n -> p (g n)").bitcast(U32), 0)
 
         def load_a(g):
             for h in range(2):
@@ -103,11 +104,11 @@ def tile_vera_merged_layer_s13_kernel(tc, x_words, x_scales, a, bmat_bytes, bmat
             c, g = divmod(r, GROUPS)
             nc.sync.dma_start(out=w_raw[r][:], in_=w_view[g][:, :, c * PANEL : (c + 1) * PANEL])
 
-        def load_x_scales():
+        def load_x_scales(i):
             for q in range(4):
                 nc.sync.dma_start(
-                    out=x_pla[32 * q : 32 * q + 4, :, :].bitcast(I32),
-                    in_=x_scales[:, 4 * q : 4 * q + 4, :].bitcast(I32).rearrange("g q n -> q g n"),
+                    out=x_pla[i][32 * q : 32 * q + 4, :, :].bitcast(I32),
+                    in_=x_scales[:, 4 * q : 4 * q + 4, i * T // 2 : (i + 1) * T // 2].bitcast(I32).rearrange("g q n -> q g n"),
                 )
 
         def load_x(n):
@@ -130,12 +131,13 @@ def tile_vera_merged_layer_s13_kernel(tc, x_words, x_scales, a, bmat_bytes, bmat
         load_w(1)
         load_a(3)
         load_w(2)
-        load_x_scales()
+        load_x_scales(0)
         load_x(0)
         load_w(3)
         load_b(2)
         load_x(1)
         load_w(4)
+        load_x_scales(1)
         load_x(2)
         load_x(3)
         for r in range(5, ROWS):
@@ -355,7 +357,7 @@ def tile_vera_merged_layer_s13_kernel(tc, x_words, x_scales, a, bmat_bytes, bmat
             mx_pass(
                 y_banks[k][1][:],
                 x_cod[(m // 4, g // 2)][:, g % 2, m % 4 * 2 * P : (m % 4 + 1) * 2 * P].bitcast(E2M1X4),
-                x_pla[:, g, m * P : (m + 1) * P],
+                x_pla[m // 4][:, g, m % 4 * P : (m % 4 + 1) * P],
                 w_cod[:, cols].bitcast(E4M3X4),
                 w_pla[:, cols],
                 start=g == 0,
@@ -420,13 +422,13 @@ def tile_vera_merged_layer_s13_kernel(tc, x_words, x_scales, a, bmat_bytes, bmat
         warm = keep.tile([P, PANEL], BF16, name="warm")
         nc.vector.memset(warm[:], 0.0)
 
-        def warm_up(count):
-            b, bank = take(piece_free, [P, PANEL])
+        def warm_up(count, free=piece_free):
+            b, bank = take(free, [P, PANEL])
             for i in range(count):
                 nc.tensor.matmul(bank[:], lhsT=warm[:, 0:P], rhs=warm[:], start=True, stop=True)
-            piece_free.append(b)
+            free.append(b)
 
-        warm_up(4)
+        warm_up(5)
         ad_turn(0, 0)
         ad_turn(0, 1)
         col_b, col_bank = take(piece_free, [P, PIECES])
@@ -445,6 +447,7 @@ def tile_vera_merged_layer_s13_kernel(tc, x_words, x_scales, a, bmat_bytes, bmat
         for c in range(PANELS):
             spread_gain(c)
         ad_turn(1, 0)
+        warm_up(1)
         ad_turn(1, 1)
         ad_quantise(0)
         fill_all()

@@ -31,21 +31,11 @@ FLOPS = 2 * IN * R * OUT + 2 * T * IN * OUT
 
 ALIGN = 64
 PIECE_BANKS = 4
-RES_BUFS = 8
-KINDS = ["PPVS", "PPVS", "PPVV", "PPVV"] + ["PPPP", "PPVV", "PPPP", "PPVV", "PPPP", "PPVV", "PPPP", "PPPP"]
-G_COLS = [256, 256, 232, 232, 208, 256, 208, 256, 208, 256, 160, 128]
-B_DUE = {2: 1, 5: 2}
-B_WORK = {-2: [("tiles", 1, 0), ("widen", 1, 0), ("widen", 1, 1)], -0.5: [("widen", 1, 2)], -1: [("widen", 1, 3)], 0: [("weave", 1, 0), ("weave", 1, 1)], 1: [("tiles", 2, 0), ("widen", 2, 0), ("widen", 2, 1)], 2: [("widen", 2, 2), ("widen", 2, 3)], 3.5: [("weave", 2, 0)], 4.5: [("weave", 2, 1)]}
-AD_AT = {-1: [0, 0], 0: [0, 1]}
-Y_RATE = {-1: [0], 0: [0, 0, 2], 1: [1, 1, 2, 2], 2: [1], 3: [1, 3, 0, 4], 4: [2, 2, 3, 3], 5: [1, 3, 0, 4], 6: [2, 2, 2, 3], 7: [1, 3, 0, 4], 8: [2, 2, 2, 3], 9: [2, 2, 2, 4], 10: [3]}
-Y_OPEN = {-1: 0, 0: 2, 1: 4, 2: 4, 3: 4, 4: 4, 5: 4, 6: 4, 7: 4, 8: 4, 9: 4, 10: 8}
-TAIL_EARLY = 4
-TURN_AT = {3: 2, 5: 2, 7: 2}
-PAIRS = True
-SPLIT_SOON = []
-LEND_AT = None
-RETURN_AT = None
-RAW_ROWS = [0, 1, 2, 3]
+RES_BUFS = T_TILES
+KINDS = ["PPVS"] * 2 + ["PPVV"] * 2 + ["PPPP", "PPVV"] * 3 + ["PPPP"] * 2
+COLUMNS_PER_BANK = 52
+PASSES_PER_BANK = 3
+WARM_UPS = 5
 
 
 def tile_vera_merged_layer_s13_kernel(tc, x_words, x_scales, a, bmat_bytes, bmat_scale, d_gain, b_gain, w0, out):
@@ -217,7 +207,7 @@ def tile_vera_merged_layer_s13_kernel(tc, x_words, x_scales, a, bmat_bytes, bmat
             return [u for u in range(SLOTS) if 0 <= r < ROWS and KINDS[r][u] in kinds]
 
         def paired(r, u):
-            return PAIRS and u >= 2 and KINDS[r] == "PPPP"
+            return u >= 2 and KINDS[r] == "PPPP"
 
         unturned = []
 
@@ -321,28 +311,30 @@ def tile_vera_merged_layer_s13_kernel(tc, x_words, x_scales, a, bmat_bytes, bmat
 
         def add_gpsimd(r):
             cols = g_cols(r)
-            if cols:
+            if r < GROUPS:
                 nc.gpsimd.tensor_tensor(
                     out=wm_cols(r, 0, cols).rearrange("p (m f) t -> p m t f", f=2),
                     in0=gained[r][:, 0:cols, :].rearrange("p (m f) t -> p m t f", f=2),
                     in1=w_raw[r][:, :, 0:cols].rearrange("p t (m f) -> p m t f", f=2),
                     op=ADD,
                 )
+            else:
+                add_plain(nc.gpsimd, r, 0, cols)
 
         quantised = []
 
-        def wm_quantise(r, lo=0, hi=PANEL):
-            quantise(w_cod, w_pla, r * PANEL + lo, wm_cols(r, lo, hi))
-            if hi == PANEL:
-                quantised.append(r)
+        def wm_quantise(r):
+            for lo in (0, HALF):
+                quantise(w_cod, w_pla, r * PANEL + lo, wm_cols(r, lo, lo + HALF))
+            quantised.append(r)
 
         waiting = [(c, m) for c in range(PANELS) for m in range(T_TILES)]
         opened, y_banks, y_next, closed = [], {}, {}, []
 
-        def y_pass(most_open):
+        def y_pass():
             ready = [k for k in opened if k[0] * GROUPS + y_next[k] in quantised]
             if not ready:
-                if not waiting or not ring_free or len(opened) >= most_open or waiting[0][0] * GROUPS not in quantised:
+                if not waiting or not ring_free or waiting[0][0] * GROUPS not in quantised:
                     return
                 k = waiting[0]
                 waiting.remove(k)
@@ -381,29 +373,41 @@ def tile_vera_merged_layer_s13_kernel(tc, x_words, x_scales, a, bmat_bytes, bmat
             for k in list(closed):
                 y_store(nc.scalar.copy)
 
-        def y_passes(count, most_open, store=True):
+        def y_passes(count, store=True):
             for i in range(count):
                 if store:
                     store_closed()
-                y_pass(most_open)
+                y_pass()
 
         def spread_gain(c):
             count = max(kinds.count("P") for kinds in KINDS[c * GROUPS : (c + 1) * GROUPS])
-            if count:
-                b, bank = take(piece_free, [P, count, P])
-                for u in range(count):
-                    j = c * SLOTS + u
-                    nc.tensor.matmul(bank[:, u, :], lhsT=ident_bf[:, j : j + 1].to_broadcast([P, P]), rhs=gain_rows[:], start=True, stop=True)
-                nc.scalar.copy(out=gain_all[c][:, 0 : count * P], in_=bank[:].rearrange("p u o -> p (u o)"))
-                piece_free.append(b)
+            b, bank = take(piece_free, [P, SLOTS, P])
+            if c == 0:
+                nc.tensor.matmul(bank[:, count, 0:PIECES], lhsT=gain_rows[:], rhs=ident_bf[:, 0:PIECES], start=True, stop=True)
+            for u in range(count):
+                j = c * SLOTS + u
+                nc.tensor.matmul(bank[:, u, :], lhsT=ident_bf[:, j : j + 1].to_broadcast([P, P]), rhs=gain_rows[:], start=True, stop=True)
+            nc.scalar.copy(out=gain_all[c][:, 0 : count * P], in_=bank[:, 0:count, :].rearrange("p u o -> p (u o)"))
+            if c == 0:
+                nc.scalar.copy(out=gain_col[:], in_=bank[:, count, 0:PIECES])
+            piece_free.append(b)
 
         def early(r, u):
-            return u * P < G_COLS[r] and KINDS[r][u] == "P"
+            return u < (1 if r == ROWS - 1 else 2)
 
         def emptied(w):
-            soon = [(w + 2, u) for u in pieces(w + 2, "P") if early(w + 2, u)]
             rest = [(w + 1, u) for u in pieces(w + 1, "S") + pieces(w + 1, "PV") if not early(w + 1, u)]
-            return soon[:1] + rest + soon[1:] if w in SPLIT_SOON else rest + soon
+            return rest + [(w + 2, u) for u in pieces(w + 2, "P") if early(w + 2, u)]
+
+        def plain_cols(r):
+            return P * len(pieces(r, "P"))
+
+        def g_cols(r):
+            if not 0 <= r < ROWS:
+                return 0
+            if "S" in KINDS[r] or (r >= GROUPS and "V" in KINDS[r]):
+                return HALF
+            return min(COLUMNS_PER_BANK * len(emptied(r - 1)), P * len([u for u in range(SLOTS) if early(r, u)]))
 
         unfilled = [k for w in range(-2, ROWS - 1) for k in emptied(w)]
 
@@ -421,37 +425,29 @@ def tile_vera_merged_layer_s13_kernel(tc, x_words, x_scales, a, bmat_bytes, bmat
         nc.scalar.activation(out=ident_bf[:], in_=ident[:], func=COPY)
         warm = keep.tile([P, PANEL], BF16, name="warm")
         nc.vector.memset(warm[:], 0.0)
-
-        def warm_up(count, free=piece_free):
-            b, bank = take(free, [P, PANEL])
-            for i in range(count):
-                nc.tensor.matmul(bank[:], lhsT=warm[:, 0:P], rhs=warm[:], start=True, stop=True)
-            free.append(b)
-
-        warm_up(5)
+        warm_b, warm_bank = take(piece_free, [P, PANEL])
+        for i in range(WARM_UPS):
+            nc.tensor.matmul(warm_bank[:], lhsT=warm[:, 0:P], rhs=warm[:], start=True, stop=True)
         ad_turn(0, 0)
         ad_turn(0, 1)
-        col_b, col_bank = take(piece_free, [P, PIECES])
-        nc.tensor.matmul(col_bank[:], lhsT=gain_rows[:], rhs=ident_bf[:, 0:PIECES], start=True, stop=True)
         b_tiles(0)
         for t in range(SLOTS):
             b_widen_halves(t)
         b_interleave(nc.vector.tensor_copy, 0, 0)
         b_interleave(nc.scalar.copy, 0, 1)
-        ad_product(0, 0)
-        b_quantise(0, 0)
-        ad_product(0, 1)
-        b_quantise(0, 1)
-        nc.scalar.copy(out=gain_col[:], in_=col_bank[:])
-        piece_free.append(col_b)
         for c in range(PANELS):
             spread_gain(c)
+        ad_product(0, 0)
+        ad_product(0, 1)
         ad_turn(1, 0)
-        warm_up(1)
+        piece_free.insert(0, warm_b)
         ad_turn(1, 1)
+        b_quantise(0, 0)
         ad_quantise(0)
         fill_all()
         ad_product(1, 0)
+        b_quantise(0, 1)
+        fill_all()
         ad_product(1, 1)
         ad_turn(2, 0)
         ad_turn(2, 1)
@@ -459,83 +455,79 @@ def tile_vera_merged_layer_s13_kernel(tc, x_words, x_scales, a, bmat_bytes, bmat
         for r, u in emptied(-2):
             empty(r, u)
 
-        def scalar_extras(w):
-            for kind, c, i in B_WORK.get(w, []):
-                if kind == "tiles":
-                    b_tiles(c)
-                elif kind == "gain":
-                    spread_gain(c)
-                elif kind == "widen":
-                    b_widen_scalar(c, i)
-                else:
-                    b_interleave(nc.scalar.copy, c, i)
+        def b_widen(c, slots):
+            if slots[0] == 0:
+                b_tiles(c)
+            for t in slots:
+                b_widen_scalar(c, t)
 
-        def plain_cols(r):
-            return P * len(pieces(r, "P"))
-
-        def g_cols(r):
-            return G_COLS[r] if 0 <= r < ROWS else 0
-
-        def locked(w):
+        def holding_the_port(w):
             add_plain(nc.vector, w, g_cols(w), min(HALF, plain_cols(w)))
-            if w in B_DUE:
-                b_quantise_whole(B_DUE[w])
+            if w == GROUPS - 2:
+                b_quantise_whole(1)
+            if w == 2 * GROUPS - 3:
+                b_quantise_whole(2)
             if w + 2 < GROUPS:
                 ad_quantise(w + 2)
             if w >= 0:
                 add_plain(nc.vector, w, max(HALF, g_cols(w)), plain_cols(w))
-                wm_quantise(w, 0, HALF)
-                wm_quantise(w, HALF, PANEL)
+                wm_quantise(w)
 
-        scalar_extras(-2)
+        def passes_behind(w, i):
+            count = PASSES_PER_BANK - 1 if w + 2 < ROWS else PASSES_PER_BANK
+            if turning(w):
+                return (count - 1, count + 1, 0, 2 * count)[i]
+            return count + 1 if i == PIECE_BANKS - 1 else count
+
+        def turning(w):
+            return w >= 0 and len(pieces(w + 2, "VS")) > 0
+
+        b_widen(1, (0, 1))
         for w in range(-1, ROWS - 1):
-            locked(w)
-            if w + 1 in RAW_ROWS:
-                add_gpsimd(w + 1)
-            else:
-                add_plain(nc.gpsimd, w + 1, 0, g_cols(w + 1))
+            holding_the_port(w)
+            add_gpsimd(w + 1)
             for u in pieces(w + 1, "S"):
                 empty(w + 1, u)
-            scalar_extras(w + 0.5)
-            if w + 2 in RAW_ROWS:
+            if w == GROUPS:
+                b_interleave(nc.scalar.copy, 2, 1)
+            if w + 2 < GROUPS:
                 weave(w + 2, g_cols(w + 2), plain_cols(w + 2))
             else:
                 weave(w + 2, 0, min(HALF, plain_cols(w + 2)))
                 weave(w + 2, HALF, plain_cols(w + 2))
             fill_all()
-            todo = [(r, u) for r, u in emptied(w) if KINDS[r][u] != "S"]
-            for i, (r, u) in enumerate(todo):
-                if w + 3 < GROUPS and i in AD_AT[w]:
-                    ad_product(w + 3, AD_AT[w].index(i))
-                    if AD_AT[w] == [i, i]:
-                        ad_product(w + 3, 1)
+            if w == -1:
+                ad_product(2, 0)
+                ad_product(2, 1)
+            for i, (r, u) in enumerate([(r, u) for r, u in emptied(w) if KINDS[r][u] != "S"]):
+                if w == 0 and i < 2:
+                    ad_product(3, i)
                 empty(r, u)
-                if (w, i) == LEND_AT:
-                    ring_free.append(piece_free[-1])
-                    piece_free.remove(piece_free[-1])
-                if (w, i) == RETURN_AT:
-                    store_closed()
-                    piece_free.append(ring_free[0])
-                    ring_free.remove(ring_free[0])
-                if i == TURN_AT.get(w):
+                if turning(w) and i == 2:
                     turn_back()
                 fill_next()
-                y_passes(Y_RATE[w][min(i, len(Y_RATE[w]) - 1)], Y_OPEN[w], i > 0 or w not in TURN_AT)
-            if w + 4 < GROUPS:
-                ad_turn(w + 4, 0)
-                ad_turn(w + 4, 1)
-            turn_back()
-            scalar_extras(w)
+                y_passes(passes_behind(w, i), i > 0 or not turning(w))
+            if w == -1:
+                ad_turn(3, 0)
+                ad_turn(3, 1)
+                turn_back()
+                b_widen(1, (2, 3))
+            if w == 0:
+                b_interleave(nc.scalar.copy, 1, 0)
+                b_interleave(nc.scalar.copy, 1, 1)
+            if w == 1:
+                b_widen(2, range(SLOTS))
+            if w == 2:
+                b_interleave(nc.scalar.copy, 2, 0)
             if not unfilled:
                 ring_free.extend(piece_free)
                 piece_free.clear()
 
-        y_passes(TAIL_EARLY, 8)
-        locked(ROWS - 1)
-        for k in list(closed):
-            y_store(nc.scalar.copy)
+        y_passes(PIECE_BANKS)
+        holding_the_port(ROWS - 1)
+        store_closed()
         for i in range(T_TILES * GROUPS):
-            y_pass(8)
+            y_pass()
             if closed:
                 y_store(nc.scalar.copy if closed[0][1] % 2 == 0 else nc.vector.tensor_copy)
         assert not waiting and not opened and not closed

@@ -56,7 +56,7 @@ def tile_vera_merged_layer_s13_kernel(tc, x_words, x_scales, a, bmat_bytes, bmat
         b_raw = [keep.tile([P, SLOTS, PANEL], U8, name="b_raw%d" % c, align_bytes=ALIGN) for c in range(PANELS)]
         b_cod = keep.tile([P, OUT], U32, name="b_cod", align_bytes=ALIGN)
         b_pla = keep.tile([P, OUT], U8, name="b_pla", align_bytes=ALIGN)
-        a_raw = {(g, h): keep.tile([P, 2, R], BF16, name="a_raw%d%d" % (g, h), align_bytes=ALIGN) for g in range(GROUPS) for h in range(2)}
+        a_raw = [keep.tile([P, SLOTS, R], BF16, name="a_raw%d" % g, align_bytes=ALIGN) for g in range(GROUPS)]
         a_cod = keep.tile([P, IN], U32, name="a_cod", align_bytes=ALIGN)
         a_pla = keep.tile([P, IN], U8, name="a_pla", align_bytes=ALIGN)
         w_raw = [keep.tile([P, SLOTS, PANEL], BF16, name="w_raw%d" % r, align_bytes=ALIGN) for r in range(ROWS)]
@@ -84,8 +84,11 @@ def tile_vera_merged_layer_s13_kernel(tc, x_words, x_scales, a, bmat_bytes, bmat
             nc.gpsimd.memset(plane[:].rearrange("p g n -> p (g n)").bitcast(U32), 0)
 
         def load_a(g):
-            for h in range(2):
-                nc.sync.dma_start(out=a_raw[(g, h)][:], in_=a_view[g][:, 2 * h : 2 * h + 2, :])
+            if g == 0:
+                for h in range(2):
+                    nc.sync.dma_start(out=a_raw[g][:, 2 * h : 2 * h + 2, :], in_=a_view[g][:, 2 * h : 2 * h + 2, :])
+            else:
+                nc.sync.dma_start(out=a_raw[g][:], in_=a_view[g])
 
         def load_b(c):
             nc.sync.dma_start(out=b_raw[c][:], in_=b_view[:, :, c * PANEL : (c + 1) * PANEL])
@@ -108,18 +111,18 @@ def tile_vera_merged_layer_s13_kernel(tc, x_words, x_scales, a, bmat_bytes, bmat
             )
 
         gain_view = b_gain.rearrange("(j p) -> j p", p=P)
-        nc.sync.dma_start(out=b_sc[:], in_=bmat_scale.rearrange("(p t) o -> p (t o)", t=SLOTS))
+        nc.scalar.dma_start(out=b_sc[:], in_=bmat_scale.rearrange("(p t) o -> p (t o)", t=SLOTS))
+        nc.scalar.dma_start(out=d_col[:], in_=d_gain.rearrange("(p t) -> p t", t=SLOTS))
+        nc.scalar.dma_start(out=gain_rows[0:8, :], in_=gain_view[0:8])
+        nc.scalar.dma_start(out=gain_rows[8:PIECES, :], in_=gain_view[8:PIECES])
         load_b(0)
         load_a(0)
-        nc.sync.dma_start(out=d_col[:], in_=d_gain.rearrange("(p t) -> p t", t=SLOTS))
-        nc.sync.dma_start(out=gain_rows[0:8, :], in_=gain_view[0:8])
-        nc.sync.dma_start(out=gain_rows[8:PIECES, :], in_=gain_view[8:PIECES])
         load_a(1)
-        load_w(0)
         load_a(2)
+        load_w(0)
         load_b(1)
-        load_w(1)
         load_a(3)
+        load_w(1)
         load_w(2)
         load_x_scales(0)
         load_x(0)
@@ -147,7 +150,7 @@ def tile_vera_merged_layer_s13_kernel(tc, x_words, x_scales, a, bmat_bytes, bmat
                 ad_grp[g] = work.tile([P, PANEL, SLOTS], BF16, name="ad_grp", tag="ad_grp", align_bytes=ALIGN)
             ad_banks[(g, h)] = take(ring_free, [P, 2, HALF])
             for i in range(2):
-                words = a_raw[(g, h)][:, i, :].bitcast(F32)
+                words = a_raw[g][:, 2 * h + i, :].bitcast(F32)
                 for u in range(2):
                     nc.tensor.transpose(ad_banks[(g, h)][1][:, u, i * P : (i + 1) * P], words[:, u::2], ident[:])
 
@@ -387,6 +390,9 @@ def tile_vera_merged_layer_s13_kernel(tc, x_words, x_scales, a, bmat_bytes, bmat
             for u in range(count):
                 j = c * SLOTS + u
                 nc.tensor.matmul(bank[:, u, :], lhsT=ident_bf[:, j : j + 1].to_broadcast([P, P]), rhs=gain_rows[:], start=True, stop=True)
+            return b, bank, count
+
+        def take_out_gain(c, b, bank, count):
             nc.scalar.copy(out=gain_all[c][:, 0 : count * P], in_=bank[:, 0:count, :].rearrange("p u o -> p (u o)"))
             if c == 0:
                 nc.scalar.copy(out=gain_col[:], in_=bank[:, count, 0:PIECES])
@@ -430,13 +436,14 @@ def tile_vera_merged_layer_s13_kernel(tc, x_words, x_scales, a, bmat_bytes, bmat
             nc.tensor.matmul(warm_bank[:], lhsT=warm[:, 0:P], rhs=warm[:], start=True, stop=True)
         ad_turn(0, 0)
         ad_turn(0, 1)
+        spread = [spread_gain(c) for c in range(PANELS)]
         b_tiles(0)
         for t in range(SLOTS):
             b_widen_halves(t)
         b_interleave(nc.vector.tensor_copy, 0, 0)
         b_interleave(nc.scalar.copy, 0, 1)
         for c in range(PANELS):
-            spread_gain(c)
+            take_out_gain(c, *spread[c])
         ad_product(0, 0)
         ad_product(0, 1)
         ad_turn(1, 0)
@@ -482,12 +489,14 @@ def tile_vera_merged_layer_s13_kernel(tc, x_words, x_scales, a, bmat_bytes, bmat
         def turning(w):
             return w >= 0 and len(pieces(w + 2, "VS")) > 0
 
-        b_widen(1, (0, 1))
+        b_widen(1, (0,))
         for w in range(-1, ROWS - 1):
             holding_the_port(w)
             add_gpsimd(w + 1)
             for u in pieces(w + 1, "S"):
                 empty(w + 1, u)
+            if w == -1:
+                b_widen(1, (1,))
             if w == GROUPS:
                 b_interleave(nc.scalar.copy, 2, 1)
             if w + 2 < GROUPS:

@@ -18,23 +18,32 @@ COPY = mybir.ActivationFunctionType.Copy
 T, IN, R, OUT = 1024, 2048, 512, 1536
 P = 128
 SLOTS = 4
-GROUPS = IN // (P * SLOTS)
-PANEL = 512
+SPAN = P * SLOTS
+GROUPS = IN // SPAN
+PANEL = 256
 PANELS = OUT // PANEL
-HALF = PANEL // 2
+CELLS = PANELS * GROUPS
+ROWS = CELLS // 2
 PIECES = OUT // P
 T_TILES = T // P
-ROWS = PANELS * GROUPS
 RUN = 4
 
 FLOPS = 2 * IN * R * OUT + 2 * T * IN * OUT
 
 ALIGN = 64
-PIECE_BANKS = 4
-RES_BUFS = T_TILES
-KINDS = ["PPVS"] * 2 + ["PPVV"] * 2 + ["PPPP", "PPVV"] * 3 + ["PPPP"] * 2
-COLUMNS_PER_BANK = 52
-PASSES_PER_BANK = 3
+CELL_BANKS = 4
+RES_BUFS = 8
+SECOND = ["SS", "VV", "P", "VV", "P", "VV", "P", "VV", "P", "VV", "P", "VV"]
+G_COLS = 232
+G_LAST = 0
+WEAVE = 1
+G_TURNED = 256
+G_HEAD = 192
+AHEAD = 12
+PASSES = 2
+PASSES_ADD = 7
+PASSES_QUANT = 8
+PASSES_TURN = 6
 WARM_UPS = 5
 
 
@@ -52,36 +61,39 @@ def tile_vera_merged_layer_s13_kernel(tc, x_words, x_scales, a, bmat_bytes, bmat
         b_sc = keep.tile([P, SLOTS], F32, name="b_sc")
         d_col = keep.tile([P, SLOTS], BF16, name="d_col")
         gain_col = keep.tile([P, PIECES], F32, name="gain_col")
-        gain_all = [keep.tile([P, PANEL], BF16, name="gain_all%d" % c) for c in range(PANELS)]
-        b_raw = [keep.tile([P, SLOTS, PANEL], U8, name="b_raw%d" % c, align_bytes=ALIGN) for c in range(PANELS)]
+        gain_all = keep.tile([P, OUT], BF16, name="gain_all")
+        b_raw = [keep.tile([P, SLOTS, 2 * PANEL], U8, name="b_raw%d" % i, align_bytes=ALIGN) for i in range(PANELS // 2)]
         b_cod = keep.tile([P, OUT], U32, name="b_cod", align_bytes=ALIGN)
         b_pla = keep.tile([P, OUT], U8, name="b_pla", align_bytes=ALIGN)
         a_raw = [keep.tile([P, SLOTS, R], BF16, name="a_raw%d" % g, align_bytes=ALIGN) for g in range(GROUPS)]
         a_cod = keep.tile([P, IN], U32, name="a_cod", align_bytes=ALIGN)
         a_pla = keep.tile([P, IN], U8, name="a_pla", align_bytes=ALIGN)
-        w_raw = [keep.tile([P, SLOTS, PANEL], BF16, name="w_raw%d" % r, align_bytes=ALIGN) for r in range(ROWS)]
-        w_cod = keep.tile([P, ROWS * PANEL], U32, name="w_cod", align_bytes=ALIGN)
-        w_pla = keep.tile([P, ROWS * PANEL], U8, name="w_pla", align_bytes=ALIGN)
-        x_cod = {(i, j): keep.tile([P, 2, T], U8, name="x_cod%d%d" % (i, j), align_bytes=ALIGN) for i in range(2) for j in range(2)}
-        x_pla = [keep.tile([P, GROUPS, T // 2], U8, name="x_pla%d" % i, align_bytes=ALIGN) for i in range(2)]
+        w_cod = keep.tile([P, CELLS * PANEL], U32, name="w_cod", align_bytes=ALIGN)
+        w_pla = keep.tile([P, CELLS * PANEL], U8, name="w_pla", align_bytes=ALIGN)
+        x_cod = [keep.tile([P, 2 * T], U8, name="x_cod%d" % g, align_bytes=ALIGN) for g in range(GROUPS)]
+        x_pla = keep.tile([P, GROUPS, T], U8, name="x_pla", align_bytes=ALIGN)
 
         a_view = a.rearrange("(g p t) r -> g p t r", p=P, t=SLOTS)
         w_view = w0.rearrange("(g p t) o -> g p t o", p=P, t=SLOTS)
         b_view = bmat_bytes.rearrange("(p t) o -> p t o", t=SLOTS)
-        out_view = out.rearrange("(m p) o -> m p o", p=P)
+        out_view = out.rearrange("(m p) o -> p m o", p=P)
 
-        piece_free = list(range(PIECE_BANKS))
-        ring_free = list(range(PIECE_BANKS, 8))
+        cell_free = list(range(CELL_BANKS))
+        ring_free = list(range(CELL_BANKS, 8))
 
-        def take(free, shape):
+        def take(free, shape, dtype=F32):
             b = free[0]
             free.remove(b)
-            return b, psum.tile(shape, F32, name="bank", tag="bank%d" % b)
+            return b, psum.tile(shape, dtype, name="bank", tag="bank%d" % b)
+
+        def kind(k):
+            return "P" if k % 2 == 0 else SECOND[k // 2]
 
         nc.vector.memset(gain_rows[:], 0.0)
         make_identity(nc, ident[:])
-        for plane in x_pla:
-            nc.gpsimd.memset(plane[:].rearrange("p g n -> p (g n)").bitcast(U32), 0)
+        nc.gpsimd.memset(x_pla[:].rearrange("p g n -> p (g n)").bitcast(U32), 0)
+
+        w_raw = {}
 
         def load_a(g):
             if g == 0:
@@ -90,25 +102,24 @@ def tile_vera_merged_layer_s13_kernel(tc, x_words, x_scales, a, bmat_bytes, bmat
             else:
                 nc.sync.dma_start(out=a_raw[g][:], in_=a_view[g])
 
-        def load_b(c):
-            nc.sync.dma_start(out=b_raw[c][:], in_=b_view[:, :, c * PANEL : (c + 1) * PANEL])
+        def load_b(i):
+            nc.sync.dma_start(out=b_raw[i][:], in_=b_view[:, :, 2 * i * PANEL : 2 * (i + 1) * PANEL])
 
-        def load_w(r):
-            c, g = divmod(r, GROUPS)
-            nc.sync.dma_start(out=w_raw[r][:], in_=w_view[g][:, :, c * PANEL : (c + 1) * PANEL])
+        def load_w(c, g, panels):
+            tile = keep.tile([P, SLOTS, panels * PANEL], BF16, name="w_raw%d%d" % (c, g), align_bytes=ALIGN)
+            nc.sync.dma_start(out=tile[:], in_=w_view[g][:, :, c * PANEL : (c + panels) * PANEL])
+            for i in range(panels):
+                w_raw[(c + i) * GROUPS + g] = tile[:, :, i * PANEL : (i + 1) * PANEL]
 
-        def load_x_scales(i):
+        def load_x_scales():
             for q in range(4):
                 nc.sync.dma_start(
-                    out=x_pla[i][32 * q : 32 * q + 4, :, :].bitcast(I32),
-                    in_=x_scales[:, 4 * q : 4 * q + 4, i * T // 2 : (i + 1) * T // 2].bitcast(I32).rearrange("g q n -> q g n"),
+                    out=x_pla[32 * q : 32 * q + 4, :, :].bitcast(I32),
+                    in_=x_scales[:, 4 * q : 4 * q + 4, :].bitcast(I32).rearrange("g q n -> q g n"),
                 )
 
-        def load_x(n):
-            i, j = divmod(n, 2)
-            nc.sync.dma_start(
-                out=x_cod[(i, j)][:].bitcast(I32), in_=x_words[2 * j : 2 * j + 2, :, i * T : (i + 1) * T].bitcast(I32).rearrange("g p n -> p g n")
-            )
+        def load_x(g):
+            nc.sync.dma_start(out=x_cod[g][:].bitcast(I32), in_=x_words[g].bitcast(I32))
 
         gain_view = b_gain.rearrange("(j p) -> j p", p=P)
         nc.scalar.dma_start(out=b_sc[:], in_=bmat_scale.rearrange("(p t) o -> p (t o)", t=SLOTS))
@@ -119,22 +130,26 @@ def tile_vera_merged_layer_s13_kernel(tc, x_words, x_scales, a, bmat_bytes, bmat
         load_a(0)
         load_a(1)
         load_a(2)
-        load_w(0)
-        load_b(1)
         load_a(3)
-        load_w(1)
-        load_w(2)
-        load_x_scales(0)
+        load_w(0, 0, 1)
+        load_w(0, 1, 1)
+        load_x_scales()
         load_x(0)
-        load_w(3)
-        load_b(2)
+        load_w(0, 2, 1)
+        load_b(1)
         load_x(1)
-        load_w(4)
-        load_x_scales(1)
+        load_w(0, 3, 1)
+        load_w(1, 0, 1)
         load_x(2)
         load_x(3)
-        for r in range(5, ROWS):
-            load_w(r)
+        load_w(1, 1, 1)
+        load_w(1, 2, 1)
+        load_w(1, 3, 1)
+        load_b(2)
+        for g in range(GROUPS):
+            load_w(2, g, 2)
+        for g in range(GROUPS):
+            load_w(4, g, 2)
 
         def quantise(codes, plane, at, grouped):
             cols = slice(at, at + grouped.shape[1])
@@ -145,56 +160,59 @@ def tile_vera_merged_layer_s13_kernel(tc, x_words, x_scales, a, bmat_bytes, bmat
 
         ad_banks, ad_grp, ad_done = {}, {}, []
 
-        def ad_turn(g, h):
-            if h == 0:
-                ad_grp[g] = work.tile([P, PANEL, SLOTS], BF16, name="ad_grp", tag="ad_grp", align_bytes=ALIGN)
-            ad_banks[(g, h)] = take(ring_free, [P, 2, HALF])
-            for i in range(2):
-                words = a_raw[g][:, 2 * h + i, :].bitcast(F32)
-                for u in range(2):
-                    nc.tensor.transpose(ad_banks[(g, h)][1][:, u, i * P : (i + 1) * P], words[:, u::2], ident[:])
+        def ad_turn(g):
+            ad_grp[g] = work.tile([P, SPAN, SLOTS], BF16, name="ad_grp", tag="ad_grp", align_bytes=ALIGN)
+            for h in range(2):
+                ad_banks[(g, h)] = take(ring_free, [P, 2, 2 * P])
+                for i in range(2):
+                    words = a_raw[g][:, 2 * h + i, :].bitcast(F32)
+                    for u in range(2):
+                        nc.tensor.transpose(ad_banks[(g, h)][1][:, u, i * P : (i + 1) * P], words[:, u::2], ident[:])
 
         def ad_product(g, h):
             b, bank = ad_banks[(g, h)]
             nc.vector.tensor_tensor(
-                out=ad_grp[g][:, h * HALF : (h + 1) * HALF, :].rearrange("p n (u e) -> p n u e", u=2),
+                out=ad_grp[g][:, 2 * h * P : 2 * (h + 1) * P, :].rearrange("p n (u e) -> p n u e", u=2),
                 in0=bank[:].bitcast(BF16).rearrange("p u (n e) -> p n u e", e=2),
-                in1=d_col[:].rearrange("p (u e) -> p u e", u=2).unsqueeze(1).to_broadcast([P, HALF, 2, 2]),
+                in1=d_col[:].rearrange("p (u e) -> p u e", u=2).unsqueeze(1).to_broadcast([P, 2 * P, 2, 2]),
                 op=MULT,
             )
             ring_free.append(b)
 
         def ad_quantise(g):
-            quantise(a_cod, a_pla, g * PANEL, ad_grp[g][:])
+            quantise(a_cod, a_pla, g * SPAN, ad_grp[g][:])
             ad_done.append(g)
 
         b_wide, b_grp, b_done = {}, {}, []
 
-        def b_tiles(c):
-            b_wide[c] = work.tile([P, SLOTS, PANEL], BF16, name="b_wide", tag="b_wide", align_bytes=ALIGN)
-            b_grp[c] = work.tile([P, PANEL, SLOTS], BF16, name="b_grp", tag="b_grp", align_bytes=ALIGN)
+        def b_bytes(c, t):
+            return b_raw[c // 2][:, t, c % 2 * PANEL : (c % 2 + 1) * PANEL].bitcast(E4M3)
 
-        def b_widen_scalar(c, t):
-            nc.scalar.activation(out=b_wide[c][:, t, :], in_=b_raw[c][:, t, :].bitcast(E4M3), func=COPY, scale=b_sc[:, t : t + 1])
+        def b_widen(c, t, on_vector=False):
+            if t == 0:
+                b_wide[c] = work.tile([P, SLOTS, PANEL], BF16, name="b_wide", tag="b_wide", align_bytes=ALIGN)
+            if on_vector:
+                nc.vector.tensor_scalar(out=b_wide[c][:, t, :], in0=b_bytes(c, t), scalar1=b_sc[:, t : t + 1], scalar2=None, op0=MULT)
+            else:
+                nc.scalar.activation(out=b_wide[c][:, t, :], in_=b_bytes(c, t), func=COPY, scale=b_sc[:, t : t + 1])
 
-        def b_widen_halves(t):
-            nc.vector.tensor_scalar(out=b_wide[0][:, t, 0:HALF], in0=b_raw[0][:, t, 0:HALF].bitcast(E4M3), scalar1=b_sc[:, t : t + 1], scalar2=None, op0=MULT)
-            nc.scalar.activation(out=b_wide[0][:, t, HALF:PANEL], in_=b_raw[0][:, t, HALF:PANEL].bitcast(E4M3), func=COPY, scale=b_sc[:, t : t + 1])
-
-        def b_interleave(copy, c, h):
-            cols = slice(h * HALF, (h + 1) * HALF)
+        def b_interleave(c, lo, hi, copy):
+            if lo == 0:
+                b_grp[c] = work.tile([P, PANEL, SLOTS], BF16, name="b_grp", tag="b_grp", align_bytes=ALIGN)
             copy(
-                out=b_grp[c][:, cols, :].rearrange("p (n i) t -> p n t i", i=RUN),
-                in_=b_wide[c][:, :, cols].rearrange("p t (n i) -> p n t i", i=RUN),
+                out=b_grp[c][:, lo:hi, :].rearrange("p (n i) t -> p n t i", i=RUN),
+                in_=b_wide[c][:, :, lo:hi].rearrange("p t (n i) -> p n t i", i=RUN),
             )
 
-        def b_quantise(c, h):
-            quantise(b_cod, b_pla, c * PANEL + h * HALF, b_grp[c][:, h * HALF : (h + 1) * HALF, :])
-            b_done.append((c, h))
+        def b_step(c, i):
+            if c < PANELS and 0 <= i < SLOTS:
+                b_widen(c, i)
+            elif c < PANELS and SLOTS <= i < SLOTS + 2:
+                b_interleave(c, (i - SLOTS) * P, (i - SLOTS + 1) * P, nc.scalar.copy)
 
-        def b_quantise_whole(c):
+        def b_quantise(c):
             quantise(b_cod, b_pla, c * PANEL, b_grp[c][:])
-            b_done.extend([(c, 0), (c, 1)])
+            b_done.append(c)
 
         def a_operand(lo, hi):
             return a_cod[:, lo:hi].bitcast(E4M3X4), a_pla[:, lo:hi]
@@ -203,340 +221,299 @@ def tile_vera_merged_layer_s13_kernel(tc, x_words, x_scales, a, bmat_bytes, bmat
             return b_cod[:, lo:hi].bitcast(E4M3X4), b_pla[:, lo:hi]
 
         scaled, banks, gained, woven = {}, {}, {}, {}
-        wm_first = keep.tile([P, HALF, SLOTS], BF16, name="wm_first", align_bytes=ALIGN)
-        wm_second = [keep.tile([P, HALF, SLOTS], BF16, name="wm_second%d" % i, align_bytes=ALIGN) for i in range(2)]
-
-        def pieces(r, kinds):
-            return [u for u in range(SLOTS) if 0 <= r < ROWS and KINDS[r][u] in kinds]
-
-        def paired(r, u):
-            return u >= 2 and KINDS[r] == "PPPP"
-
+        wm_first = keep.tile([P, PANEL, SLOTS], BF16, name="wm_first", align_bytes=ALIGN)
+        wm_second = [keep.tile([P, PANEL, SLOTS], BF16, name="wm_second%d" % i, align_bytes=ALIGN) for i in range(3)]
         unturned = []
 
-        def fill(r, u):
-            c, g = divmod(r, GROUPS)
-            j = c * SLOTS + u
-            if paired(r, u):
-                banks[(r, u)] = take(piece_free, [P, 2, HALF])
+        def wm_of(k):
+            return wm_first if k % 2 == 0 else wm_second[k // 2 % 3]
+
+        def fill(k, u, free=cell_free):
+            c, g = divmod(k, GROUPS)
+            if kind(k) == "P":
+                banks[(k, u)] = take(free, [P, 2, PANEL])
                 for e in range(2):
-                    at = g * PANEL + (2 * (u - 2) + e) * P
-                    mx_pass(banks[(r, u)][1][:, e, :], *a_operand(at, at + P), *b_operand(c * PANEL + HALF, (c + 1) * PANEL))
-            elif KINDS[r][u] == "P":
-                banks[(r, u)] = take(piece_free, [P, SLOTS, P])
-                for t in range(SLOTS):
-                    at = g * PANEL + t * P
-                    mx_pass(banks[(r, u)][1][:, t, :], *a_operand(at, at + P), *b_operand(j * P, (j + 1) * P))
+                    at = g * SPAN + (2 * u + e) * P
+                    mx_pass(banks[(k, u)][1][:, e, :], *a_operand(at, at + P), *b_operand(c * PANEL, (c + 1) * PANEL))
             else:
-                b, bank = take(piece_free, [P, PANEL])
-                mx_pass(bank[:], *b_operand(j * P, (j + 1) * P), *a_operand(g * PANEL, (g + 1) * PANEL))
-                scaled[(r, u)] = work.tile([P, PANEL], F32, name="scaled", tag="scaled", bufs=4)
-                nc.scalar.activation(out=scaled[(r, u)][:], in_=bank[:], func=COPY, scale=gain_col[:, j : j + 1])
-                unturned.append((r, u, b))
+                j = 2 * c + u
+                b, bank = take(free, [P, SPAN])
+                mx_pass(bank[:], *b_operand(j * P, (j + 1) * P), *a_operand(g * SPAN, (g + 1) * SPAN))
+                scaled[(k, u)] = work.tile([P, SPAN], F32, name="scaled", tag="scaled", bufs=4)
+                nc.scalar.activation(out=scaled[(k, u)][:], in_=bank[:], func=COPY, scale=gain_col[:, j : j + 1])
+                unturned.append((k, u, b))
 
         def turn_back():
-            for r, u, b in unturned:
-                banks[(r, u)] = take([b], [P, SLOTS, P])
-                if KINDS[r][u] == "S":
-                    nc.tensor.matmul(banks[(r, u)][1][:], lhsT=ident_bf[:], rhs=w_raw[r][:, :, u * P : (u + 1) * P], start=True, stop=False)
-            for r, u, b in sorted(unturned):
-                kind = KINDS[r][u]
+            for k, u, b in unturned:
+                banks[(k, u)] = take([b], [P, SLOTS, P])
+                if kind(k)[u] == "S":
+                    nc.tensor.matmul(banks[(k, u)][1][:], lhsT=ident_bf[:], rhs=w_raw[k][:, :, u * P : (u + 1) * P], start=True, stop=False)
+            for k, u, b in unturned:
+                laid = kind(k)[u] == "S"
                 for t in range(SLOTS):
                     nc.tensor.matmul(
-                        banks[(r, u)][1][:, t, :],
-                        lhsT=scaled[(r, u)][:, t * P : (t + 1) * P],
+                        banks[(k, u)][1][:, t, :],
+                        lhsT=scaled[(k, u)][:, t * P : (t + 1) * P],
                         rhs=ident[:],
                         is_transpose=True,
-                        start=kind == "V",
-                        stop=kind == "V" or t == SLOTS - 1,
+                        start=not laid,
+                        stop=not laid or t == SLOTS - 1,
                     )
             unturned.clear()
 
-        def weave(r, lo, hi):
-            if 0 <= r < ROWS and lo < hi:
-                if r not in woven:
-                    woven[r] = work.tile([P, HALF, SLOTS], F32, name="woven", tag="woven", bufs=3, align_bytes=ALIGN)
+        def weaves(k):
+            return 0 < k < CELLS and kind(k) == "P" and (WEAVE == 2 or (WEAVE == 1 and k % 2 == 0))
+
+        def weave(k):
+            if weaves(k):
+                woven[k] = work.tile([P, PANEL // 2, SLOTS], F32, name="woven", tag="woven", bufs=5, align_bytes=ALIGN)
                 nc.scalar.copy(
-                    out=woven[r][:, lo // 2 : hi // 2, :].rearrange("p (n i) t -> p n t i", i=RUN // 2),
-                    in_=w_raw[r][:].bitcast(F32)[:, :, lo // 2 : hi // 2].rearrange("p t (n i) -> p n t i", i=RUN // 2),
+                    out=woven[k][:].rearrange("p (n i) t -> p n t i", i=RUN // 2),
+                    in_=w_raw[k].bitcast(F32).rearrange("p t (n i) -> p n t i", i=RUN // 2),
                 )
 
-        def wm_cols(r, lo, hi):
-            if lo < HALF:
-                return wm_first[:, lo:hi, :]
-            return wm_second[r % 2][:, lo - HALF : hi - HALF, :]
-
-        def empty(r, u):
-            c = r // GROUPS
-            kind = KINDS[r][u]
-            b, bank = banks[(r, u)]
+        def empty(k, u, free=cell_free):
+            c = k // GROUPS
+            b, bank = banks[(k, u)]
             cols = slice(u * P, (u + 1) * P)
-            by_column = bank[:].rearrange("p t o -> p o t")
-            if kind == "P" and u == 0:
-                gained[r] = work.tile([P, PANEL, SLOTS], F32, name="gained", tag="gained", bufs=3)
-            if paired(r, u):
+            if weaves(k):
+                if u == 0:
+                    gained[k] = work.tile([P, 2, PANEL, 2], F32, name="gained", tag="gained", bufs=7)
                 nc.vector.tensor_tensor(
-                    out=gained[r][:, HALF:PANEL, :].rearrange("p o t -> p (o t)").rearrange("p (h o e) -> p h o e", h=2, e=2)[:, u - 2, :, :],
-                    in0=by_column,
-                    in1=gain_all[c][:, HALF:PANEL].unsqueeze(2).to_broadcast([P, HALF, 2]),
+                    out=gained[k][:, u, :, :],
+                    in0=bank[:].rearrange("p e o -> p o e"),
+                    in1=gain_all[:, c * PANEL : (c + 1) * PANEL].unsqueeze(2).to_broadcast([P, PANEL, 2]),
                     op=MULT,
                 )
-            elif kind == "P":
+            elif kind(k) == "P":
+                if u == 0:
+                    gained[k] = work.tile([P, PANEL // RUN, SLOTS, RUN], F32, name="gained", tag="gained", bufs=7)
                 nc.vector.tensor_tensor(
-                    out=gained[r][:, cols, :], in0=by_column, in1=gain_all[c][:, cols].unsqueeze(2).to_broadcast([P, P, SLOTS]), op=MULT
+                    out=gained[k][:, :, 2 * u : 2 * u + 2, :],
+                    in0=bank[:].rearrange("p e (n i) -> p n e i", i=RUN),
+                    in1=gain_all[:, c * PANEL : (c + 1) * PANEL].rearrange("p (n i) -> p n i", i=RUN).unsqueeze(2).to_broadcast([P, PANEL // RUN, 2, RUN]),
+                    op=MULT,
                 )
-            elif kind == "S":
-                nc.scalar.copy(out=wm_cols(r, u * P, (u + 1) * P), in_=by_column)
+            elif kind(k)[u] == "S":
+                nc.scalar.copy(out=wm_of(k)[:, cols, :], in_=bank[:].rearrange("p t o -> p o t"))
             else:
                 nc.vector.tensor_tensor(
-                    out=wm_cols(r, u * P, (u + 1) * P).rearrange("p (n i) t -> p n t i", i=RUN),
+                    out=wm_of(k)[:, cols, :].rearrange("p (n i) t -> p n t i", i=RUN),
                     in0=bank[:].rearrange("p t (n i) -> p n t i", i=RUN),
-                    in1=w_raw[r][:, :, cols].rearrange("p t (n i) -> p n t i", i=RUN),
+                    in1=w_raw[k][:, :, cols].rearrange("p t (n i) -> p n t i", i=RUN),
                     op=ADD,
                 )
-            piece_free.append(b)
+            free.append(b)
 
-        def add_plain(engine, r, lo, hi):
-            if 0 <= r < ROWS and lo == HALF and paired(r, 2):
+        def add_plain(engine, k, lo, hi):
+            if weaves(k) and lo < hi:
                 engine.tensor_tensor(
-                    out=wm_cols(r, lo, hi).rearrange("p (m f) (h e) -> p m f h e", f=2, h=2),
-                    in0=gained[r][:, HALF:PANEL, :].rearrange("p o t -> p (o t)").rearrange("p (h m f e) -> p m f h e", h=2, f=2, e=2),
-                    in1=woven[r][:].bitcast(BF16)[:, lo // 2 : hi // 2, :].rearrange("p m (h e f) -> p m f h e", h=2, f=2),
+                    out=wm_of(k)[:, lo:hi, :].rearrange("p (m f) (h e) -> p m f h e", f=2, h=2),
+                    in0=gained[k][:, :, lo:hi, :].rearrange("p h (m f) e -> p m f h e", f=2),
+                    in1=woven[k][:].bitcast(BF16)[:, lo // 2 : hi // 2, :].rearrange("p m (h e f) -> p m f h e", h=2, f=2),
                     op=ADD,
                 )
-            elif 0 <= r < ROWS and lo < hi:
+            elif kind(k) == "P" and lo < hi:
                 engine.tensor_tensor(
-                    out=wm_cols(r, lo, hi).rearrange("p (m f) t -> p m f t", f=2),
-                    in0=gained[r][:, lo:hi, :].rearrange("p (m f) t -> p m f t", f=2),
-                    in1=woven[r][:].bitcast(BF16)[:, lo // 2 : hi // 2, :].rearrange("p m (t f) -> p m f t", f=2),
+                    out=wm_of(k)[:, lo:hi, :].rearrange("p (n i) t -> p n t i", i=RUN),
+                    in0=gained[k][:, lo // RUN : hi // RUN, :, :],
+                    in1=w_raw[k][:, :, lo:hi].rearrange("p t (n i) -> p n t i", i=RUN),
                     op=ADD,
                 )
-
-        def add_gpsimd(r):
-            cols = g_cols(r)
-            if r < GROUPS:
-                nc.gpsimd.tensor_tensor(
-                    out=wm_cols(r, 0, cols).rearrange("p (m f) t -> p m t f", f=2),
-                    in0=gained[r][:, 0:cols, :].rearrange("p (m f) t -> p m t f", f=2),
-                    in1=w_raw[r][:, :, 0:cols].rearrange("p t (m f) -> p m t f", f=2),
-                    op=ADD,
-                )
-            else:
-                add_plain(nc.gpsimd, r, 0, cols)
 
         quantised = []
 
-        def wm_quantise(r):
-            for lo in (0, HALF):
-                quantise(w_cod, w_pla, r * PANEL + lo, wm_cols(r, lo, lo + HALF))
-            quantised.append(r)
+        def wm_quantise(k):
+            quantise(w_cod, w_pla, k * PANEL, wm_of(k)[:])
+            quantised.append(k)
 
-        waiting = [(c, m) for c in range(PANELS) for m in range(T_TILES)]
-        opened, y_banks, y_next, closed = [], {}, {}, []
+        todo = []
+        for r in range(ROWS - 2):
+            if r == 0:
+                todo.extend([(2 * r + h, m) for h in range(2) for m in range(T_TILES)])
+            else:
+                todo.extend([(2 * r + h, 2 * j + i) for j in range(T_TILES // 2) for h in range(2) for i in range(2)])
+        by_group = [(CELLS - GROUPS + g, m) for g in range(GROUPS) for m in range(T_TILES)]
+        todo.extend(by_group[:AHEAD])
+        todo.extend(sorted(by_group[AHEAD:], key=lambda p: (p[1], p[0])))
+        y_banks, closed = {}, []
 
         def y_pass():
-            ready = [k for k in opened if k[0] * GROUPS + y_next[k] in quantised]
-            if not ready:
-                if not waiting or not ring_free or waiting[0][0] * GROUPS not in quantised:
+            if not todo or todo[0][0] not in quantised:
+                return
+            k, m = todo[0]
+            c, g = divmod(k, GROUPS)
+            tiles = 1 if c == PANELS - 1 else 2
+            at = m - m % tiles
+            first = g == 0 and m == at
+            last = g == GROUPS - 1 and m == at + tiles - 1
+            if first:
+                if not ring_free:
                     return
-                k = waiting[0]
-                waiting.remove(k)
-                opened.append(k)
-                y_banks[k] = take(ring_free, [P, PANEL])
-                y_next[k] = 0
-                ready = [k]
-            k = ready[0]
-            c, m = k
-            g = y_next[k]
-            cols = slice((c * GROUPS + g) * PANEL, (c * GROUPS + g + 1) * PANEL)
+                y_banks[(c, at)] = take(ring_free, [P, tiles, PANEL])
+            todo.remove((k, m))
+            cols = slice(k * PANEL, (k + 1) * PANEL)
             mx_pass(
-                y_banks[k][1][:],
-                x_cod[(m // 4, g // 2)][:, g % 2, m % 4 * 2 * P : (m % 4 + 1) * 2 * P].bitcast(E2M1X4),
-                x_pla[m // 4][:, g, m % 4 * P : (m % 4 + 1) * P],
+                y_banks[(c, at)][1][:, m - at, :],
+                x_cod[g][:, m * 2 * P : (m + 1) * 2 * P].bitcast(E2M1X4),
+                x_pla[:, g, m * P : (m + 1) * P],
                 w_cod[:, cols].bitcast(E4M3X4),
                 w_pla[:, cols],
-                start=g == 0,
-                stop=g == GROUPS - 1,
+                start=first,
+                stop=last,
             )
-            y_next[k] = g + 1
-            if g == GROUPS - 1:
-                opened.remove(k)
-                closed.append(k)
+            if last:
+                closed.append((c, at, tiles))
 
         def y_store(copy):
-            k = closed[0]
-            closed.remove(k)
-            c, m = k
-            res = work.tile([P, PANEL], F32, name="res", tag="res", bufs=RES_BUFS)
-            copy(out=res[:], in_=y_banks[k][1][:])
-            ring_free.append(y_banks[k][0])
-            nc.sync.dma_start(out=out_view[m][:, c * PANEL : (c + 1) * PANEL], in_=res[:])
-
-        def store_closed():
-            for k in list(closed):
-                y_store(nc.scalar.copy)
+            c, at, tiles = closed[0]
+            closed.remove((c, at, tiles))
+            res = work.tile([P, tiles, PANEL], F32, name="res", tag="res", bufs=RES_BUFS)
+            copy(out=res[:], in_=y_banks[(c, at)][1][:])
+            ring_free.append(y_banks[(c, at)][0])
+            nc.sync.dma_start(out=out_view[:, at : at + tiles, c * PANEL : (c + 1) * PANEL], in_=res[:])
 
         def y_passes(count, store=True):
             for i in range(count):
                 if store:
-                    store_closed()
+                    for tile in list(closed):
+                        y_store(nc.scalar.copy)
                 y_pass()
 
-        def spread_gain(c):
-            count = max(kinds.count("P") for kinds in KINDS[c * GROUPS : (c + 1) * GROUPS])
-            b, bank = take(piece_free, [P, SLOTS, P])
-            if c == 0:
-                nc.tensor.matmul(bank[:, count, 0:PIECES], lhsT=gain_rows[:], rhs=ident_bf[:, 0:PIECES], start=True, stop=True)
-            for u in range(count):
-                j = c * SLOTS + u
-                nc.tensor.matmul(bank[:, u, :], lhsT=ident_bf[:, j : j + 1].to_broadcast([P, P]), rhs=gain_rows[:], start=True, stop=True)
-            return b, bank, count
+        def spread_gain(lo, hi):
+            b, bank = take(cell_free, [P, 2 * SPAN], BF16)
+            for j in range(lo, hi):
+                nc.tensor.matmul(bank[:, (j - lo) * P : (j - lo + 1) * P], lhsT=ident_bf[:, j : j + 1].to_broadcast([P, P]), rhs=gain_rows[:], start=True, stop=True)
+            if lo == 0:
+                nc.tensor.matmul(bank[:, hi * P : hi * P + PIECES], lhsT=gain_rows[:], rhs=ident_bf[:, 0:PIECES], start=True, stop=True)
+            return b, bank, lo, hi
 
-        def take_out_gain(c, b, bank, count):
-            nc.scalar.copy(out=gain_all[c][:, 0 : count * P], in_=bank[:, 0:count, :].rearrange("p u o -> p (u o)"))
-            if c == 0:
-                nc.scalar.copy(out=gain_col[:], in_=bank[:, count, 0:PIECES])
-            piece_free.append(b)
-
-        def early(r, u):
-            return u < (1 if r == ROWS - 1 else 2)
-
-        def emptied(w):
-            rest = [(w + 1, u) for u in pieces(w + 1, "S") + pieces(w + 1, "PV") if not early(w + 1, u)]
-            return rest + [(w + 2, u) for u in pieces(w + 2, "P") if early(w + 2, u)]
-
-        def plain_cols(r):
-            return P * len(pieces(r, "P"))
+        def take_out_gain(b, bank, lo, hi):
+            nc.scalar.copy(out=gain_all[:, lo * P : hi * P], in_=bank[:, 0 : (hi - lo) * P])
+            if lo == 0:
+                nc.scalar.copy(out=gain_col[:], in_=bank[:, hi * P : hi * P + PIECES])
+            cell_free.append(b)
 
         def g_cols(r):
-            if not 0 <= r < ROWS:
-                return 0
-            if "S" in KINDS[r] or (r >= GROUPS and "V" in KINDS[r]):
-                return HALF
-            return min(COLUMNS_PER_BANK * len(emptied(r - 1)), P * len([u for u in range(SLOTS) if early(r, u)]))
+            if r == ROWS - 1:
+                return G_LAST
+            return G_HEAD if r == 0 else G_COLS if SECOND[r] == "P" else G_TURNED
 
-        unfilled = [k for w in range(-2, ROWS - 1) for k in emptied(w)]
+        def both(step, k, *more):
+            for u in range(2):
+                step(k, u, *more)
 
-        def fill_next():
-            if unfilled and piece_free:
-                r, u = unfilled[0]
-                if r % GROUPS in ad_done and (r // GROUPS, u // 2) in b_done:
-                    unfilled.remove((r, u))
-                    fill(r, u)
-
-        def fill_all():
-            for i in range(PIECE_BANKS):
-                fill_next()
+        def finish(w):
+            first, second = 2 * w, 2 * w + 1
+            add_plain(nc.vector, first, g_cols(w), PANEL)
+            if w % 2 == 1 and (w + 3) // 2 < PANELS:
+                b_quantise((w + 3) // 2)
+            add_plain(nc.vector, second, 0, PANEL)
+            wm_quantise(first)
+            wm_quantise(second)
 
         nc.scalar.activation(out=ident_bf[:], in_=ident[:], func=COPY)
-        warm = keep.tile([P, PANEL], BF16, name="warm")
+        warm = keep.tile([P, SPAN], BF16, name="warm")
         nc.vector.memset(warm[:], 0.0)
-        warm_b, warm_bank = take(piece_free, [P, PANEL])
+        warm_b, warm_bank = take(cell_free, [P, SPAN])
         for i in range(WARM_UPS):
             nc.tensor.matmul(warm_bank[:], lhsT=warm[:, 0:P], rhs=warm[:], start=True, stop=True)
-        ad_turn(0, 0)
-        ad_turn(0, 1)
-        spread = [spread_gain(c) for c in range(PANELS)]
-        b_tiles(0)
+        ad_turn(0)
+        spread = [spread_gain(0, 4), spread_gain(4, PIECES)]
+        cell_free.append(warm_b)
         for t in range(SLOTS):
-            b_widen_halves(t)
-        b_interleave(nc.vector.tensor_copy, 0, 0)
-        b_interleave(nc.scalar.copy, 0, 1)
-        for c in range(PANELS):
-            take_out_gain(c, *spread[c])
-        ad_product(0, 0)
-        ad_product(0, 1)
-        ad_turn(1, 0)
-        piece_free.insert(0, warm_b)
-        ad_turn(1, 1)
-        b_quantise(0, 0)
+            b_widen(0, t, on_vector=True)
+            b_widen(1, t)
+        b_interleave(0, 0, PANEL, nc.vector.tensor_copy)
+        take_out_gain(*spread[0])
+        b_interleave(1, 0, PANEL, nc.scalar.copy)
+        take_out_gain(*spread[1])
+        both(ad_product, 0)
+        ad_turn(1)
+        b_quantise(0)
         ad_quantise(0)
-        fill_all()
-        ad_product(1, 0)
-        b_quantise(0, 1)
-        fill_all()
-        ad_product(1, 1)
-        ad_turn(2, 0)
-        ad_turn(2, 1)
+        both(fill, 0)
+        both(ad_product, 1)
+        ad_turn(2)
+        b_quantise(1)
+        ad_quantise(1)
+        both(fill, 1)
+        ad_turn(3)
+        both(empty, 0)
+        add_plain(nc.gpsimd, 0, 0, g_cols(0))
+        both(fill, 4)
         turn_back()
-        for r, u in emptied(-2):
-            empty(r, u)
+        both(ad_product, 2)
+        both(empty, 1, ring_free)
+        weave(2)
+        for i in range(4):
+            b_step(2, i)
+        both(ad_product, 3)
+        add_plain(nc.vector, 0, g_cols(0), PANEL)
+        ad_quantise(2)
+        for b in (4, 5):
+            ring_free.remove(b)
+            cell_free.append(b)
+        both(fill, 2)
+        wm_quantise(0)
+        y_passes(4)
+        ad_quantise(3)
+        wm_quantise(1)
+        y_passes(4)
+        for u in range(2):
+            empty(2, u)
+            fill(3, u)
+            y_passes(PASSES)
+        for i in range(4, 6):
+            b_step(2, i)
+        weave(4)
 
-        def b_widen(c, slots):
-            if slots[0] == 0:
-                b_tiles(c)
-            for t in slots:
-                b_widen_scalar(c, t)
+        def turns(w):
+            return w + 3 < ROWS and kind(2 * w + 7) != "P"
 
-        def holding_the_port(w):
-            add_plain(nc.vector, w, g_cols(w), min(HALF, plain_cols(w)))
-            if w == GROUPS - 2:
-                b_quantise_whole(1)
-            if w == 2 * GROUPS - 3:
-                b_quantise_whole(2)
-            if w + 2 < GROUPS:
-                ad_quantise(w + 2)
-            if w >= 0:
-                add_plain(nc.vector, w, max(HALF, g_cols(w)), plain_cols(w))
-                wm_quantise(w)
+        def b_steps(w):
+            for i in range(4) if w % 2 == 0 else range(4, 6):
+                b_step(w // 2 + 3, i)
+            weave(2 * w + 6)
 
-        def passes_behind(w, i):
-            count = PASSES_PER_BANK - 1 if w + 2 < ROWS else PASSES_PER_BANK
-            if turning(w):
-                return (count - 1, count + 1, 0, 2 * count)[i]
-            return count + 1 if i == PIECE_BANKS - 1 else count
-
-        def turning(w):
-            return w >= 0 and len(pieces(w + 2, "VS")) > 0
-
-        b_widen(1, (0,))
-        for w in range(-1, ROWS - 1):
-            holding_the_port(w)
-            add_gpsimd(w + 1)
-            for u in pieces(w + 1, "S"):
-                empty(w + 1, u)
-            if w == -1:
-                b_widen(1, (1,))
-            if w == GROUPS:
-                b_interleave(nc.scalar.copy, 2, 1)
-            if w + 2 < GROUPS:
-                weave(w + 2, g_cols(w + 2), plain_cols(w + 2))
-            else:
-                weave(w + 2, 0, min(HALF, plain_cols(w + 2)))
-                weave(w + 2, HALF, plain_cols(w + 2))
-            fill_all()
-            if w == -1:
-                ad_product(2, 0)
-                ad_product(2, 1)
-            for i, (r, u) in enumerate([(r, u) for r, u in emptied(w) if KINDS[r][u] != "S"]):
-                if w == 0 and i < 2:
-                    ad_product(3, i)
-                empty(r, u)
-                if turning(w) and i == 2:
-                    turn_back()
-                fill_next()
-                y_passes(passes_behind(w, i), i > 0 or not turning(w))
-            if w == -1:
-                ad_turn(3, 0)
-                ad_turn(3, 1)
-                turn_back()
-                b_widen(1, (2, 3))
+        for w in range(ROWS - 2):
+            first, second = 2 * w, 2 * w + 1
+            if w > 0:
+                finish(w)
+            add_plain(nc.gpsimd, first + 2, 0, g_cols(w + 1))
+            turning = turns(w)
+            if not turning:
+                b_steps(w)
+            leaving = [(first + 4, 0), (first + 4, 1), (second + 4, 0), (second + 4, 1)]
+            coming = [(k + 2, u) for k, u in leaving]
+            if turning:
+                coming = coming[2:] + coming[:2]
             if w == 0:
-                b_interleave(nc.scalar.copy, 1, 0)
-                b_interleave(nc.scalar.copy, 1, 1)
-            if w == 1:
-                b_widen(2, range(SLOTS))
-            if w == 2:
-                b_interleave(nc.scalar.copy, 2, 0)
-            if not unfilled:
-                ring_free.extend(piece_free)
-                piece_free.clear()
+                leaving, coming = leaving + [(3, 0), (3, 1)], [(5, 0), (5, 1)] + coming
+            for i in range(len(leaving)):
+                empty(*leaving[i], cell_free if coming[i][0] < CELLS else ring_free)
+                if coming[i][0] < CELLS:
+                    fill(*coming[i])
+                if w == 0 and i == 1:
+                    turn_back()
+                if i == len(leaving) - 3 and turning:
+                    b_steps(w)
+                if i == len(leaving) - 1:
+                    turn_back()
+                y_passes(PASSES)
+            y_passes(PASSES_QUANT + (PASSES_ADD if kind(second + 2) == "P" else 0) - (PASSES_TURN if turning else 0))
+        finish(ROWS - 2)
 
-        y_passes(PIECE_BANKS)
-        holding_the_port(ROWS - 1)
-        store_closed()
-        for i in range(T_TILES * GROUPS):
+        last = CELLS - 1
+        add_plain(nc.vector, last - 1, g_cols(ROWS - 1), PANEL)
+        y_passes(len(todo))
+        add_plain(nc.vector, last, 0, PANEL // 2)
+        wm_quantise(last - 1)
+        add_plain(nc.vector, last, PANEL // 2, PANEL)
+        y_passes(len(todo))
+        wm_quantise(last)
+        for i in range(len(todo)):
             y_pass()
-            if closed:
-                y_store(nc.scalar.copy if closed[0][1] % 2 == 0 else nc.vector.tensor_copy)
-        assert not waiting and not opened and not closed
+            for c, at, tiles in list(closed):
+                y_store(nc.scalar.copy if at % 2 == 0 else nc.vector.tensor_copy)
+        assert not todo and not closed

@@ -24,7 +24,8 @@ PANEL = 256
 PANELS = OUT // PANEL
 CELLS = PANELS * GROUPS
 ROWS = CELLS // 2
-PIECES = OUT // P
+GAIN_ROWS = 4
+GAIN_ROW = OUT // GAIN_ROWS
 T_TILES = T // P
 RUN = 4
 
@@ -33,13 +34,15 @@ FLOPS = 2 * IN * R * OUT + 2 * T * IN * OUT
 ALIGN = 64
 CELL_BANKS = 4
 RES_BUFS = 8
-SECOND = ["SS", "VV", "P", "VV", "P", "VV", "P", "VV", "P", "VV", "P", "VV"]
+SECOND = ["SS", "VV", "P", "VV", "P", "VV", "P", "VV", "P", "VV", "P", "P"]
 G_COLS = 232
-G_LAST = 0
+G_LAST = 96
 WEAVE = 1
 G_TURNED = 256
-G_HEAD = 192
-AHEAD = 12
+G_HEAD = 160
+G_ONE = 208
+AHEAD = 16
+HEAD_PASSES = 6
 PASSES = 2
 PASSES_ADD = 7
 PASSES_QUANT = 8
@@ -55,14 +58,13 @@ def tile_vera_merged_layer_s13_kernel(tc, x_words, x_scales, a, bmat_bytes, bmat
         psum = ctx.enter_context(tc.psum_pool(name="psum", bufs=1))
         ctx.enter_context(tc.manual_schedule())
 
-        gain_rows = keep.tile([P, P], BF16, name="gain_rows")
+        gain_rows = keep.tile([P, GAIN_ROW], BF16, name="gain_rows")
         ident = keep.tile([P, P], F32, name="ident")
         ident_bf = keep.tile([P, P], BF16, name="ident_bf")
         b_sc = keep.tile([P, SLOTS], F32, name="b_sc")
         d_col = keep.tile([P, SLOTS], BF16, name="d_col")
-        gain_col = keep.tile([P, PIECES], F32, name="gain_col")
+        gain_col = keep.tile([P, GAIN_ROW // P, GAIN_ROWS], F32, name="gain_col")
         gain_all = keep.tile([P, OUT], BF16, name="gain_all")
-        b_raw = [keep.tile([P, SLOTS, 2 * PANEL], U8, name="b_raw%d" % i, align_bytes=ALIGN) for i in range(PANELS // 2)]
         b_cod = keep.tile([P, OUT], U32, name="b_cod", align_bytes=ALIGN)
         b_pla = keep.tile([P, OUT], U8, name="b_pla", align_bytes=ALIGN)
         a_raw = [keep.tile([P, SLOTS, R], BF16, name="a_raw%d" % g, align_bytes=ALIGN) for g in range(GROUPS)]
@@ -90,10 +92,10 @@ def tile_vera_merged_layer_s13_kernel(tc, x_words, x_scales, a, bmat_bytes, bmat
             return "P" if k % 2 == 0 else SECOND[k // 2]
 
         nc.vector.memset(gain_rows[:], 0.0)
-        make_identity(nc, ident[:])
+        make_identity(nc, ident_bf[:])
         nc.gpsimd.memset(x_pla[:].rearrange("p g n -> p (g n)").bitcast(U32), 0)
 
-        w_raw = {}
+        w_raw, b_raw = {}, {}
 
         def load_a(g):
             if g == 0:
@@ -102,8 +104,11 @@ def tile_vera_merged_layer_s13_kernel(tc, x_words, x_scales, a, bmat_bytes, bmat
             else:
                 nc.sync.dma_start(out=a_raw[g][:], in_=a_view[g])
 
-        def load_b(i):
-            nc.sync.dma_start(out=b_raw[i][:], in_=b_view[:, :, 2 * i * PANEL : 2 * (i + 1) * PANEL])
+        def load_b(c, panels):
+            tile = keep.tile([P, SLOTS, panels * PANEL], U8, name="b_raw%d" % c, align_bytes=ALIGN)
+            nc.sync.dma_start(out=tile[:], in_=b_view[:, :, c * PANEL : (c + panels) * PANEL])
+            for i in range(panels):
+                b_raw[c + i] = tile[:, :, i * PANEL : (i + 1) * PANEL]
 
         def load_w(c, g, panels):
             tile = keep.tile([P, SLOTS, panels * PANEL], BF16, name="w_raw%d%d" % (c, g), align_bytes=ALIGN)
@@ -121,31 +126,30 @@ def tile_vera_merged_layer_s13_kernel(tc, x_words, x_scales, a, bmat_bytes, bmat
         def load_x(g):
             nc.sync.dma_start(out=x_cod[g][:].bitcast(I32), in_=x_words[g].bitcast(I32))
 
-        gain_view = b_gain.rearrange("(j p) -> j p", p=P)
         nc.scalar.dma_start(out=b_sc[:], in_=bmat_scale.rearrange("(p t) o -> p (t o)", t=SLOTS))
         nc.scalar.dma_start(out=d_col[:], in_=d_gain.rearrange("(p t) -> p t", t=SLOTS))
-        nc.scalar.dma_start(out=gain_rows[0:8, :], in_=gain_view[0:8])
-        nc.scalar.dma_start(out=gain_rows[8:PIECES, :], in_=gain_view[8:PIECES])
-        load_b(0)
+        nc.scalar.dma_start(out=gain_rows[0:GAIN_ROWS, :], in_=b_gain.rearrange("(j n) -> j n", j=GAIN_ROWS))
+        load_b(0, 1)
         load_a(0)
         load_a(1)
-        load_a(2)
+        load_b(1, 2)
         load_a(3)
+        load_a(2)
         load_w(0, 0, 1)
         load_w(0, 1, 1)
+        load_w(0, 2, 1)
         load_x_scales()
         load_x(0)
-        load_w(0, 2, 1)
-        load_b(1)
         load_x(1)
         load_w(0, 3, 1)
         load_w(1, 0, 1)
         load_x(2)
         load_x(3)
+        load_b(3, 2)
         load_w(1, 1, 1)
         load_w(1, 2, 1)
         load_w(1, 3, 1)
-        load_b(2)
+        load_b(5, 1)
         for g in range(GROUPS):
             load_w(2, g, 2)
         for g in range(GROUPS):
@@ -185,16 +189,16 @@ def tile_vera_merged_layer_s13_kernel(tc, x_words, x_scales, a, bmat_bytes, bmat
 
         b_wide, b_grp, b_done = {}, {}, []
 
-        def b_bytes(c, t):
-            return b_raw[c // 2][:, t, c % 2 * PANEL : (c % 2 + 1) * PANEL].bitcast(E4M3)
+        def b_bytes(c, t, lo, hi):
+            return b_raw[c][:, t, lo:hi].bitcast(E4M3)
 
-        def b_widen(c, t, on_vector=False):
+        def b_widen(c, t, shared=False):
             if t == 0:
                 b_wide[c] = work.tile([P, SLOTS, PANEL], BF16, name="b_wide", tag="b_wide", align_bytes=ALIGN)
-            if on_vector:
-                nc.vector.tensor_scalar(out=b_wide[c][:, t, :], in0=b_bytes(c, t), scalar1=b_sc[:, t : t + 1], scalar2=None, op0=MULT)
-            else:
-                nc.scalar.activation(out=b_wide[c][:, t, :], in_=b_bytes(c, t), func=COPY, scale=b_sc[:, t : t + 1])
+            lo = P if shared else 0
+            if shared:
+                nc.vector.tensor_scalar(out=b_wide[c][:, t, 0:lo], in0=b_bytes(c, t, 0, lo), scalar1=b_sc[:, t : t + 1], scalar2=None, op0=MULT)
+            nc.scalar.activation(out=b_wide[c][:, t, lo:PANEL], in_=b_bytes(c, t, lo, PANEL), func=COPY, scale=b_sc[:, t : t + 1])
 
         def b_interleave(c, lo, hi, copy):
             if lo == 0:
@@ -222,11 +226,11 @@ def tile_vera_merged_layer_s13_kernel(tc, x_words, x_scales, a, bmat_bytes, bmat
 
         scaled, banks, gained, woven = {}, {}, {}, {}
         wm_first = keep.tile([P, PANEL, SLOTS], BF16, name="wm_first", align_bytes=ALIGN)
-        wm_second = [keep.tile([P, PANEL, SLOTS], BF16, name="wm_second%d" % i, align_bytes=ALIGN) for i in range(3)]
+        wm_second = [keep.tile([P, PANEL, SLOTS], BF16, name="wm_second%d" % i, align_bytes=ALIGN) for i in range(2)]
         unturned = []
 
         def wm_of(k):
-            return wm_first if k % 2 == 0 else wm_second[k // 2 % 3]
+            return wm_first if k % 2 == 0 else wm_second[k // 2 % 2]
 
         def fill(k, u, free=cell_free):
             c, g = divmod(k, GROUPS)
@@ -240,7 +244,7 @@ def tile_vera_merged_layer_s13_kernel(tc, x_words, x_scales, a, bmat_bytes, bmat
                 b, bank = take(free, [P, SPAN])
                 mx_pass(bank[:], *b_operand(j * P, (j + 1) * P), *a_operand(g * SPAN, (g + 1) * SPAN))
                 scaled[(k, u)] = work.tile([P, SPAN], F32, name="scaled", tag="scaled", bufs=4)
-                nc.scalar.activation(out=scaled[(k, u)][:], in_=bank[:], func=COPY, scale=gain_col[:, j : j + 1])
+                nc.scalar.activation(out=scaled[(k, u)][:], in_=bank[:], func=COPY, scale=gain_col[:, j % 3, j // 3 : j // 3 + 1])
                 unturned.append((k, u, b))
 
         def turn_back():
@@ -329,10 +333,7 @@ def tile_vera_merged_layer_s13_kernel(tc, x_words, x_scales, a, bmat_bytes, bmat
 
         todo = []
         for r in range(ROWS - 2):
-            if r == 0:
-                todo.extend([(2 * r + h, m) for h in range(2) for m in range(T_TILES)])
-            else:
-                todo.extend([(2 * r + h, 2 * j + i) for j in range(T_TILES // 2) for h in range(2) for i in range(2)])
+            todo.extend([(2 * r + h, 2 * j + i) for j in range(T_TILES // 2) for h in range(2) for i in range(2)])
         by_group = [(CELLS - GROUPS + g, m) for g in range(GROUPS) for m in range(T_TILES)]
         todo.extend(by_group[:AHEAD])
         todo.extend(sorted(by_group[AHEAD:], key=lambda p: (p[1], p[0])))
@@ -380,24 +381,29 @@ def tile_vera_merged_layer_s13_kernel(tc, x_words, x_scales, a, bmat_bytes, bmat
                         y_store(nc.scalar.copy)
                 y_pass()
 
-        def spread_gain(lo, hi):
+        def spread_gain(half):
             b, bank = take(cell_free, [P, 2 * SPAN], BF16)
-            for j in range(lo, hi):
-                nc.tensor.matmul(bank[:, (j - lo) * P : (j - lo + 1) * P], lhsT=ident_bf[:, j : j + 1].to_broadcast([P, P]), rhs=gain_rows[:], start=True, stop=True)
-            if lo == 0:
-                nc.tensor.matmul(bank[:, hi * P : hi * P + PIECES], lhsT=gain_rows[:], rhs=ident_bf[:, 0:PIECES], start=True, stop=True)
-            return b, bank, lo, hi
+            for i in range(2):
+                j = 2 * half + i
+                nc.tensor.matmul(
+                    bank[:, i * GAIN_ROW : (i + 1) * GAIN_ROW], lhsT=ident_bf[:, j : j + 1].to_broadcast([P, P]), rhs=gain_rows[:], start=True, stop=True
+                )
+            if half == 0:
+                for i in range(GAIN_ROW // P):
+                    at = OUT // 2 + i * GAIN_ROWS
+                    nc.tensor.matmul(bank[:, at : at + GAIN_ROWS], lhsT=gain_rows[:, i * P : (i + 1) * P], rhs=ident_bf[:, 0:GAIN_ROWS], start=True, stop=True)
+            return b, bank, half
 
-        def take_out_gain(b, bank, lo, hi):
-            nc.scalar.copy(out=gain_all[:, lo * P : hi * P], in_=bank[:, 0 : (hi - lo) * P])
-            if lo == 0:
-                nc.scalar.copy(out=gain_col[:], in_=bank[:, hi * P : hi * P + PIECES])
+        def take_out_gain(b, bank, half):
+            nc.scalar.copy(out=gain_all[:, half * OUT // 2 : (half + 1) * OUT // 2], in_=bank[:, 0 : OUT // 2])
+            if half == 0:
+                nc.scalar.copy(out=gain_col[:].rearrange("p i j -> p (i j)"), in_=bank[:, OUT // 2 : OUT // 2 + OUT // P])
             cell_free.append(b)
 
         def g_cols(r):
             if r == ROWS - 1:
                 return G_LAST
-            return G_HEAD if r == 0 else G_COLS if SECOND[r] == "P" else G_TURNED
+            return G_HEAD if r == 0 else G_ONE if r == 1 else G_COLS if SECOND[r] == "P" else G_TURNED
 
         def both(step, k, *more):
             for u in range(2):
@@ -412,97 +418,88 @@ def tile_vera_merged_layer_s13_kernel(tc, x_words, x_scales, a, bmat_bytes, bmat
             wm_quantise(first)
             wm_quantise(second)
 
-        nc.scalar.activation(out=ident_bf[:], in_=ident[:], func=COPY)
+        nc.scalar.activation(out=ident[:], in_=ident_bf[:], func=COPY)
         warm = keep.tile([P, SPAN], BF16, name="warm")
         nc.vector.memset(warm[:], 0.0)
         warm_b, warm_bank = take(cell_free, [P, SPAN])
         for i in range(WARM_UPS):
             nc.tensor.matmul(warm_bank[:], lhsT=warm[:, 0:P], rhs=warm[:], start=True, stop=True)
         ad_turn(0)
-        spread = [spread_gain(0, 4), spread_gain(4, PIECES)]
+        spread = [spread_gain(0), spread_gain(1)]
         cell_free.append(warm_b)
         for t in range(SLOTS):
-            b_widen(0, t, on_vector=True)
-            b_widen(1, t)
-        b_interleave(0, 0, PANEL, nc.vector.tensor_copy)
+            b_widen(0, t, shared=True)
+        b_interleave(0, 0, P, nc.vector.tensor_copy)
+        b_interleave(0, P, PANEL, nc.scalar.copy)
         take_out_gain(*spread[0])
-        b_interleave(1, 0, PANEL, nc.scalar.copy)
         take_out_gain(*spread[1])
         both(ad_product, 0)
         ad_turn(1)
         b_quantise(0)
         ad_quantise(0)
         both(fill, 0)
+        for i in range(6):
+            b_step(1, i)
         both(ad_product, 1)
-        ad_turn(2)
-        b_quantise(1)
+        ad_turn(3)
+        empty(0, 0)
         ad_quantise(1)
         both(fill, 1)
-        ad_turn(3)
-        both(empty, 0)
+        ad_turn(2)
+        empty(0, 1)
+        b_quantise(1)
         add_plain(nc.gpsimd, 0, 0, g_cols(0))
-        both(fill, 4)
-        turn_back()
-        both(ad_product, 2)
-        both(empty, 1, ring_free)
-        weave(2)
         for i in range(4):
             b_step(2, i)
+        turn_back()
+        both(fill, 4)
         both(ad_product, 3)
+        both(empty, 1, ring_free)
+        weave(2)
+        both(ad_product, 2)
         add_plain(nc.vector, 0, g_cols(0), PANEL)
-        ad_quantise(2)
-        for b in (4, 5):
-            ring_free.remove(b)
-            cell_free.append(b)
-        both(fill, 2)
-        wm_quantise(0)
-        y_passes(4)
         ad_quantise(3)
+        both(fill, 3, ring_free)
+        ad_quantise(2)
+        both(fill, 2, ring_free)
+        wm_quantise(0)
+        turn_back()
         wm_quantise(1)
-        y_passes(4)
-        for u in range(2):
-            empty(2, u)
-            fill(3, u)
-            y_passes(PASSES)
         for i in range(4, 6):
             b_step(2, i)
         weave(4)
+        both(empty, 2, ring_free)
+        y_passes(HEAD_PASSES)
 
         def turns(w):
-            return w + 3 < ROWS and kind(2 * w + 7) != "P"
+            return w + 2 < ROWS and kind(2 * w + 5) != "P"
 
         def b_steps(w):
             for i in range(4) if w % 2 == 0 else range(4, 6):
                 b_step(w // 2 + 3, i)
             weave(2 * w + 6)
 
-        for w in range(ROWS - 2):
+        for w in range(ROWS - 1):
             first, second = 2 * w, 2 * w + 1
             if w > 0:
                 finish(w)
             add_plain(nc.gpsimd, first + 2, 0, g_cols(w + 1))
             turning = turns(w)
-            if not turning:
+            if not turning and w > 0:
                 b_steps(w)
-            leaving = [(first + 4, 0), (first + 4, 1), (second + 4, 0), (second + 4, 1)]
-            coming = [(k + 2, u) for k, u in leaving]
-            if turning:
-                coming = coming[2:] + coming[:2]
-            if w == 0:
-                leaving, coming = leaving + [(3, 0), (3, 1)], [(5, 0), (5, 1)] + coming
-            for i in range(len(leaving)):
-                empty(*leaving[i], cell_free if coming[i][0] < CELLS else ring_free)
+            leaving = [(k, u) for k in sorted((second + 2, first + 4), reverse=kind(second + 2) != "P") for u in range(2)]
+            coming = [(k, u) for k in (second + 4, first + 6) for u in range(2)]
+            for i in range(CELL_BANKS):
+                if leaving[i][0] < CELLS:
+                    empty(*leaving[i], cell_free if coming[i][0] < CELLS else ring_free)
                 if coming[i][0] < CELLS:
                     fill(*coming[i])
-                if w == 0 and i == 1:
-                    turn_back()
-                if i == len(leaving) - 3 and turning:
+                if i == 1 and (turning or w == 0):
                     b_steps(w)
-                if i == len(leaving) - 1:
+                if i == CELL_BANKS - 1:
                     turn_back()
                 y_passes(PASSES)
             y_passes(PASSES_QUANT + (PASSES_ADD if kind(second + 2) == "P" else 0) - (PASSES_TURN if turning else 0))
-        finish(ROWS - 2)
 
         last = CELLS - 1
         add_plain(nc.vector, last - 1, g_cols(ROWS - 1), PANEL)

@@ -37,7 +37,7 @@ RES_BUFS = 8
 SECOND = ["SS", "VV", "P", "VV", "P", "VV", "P", "VV", "P", "VV", "P", "P"]
 G_COLS = 232
 G_LAST = 96
-WEAVE = 1
+WEAVE_FROM = 4
 G_TURNED = 256
 G_HEAD = 160
 G_ONE = 208
@@ -266,11 +266,11 @@ def tile_vera_merged_layer_s13_kernel(tc, x_words, x_scales, a, bmat_bytes, bmat
             unturned.clear()
 
         def weaves(k):
-            return 0 < k < CELLS and kind(k) == "P" and (WEAVE == 2 or (WEAVE == 1 and k % 2 == 0))
+            return 0 < k < CELLS and kind(k) == "P" and (k % 2 == 0 or k >= WEAVE_FROM)
 
         def weave(k):
             if weaves(k):
-                woven[k] = work.tile([P, PANEL // 2, SLOTS], F32, name="woven", tag="woven", bufs=5, align_bytes=ALIGN)
+                woven[k] = work.tile([P, PANEL // 2, SLOTS], F32, name="woven", tag="woven", bufs=6, align_bytes=ALIGN)
                 nc.scalar.copy(
                     out=woven[k][:].rearrange("p (n i) t -> p n t i", i=RUN // 2),
                     in_=w_raw[k].bitcast(F32).rearrange("p t (n i) -> p n t i", i=RUN // 2),
@@ -478,6 +478,7 @@ def tile_vera_merged_layer_s13_kernel(tc, x_words, x_scales, a, bmat_bytes, bmat
             for i in range(4) if w % 2 == 0 else range(4, 6):
                 b_step(w // 2 + 3, i)
             weave(2 * w + 6)
+            weave(2 * w + 5)
 
         for w in range(ROWS - 1):
             first, second = 2 * w, 2 * w + 1

@@ -34,18 +34,20 @@ FLOPS = 2 * IN * R * OUT + 2 * T * IN * OUT
 ALIGN = 64
 CELL_BANKS = 4
 RES_BUFS = 8
-SECOND = ["SS", "VV", "P", "VV", "P", "VV", "P", "VV", "P", "VV", "P", "P"]
-G_COLS = 232
-G_LAST = 96
+TURNED_PANELS = 5
+TURN_AFTER = 4
+RING = 3
 WEAVE_FROM = 4
-G_TURNED = 256
-G_HEAD = 160
-G_ONE = 208
-AHEAD = 16
+G_HEAD = 144
+G_ONE = 256
+G_COLS = 496
+G_LAST = 208
+AHEAD = 12
 HEAD_PASSES = 6
 PASSES = 2
+PASSES_PORT = 6
+PASSES_OPEN = 4
 PASSES_ADD = 7
-PASSES_QUANT = 8
 PASSES_TURN = 6
 WARM_UPS = 5
 
@@ -89,7 +91,7 @@ def tile_vera_merged_layer_s13_kernel(tc, x_words, x_scales, a, bmat_bytes, bmat
             return b, psum.tile(shape, dtype, name="bank", tag="bank%d" % b)
 
         def kind(k):
-            return "P" if k % 2 == 0 else SECOND[k // 2]
+            return "SS" if k == 1 else "VV" if k % GROUPS == GROUPS - 1 and k // GROUPS < TURNED_PANELS else "P"
 
         nc.vector.memset(gain_rows[:], 0.0)
         make_identity(nc, ident_bf[:])
@@ -138,17 +140,15 @@ def tile_vera_merged_layer_s13_kernel(tc, x_words, x_scales, a, bmat_bytes, bmat
         load_w(0, 0, 1)
         load_w(0, 1, 1)
         load_w(0, 2, 1)
-        load_x_scales()
-        load_x(0)
-        load_x(1)
-        load_w(0, 3, 1)
         load_w(1, 0, 1)
-        load_x(2)
-        load_x(3)
-        load_b(3, 2)
+        load_w(0, 3, 1)
         load_w(1, 1, 1)
-        load_w(1, 2, 1)
+        load_b(3, 2)
+        load_x_scales()
+        for g in range(GROUPS):
+            load_x(g)
         load_w(1, 3, 1)
+        load_w(1, 2, 1)
         load_b(5, 1)
         for g in range(GROUPS):
             load_w(2, g, 2)
@@ -225,12 +225,21 @@ def tile_vera_merged_layer_s13_kernel(tc, x_words, x_scales, a, bmat_bytes, bmat
             return b_cod[:, lo:hi].bitcast(E4M3X4), b_pla[:, lo:hi]
 
         scaled, banks, gained, woven = {}, {}, {}, {}
-        wm_first = keep.tile([P, PANEL, SLOTS], BF16, name="wm_first", align_bytes=ALIGN)
-        wm_second = [keep.tile([P, PANEL, SLOTS], BF16, name="wm_second%d" % i, align_bytes=ALIGN) for i in range(2)]
-        unturned = []
+        wm_pool = keep.tile([P, 2 * PANEL, SLOTS], BF16, name="wm_pool", align_bytes=ALIGN)
+        wm_vec = [keep.tile([P, 2 * PANEL, SLOTS], BF16, name="wm_vec%d" % i, align_bytes=ALIGN) for i in range(2)]
+        waiting = []
+
+        def pair(k):
+            return k if k < GROUPS else k - k % 2
+
+        def wm_pair(k):
+            if k < GROUPS:
+                return wm_pool[:] if k % 2 == 0 else wm_vec[0][:, k // 2 * PANEL : 2 * PANEL, :]
+            return wm_pool[:] if k % GROUPS < 2 else wm_vec[k // GROUPS % 2][:]
 
         def wm_of(k):
-            return wm_first if k % 2 == 0 else wm_second[k // 2 % 2]
+            at = (k - pair(k)) * PANEL
+            return wm_pair(k)[:, at : at + PANEL, :]
 
         def fill(k, u, free=cell_free):
             c, g = divmod(k, GROUPS)
@@ -245,9 +254,12 @@ def tile_vera_merged_layer_s13_kernel(tc, x_words, x_scales, a, bmat_bytes, bmat
                 mx_pass(bank[:], *b_operand(j * P, (j + 1) * P), *a_operand(g * SPAN, (g + 1) * SPAN))
                 scaled[(k, u)] = work.tile([P, SPAN], F32, name="scaled", tag="scaled", bufs=4)
                 nc.scalar.activation(out=scaled[(k, u)][:], in_=bank[:], func=COPY, scale=gain_col[:, j % 3, j // 3 : j // 3 + 1])
-                unturned.append((k, u, b))
+                waiting.append((k, u, b))
 
-        def turn_back():
+        def turn_back(cell=None):
+            unturned = [x for x in waiting if cell is None or x[0] == cell]
+            for x in unturned:
+                waiting.remove(x)
             for k, u, b in unturned:
                 banks[(k, u)] = take([b], [P, SLOTS, P])
                 if kind(k)[u] == "S":
@@ -263,16 +275,17 @@ def tile_vera_merged_layer_s13_kernel(tc, x_words, x_scales, a, bmat_bytes, bmat
                         start=not laid,
                         stop=not laid or t == SLOTS - 1,
                     )
-            unturned.clear()
 
         def weaves(k):
-            return 0 < k < CELLS and kind(k) == "P" and (k % 2 == 0 or k >= WEAVE_FROM)
+            return 0 < k < CELLS and kind(k) == "P" and (k % GROUPS < 2 or k == 2 or k // GROUPS >= WEAVE_FROM)
 
         def weave(k):
             if weaves(k):
-                woven[k] = work.tile([P, PANEL // 2, SLOTS], F32, name="woven", tag="woven", bufs=6, align_bytes=ALIGN)
+                if pair(k) not in woven:
+                    woven[pair(k)] = work.tile([P, PANEL, SLOTS], F32, name="woven", tag="woven", bufs=4, align_bytes=ALIGN)
+                at = (k - pair(k)) * PANEL // 2
                 nc.scalar.copy(
-                    out=woven[k][:].rearrange("p (n i) t -> p n t i", i=RUN // 2),
+                    out=woven[pair(k)][:, at : at + PANEL // 2, :].rearrange("p (n i) t -> p n t i", i=RUN // 2),
                     in_=w_raw[k].bitcast(F32).rearrange("p t (n i) -> p n t i", i=RUN // 2),
                 )
 
@@ -280,20 +293,21 @@ def tile_vera_merged_layer_s13_kernel(tc, x_words, x_scales, a, bmat_bytes, bmat
             c = k // GROUPS
             b, bank = banks[(k, u)]
             cols = slice(u * P, (u + 1) * P)
+            at = (k - pair(k)) * PANEL
             if weaves(k):
-                if u == 0:
-                    gained[k] = work.tile([P, 2, PANEL, 2], F32, name="gained", tag="gained", bufs=7)
+                if pair(k) not in gained:
+                    gained[pair(k)] = work.tile([P, 2, 2 * PANEL, 2], F32, name="gained", tag="gained", bufs=4)
                 nc.vector.tensor_tensor(
-                    out=gained[k][:, u, :, :],
+                    out=gained[pair(k)][:, u, at : at + PANEL, :],
                     in0=bank[:].rearrange("p e o -> p o e"),
                     in1=gain_all[:, c * PANEL : (c + 1) * PANEL].unsqueeze(2).to_broadcast([P, PANEL, 2]),
                     op=MULT,
                 )
             elif kind(k) == "P":
-                if u == 0:
-                    gained[k] = work.tile([P, PANEL // RUN, SLOTS, RUN], F32, name="gained", tag="gained", bufs=7)
+                if pair(k) not in gained:
+                    gained[pair(k)] = work.tile([P, 2 * PANEL // RUN, SLOTS, RUN], F32, name="gained", tag="gained", bufs=4)
                 nc.vector.tensor_tensor(
-                    out=gained[k][:, :, 2 * u : 2 * u + 2, :],
+                    out=gained[pair(k)][:, at // RUN : (at + PANEL) // RUN, 2 * u : 2 * u + 2, :],
                     in0=bank[:].rearrange("p e (n i) -> p n e i", i=RUN),
                     in1=gain_all[:, c * PANEL : (c + 1) * PANEL].rearrange("p (n i) -> p n i", i=RUN).unsqueeze(2).to_broadcast([P, PANEL // RUN, 2, RUN]),
                     op=MULT,
@@ -310,30 +324,31 @@ def tile_vera_merged_layer_s13_kernel(tc, x_words, x_scales, a, bmat_bytes, bmat
             free.append(b)
 
         def add_plain(engine, k, lo, hi):
+            at = (k - pair(k)) * PANEL
             if weaves(k) and lo < hi:
                 engine.tensor_tensor(
-                    out=wm_of(k)[:, lo:hi, :].rearrange("p (m f) (h e) -> p m f h e", f=2, h=2),
-                    in0=gained[k][:, :, lo:hi, :].rearrange("p h (m f) e -> p m f h e", f=2),
-                    in1=woven[k][:].bitcast(BF16)[:, lo // 2 : hi // 2, :].rearrange("p m (h e f) -> p m f h e", h=2, f=2),
+                    out=wm_pair(k)[:, at + lo : at + hi, :].rearrange("p (m f) (h e) -> p m f h e", f=2, h=2),
+                    in0=gained[pair(k)][:, :, at + lo : at + hi, :].rearrange("p h (m f) e -> p m f h e", f=2),
+                    in1=woven[pair(k)][:].bitcast(BF16)[:, (at + lo) // 2 : (at + hi) // 2, :].rearrange("p m (h e f) -> p m f h e", h=2, f=2),
                     op=ADD,
                 )
             elif kind(k) == "P" and lo < hi:
                 engine.tensor_tensor(
                     out=wm_of(k)[:, lo:hi, :].rearrange("p (n i) t -> p n t i", i=RUN),
-                    in0=gained[k][:, lo // RUN : hi // RUN, :, :],
+                    in0=gained[pair(k)][:, (at + lo) // RUN : (at + hi) // RUN, :, :],
                     in1=w_raw[k][:, :, lo:hi].rearrange("p t (n i) -> p n t i", i=RUN),
                     op=ADD,
                 )
 
         quantised = []
 
-        def wm_quantise(k):
-            quantise(w_cod, w_pla, k * PANEL, wm_of(k)[:])
-            quantised.append(k)
+        def wm_quantise(k, cells=1):
+            quantise(w_cod, w_pla, k * PANEL, wm_of(k) if cells == 1 else wm_pair(k))
+            quantised.extend(range(k, k + cells))
 
         todo = []
-        for r in range(ROWS - 2):
-            todo.extend([(2 * r + h, 2 * j + i) for j in range(T_TILES // 2) for h in range(2) for i in range(2)])
+        for c in range(PANELS - 1):
+            todo.extend([(GROUPS * c + g, 2 * j + i) for j in range(T_TILES // 2) for g in range(GROUPS) for i in range(2)])
         by_group = [(CELLS - GROUPS + g, m) for g in range(GROUPS) for m in range(T_TILES)]
         todo.extend(by_group[:AHEAD])
         todo.extend(sorted(by_group[AHEAD:], key=lambda p: (p[1], p[0])))
@@ -400,23 +415,9 @@ def tile_vera_merged_layer_s13_kernel(tc, x_words, x_scales, a, bmat_bytes, bmat
                 nc.scalar.copy(out=gain_col[:].rearrange("p i j -> p (i j)"), in_=bank[:, OUT // 2 : OUT // 2 + OUT // P])
             cell_free.append(b)
 
-        def g_cols(r):
-            if r == ROWS - 1:
-                return G_LAST
-            return G_HEAD if r == 0 else G_ONE if r == 1 else G_COLS if SECOND[r] == "P" else G_TURNED
-
         def both(step, k, *more):
             for u in range(2):
                 step(k, u, *more)
-
-        def finish(w):
-            first, second = 2 * w, 2 * w + 1
-            add_plain(nc.vector, first, g_cols(w), PANEL)
-            if w % 2 == 1 and (w + 3) // 2 < PANELS:
-                b_quantise((w + 3) // 2)
-            add_plain(nc.vector, second, 0, PANEL)
-            wm_quantise(first)
-            wm_quantise(second)
 
         nc.scalar.activation(out=ident[:], in_=ident_bf[:], func=COPY)
         warm = keep.tile([P, SPAN], BF16, name="warm")
@@ -448,68 +449,121 @@ def tile_vera_merged_layer_s13_kernel(tc, x_words, x_scales, a, bmat_bytes, bmat
         ad_turn(2)
         empty(0, 1)
         b_quantise(1)
-        add_plain(nc.gpsimd, 0, 0, g_cols(0))
+        add_plain(nc.gpsimd, 0, 0, G_HEAD)
         for i in range(4):
             b_step(2, i)
         turn_back()
         both(fill, 4)
         both(ad_product, 3)
-        both(empty, 1, ring_free)
+        both(empty, 1)
         weave(2)
         both(ad_product, 2)
-        add_plain(nc.vector, 0, g_cols(0), PANEL)
         ad_quantise(3)
         both(fill, 3, ring_free)
         ad_quantise(2)
         both(fill, 2, ring_free)
-        wm_quantise(0)
+        add_plain(nc.vector, 0, G_HEAD, PANEL)
         turn_back()
         wm_quantise(1)
-        for i in range(4, 6):
-            b_step(2, i)
-        weave(4)
-        both(empty, 2, ring_free)
-        y_passes(HEAD_PASSES)
+        wm_quantise(0)
 
-        def turns(w):
-            return w + 2 < ROWS and kind(2 * w + 5) != "P"
+        def banks_of(*cells):
+            return [(k, u) for k in cells if k < CELLS for u in range(2)]
 
-        def b_steps(w):
-            for i in range(4) if w % 2 == 0 else range(4, 6):
-                b_step(w // 2 + 3, i)
-            weave(2 * w + 6)
-            weave(2 * w + 5)
+        def own(c):
+            k = GROUPS * c + 2
+            return (k + 1, k) if kind(k + 1) != "P" else (k, k + 1)
 
-        for w in range(ROWS - 1):
-            first, second = 2 * w, 2 * w + 1
-            if w > 0:
-                finish(w)
-            add_plain(nc.gpsimd, first + 2, 0, g_cols(w + 1))
-            turning = turns(w)
-            if not turning and w > 0:
-                b_steps(w)
-            leaving = [(k, u) for k in sorted((second + 2, first + 4), reverse=kind(second + 2) != "P") for u in range(2)]
-            coming = [(k, u) for k in (second + 4, first + 6) for u in range(2)]
-            for i in range(CELL_BANKS):
-                if leaving[i][0] < CELLS:
-                    empty(*leaving[i], cell_free if coming[i][0] < CELLS else ring_free)
-                if coming[i][0] < CELLS:
-                    fill(*coming[i])
-                if i == 1 and (turning or w == 0):
-                    b_steps(w)
-                if i == CELL_BANKS - 1:
-                    turn_back()
+        unfilled = banks_of(*own(1), 5, 8, 9)
+        for c in range(2, PANELS):
+            unfilled.extend(banks_of(*own(c), GROUPS * c + 4, GROUPS * c + 5))
+        due = {}
+        clock = [0]
+
+        def fill_all():
+            while_free = list(cell_free)
+            for b in while_free:
+                if unfilled and unfilled[0][0] // GROUPS in b_done:
+                    k, u = unfilled[0]
+                    unfilled.remove((k, u))
+                    fill(k, u)
+                    if u == 1 and kind(k) != "P":
+                        due[k] = clock[0] + TURN_AFTER
+
+        def turn_due(force=False):
+            for k in sorted(due):
+                if force or due[k] <= clock[0]:
+                    turn_back(k)
+            for k in [k for k in due if force or due[k] <= clock[0]]:
+                due.pop(k)
+
+        to_ring = [(5, 0), (5, 1), (own(1)[0], 0)][:RING]
+
+        def run(leaving, after, force=True):
+            fill_all()
+            for i, (k, u) in enumerate(leaving):
+                if k in due:
+                    turn_due(True)
+                empty(k, u, cell_free if unfilled and (k, u) not in to_ring else ring_free)
+                clock[0] = clock[0] + 1
+                fill_all()
+                turn_due()
+                for step in after.get(i, []):
+                    step()
                 y_passes(PASSES)
-            y_passes(PASSES_QUANT + (PASSES_ADD if kind(second + 2) == "P" else 0) - (PASSES_TURN if turning else 0))
+            turn_due(force)
 
-        last = CELLS - 1
-        add_plain(nc.vector, last - 1, g_cols(ROWS - 1), PANEL)
+        def order(c):
+            k = GROUPS * c
+            plain = [j for j in (k + 2, k + 3) if kind(j) == "P"]
+            turned = [j for j in own(c) if kind(j) != "P"]
+            return plain + turned + [k + 4, k + 5]
+
+        b_step(2, 4)
+        b_step(2, 5)
+        run(banks_of(2), {}, False)
+        add_plain(nc.gpsimd, 2, 0, G_ONE)
+        run(banks_of(4, 3, 5), {0: [lambda: weave(4)], 3: [lambda: weave(5)]})
+        add_plain(nc.vector, 2, G_ONE, PANEL)
+        b_quantise(2)
+        wm_quantise(2)
+        wm_quantise(3)
+
+        for c in range(1, PANELS - 1):
+            k = GROUPS * c
+            add_plain(nc.gpsimd, k, 0, G_COLS)
+            y_passes(PASSES_OPEN, False)
+            for i in range(6):
+                b_step(c + 2, i)
+            later = {2: [lambda: weave(k + 2)], 3: [lambda: weave(k + 3)], 4: [lambda: weave(k + 4)], 5: [lambda: weave(k + 5)]}
+            run(banks_of(*order(c)), later)
+            y_passes(PASSES_PORT + PASSES_ADD * [kind(k + 2), kind(k + 3)].count("P"))
+            add_plain(nc.vector, k, G_COLS, 2 * PANEL)
+            if c + 2 < PANELS:
+                b_quantise(c + 2)
+            add_plain(nc.vector, k + 2, 0, PANEL)
+            add_plain(nc.vector, k + 3, 0, PANEL)
+            wm_quantise(k, 2)
+            wm_quantise(k + 2, 2)
+
+        k = CELLS - GROUPS
+        add_plain(nc.gpsimd, k, 0, G_LAST)
+        weave(k + 2)
+        weave(k + 3)
+        ring_free.extend(cell_free)
+        cell_free.clear()
+        run(banks_of(*order(PANELS - 1)), {})
+        add_plain(nc.vector, k, G_LAST, PANEL)
+        for g in range(1, GROUPS - 1):
+            add_plain(nc.vector, k + g, 0, PANEL)
+            y_passes(len(todo))
+            wm_quantise(k + g - 1)
+        add_plain(nc.vector, k + 3, 0, PANEL // 2)
         y_passes(len(todo))
-        add_plain(nc.vector, last, 0, PANEL // 2)
-        wm_quantise(last - 1)
-        add_plain(nc.vector, last, PANEL // 2, PANEL)
+        wm_quantise(k + 2)
+        add_plain(nc.vector, k + 3, PANEL // 2, PANEL)
         y_passes(len(todo))
-        wm_quantise(last)
+        wm_quantise(k + 3)
         for i in range(len(todo)):
             y_pass()
             for c, at, tiles in list(closed):

@@ -43,13 +43,16 @@ G_ONE = 256
 G_COLS = 496
 G_LAST = 208
 AHEAD = 12
-HEAD_PASSES = 6
+LAG = 4
+HEAD_PASSES = 4
 PASSES = 2
-PASSES_PORT = 6
+PASSES_PLAIN = 20
+PASSES_TURNED = 11
 PASSES_OPEN = 4
 PASSES_ADD = 7
 PASSES_TURN = 6
-WARM_UPS = 5
+WARM_A = 3
+WARM_B = 2
 
 
 def tile_vera_merged_layer_s13_kernel(tc, x_words, x_scales, a, bmat_bytes, bmat_scale, d_gain, b_gain, w0, out):
@@ -74,7 +77,7 @@ def tile_vera_merged_layer_s13_kernel(tc, x_words, x_scales, a, bmat_bytes, bmat
         a_pla = keep.tile([P, IN], U8, name="a_pla", align_bytes=ALIGN)
         w_cod = keep.tile([P, CELLS * PANEL], U32, name="w_cod", align_bytes=ALIGN)
         w_pla = keep.tile([P, CELLS * PANEL], U8, name="w_pla", align_bytes=ALIGN)
-        x_cod = [keep.tile([P, 2 * T], U8, name="x_cod%d" % g, align_bytes=ALIGN) for g in range(GROUPS)]
+        x_cod = [keep.tile([P, GROUPS, T], U8, name="x_cod%d" % h, align_bytes=ALIGN) for h in range(2)]
         x_pla = keep.tile([P, GROUPS, T], U8, name="x_pla", align_bytes=ALIGN)
 
         a_view = a.rearrange("(g p t) r -> g p t r", p=P, t=SLOTS)
@@ -82,8 +85,8 @@ def tile_vera_merged_layer_s13_kernel(tc, x_words, x_scales, a, bmat_bytes, bmat
         b_view = bmat_bytes.rearrange("(p t) o -> p t o", t=SLOTS)
         out_view = out.rearrange("(m p) o -> p m o", p=P)
 
-        cell_free = list(range(CELL_BANKS))
-        ring_free = list(range(CELL_BANKS, 8))
+        cell_free = list(range(8))
+        ring_free = []
 
         def take(free, shape, dtype=F32):
             b = free[0]
@@ -91,7 +94,7 @@ def tile_vera_merged_layer_s13_kernel(tc, x_words, x_scales, a, bmat_bytes, bmat
             return b, psum.tile(shape, dtype, name="bank", tag="bank%d" % b)
 
         def kind(k):
-            return "SS" if k == 1 else "VV" if k % GROUPS == GROUPS - 1 and k // GROUPS < TURNED_PANELS else "P"
+            return "SS" if k < 2 else "VV" if k % GROUPS == GROUPS - 1 and k // GROUPS < TURNED_PANELS else "P"
 
         nc.vector.memset(gain_rows[:], 0.0)
         make_identity(nc, ident_bf[:])
@@ -119,41 +122,41 @@ def tile_vera_merged_layer_s13_kernel(tc, x_words, x_scales, a, bmat_bytes, bmat
                 w_raw[(c + i) * GROUPS + g] = tile[:, :, i * PANEL : (i + 1) * PANEL]
 
         def load_x_scales():
-            for q in range(4):
+            for j in range(4):
                 nc.sync.dma_start(
-                    out=x_pla[32 * q : 32 * q + 4, :, :].bitcast(I32),
-                    in_=x_scales[:, 4 * q : 4 * q + 4, :].bitcast(I32).rearrange("g q n -> q g n"),
+                    out=x_pla[j:P:32, :, :].bitcast(I32),
+                    in_=x_scales[:, j:16:4, :].bitcast(I32).rearrange("g q n -> q g n"),
                 )
 
-        def load_x(g):
-            nc.sync.dma_start(out=x_cod[g][:].bitcast(I32), in_=x_words[g].bitcast(I32))
+        def load_gain():
+            nc.sync.dma_start(out=gain_rows[0:GAIN_ROWS, :], in_=b_gain.rearrange("(j n) -> j n", j=GAIN_ROWS))
+
+        def load_x(h):
+            nc.sync.dma_start(out=x_cod[h][:].bitcast(I32), in_=x_words[:, :, h * T : (h + 1) * T].bitcast(I32).rearrange("g p n -> p g n"))
 
         nc.scalar.dma_start(out=b_sc[:], in_=bmat_scale.rearrange("(p t) o -> p (t o)", t=SLOTS))
         nc.scalar.dma_start(out=d_col[:], in_=d_gain.rearrange("(p t) -> p t", t=SLOTS))
-        nc.scalar.dma_start(out=gain_rows[0:GAIN_ROWS, :], in_=b_gain.rearrange("(j n) -> j n", j=GAIN_ROWS))
-        load_b(0, 1)
+        load_b(0, 2)
+        load_gain()
         load_a(0)
         load_a(1)
-        load_b(1, 2)
-        load_a(3)
+        load_b(2, 1)
         load_a(2)
-        load_w(0, 0, 1)
-        load_w(0, 1, 1)
+        load_a(3)
+        load_w(0, 0, 2)
+        load_w(0, 1, 2)
         load_w(0, 2, 1)
-        load_w(1, 0, 1)
         load_w(0, 3, 1)
-        load_w(1, 1, 1)
-        load_b(3, 2)
         load_x_scales()
-        for g in range(GROUPS):
-            load_x(g)
+        load_x(0)
+        load_b(3, 1)
         load_w(1, 3, 1)
+        load_x(1)
         load_w(1, 2, 1)
-        load_b(5, 1)
-        for g in range(GROUPS):
-            load_w(2, g, 2)
-        for g in range(GROUPS):
-            load_w(4, g, 2)
+        load_b(4, 2)
+        for c in (2, 4):
+            for g in (0, 1, 3, 2):
+                load_w(c, g, 2)
 
         def quantise(codes, plane, at, grouped):
             cols = slice(at, at + grouped.shape[1])
@@ -164,10 +167,11 @@ def tile_vera_merged_layer_s13_kernel(tc, x_words, x_scales, a, bmat_bytes, bmat
 
         ad_banks, ad_grp, ad_done = {}, {}, []
 
-        def ad_turn(g):
-            ad_grp[g] = work.tile([P, SPAN, SLOTS], BF16, name="ad_grp", tag="ad_grp", align_bytes=ALIGN)
-            for h in range(2):
-                ad_banks[(g, h)] = take(ring_free, [P, 2, 2 * P])
+        def ad_turn(g, halves=(0, 1)):
+            if 0 in halves:
+                ad_grp[g] = work.tile([P, SPAN, SLOTS], BF16, name="ad_grp", tag="ad_grp", align_bytes=ALIGN)
+            for h in halves:
+                ad_banks[(g, h)] = take(cell_free, [P, 2, 2 * P])
                 for i in range(2):
                     words = a_raw[g][:, 2 * h + i, :].bitcast(F32)
                     for u in range(2):
@@ -181,7 +185,7 @@ def tile_vera_merged_layer_s13_kernel(tc, x_words, x_scales, a, bmat_bytes, bmat
                 in1=d_col[:].rearrange("p (u e) -> p u e", u=2).unsqueeze(1).to_broadcast([P, 2 * P, 2, 2]),
                 op=MULT,
             )
-            ring_free.append(b)
+            cell_free.append(b)
 
         def ad_quantise(g):
             quantise(a_cod, a_pla, g * SPAN, ad_grp[g][:])
@@ -192,13 +196,13 @@ def tile_vera_merged_layer_s13_kernel(tc, x_words, x_scales, a, bmat_bytes, bmat
         def b_bytes(c, t, lo, hi):
             return b_raw[c][:, t, lo:hi].bitcast(E4M3)
 
-        def b_widen(c, t, shared=False):
-            if t == 0:
+        def b_widen(c, t, engine=nc.scalar, lo=0, hi=PANEL):
+            if t == 0 and lo == 0:
                 b_wide[c] = work.tile([P, SLOTS, PANEL], BF16, name="b_wide", tag="b_wide", align_bytes=ALIGN)
-            lo = P if shared else 0
-            if shared:
-                nc.vector.tensor_scalar(out=b_wide[c][:, t, 0:lo], in0=b_bytes(c, t, 0, lo), scalar1=b_sc[:, t : t + 1], scalar2=None, op0=MULT)
-            nc.scalar.activation(out=b_wide[c][:, t, lo:PANEL], in_=b_bytes(c, t, lo, PANEL), func=COPY, scale=b_sc[:, t : t + 1])
+            if engine is nc.vector:
+                nc.vector.tensor_scalar(out=b_wide[c][:, t, lo:hi], in0=b_bytes(c, t, lo, hi), scalar1=b_sc[:, t : t + 1], scalar2=None, op0=MULT)
+            else:
+                nc.scalar.activation(out=b_wide[c][:, t, lo:hi], in_=b_bytes(c, t, lo, hi), func=COPY, scale=b_sc[:, t : t + 1])
 
         def b_interleave(c, lo, hi, copy):
             if lo == 0:
@@ -227,14 +231,14 @@ def tile_vera_merged_layer_s13_kernel(tc, x_words, x_scales, a, bmat_bytes, bmat
         scaled, banks, gained, woven = {}, {}, {}, {}
         wm_pool = keep.tile([P, 2 * PANEL, SLOTS], BF16, name="wm_pool", align_bytes=ALIGN)
         wm_vec = [keep.tile([P, 2 * PANEL, SLOTS], BF16, name="wm_vec%d" % i, align_bytes=ALIGN) for i in range(2)]
-        waiting = []
+        waiting = {}
 
         def pair(k):
-            return k if k < GROUPS else k - k % 2
+            return k - k % 2
 
         def wm_pair(k):
             if k < GROUPS:
-                return wm_pool[:] if k % 2 == 0 else wm_vec[0][:, k // 2 * PANEL : 2 * PANEL, :]
+                return wm_pool[:] if k < 2 else wm_vec[0][:]
             return wm_pool[:] if k % GROUPS < 2 else wm_vec[k // GROUPS % 2][:]
 
         def wm_of(k):
@@ -254,30 +258,35 @@ def tile_vera_merged_layer_s13_kernel(tc, x_words, x_scales, a, bmat_bytes, bmat
                 mx_pass(bank[:], *b_operand(j * P, (j + 1) * P), *a_operand(g * SPAN, (g + 1) * SPAN))
                 scaled[(k, u)] = work.tile([P, SPAN], F32, name="scaled", tag="scaled", bufs=4)
                 nc.scalar.activation(out=scaled[(k, u)][:], in_=bank[:], func=COPY, scale=gain_col[:, j % 3, j // 3 : j // 3 + 1])
-                waiting.append((k, u, b))
+                waiting[(k, u)] = b
 
-        def turn_back(cell=None):
-            unturned = [x for x in waiting if cell is None or x[0] == cell]
-            for x in unturned:
-                waiting.remove(x)
-            for k, u, b in unturned:
-                banks[(k, u)] = take([b], [P, SLOTS, P])
-                if kind(k)[u] == "S":
-                    nc.tensor.matmul(banks[(k, u)][1][:], lhsT=ident_bf[:], rhs=w_raw[k][:, :, u * P : (u + 1) * P], start=True, stop=False)
-            for k, u, b in unturned:
-                laid = kind(k)[u] == "S"
-                for t in range(SLOTS):
-                    nc.tensor.matmul(
-                        banks[(k, u)][1][:, t, :],
-                        lhsT=scaled[(k, u)][:, t * P : (t + 1) * P],
-                        rhs=ident[:],
-                        is_transpose=True,
-                        start=not laid,
-                        stop=not laid or t == SLOTS - 1,
-                    )
+        def lay(k, u):
+            b = waiting.pop((k, u))
+            banks[(k, u)] = take([b], [P, SLOTS, P])
+            if kind(k) == "SS":
+                nc.tensor.matmul(banks[(k, u)][1][:], lhsT=ident_bf[:], rhs=w_raw[k][:, :, u * P : (u + 1) * P], start=True, stop=False)
+
+        def turn(k, u):
+            if (k, u) in waiting:
+                lay(k, u)
+            laid = kind(k) == "SS"
+            for t in range(SLOTS):
+                nc.tensor.matmul(
+                    banks[(k, u)][1][:, t, :],
+                    lhsT=scaled[(k, u)][:, t * P : (t + 1) * P],
+                    rhs=ident[:],
+                    is_transpose=True,
+                    start=not laid,
+                    stop=not laid or t == SLOTS - 1,
+                )
+
+        def turn_back(k):
+            for step in (lay, turn):
+                for u in range(2):
+                    step(k, u)
 
         def weaves(k):
-            return 0 < k < CELLS and kind(k) == "P" and (k % GROUPS < 2 or k == 2 or k // GROUPS >= WEAVE_FROM)
+            return 0 < k < CELLS and kind(k) == "P" and k >= GROUPS and (k % GROUPS < 2 or k // GROUPS >= WEAVE_FROM)
 
         def weave(k):
             if weaves(k):
@@ -346,13 +355,16 @@ def tile_vera_merged_layer_s13_kernel(tc, x_words, x_scales, a, bmat_bytes, bmat
             quantise(w_cod, w_pla, k * PANEL, wm_of(k) if cells == 1 else wm_pair(k))
             quantised.extend(range(k, k + cells))
 
+        def group_order(c):
+            return (2, 3, 0, 1) if c == 0 else (0, 1, 2, 3)
+
         todo = []
         for c in range(PANELS - 1):
-            todo.extend([(GROUPS * c + g, 2 * j + i) for j in range(T_TILES // 2) for g in range(GROUPS) for i in range(2)])
+            todo.extend([(GROUPS * c + g, 2 * j + i) for j in range(T_TILES // 2) for g in group_order(c) for i in range(2)])
         by_group = [(CELLS - GROUPS + g, m) for g in range(GROUPS) for m in range(T_TILES)]
         todo.extend(by_group[:AHEAD])
         todo.extend(sorted(by_group[AHEAD:], key=lambda p: (p[1], p[0])))
-        y_banks, closed = {}, []
+        y_banks, closed, closed_at = {}, [], {}
 
         def y_pass():
             if not todo or todo[0][0] not in quantised:
@@ -361,8 +373,8 @@ def tile_vera_merged_layer_s13_kernel(tc, x_words, x_scales, a, bmat_bytes, bmat
             c, g = divmod(k, GROUPS)
             tiles = 1 if c == PANELS - 1 else 2
             at = m - m % tiles
-            first = g == 0 and m == at
-            last = g == GROUPS - 1 and m == at + tiles - 1
+            first = g == group_order(c)[0] and m == at
+            last = g == group_order(c)[-1] and m == at + tiles - 1
             if first:
                 if not ring_free:
                     return
@@ -371,7 +383,7 @@ def tile_vera_merged_layer_s13_kernel(tc, x_words, x_scales, a, bmat_bytes, bmat
             cols = slice(k * PANEL, (k + 1) * PANEL)
             mx_pass(
                 y_banks[(c, at)][1][:, m - at, :],
-                x_cod[g][:, m * 2 * P : (m + 1) * 2 * P].bitcast(E2M1X4),
+                x_cod[m // 4][:, g, m % 4 * 2 * P : (m % 4 + 1) * 2 * P].bitcast(E2M1X4),
                 x_pla[:, g, m * P : (m + 1) * P],
                 w_cod[:, cols].bitcast(E4M3X4),
                 w_pla[:, cols],
@@ -380,6 +392,7 @@ def tile_vera_merged_layer_s13_kernel(tc, x_words, x_scales, a, bmat_bytes, bmat
             )
             if last:
                 closed.append((c, at, tiles))
+                closed_at[(c, at, tiles)] = len(todo)
 
         def y_store(copy):
             c, at, tiles = closed[0]
@@ -393,7 +406,8 @@ def tile_vera_merged_layer_s13_kernel(tc, x_words, x_scales, a, bmat_bytes, bmat
             for i in range(count):
                 if store:
                     for tile in list(closed):
-                        y_store(nc.scalar.copy)
+                        if closed_at[tile] - len(todo) >= LAG or not ring_free:
+                            y_store(nc.scalar.copy)
                 y_pass()
 
         def spread_gain(half):
@@ -423,49 +437,75 @@ def tile_vera_merged_layer_s13_kernel(tc, x_words, x_scales, a, bmat_bytes, bmat
         warm = keep.tile([P, SPAN], BF16, name="warm")
         nc.vector.memset(warm[:], 0.0)
         warm_b, warm_bank = take(cell_free, [P, SPAN])
-        for i in range(WARM_UPS):
-            nc.tensor.matmul(warm_bank[:], lhsT=warm[:, 0:P], rhs=warm[:], start=True, stop=True)
-        ad_turn(0)
-        spread = [spread_gain(0), spread_gain(1)]
+
+        def warm_up(count):
+            for i in range(count):
+                nc.tensor.matmul(warm_bank[:], lhsT=warm[:, 0:P], rhs=warm[:], start=True, stop=True)
+
+        warm_up(WARM_A)
+        spread = [spread_gain(0)]
+        ad_turn(0, [0])
+        spread.append(spread_gain(1))
+        ad_turn(0, [1])
+        warm_up(WARM_B)
         cell_free.append(warm_b)
         for t in range(SLOTS):
-            b_widen(0, t, shared=True)
-        b_interleave(0, 0, P, nc.vector.tensor_copy)
-        b_interleave(0, P, PANEL, nc.scalar.copy)
+            b_widen(0, t, nc.vector)
+        for i in range(SLOTS):
+            b_step(1, i)
         take_out_gain(*spread[0])
+        b_step(1, 4)
+        b_step(1, 5)
         take_out_gain(*spread[1])
+        b_interleave(0, 0, PANEL, nc.vector.tensor_copy)
         both(ad_product, 0)
         ad_turn(1)
         b_quantise(0)
         ad_quantise(0)
-        both(fill, 0)
-        for i in range(6):
-            b_step(1, i)
-        both(ad_product, 1)
-        ad_turn(3)
-        empty(0, 0)
-        ad_quantise(1)
-        both(fill, 1)
-        ad_turn(2)
-        empty(0, 1)
-        b_quantise(1)
-        add_plain(nc.gpsimd, 0, 0, G_HEAD)
-        for i in range(4):
+        for i in range(SLOTS):
             b_step(2, i)
-        turn_back()
-        both(fill, 4)
-        both(ad_product, 3)
-        both(empty, 1)
-        weave(2)
+        both(fill, 0)
+        both(ad_product, 1)
+        ad_turn(2)
+        b_quantise(1)
+        ad_quantise(1)
+        b_step(2, 4)
+        b_step(2, 5)
+        both(fill, 1)
+        ad_turn(3)
         both(ad_product, 2)
-        ad_quantise(3)
-        both(fill, 3, ring_free)
         ad_quantise(2)
-        both(fill, 2, ring_free)
-        add_plain(nc.vector, 0, G_HEAD, PANEL)
-        turn_back()
-        wm_quantise(1)
-        wm_quantise(0)
+        weave(4)
+        both(lay, 0)
+        both(fill, 2)
+        both(turn, 0)
+        both(ad_product, 3)
+        both(fill, 4)
+        empty(2, 0)
+        ad_quantise(3)
+        empty(2, 1)
+        add_plain(nc.gpsimd, 2, 0, G_ONE)
+        both(empty, 0)
+        both(fill, 3)
+        both(fill, 5)
+        weave(5)
+        both(lay, 1)
+        for u in range(2):
+            turn(3, u)
+            turn(1, u)
+        both(empty, 4)
+        both(empty, 1)
+        both(fill, 7)
+        both(fill, 6)
+        both(empty, 5, ring_free)
+        empty(3, 0, ring_free)
+        empty(3, 1)
+        add_plain(nc.vector, 2, G_ONE, PANEL)
+        b_quantise(2)
+        wm_quantise(2, 2)
+        y_passes(HEAD_PASSES, False)
+        turn_back(7)
+        wm_quantise(0, 2)
 
         def banks_of(*cells):
             return [(k, u) for k in cells if k < CELLS for u in range(2)]
@@ -474,7 +514,7 @@ def tile_vera_merged_layer_s13_kernel(tc, x_words, x_scales, a, bmat_bytes, bmat
             k = GROUPS * c + 2
             return (k + 1, k) if kind(k + 1) != "P" else (k, k + 1)
 
-        unfilled = banks_of(*own(1), 5, 8, 9)
+        unfilled = banks_of(8, 9)
         for c in range(2, PANELS):
             unfilled.extend(banks_of(*own(c), GROUPS * c + 4, GROUPS * c + 5))
         due = {}
@@ -497,14 +537,12 @@ def tile_vera_merged_layer_s13_kernel(tc, x_words, x_scales, a, bmat_bytes, bmat
             for k in [k for k in due if force or due[k] <= clock[0]]:
                 due.pop(k)
 
-        to_ring = [(5, 0), (5, 1), (own(1)[0], 0)][:RING]
-
         def run(leaving, after, force=True):
             fill_all()
             for i, (k, u) in enumerate(leaving):
                 if k in due:
                     turn_due(True)
-                empty(k, u, cell_free if unfilled and (k, u) not in to_ring else ring_free)
+                empty(k, u, cell_free if unfilled else ring_free)
                 clock[0] = clock[0] + 1
                 fill_all()
                 turn_due()
@@ -519,16 +557,6 @@ def tile_vera_merged_layer_s13_kernel(tc, x_words, x_scales, a, bmat_bytes, bmat
             turned = [j for j in own(c) if kind(j) != "P"]
             return plain + turned + [k + 4, k + 5]
 
-        b_step(2, 4)
-        b_step(2, 5)
-        run(banks_of(2), {}, False)
-        add_plain(nc.gpsimd, 2, 0, G_ONE)
-        run(banks_of(4, 3, 5), {0: [lambda: weave(4)], 3: [lambda: weave(5)]})
-        add_plain(nc.vector, 2, G_ONE, PANEL)
-        b_quantise(2)
-        wm_quantise(2)
-        wm_quantise(3)
-
         for c in range(1, PANELS - 1):
             k = GROUPS * c
             add_plain(nc.gpsimd, k, 0, G_COLS)
@@ -537,12 +565,12 @@ def tile_vera_merged_layer_s13_kernel(tc, x_words, x_scales, a, bmat_bytes, bmat
                 b_step(c + 2, i)
             later = {2: [lambda: weave(k + 2)], 3: [lambda: weave(k + 3)], 4: [lambda: weave(k + 4)], 5: [lambda: weave(k + 5)]}
             run(banks_of(*order(c)), later)
-            y_passes(PASSES_PORT + PASSES_ADD * [kind(k + 2), kind(k + 3)].count("P"))
+            y_passes(PASSES_PLAIN if kind(k + 3) == "P" else PASSES_TURNED)
             add_plain(nc.vector, k, G_COLS, 2 * PANEL)
-            if c + 2 < PANELS:
-                b_quantise(c + 2)
             add_plain(nc.vector, k + 2, 0, PANEL)
             add_plain(nc.vector, k + 3, 0, PANEL)
+            if c + 2 < PANELS:
+                b_quantise(c + 2)
             wm_quantise(k, 2)
             wm_quantise(k + 2, 2)
 
@@ -554,14 +582,10 @@ def tile_vera_merged_layer_s13_kernel(tc, x_words, x_scales, a, bmat_bytes, bmat
         cell_free.clear()
         run(banks_of(*order(PANELS - 1)), {})
         add_plain(nc.vector, k, G_LAST, PANEL)
-        for g in range(1, GROUPS - 1):
+        for g in range(1, GROUPS):
             add_plain(nc.vector, k + g, 0, PANEL)
             y_passes(len(todo))
             wm_quantise(k + g - 1)
-        add_plain(nc.vector, k + 3, 0, PANEL // 2)
-        y_passes(len(todo))
-        wm_quantise(k + 2)
-        add_plain(nc.vector, k + 3, PANEL // 2, PANEL)
         y_passes(len(todo))
         wm_quantise(k + 3)
         for i in range(len(todo)):

@@ -46,6 +46,7 @@ AHEAD = 12
 LAG = 4
 HEAD_PASSES = 4
 PASSES = 2
+FILL_AT = 0
 PASSES_PLAIN = 20
 PASSES_TURNED = 11
 PASSES_OPEN = 4
@@ -544,7 +545,8 @@ def tile_vera_merged_layer_s13_kernel(tc, x_words, x_scales, a, bmat_bytes, bmat
                     turn_due(True)
                 empty(k, u, cell_free if unfilled else ring_free)
                 clock[0] = clock[0] + 1
-                fill_all()
+                if u == FILL_AT:
+                    fill_all()
                 turn_due()
                 for step in after.get(i, []):
                     step()

@@ -47,6 +47,7 @@ LAG = 4
 HEAD_PASSES = 4
 PASSES = 2
 FILL_AT = 0
+LENT = 2
 PASSES_PLAIN = 20
 PASSES_TURNED = 11
 PASSES_OPEN = 4
@@ -267,11 +268,11 @@ def tile_vera_merged_layer_s13_kernel(tc, x_words, x_scales, a, bmat_bytes, bmat
             if kind(k) == "SS":
                 nc.tensor.matmul(banks[(k, u)][1][:], lhsT=ident_bf[:], rhs=w_raw[k][:, :, u * P : (u + 1) * P], start=True, stop=False)
 
-        def turn(k, u):
+        def turn(k, u, slots=range(SLOTS)):
             if (k, u) in waiting:
                 lay(k, u)
             laid = kind(k) == "SS"
-            for t in range(SLOTS):
+            for t in slots:
                 nc.tensor.matmul(
                     banks[(k, u)][1][:, t, :],
                     lhsT=scaled[(k, u)][:, t * P : (t + 1) * P],
@@ -463,18 +464,17 @@ def tile_vera_merged_layer_s13_kernel(tc, x_words, x_scales, a, bmat_bytes, bmat
         ad_turn(1)
         b_quantise(0)
         ad_quantise(0)
-        for i in range(SLOTS):
+        for i in range(6):
             b_step(2, i)
         both(fill, 0)
         both(ad_product, 1)
         ad_turn(2)
         b_quantise(1)
         ad_quantise(1)
-        b_step(2, 4)
-        b_step(2, 5)
         both(fill, 1)
         ad_turn(3)
         both(ad_product, 2)
+        b_quantise(2)
         ad_quantise(2)
         weave(4)
         both(lay, 0)
@@ -490,19 +490,23 @@ def tile_vera_merged_layer_s13_kernel(tc, x_words, x_scales, a, bmat_bytes, bmat
         both(fill, 3)
         both(fill, 5)
         weave(5)
-        both(lay, 1)
         for u in range(2):
-            turn(3, u)
-            turn(1, u)
+            lay(1, u)
+            turn(3, 0, range(2 * u, 2 * u + 2))
+        turn(1, 0)
+        turn(3, 1)
+        turn(1, 1)
         both(empty, 4)
         both(empty, 1)
         both(fill, 7)
         both(fill, 6)
-        both(empty, 5, ring_free)
-        empty(3, 0, ring_free)
+        empty(5, 0, ring_free)
+        empty(5, 1, cell_free)
+        empty(3, 0, cell_free)
         empty(3, 1)
         add_plain(nc.vector, 2, G_ONE, PANEL)
-        b_quantise(2)
+        for k, u in [(8, 0), (8, 1), (9, 0)][: LENT + 1]:
+            fill(k, u)
         wm_quantise(2, 2)
         y_passes(HEAD_PASSES, False)
         turn_back(7)
@@ -515,10 +519,11 @@ def tile_vera_merged_layer_s13_kernel(tc, x_words, x_scales, a, bmat_bytes, bmat
             k = GROUPS * c + 2
             return (k + 1, k) if kind(k + 1) != "P" else (k, k + 1)
 
-        unfilled = banks_of(8, 9)
+        unfilled = [x for x in banks_of(8, 9) if x not in banks]
         for c in range(2, PANELS):
             unfilled.extend(banks_of(*own(c), GROUPS * c + 4, GROUPS * c + 5))
         due = {}
+        lent = banks_of(6)[:LENT]
         clock = [0]
 
         def fill_all():
@@ -543,7 +548,7 @@ def tile_vera_merged_layer_s13_kernel(tc, x_words, x_scales, a, bmat_bytes, bmat
             for i, (k, u) in enumerate(leaving):
                 if k in due:
                     turn_due(True)
-                empty(k, u, cell_free if unfilled else ring_free)
+                empty(k, u, cell_free if unfilled and (k, u) not in lent else ring_free)
                 clock[0] = clock[0] + 1
                 if u == FILL_AT:
                     fill_all()

@@ -41,6 +41,7 @@ WEAVE_FROM = 4
 G_HEAD = 144
 G_ONE = 256
 G_COLS = 496
+G_FIRST = 464
 G_LAST = 208
 AHEAD = 12
 LAG = 4
@@ -364,7 +365,7 @@ def tile_vera_merged_layer_s13_kernel(tc, x_words, x_scales, a, bmat_bytes, bmat
         for c in range(PANELS - 1):
             todo.extend([(GROUPS * c + g, 2 * j + i) for j in range(T_TILES // 2) for g in group_order(c) for i in range(2)])
         by_group = [(CELLS - GROUPS + g, m) for g in range(GROUPS) for m in range(T_TILES)]
-        todo.extend(by_group[:AHEAD])
+        todo.extend(sorted(by_group[:AHEAD], key=lambda p: (p[1] // (T_TILES // 2), p[0], p[1])))
         todo.extend(sorted(by_group[AHEAD:], key=lambda p: (p[1], p[0])))
         y_banks, closed, closed_at = {}, [], {}
 
@@ -447,7 +448,6 @@ def tile_vera_merged_layer_s13_kernel(tc, x_words, x_scales, a, bmat_bytes, bmat
         warm_up(WARM_A)
         spread = [spread_gain(0)]
         ad_turn(0, [0])
-        spread.append(spread_gain(1))
         ad_turn(0, [1])
         warm_up(WARM_B)
         cell_free.append(warm_b)
@@ -458,14 +458,17 @@ def tile_vera_merged_layer_s13_kernel(tc, x_words, x_scales, a, bmat_bytes, bmat
         take_out_gain(*spread[0])
         b_step(1, 4)
         b_step(1, 5)
-        take_out_gain(*spread[1])
         b_interleave(0, 0, PANEL, nc.vector.tensor_copy)
         both(ad_product, 0)
         ad_turn(1)
+        spread.append(spread_gain(1))
         b_quantise(0)
         ad_quantise(0)
-        for i in range(6):
+        for i in range(SLOTS):
             b_step(2, i)
+        take_out_gain(*spread[1])
+        b_step(2, 4)
+        b_step(2, 5)
         both(fill, 0)
         both(ad_product, 1)
         ad_turn(2)
@@ -487,22 +490,24 @@ def tile_vera_merged_layer_s13_kernel(tc, x_words, x_scales, a, bmat_bytes, bmat
         empty(2, 1)
         add_plain(nc.gpsimd, 2, 0, G_ONE)
         both(empty, 0)
-        both(fill, 3)
+        fill(3, 0)
+        lay(1, 0)
+        fill(3, 1)
         both(fill, 5)
         weave(5)
+        lay(1, 1)
         for u in range(2):
-            lay(1, u)
-            turn(3, 0, range(2 * u, 2 * u + 2))
-        turn(1, 0)
-        turn(3, 1)
-        turn(1, 1)
+            turn(3, u)
+            turn(1, u)
         both(empty, 4)
-        both(empty, 1)
+        late = []
+        both(empty, 1, late)
         both(fill, 7)
-        both(fill, 6)
         empty(5, 0, ring_free)
-        empty(5, 1, cell_free)
-        empty(3, 0, cell_free)
+        empty(5, 1)
+        empty(3, 0)
+        both(fill, 6)
+        cell_free.extend(late)
         empty(3, 1)
         add_plain(nc.vector, 2, G_ONE, PANEL)
         for k, u in [(8, 0), (8, 1), (9, 0)][: LENT + 1]:
@@ -566,14 +571,15 @@ def tile_vera_merged_layer_s13_kernel(tc, x_words, x_scales, a, bmat_bytes, bmat
 
         for c in range(1, PANELS - 1):
             k = GROUPS * c
-            add_plain(nc.gpsimd, k, 0, G_COLS)
+            cols = G_FIRST if c == 1 else G_COLS
+            add_plain(nc.gpsimd, k, 0, cols)
             y_passes(PASSES_OPEN, False)
             for i in range(6):
                 b_step(c + 2, i)
             later = {2: [lambda: weave(k + 2)], 3: [lambda: weave(k + 3)], 4: [lambda: weave(k + 4)], 5: [lambda: weave(k + 5)]}
             run(banks_of(*order(c)), later)
             y_passes(PASSES_PLAIN if kind(k + 3) == "P" else PASSES_TURNED)
-            add_plain(nc.vector, k, G_COLS, 2 * PANEL)
+            add_plain(nc.vector, k, cols, 2 * PANEL)
             add_plain(nc.vector, k + 2, 0, PANEL)
             add_plain(nc.vector, k + 3, 0, PANEL)
             if c + 2 < PANELS:

from contextlib import ExitStack

import concourse.mybir as mybir
from concourse.masks import make_identity

F32 = mybir.dt.float32
BF16 = mybir.dt.bfloat16
I32 = mybir.dt.int32
U32 = mybir.dt.uint32
U8 = mybir.dt.uint8
E4M3 = mybir.dt.float8_e4m3fn
E4M3X4 = mybir.dt.float8_e4m3fn_x4
E2M1X4 = mybir.dt.float4_e2m1fn_x4
MULT = mybir.AluOpType.mult
ADD = mybir.AluOpType.add
COPY = mybir.ActivationFunctionType.Copy

T, IN, R, OUT = 1024, 2048, 512, 1536
P = 128
SLOTS = 4
SPAN = P * SLOTS
GROUPS = IN // SPAN
PANEL = 256
PANELS = OUT // PANEL
CELLS = PANELS * GROUPS
ROWS = CELLS // 2
GAIN_ROWS = 4
GAIN_ROW = OUT // GAIN_ROWS
T_TILES = T // P
RUN = 4

FLOPS = 2 * IN * R * OUT + 2 * T * IN * OUT

ALIGN = 64
CELL_BANKS = 4
RES_BUFS = 8
TURNED_PANELS = 5
TURN_AFTER = 4
RING = 3
WEAVE_FROM = 4
G_HEAD = 144
G_ONE = 256
G_COLS = 496
G_FIRST = 464
G_LAST = 208
AHEAD = 12
LAG = 4
HEAD_PASSES = 4
PASSES = 2
FILL_AT = 0
LENT = 2
PASSES_PLAIN = 20
PASSES_TURNED = 11
PASSES_OPEN = 4
PASSES_ADD = 7
PASSES_TURN = 6
WARM_A = 3
WARM_B = 2


def tile_vera_merged_layer_s13_kernel(tc, x_words, x_scales, a, bmat_bytes, bmat_scale, d_gain, b_gain, w0, out):
    nc = tc.nc
    with ExitStack() as ctx:
        keep = ctx.enter_context(tc.tile_pool(name="keep", bufs=1))
        work = ctx.enter_context(tc.tile_pool(name="work", bufs=2))
        psum = ctx.enter_context(tc.psum_pool(name="psum", bufs=1))
        ctx.enter_context(tc.manual_schedule())

        gain_rows = keep.tile([P, GAIN_ROW], BF16, name="gain_rows")
        ident = keep.tile([P, P], F32, name="ident")
        ident_bf = keep.tile([P, P], BF16, name="ident_bf")
        b_sc = keep.tile([P, SLOTS], F32, name="b_sc")
        d_col = keep.tile([P, SLOTS], BF16, name="d_col")
        gain_col = keep.tile([P, GAIN_ROW // P, GAIN_ROWS], F32, name="gain_col")
        gain_all = keep.tile([P, OUT], BF16, name="gain_all")
        b_cod = keep.tile([P, OUT], U32, name="b_cod", align_bytes=ALIGN)
        b_pla = keep.tile([P, OUT], U8, name="b_pla", align_bytes=ALIGN)
        a_raw = [keep.tile([P, SLOTS, R], BF16, name="a_raw%d" % g, align_bytes=ALIGN) for g in range(GROUPS)]
        a_cod = keep.tile([P, IN], U32, name="a_cod", align_bytes=ALIGN)
        a_pla = keep.tile([P, IN], U8, name="a_pla", align_bytes=ALIGN)
        w_cod = keep.tile([P, CELLS * PANEL], U32, name="w_cod", align_bytes=ALIGN)
        w_pla = keep.tile([P, CELLS * PANEL], U8, name="w_pla", align_bytes=ALIGN)
        x_cod = [keep.tile([P, GROUPS, T], U8, name="x_cod%d" % h, align_bytes=ALIGN) for h in range(2)]
        x_pla = keep.tile([P, GROUPS, T], U8, name="x_pla", align_bytes=ALIGN)

        a_view = a.rearrange("(g p t) r -> g p t r", p=P, t=SLOTS)
        w_view = w0.rearrange("(g p t) o -> g p t o", p=P, t=SLOTS)
        b_view = bmat_bytes.rearrange("(p t) o -> p t o", t=SLOTS)
        out_view = out.rearrange("(m p) o -> p m o", p=P)

        cell_free = list(range(8))
        ring_free = []

        def take(free, shape, dtype=F32):
            b = free[0]
            free.remove(b)
            return b, psum.tile(shape, dtype, name="bank", tag="bank%d" % b)

        def kind(k):
            return "SS" if k < 2 else "VV" if k % GROUPS == GROUPS - 1 and k // GROUPS < TURNED_PANELS else "P"

        nc.vector.memset(gain_rows[:], 0.0)
        make_identity(nc, ident_bf[:])
        nc.gpsimd.memset(x_pla[:].rearrange("p g n -> p (g n)").bitcast(U32), 0)

        w_raw, b_raw = {}, {}

        def load_a(g):
            if g == 0:
                for h in range(2):
                    nc.sync.dma_start(out=a_raw[g][:, 2 * h : 2 * h + 2, :], in_=a_view[g][:, 2 * h : 2 * h + 2, :])
            else:
                nc.sync.dma_start(out=a_raw[g][:], in_=a_view[g])

        def load_b(c, panels):
            tile = keep.tile([P, SLOTS, panels * PANEL], U8, name="b_raw%d" % c, align_bytes=ALIGN)
            nc.sync.dma_start(out=tile[:], in_=b_view[:, :, c * PANEL : (c + panels) * PANEL])
            for i in range(panels):
                b_raw[c + i] = tile[:, :, i * PANEL : (i + 1) * PANEL]

        def load_w(c, g, panels):
            tile = keep.tile([P, SLOTS, panels * PANEL], BF16, name="w_raw%d%d" % (c, g), align_bytes=ALIGN)
            nc.sync.dma_start(out=tile[:], in_=w_view[g][:, :, c * PANEL : (c + panels) * PANEL])
            for i in range(panels):
                w_raw[(c + i) * GROUPS + g] = tile[:, :, i * PANEL : (i + 1) * PANEL]

        def load_x_scales():
            for j in range(4):
                nc.sync.dma_start(
                    out=x_pla[j:P:32, :, :].bitcast(I32),
                    in_=x_scales[:, j:16:4, :].bitcast(I32).rearrange("g q n -> q g n"),
                )

        def load_gain():
            nc.sync.dma_start(out=gain_rows[0:GAIN_ROWS, :], in_=b_gain.rearrange("(j n) -> j n", j=GAIN_ROWS))

        def load_x(h):
            nc.sync.dma_start(out=x_cod[h][:].bitcast(I32), in_=x_words[:, :, h * T : (h + 1) * T].bitcast(I32).rearrange("g p n -> p g n"))

        nc.scalar.dma_start(out=b_sc[:], in_=bmat_scale.rearrange("(p t) o -> p (t o)", t=SLOTS))
        nc.scalar.dma_start(out=d_col[:], in_=d_gain.rearrange("(p t) -> p t", t=SLOTS))
        load_b(0, 2)
        load_gain()
        load_a(0)
        load_a(1)
        load_b(2, 1)
        load_a(2)
        load_a(3)
        load_w(0, 0, 2)
        load_w(0, 1, 2)
        load_w(0, 2, 1)
        load_w(0, 3, 1)
        load_x_scales()
        load_x(0)
        load_b(3, 1)
        load_w(1, 3, 1)
        load_x(1)
        load_w(1, 2, 1)
        load_b(4, 2)
        for c in (2, 4):
            for g in (0, 1, 3, 2):
                load_w(c, g, 2)

        def quantise(codes, plane, at, grouped):
            cols = slice(at, at + grouped.shape[1])
            nc.vector.quantize_mx(out=codes[:, cols].bitcast(E4M3X4), scales=plane[:, cols], in_=grouped.rearrange("p n t -> p (n t)"))

        def mx_pass(bank, lhs, lhs_plane, rhs, rhs_plane, start=True, stop=True):
            nc.tensor.matmul_mx(out=bank, lhsT=lhs, lhsT_scale=lhs_plane, rhs=rhs, rhs_scale=rhs_plane, start=start, stop=stop)

        ad_banks, ad_grp, ad_done = {}, {}, []

        def ad_turn(g, halves=(0, 1)):
            if 0 in halves:
                ad_grp[g] = work.tile([P, SPAN, SLOTS], BF16, name="ad_grp", tag="ad_grp", align_bytes=ALIGN)
            for h in halves:
                ad_banks[(g, h)] = take(cell_free, [P, 2, 2 * P])
                for i in range(2):
                    words = a_raw[g][:, 2 * h + i, :].bitcast(F32)
                    for u in range(2):
                        nc.tensor.transpose(ad_banks[(g, h)][1][:, u, i * P : (i + 1) * P], words[:, u::2], ident[:])

        def ad_product(g, h):
            b, bank = ad_banks[(g, h)]
            nc.vector.tensor_tensor(
                out=ad_grp[g][:, 2 * h * P : 2 * (h + 1) * P, :].rearrange("p n (u e) -> p n u e", u=2),
                in0=bank[:].bitcast(BF16).rearrange("p u (n e) -> p n u e", e=2),
                in1=d_col[:].rearrange("p (u e) -> p u e", u=2).unsqueeze(1).to_broadcast([P, 2 * P, 2, 2]),
                op=MULT,
            )
            cell_free.append(b)

        def ad_quantise(g):
            quantise(a_cod, a_pla, g * SPAN, ad_grp[g][:])
            ad_done.append(g)

        b_wide, b_grp, b_done = {}, {}, []

        def b_bytes(c, t, lo, hi):
            return b_raw[c][:, t, lo:hi].bitcast(E4M3)

        def b_widen(c, t, engine=nc.scalar, lo=0, hi=PANEL):
            if t == 0 and lo == 0:
                b_wide[c] = work.tile([P, SLOTS, PANEL], BF16, name="b_wide", tag="b_wide", align_bytes=ALIGN)
            if engine is nc.vector:
                nc.vector.tensor_scalar(out=b_wide[c][:, t, lo:hi], in0=b_bytes(c, t, lo, hi), scalar1=b_sc[:, t : t + 1], scalar2=None, op0=MULT)
            else:
                nc.scalar.activation(out=b_wide[c][:, t, lo:hi], in_=b_bytes(c, t, lo, hi), func=COPY, scale=b_sc[:, t : t + 1])

        def b_interleave(c, lo, hi, copy):
            if lo == 0:
                b_grp[c] = work.tile([P, PANEL, SLOTS], BF16, name="b_grp", tag="b_grp", align_bytes=ALIGN)
            copy(
                out=b_grp[c][:, lo:hi, :].rearrange("p (n i) t -> p n t i", i=RUN),
                in_=b_wide[c][:, :, lo:hi].rearrange("p t (n i) -> p n t i", i=RUN),
            )

        def b_step(c, i):
            if c < PANELS and 0 <= i < SLOTS:
                b_widen(c, i)
            elif c < PANELS and SLOTS <= i < SLOTS + 2:
                b_interleave(c, (i - SLOTS) * P, (i - SLOTS + 1) * P, nc.scalar.copy)

        def b_quantise(c):
            quantise(b_cod, b_pla, c * PANEL, b_grp[c][:])
            b_done.append(c)

        def a_operand(lo, hi):
            return a_cod[:, lo:hi].bitcast(E4M3X4), a_pla[:, lo:hi]

        def b_operand(lo, hi):
            return b_cod[:, lo:hi].bitcast(E4M3X4), b_pla[:, lo:hi]

        scaled, banks, gained, woven = {}, {}, {}, {}
        wm_pool = keep.tile([P, 2 * PANEL, SLOTS], BF16, name="wm_pool", align_bytes=ALIGN)
        wm_vec = [keep.tile([P, 2 * PANEL, SLOTS], BF16, name="wm_vec%d" % i, align_bytes=ALIGN) for i in range(2)]
        waiting = {}

        def pair(k):
            return k - k % 2

        def wm_pair(k):
            if k < GROUPS:
                return wm_pool[:] if k < 2 else wm_vec[0][:]
            return wm_pool[:] if k % GROUPS < 2 else wm_vec[k // GROUPS % 2][:]

        def wm_of(k):
            at = (k - pair(k)) * PANEL
            return wm_pair(k)[:, at : at + PANEL, :]

        def fill(k, u, free=cell_free):
            c, g = divmod(k, GROUPS)
            if kind(k) == "P":
                banks[(k, u)] = take(free, [P, 2, PANEL])
                for e in range(2):
                    at = g * SPAN + (2 * u + e) * P
                    mx_pass(banks[(k, u)][1][:, e, :], *a_operand(at, at + P), *b_operand(c * PANEL, (c + 1) * PANEL))
            else:
                j = 2 * c + u
                b, bank = take(free, [P, SPAN])
                mx_pass(bank[:], *b_operand(j * P, (j + 1) * P), *a_operand(g * SPAN, (g + 1) * SPAN))
                scaled[(k, u)] = work.tile([P, SPAN], F32, name="scaled", tag="scaled", bufs=4)
                nc.scalar.activation(out=scaled[(k, u)][:], in_=bank[:], func=COPY, scale=gain_col[:, j % 3, j // 3 : j // 3 + 1])
                waiting[(k, u)] = b

        def lay(k, u):
            b = waiting.pop((k, u))
            banks[(k, u)] = take([b], [P, SLOTS, P])
            if kind(k) == "SS":
                nc.tensor.matmul(banks[(k, u)][1][:], lhsT=ident_bf[:], rhs=w_raw[k][:, :, u * P : (u + 1) * P], start=True, stop=False)

        def turn(k, u, slots=range(SLOTS)):
            if (k, u) in waiting:
                lay(k, u)
            laid = kind(k) == "SS"
            for t in slots:
                nc.tensor.matmul(
                    banks[(k, u)][1][:, t, :],
                    lhsT=scaled[(k, u)][:, t * P : (t + 1) * P],
                    rhs=ident[:],
                    is_transpose=True,
                    start=not laid,
                    stop=not laid or t == SLOTS - 1,
                )

        def turn_back(k):
            for step in (lay, turn):
                for u in range(2):
                    step(k, u)

        def weaves(k):
            return 0 < k < CELLS and kind(k) == "P" and k >= GROUPS and (k % GROUPS < 2 or k // GROUPS >= WEAVE_FROM)

        def weave(k):
            if weaves(k):
                if pair(k) not in woven:
                    woven[pair(k)] = work.tile([P, PANEL, SLOTS], F32, name="woven", tag="woven", bufs=4, align_bytes=ALIGN)
                at = (k - pair(k)) * PANEL // 2
                nc.scalar.copy(
                    out=woven[pair(k)][:, at : at + PANEL // 2, :].rearrange("p (n i) t -> p n t i", i=RUN // 2),
                    in_=w_raw[k].bitcast(F32).rearrange("p t (n i) -> p n t i", i=RUN // 2),
                )

        def empty(k, u, free=cell_free):
            c = k // GROUPS
            b, bank = banks[(k, u)]
            cols = slice(u * P, (u + 1) * P)
            at = (k - pair(k)) * PANEL
            if weaves(k):
                if pair(k) not in gained:
                    gained[pair(k)] = work.tile([P, 2, 2 * PANEL, 2], F32, name="gained", tag="gained", bufs=4)
                nc.vector.tensor_tensor(
                    out=gained[pair(k)][:, u, at : at + PANEL, :],
                    in0=bank[:].rearrange("p e o -> p o e"),
                    in1=gain_all[:, c * PANEL : (c + 1) * PANEL].unsqueeze(2).to_broadcast([P, PANEL, 2]),
                    op=MULT,
                )
            elif kind(k) == "P":
                if pair(k) not in gained:
                    gained[pair(k)] = work.tile([P, 2 * PANEL // RUN, SLOTS, RUN], F32, name="gained", tag="gained", bufs=4)
                nc.vector.tensor_tensor(
                    out=gained[pair(k)][:, at // RUN : (at + PANEL) // RUN, 2 * u : 2 * u + 2, :],
                    in0=bank[:].rearrange("p e (n i) -> p n e i", i=RUN),
                    in1=gain_all[:, c * PANEL : (c + 1) * PANEL].rearrange("p (n i) -> p n i", i=RUN).unsqueeze(2).to_broadcast([P, PANEL // RUN, 2, RUN]),
                    op=MULT,
                )
            elif kind(k)[u] == "S":
                nc.scalar.copy(out=wm_of(k)[:, cols, :], in_=bank[:].rearrange("p t o -> p o t"))
            else:
                nc.vector.tensor_tensor(
                    out=wm_of(k)[:, cols, :].rearrange("p (n i) t -> p n t i", i=RUN),
                    in0=bank[:].rearrange("p t (n i) -> p n t i", i=RUN),
                    in1=w_raw[k][:, :, cols].rearrange("p t (n i) -> p n t i", i=RUN),
                    op=ADD,
                )
            free.append(b)

        def add_plain(engine, k, lo, hi):
            at = (k - pair(k)) * PANEL
            if weaves(k) and lo < hi:
                engine.tensor_tensor(
                    out=wm_pair(k)[:, at + lo : at + hi, :].rearrange("p (m f) (h e) -> p m f h e", f=2, h=2),
                    in0=gained[pair(k)][:, :, at + lo : at + hi, :].rearrange("p h (m f) e -> p m f h e", f=2),
                    in1=woven[pair(k)][:].bitcast(BF16)[:, (at + lo) // 2 : (at + hi) // 2, :].rearrange("p m (h e f) -> p m f h e", h=2, f=2),
                    op=ADD,
                )
            elif kind(k) == "P" and lo < hi:
                engine.tensor_tensor(
                    out=wm_of(k)[:, lo:hi, :].rearrange("p (n i) t -> p n t i", i=RUN),
                    in0=gained[pair(k)][:, (at + lo) // RUN : (at + hi) // RUN, :, :],
                    in1=w_raw[k][:, :, lo:hi].rearrange("p t (n i) -> p n t i", i=RUN),
                    op=ADD,
                )

        quantised = []

        def wm_quantise(k, cells=1):
            quantise(w_cod, w_pla, k * PANEL, wm_of(k) if cells == 1 else wm_pair(k))
            quantised.extend(range(k, k + cells))

        def group_order(c):
            return (2, 3, 0, 1) if c == 0 else (0, 1, 2, 3)

        todo = []
        for c in range(PANELS - 1):
            todo.extend([(GROUPS * c + g, 2 * j + i) for j in range(T_TILES // 2) for g in group_order(c) for i in range(2)])
        by_group = [(CELLS - GROUPS + g, m) for g in range(GROUPS) for m in range(T_TILES)]
        todo.extend(sorted(by_group[:AHEAD], key=lambda p: (p[1] // (T_TILES // 2), p[0], p[1])))
        todo.extend(sorted(by_group[AHEAD:], key=lambda p: (p[1], p[0])))
        y_banks, closed, closed_at = {}, [], {}

        def y_pass():
            if not todo or todo[0][0] not in quantised:
                return
            k, m = todo[0]
            c, g = divmod(k, GROUPS)
            tiles = 1 if c == PANELS - 1 else 2
            at = m - m % tiles
            first = g == group_order(c)[0] and m == at
            last = g == group_order(c)[-1] and m == at + tiles - 1
            if first:
                if not ring_free:
                    return
                y_banks[(c, at)] = take(ring_free, [P, tiles, PANEL])
            todo.remove((k, m))
            cols = slice(k * PANEL, (k + 1) * PANEL)
            mx_pass(
                y_banks[(c, at)][1][:, m - at, :],
                x_cod[m // 4][:, g, m % 4 * 2 * P : (m % 4 + 1) * 2 * P].bitcast(E2M1X4),
                x_pla[:, g, m * P : (m + 1) * P],
                w_cod[:, cols].bitcast(E4M3X4),
                w_pla[:, cols],
                start=first,
                stop=last,
            )
            if last:
                closed.append((c, at, tiles))
                closed_at[(c, at, tiles)] = len(todo)

        def y_store(copy):
            c, at, tiles = closed[0]
            closed.remove((c, at, tiles))
            res = work.tile([P, tiles, PANEL], F32, name="res", tag="res", bufs=RES_BUFS)
            copy(out=res[:], in_=y_banks[(c, at)][1][:])
            ring_free.append(y_banks[(c, at)][0])
            nc.sync.dma_start(out=out_view[:, at : at + tiles, c * PANEL : (c + 1) * PANEL], in_=res[:])

        def y_passes(count, store=True):
            for i in range(count):
                if store:
                    for tile in list(closed):
                        if closed_at[tile] - len(todo) >= LAG or not ring_free:
                            y_store(nc.scalar.copy)
                y_pass()

        def spread_gain(half):
            b, bank = take(cell_free, [P, 2 * SPAN], BF16)
            for i in range(2):
                j = 2 * half + i
                nc.tensor.matmul(
                    bank[:, i * GAIN_ROW : (i + 1) * GAIN_ROW], lhsT=ident_bf[:, j : j + 1].to_broadcast([P, P]), rhs=gain_rows[:], start=True, stop=True
                )
            if half == 0:
                for i in range(GAIN_ROW // P):
                    at = OUT // 2 + i * GAIN_ROWS
                    nc.tensor.matmul(bank[:, at : at + GAIN_ROWS], lhsT=gain_rows[:, i * P : (i + 1) * P], rhs=ident_bf[:, 0:GAIN_ROWS], start=True, stop=True)
            return b, bank, half

        def take_out_gain(b, bank, half):
            nc.scalar.copy(out=gain_all[:, half * OUT // 2 : (half + 1) * OUT // 2], in_=bank[:, 0 : OUT // 2])
            if half == 0:
                nc.scalar.copy(out=gain_col[:].rearrange("p i j -> p (i j)"), in_=bank[:, OUT // 2 : OUT // 2 + OUT // P])
            cell_free.append(b)

        def both(step, k, *more):
            for u in range(2):
                step(k, u, *more)

        nc.scalar.activation(out=ident[:], in_=ident_bf[:], func=COPY)
        warm = keep.tile([P, SPAN], BF16, name="warm")
        nc.vector.memset(warm[:], 0.0)
        warm_b, warm_bank = take(cell_free, [P, SPAN])

        def warm_up(count):
            for i in range(count):
                nc.tensor.matmul(warm_bank[:], lhsT=warm[:, 0:P], rhs=warm[:], start=True, stop=True)

        warm_up(WARM_A)
        spread = [spread_gain(0)]
        ad_turn(0, [0])
        ad_turn(0, [1])
        warm_up(WARM_B)
        cell_free.append(warm_b)
        for t in range(SLOTS):
            b_widen(0, t, nc.vector)
        for i in range(SLOTS):
            b_step(1, i)
        take_out_gain(*spread[0])
        b_step(1, 4)
        b_step(1, 5)
        b_interleave(0, 0, PANEL, nc.vector.tensor_copy)
        both(ad_product, 0)
        ad_turn(1)
        spread.append(spread_gain(1))
        b_quantise(0)
        ad_quantise(0)
        for i in range(SLOTS):
            b_step(2, i)
        take_out_gain(*spread[1])
        b_step(2, 4)
        b_step(2, 5)
        both(fill, 0)
        both(ad_product, 1)
        ad_turn(2)
        b_quantise(1)
        ad_quantise(1)
        both(fill, 1)
        ad_turn(3)
        both(ad_product, 2)
        b_quantise(2)
        ad_quantise(2)
        weave(4)
        both(lay, 0)
        both(fill, 2)
        both(turn, 0)
        both(ad_product, 3)
        both(fill, 4)
        empty(2, 0)
        ad_quantise(3)
        empty(2, 1)
        add_plain(nc.gpsimd, 2, 0, G_ONE)
        both(empty, 0)
        fill(3, 0)
        lay(1, 0)
        fill(3, 1)
        both(fill, 5)
        weave(5)
        lay(1, 1)
        for u in range(2):
            turn(3, u)
            turn(1, u)
        both(empty, 4)
        late = []
        both(empty, 1, late)
        both(fill, 7)
        empty(5, 0, ring_free)
        empty(5, 1)
        empty(3, 0)
        both(fill, 6)
        cell_free.extend(late)
        empty(3, 1)
        add_plain(nc.vector, 2, G_ONE, PANEL)
        for k, u in [(8, 0), (8, 1), (9, 0)][: LENT + 1]:
            fill(k, u)
        wm_quantise(2, 2)
        y_passes(HEAD_PASSES, False)
        turn_back(7)
        wm_quantise(0, 2)

        def banks_of(*cells):
            return [(k, u) for k in cells if k < CELLS for u in range(2)]

        def own(c):
            k = GROUPS * c + 2
            return (k + 1, k) if kind(k + 1) != "P" else (k, k + 1)

        unfilled = [x for x in banks_of(8, 9) if x not in banks]
        for c in range(2, PANELS):
            unfilled.extend(banks_of(*own(c), GROUPS * c + 4, GROUPS * c + 5))
        due = {}
        lent = banks_of(6)[:LENT]
        clock = [0]

        def fill_all():
            while_free = list(cell_free)
            for b in while_free:
                if unfilled and unfilled[0][0] // GROUPS in b_done:
                    k, u = unfilled[0]
                    unfilled.remove((k, u))
                    fill(k, u)
                    if u == 1 and kind(k) != "P":
                        due[k] = clock[0] + TURN_AFTER

        def turn_due(force=False):
            for k in sorted(due):
                if force or due[k] <= clock[0]:
                    turn_back(k)
            for k in [k for k in due if force or due[k] <= clock[0]]:
                due.pop(k)

        def run(leaving, after, force=True):
            fill_all()
            for i, (k, u) in enumerate(leaving):
                if k in due:
                    turn_due(True)
                empty(k, u, cell_free if unfilled and (k, u) not in lent else ring_free)
                clock[0] = clock[0] + 1
                if u == FILL_AT:
                    fill_all()
                turn_due()
                for step in after.get(i, []):
                    step()
                y_passes(PASSES)
            turn_due(force)

        def order(c):
            k = GROUPS * c
            plain = [j for j in (k + 2, k + 3) if kind(j) == "P"]
            turned = [j for j in own(c) if kind(j) != "P"]
            return plain + turned + [k + 4, k + 5]

        for c in range(1, PANELS - 1):
            k = GROUPS * c
            cols = G_FIRST if c == 1 else G_COLS
            add_plain(nc.gpsimd, k, 0, cols)
            y_passes(PASSES_OPEN, False)
            for i in range(6):
                b_step(c + 2, i)
            later = {2: [lambda: weave(k + 2)], 3: [lambda: weave(k + 3)], 4: [lambda: weave(k + 4)], 5: [lambda: weave(k + 5)]}
            run(banks_of(*order(c)), later)
            y_passes(PASSES_PLAIN if kind(k + 3) == "P" else PASSES_TURNED)
            add_plain(nc.vector, k, cols, 2 * PANEL)
            add_plain(nc.vector, k + 2, 0, PANEL)
            add_plain(nc.vector, k + 3, 0, PANEL)
            if c + 2 < PANELS:
                b_quantise(c + 2)
            wm_quantise(k, 2)
            wm_quantise(k + 2, 2)

        k = CELLS - GROUPS
        add_plain(nc.gpsimd, k, 0, G_LAST)
        weave(k + 2)
        weave(k + 3)
        ring_free.extend(cell_free)
        cell_free.clear()
        run(banks_of(*order(PANELS - 1)), {})
        add_plain(nc.vector, k, G_LAST, PANEL)
        for g in range(1, GROUPS):
            add_plain(nc.vector, k + g, 0, PANEL)
            y_passes(len(todo))
            wm_quantise(k + g - 1)
        y_passes(len(todo))
        wm_quantise(k + 3)
        for i in range(len(todo)):
            y_pass()
            for c, at, tiles in list(closed):
                y_store(nc.scalar.copy if at % 2 == 0 else nc.vector.tensor_copy)
        assert not todo and not closed
